import numpy as np, ml_dtypes
CORES = [24,25,26,27,28,29,30,31]
N = 8
BF = ml_dtypes.bfloat16
S, U, CH, CP, MS, Q, D, T, SH = 192, 64, 2048, 4096, 8, 16, 3, 4, 5
MX = 16 * MS
def base(rng):
    top = rng.choice(np.array([4, 8, 16, 16]), (N, 8, 1, S)); v = (rng.random((N, 8, 16 + T, S)) * top).astype(np.int64)
    return {"hist": rng.integers(0, 16, (N, 8, 16, CH)), "score": 4 * rng.random((N, 8, 16, CP)) - 2, "weight": (0.0625 + 0.9375 * rng.random((N, 8, 16, 16 * MX))) * (2 * rng.integers(0, 2, (N, 8, 16, 16 * MX)) - 1),
            "past": np.array(v[:, :, :16]), "coming": np.array(v[:, :, 16:]), "kap": rng.integers(0, 65536, (N, 8, 16)), "lam": rng.integers(0, 65536, (N, 8, 16))}
def pack(d):
    out = {k: np.ascontiguousarray(d[k].reshape(N, 128, -1)).astype(np.float32).astype(BF) for k in ("hist", "score", "weight", "past")}
    out["coming"] = np.ascontiguousarray(d["coming"].reshape(N, 8, T * S)).astype(np.float32).astype(BF)
    for k in ("kap", "lam"): out[k] = np.ascontiguousarray(d[k].reshape(N, 128, 1)).astype(np.int32)
    return out
def setup_inputs(rng):
    return pack(base(rng))
def setup_inputs_spread(rng):
    d = base(rng)
    for k, n in (("score", CP), ("weight", 16 * MX)):
        d[k] = d[k] * np.exp2(-rng.integers(0, 3, (N, 8, 1, n)).astype(np.float64))
    for k in ("kap", "lam"): d[k] = np.minimum(np.exp2(4 + 12 * rng.random((N, 8, 16))).astype(np.int64), 65535)
    d["hist"] = np.minimum((np.exp2(4 * rng.random((N, 8, 1, CH))) * rng.random((N, 8, 16, CH))).astype(np.int64), 15)
    return pack(d)
def setup_inputs_ends(rng):
    d = base(rng)
    c = rng.integers(0, 3, (N, 8, 1, CH)); d["hist"] = 15 * np.where(c == 2, rng.integers(0, 2, (N, 8, 16, CH)), c)
    c = rng.integers(0, 6, (N, 8, 1, S)); v = 15 * np.where(c >= 2, rng.integers(0, 2, (N, 8, 16 + T, S)), c)
    d["past"] = np.array(v[:, :, :16]); d["coming"] = np.array(v[:, :, 16:])
    d["kap"] = 65535 * rng.integers(0, 2, (N, 8, 16)); d["lam"] = 65535 * rng.integers(0, 2, (N, 8, 16))
    d["score"] = 4.0 * rng.integers(0, 2, (N, 8, 16, CP)) - 2; d["weight"] = 2.0 * rng.integers(0, 2, (N, 8, 16, 16 * MX)) - 1
    z = N - 1; d["kap"][z, 7] = 65535; d["lam"][z, 7] = 65535
    for u in (0, 1, U - 1, U, U + 1, S - 2, S - 1): d["past"][:, 6:8, :, u] = 15; d["coming"][:, 6:8, :, u] = 15
    d["hist"][z, 7, :, CH - 17:] = 15; d["hist"][z, 7, :, 0] = 0
    cols = (37 * 3600 + 3681 * np.arange(16)) & (CP - 1)
    d["score"][z, 7][:8][:, cols] = 2.0; d["score"][z, 7][8:][:, cols] = -2.0; d["weight"][z, 7, :, 16 * MX - 16:] = 1.0
    return pack(d)
def setup_inputs_corners(rng):
    d = base(rng); h, p, n, ka, la = d["hist"], d["past"], d["coming"], d["kap"], d["lam"]
    ka[:, 0] = 0; la[:, 0] = 0; p[:, 0] = np.maximum(p[:, 0], 1); n[:, 0] = np.maximum(n[:, 0], 1)
    ka[:, 1] = 0; la[:, 1] = 64 * np.arange(16); p[:, 1] |= 1; n[:, 1] |= 1; h[:, 1] = 0; h[:, 1, 0, 1:] = 1
    h[:, 2] = 0; n[:, 2] = 15
    h[:, 3] = 15; p[:, 3] = 15; n[:, 3] = 15; ka[:, 3] = 65535; la[:, 3] = 65535
    ka[:, 4, 1:] = 0; la[:, 4] = 0
    ka[:, 5, :15] = 0; la[:, 5] = 0
    p[:, 6] = 0; n[:, 6] = 0
    few = np.array([0, 1, 15, 16, 65535]); ka[:, 7] = rng.choice(few, (N, 16)); la[:, 7] = rng.choice(few, (N, 16)); p[:, 7] = rng.choice(np.array([0, 1, 14, 15]), (N, 16, S))
    ka[1] = rng.integers(0, 65536, (8, 16)); la[1] = rng.integers(0, 65536, (8, 16))
    return pack(d)
def setup_inputs_crowd(rng):
    d = base(rng); kind = rng.integers(0, 4, S)
    for k in ("past", "coming"):
        a = d[k]; old = np.array(a)
        for g in range(6): a[:, g] = old[:1, g, :, :1]
        for q in range(N):
            for s in range(S // U):
                u = U * s + (0 if q % 2 == 0 else U - 1)
                a[q, 4:6, :, u] = (old[q, 4:6, :, u] + 1 + a[q, 4:6, :, u]) & 15
        a[:, 6] = old[:, 6][:, :, kind]
    d["coming"][:, 6] = np.maximum(d["coming"][:, 6], 1)
    pr = np.array([17, 19, 23, 29, 31, 37, 41, 43, 47, 53, 59, 61, 67, 71, 73, 79]); d["kap"][:, 7] = 0; d["lam"][:, 7] = pr << SH
    low = Q * rng.integers(0, 16 // Q, (N, 16, 16, 15)) + np.eye(16, dtype=np.int64)[None, :, :, None]
    d["hist"][:, 7][:, :, pr[:, None] * np.arange(1, 16)[None, :]] = low
    want = np.stack([np.concatenate([rng.permutation(max(U, MX))[:U] & (MX - 1) for s in range(S // U)]) for q in range(N)])
    m = (want // MS)[:, None, :]; v = (want % MS + MS * rng.integers(0, 16 // MS, (N, S)))[:, None, :]; o = np.arange(16)[None, :, None]
    d["past"][:, 7] = np.where(o > m, v + rng.integers(1, Q, (N, 16, S)), np.where((o == m) | (o == 0), v, rng.integers(0, 16, (N, 16, S)))) & 15
    return pack(d)
def setup_inputs_calm(rng):
    d = base(rng); val = ((np.arange(N)[:, None] + np.arange(8)[None, :]) & 3)[:, :, None, None]
    v = np.where(rng.random((N, 8, 16 + T, S)) < 0.6, val, rng.integers(0, 4, (N, 8, 16 + T, S)))
    v[:, :, 2:16] *= rng.integers(0, 2, (N, 8, 1, S))
    d["past"] = np.array(v[:, :, :16]); d["coming"] = np.array(v[:, :, 16:]); d["hist"] = rng.integers(0, 4, (N, 8, 16, CH))
    return pack(d)
def check_ranges(d):
    bad = []
    for k, lo, hi in (("hist", 0, 15), ("past", 0, 15), ("coming", 0, 15), ("kap", 0, 65535), ("lam", 0, 65535), ("score", -2, 2), ("weight", -1, 1)):
        v = np.asarray(d[k]).astype(np.float64)
        if not (np.min(v) >= lo and np.max(v) <= hi): bad.append("range of " + k)
        elif k == "weight" and np.min(np.abs(v)) < 0.015625: bad.append("least size of " + k)
        elif k not in ("score", "weight") and np.any(v != np.floor(v)): bad.append("whole numbers in " + k)
    return bad
def reference(hist, score, weight, past, coming, kap, lam):
    H = hist.astype(np.float32).astype(np.int64).reshape(N, 8, 16, CH); P = score.astype(np.float64).reshape(N, 8, 16, CP); W = weight.astype(np.float64).reshape(N, 8, 16, 16 * MX)
    X = past.astype(np.float32).astype(np.int64).reshape(N, 8, 16, S); C = coming.astype(np.float32).astype(np.int64).reshape(N, 8, T, S)
    K = kap.astype(np.int64).reshape(N, 8, 16, 1); L = lam.astype(np.int64).reshape(N, 8, 16, 1)
    B = np.zeros((N, 8, 16, S)); kk = np.arange(16).reshape(1, 1, 16, 1)
    for t in range(T):
        home = np.array([(q - D * t) % N for q in range(N)])
        x = X[home]; s = C[home, :, t]; b = B[home]
        sig = np.add.accumulate(K * x, axis=2) + L * np.roll(s, 1, axis=1)[:, :, None, :]
        c = (sig >> SH) & (CH - 1)
        hp = np.take_along_axis(H, c.reshape(N, 8, 1, 16 * S), 3).reshape(N, 8, 16, 16, S)
        z = np.add.reduce(hp * x[:, :, :, None, :], axis=2)
        a = (37 * z + 3681 * kk) & (CP - 1)
        m = np.max(np.where((z & (Q - 1)) == (z[:, :, :1] & (Q - 1)), kk, 0), axis=2)
        e = MS * m + (x[:, :, 0] & (MS - 1))
        p = np.take_along_axis(P, a.reshape(N, 8, 1, 16 * S), 3).reshape(N, 8, 16, 16, S)
        w = np.take_along_axis(W, (16 * e[:, :, None, :] + kk).reshape(N, 8, 1, 16 * S), 3).reshape(N, 8, 16, 16, S)
        logit = np.add.reduce(w * p, axis=3) + np.roll(b, 1, axis=1)
        y = np.reciprocal(1.0 + np.exp(-logit))
        err = (kk == s[:, :, None, :]) - y
        B[home] = 0.5 * b + err
        cm = np.take_along_axis(c, m[:, :, None, :], 2)[:, :, 0]; lo = U * (t % (S // U))
        for q in range(N):
            for g in range(8):
                u = lo + np.unique(e[q, g, lo:lo + U], return_index=True)[1]
                cols = (16 * e[q, g, u][None, :] + np.arange(16)[:, None]).reshape(-1)
                W[q, g][:, cols] += (0.03125 * err[q, g][:, None, u] * p[q, g][:, :, u]).reshape(16, -1)
                if t < T - 1:
                    u = lo + np.unique(cm[q, g, lo:lo + U], return_index=True)[1]
                    col = cm[q, g, u]; old = H[q, g][:, col]
                    H[q, g][:, col] = np.concatenate([s[q, g, u][None, :], old[:15]], axis=0)
        X = np.concatenate([C[:, :, t][:, :, None, :], X[:, :, :15]], axis=2)
    return {"yw": W.reshape(N, 128, 16 * MX).astype(np.float32), "yb": B.reshape(N, 128, S).astype(np.float32)}

def check_inputs(d):
    bad = list(check_ranges(d))
    if not bad:
        for name, y in reference(**d).items():
            for q in range(N):
                v = np.abs(np.asarray(y[q], np.float64)); s = np.sqrt(np.mean(v * v))
                if v.max() > 4 * s or s < 2.0 ** -3: bad.append('%s of rank %d is uneven or too small' % (name, q))
    return bad

@@ -1,0 +1,726 @@
+import numpy as np
+from concourse.bass import DstId, RemoteDMATransfer
+from concourse.mybir import AluOpType, ActivationFunctionType
+
+S, U, CH, CP, STEPS, HOP, NR = 192, 64, 2048, 4096, 4, 3, 8
+SEG = 66
+BIG = 1.0e6
+
+SCRATCH = {
+    "snd": ("sbuf", [128, 240], "bfloat16"),
+    "lnd": ("sbuf", [128, 3 * 240], "bfloat16"),
+    "com": ("sbuf", [128, 4 * 768], "bfloat16"),
+    "kl": ("sbuf", [128, 8], "int32"),
+    "kli": ("sbuf", [128, 4], "int32"),
+    "klf": ("sbuf", [128, 4], "float32"),
+    "Hs": ("sbuf", [128, 64 + CH], "bfloat16"),
+    "Ps": ("sbuf", [128, CP], "bfloat16"),
+    "W0": ("sbuf", [128, 2048], "bfloat16"),
+    "Wt": ("sbuf", [128, 2048 + 4096], "float32"),
+    "ptr": ("sbuf", [128, 64 + 128], "float32"),
+    "pval": ("sbuf", [128, 256], "float32"),
+    "Dm": ("sbuf", [128, 144], "bfloat16"),
+    "Pm": ("sbuf", [128, 128], "bfloat16"),
+    "Em": ("sbuf", [128, 144], "bfloat16"),
+    "Gi": ("sbuf", [128, 128], "bfloat16"),
+    "Rw": ("sbuf", [128, 64], "float32"),
+    "pi": ("sbuf", [128, 2], "int32"),
+    "col": ("sbuf", [128, 16], "float32"),
+    "mn": ("sbuf", [128, 128], "bfloat16"),
+    "KL": ("sbuf", [128, 4 * 128], "bfloat16"),
+    "Sh": ("sbuf", [128, 4 * 128], "bfloat16"),
+    "Zw": ("sbuf", [128, 144], "bfloat16"),
+    "Sr": ("sbuf", [128, 2 * 128], "bfloat16"),
+    "Y37": ("sbuf", [128, 144], "bfloat16"),
+    "Y1": ("sbuf", [128, 144], "float16"),
+    "B37": ("sbuf", [128, 128], "bfloat16"),
+    "B1": ("sbuf", [128, 128], "float16"),
+    "ut": ("sbuf", [128, 3 * 128], "bfloat16"),
+    "Um": ("sbuf", [128, 2 * 128], "bfloat16"),
+    "S0": ("sbuf", [128, 2 * 128], "bfloat16"),
+    "Mk": ("sbuf", [128, 64], "bfloat16"),
+    "F32": ("sbuf", [128, 3 * 128], "float32"),
+    "Cs": ("sbuf", [128, 8 * SEG], "float32"),
+    "tb": ("sbuf", [128, 8 * SEG], "float32"),
+    "so": ("sbuf", [128, 8 * SEG], "float32"),
+    "xs": ("sbuf", [128, 2 * 384], "bfloat16"),
+    "ge": ("sbuf", [128, 2 * 192], "bfloat16"),
+    "oh": ("sbuf", [128, 4 * 192], "bfloat16"),
+    "oa": ("sbuf", [128, 192], "bfloat16"),
+    "ci": ("sbuf", [128, 192], "int32"),
+    "cj": ("sbuf", [128, 2 * 192], "int32"),
+    "coff": ("sbuf", [128, 2 * 192], "uint16"),
+    "hp": ("sbuf", [128, 2 * 3072], "bfloat16"),
+    "ph": ("sbuf", [128, 3072], "bfloat16"),
+    "ai": ("sbuf", [128, 192], "int32"),
+    "am": ("sbuf", [128, 192], "int32"),
+    "di": ("sbuf", [128, 192], "int32"),
+    "dj": ("sbuf", [128, 192], "int32"),
+    "aoff": ("sbuf", [128, 2 * 192], "uint16"),
+    "eq": ("sbuf", [128, 192], "bfloat16"),
+    "tmp": ("sbuf", [128, 64], "float32"),
+    "src": ("sbuf", [128, 256], "float16"),
+    "vdb": ("sbuf", [128, 8], "float32"),
+    "doff": ("sbuf", [128, 16], "uint16"),
+    "soff": ("sbuf", [128, 8], "uint16"),
+    "woff": ("sbuf", [128, 2 * 192], "uint16"),
+    "foff": ("sbuf", [128, 128], "uint16"),
+    "hold": ("sbuf", [128, 64], "bfloat16"),
+    "hnew": ("sbuf", [128, 64], "bfloat16"),
+    "pg": ("sbuf", [128, 2 * 3072], "bfloat16"),
+    "wg": ("sbuf", [128, 1024], "float32"),
+    "pw": ("sbuf", [128, 2 * 3072], "float32"),
+    "ys": ("sbuf", [128, 192], "float32"),
+    "Bo": ("sbuf", [128, 4 * 192], "float32"),
+    "Bi": ("sbuf", [128, 4 * 192], "float32"),
+    "wo": ("sbuf", [128, 2048], "float32"),
+    "p0": ("psum", [128, 512], "float32"),
+    "p1": ("psum", [128, 512], "float32"),
+    "p3": ("psum", [128, 512], "float32"),
+    "p4": ("psum", [128, 512], "float32"),
+    "p5": ("psum", [128, 512], "float32"),
+    "p7": ("psum", [128, 512], "float32"),
+    "pd": ("psum", [128, 1024], "float32"),
+}
+NDMA = 40
+SEMAPHORES = ["e_pe", "e_v", "e_s", "e_g", "loc"] + ["d%d" % i for i in range(NDMA)]
+
+CFG = {
+    "ich": [[(0, 64), (64, 128), (128, 192)], [(0, 64), (64, 192)], [(0, 64), (64, 192)], [(0, 64), (64, 192)]],
+    "hg_v": {(0, 64)},
+    "pg_v": {(0, 64)},
+    "rch": [[(0, 64), (64, 128), (128, 192)]] * 4,
+    "a_late": {0},
+    "oh_s": set(),
+    "fin": [("v", 0, 32), ("s", 32, 64), ("v", 64, 96), ("s", 96, 128)],
+    "G": 1.5, "SC": 3.8, "CY": 1.0, "OV": 50.0, "PE": 0.42, "WK": 120.0, "look": 100.0,
+    "OV2": 0.0, "DF": 2000.0, "BW": 200.0, "RF": 2500.0, "rounds": 2500, "bias": {},
+}
+VARIANTS = [{}, {"G": 1.15, "SC": 2.5, "CY": 1.3, "BW": 300.0}, {"G": 1.95, "SC": 5.0, "CY": 1.1, "WK": 200.0},
+            {"CY": 1.25, "OV2": 30.0, "BW": 150.0, "RF": 3500.0}]
+ALU = AluOpType
+ACT = ActivationFunctionType
+
+
+def A(name, c0, c1, step=1, p0=0, p1=128):
+    n = (c1 - c0 + step - 1) // step
+    return {"b": name, "c0": c0, "c1": c0 + (n - 1) * step + 1, "st": step, "p0": p0, "p1": p1, "n": n}
+
+
+def IND(win, off):
+    return {"b": win["b"], "win": win, "off": off, "n": 16 * off["n"]}
+
+
+def real(T, a):
+    if "win" in a:
+        return real(T, a["win"]).indirect(real(T, a["off"]))
+    if "ext" in a:
+        return T[a["b"]][:, a["c0"]:a["c1"]] if a["ext"] == "cols" else T[a["b"]][:]
+    if a["st"] == 1:
+        return T[a["b"]][a["p0"]:a["p1"], a["c0"]:a["c1"]]
+    return T[a["b"]][a["p0"]:a["p1"], a["c0"]:a["c1"]:a["st"]]
+
+
+def EXT(name, c0=None, c1=None):
+    return {"b": name, "ext": "all" if c0 is None else "cols", "c0": c0, "c1": c1}
+
+
+def in_psum(a):
+    return SCRATCH[a["b"]][0] == "psum"
+
+
+def width(a):
+    return 2 if SCRATCH[a["b"]][2] in ("bfloat16", "float16", "uint16") else 4
+
+
+def build(cfg):
+    ops = []
+    hist = {}
+    bank = {}
+    ndma = [0]
+    ph = [0]
+
+    def flat(aps):
+        out = []
+        for a in aps:
+            if not isinstance(a, dict) or "ext" in a:
+                continue
+            if "win" in a:
+                out.append(a["win"])
+                out.append(a["off"])
+            else:
+                out.append(a)
+        return out
+
+    def add(eng, call, reads, writes, dur, kind="c", after=(), nbytes=0):
+        i = len(ops)
+        o = {"i": i, "eng": eng, "call": call, "dur": dur, "kind": kind, "sem": set(after), "ord": set(), "bytes": nbytes, "key": (call[1]["b"], ph[0])}
+        rd = flat(reads)
+        wr = []
+        for a in writes:
+            if "ext" in a:
+                continue
+            if "win" in a:
+                wr.append(a["win"])
+                rd.append(a["off"])
+            else:
+                wr.append(a)
+
+        def dep(j, raw):
+            if j == i:
+                return
+            p = ops[j]
+            if eng == "pe" and p["eng"] == "pe" and call[1] is p["call"][1]:
+                o["ord"].add(j)
+            else:
+                o["sem"].add(j)
+
+        def meet(a, lo, hi, st):
+            if not (lo < a["c1"] and a["c0"] < hi):
+                return False
+            return st == 1 or st != a["st"] or (lo - a["c0"]) % st == 0
+        for a in rd:
+            for (j, w, lo, hi, st) in hist.get(a["b"], []):
+                if w and meet(a, lo, hi, st):
+                    dep(j, True)
+        for a in wr:
+            for (j, w, lo, hi, st) in hist.get(a["b"], []):
+                if meet(a, lo, hi, st):
+                    dep(j, False)
+        for a in wr:
+            h = hist.setdefault(a["b"], [])
+            if a["p0"] == 0 and a["p1"] == 128:
+                h[:] = [e for e in h if e[0] == i or not (a["c0"] <= e[2] and e[3] <= a["c1"] and (a["st"] == 1 or (e[4] == a["st"] and meet(a, e[2], e[3], e[4]))))]
+            h.append((i, True, a["c0"], a["c1"], a["st"]))
+        for a in rd:
+            hist.setdefault(a["b"], []).append((i, False, a["c0"], a["c1"], a["st"]))
+        for name in sorted({a["b"] for a in rd + wr if in_psum(a)}):
+            st = bank.setdefault(name, {"eng": None, "cur": [], "prev": []})
+            if st["eng"] != eng:
+                st["prev"] = st["cur"]
+                st["cur"] = []
+                st["eng"] = eng
+            elif eng == "pe" and st["cur"]:
+                o["ord"].add(st["cur"][-1])
+            for j in st["prev"]:
+                o["sem"].add(j)
+            st["cur"].append(i)
+        o["ord"] -= o["sem"]
+        if kind != "c":
+            o["tok"] = "d%d" % ndma[0]
+            ndma[0] += 1
+        ops.append(o)
+        return i
+
+    cy, ov = 0.83 * cfg["CY"], cfg["OV"]
+
+    def vcost(out, ins, two=False):
+        n = out["n"]
+        if "win" in out:
+            return ov + n * cfg["SC"] * cy
+        if any("win" in a for a in ins):
+            return ov + n * cfg["G"] * cy
+        if two:
+            f = 1.0 if any(in_psum(a) for a in ins) else 2.0
+        else:
+            f = 0.5 if all(width(a) == 2 for a in [out] + ins) else 1.0
+        return cfg["OV2"] + max(n * f, 64) * cy
+
+    def cp(out, a):
+        return add("v", ("tensor_copy", out, a), [a], [out], vcost(out, [a]))
+
+    def ts(out, a, s1, s2, o0, o1=None):
+        c = ("tensor_scalar", out, a, s1, s2, o0) + (() if o1 is None else (o1,))
+        return add("v", c, [a, s1, s2], [out], vcost(out, [a]))
+
+    def tt(out, a, b, o):
+        return add("v", ("tensor_tensor", out, a, b, o), [a, b], [out], vcost(out, [a, b], True))
+
+    def mset(out, val):
+        return add("v", ("memset", out, val), [], [out], vcost(out, []))
+
+    def act(out, a, f, bias=None, scale=None):
+        return add("s", ("activation", out, a, f, bias, scale), [a, bias, scale], [out], 15 + vcost(out, [a, A("tb", 0, 1)]))
+
+    def mm(out, pairs):
+        for n, (l, r) in enumerate(pairs):
+            f = 4 if SCRATCH[r["b"]][2] == "float32" else 1
+            add("pe", ("matmul", out, l, r, n == 0, n == len(pairs) - 1), [l, r], [out], max(64, r["n"]) * f * cfg["PE"] * cfg["CY"])
+
+    def iota(out, pat, base, cm):
+        return add("g", ("iota", out, pat, base, cm), [], [out], 130 + 2 * out["n"] * cy)
+
+    def dma(q, out, a, nbytes, after=(), behind=()):
+        i = add(q, ("dma_start", out, a), [a], [out], 100.0 if q != "g" else 1000.0, "dma", after, nbytes)
+        ops[i]["ord"] |= set(behind)
+        return i
+
+    def rem(srcap, dsts, nbytes):
+        return add("g", ("remote", srcap, dsts), [srcap], [d[0] for d in dsts], 500.0, "rem", (), nbytes)
+
+    def gather(eng, out, win, off, scale=None):
+        if eng == "s":
+            return act(out, IND(win, off), ACT.Copy if scale is None else ACT.Identity, None, scale)
+        if scale is None:
+            return cp(out, IND(win, off))
+        return ts(out, IND(win, off), scale, None, ALU.mult)
+
+    l_past = dma("sync", A("snd", 0, 192), EXT("past"), 49152)
+    dma("s", A("com", 0, 768, 1, 0, 8), EXT("coming"), 12288)
+    l_kap = dma("sync", A("kl", 0, 1), EXT("kap"), 8192, (), (l_past,))
+    dma("s", A("kl", 1, 2), EXT("lam"), 8192)
+    l_snd = dma("sync", A("snd", 192, 240), EXT("coming"), 12288, (), (l_kap,))
+    l_hist = dma("sync", A("Hs", 64, 64 + CH), EXT("hist"), 524288, (), (l_snd,))
+    l_score = dma("sync", A("Ps", 0, CP), EXT("score"), 1048576, (), (l_hist,))
+    dma("sync", A("W0", 0, 2048), EXT("weight"), 524288, (l_hist,), (l_score,))
+    iota(A("Dm", 0, 144), [[1, 144]], 0, -1)
+    iota(A("pi", 0, 1), [[1, 1]], 0, 1)
+    iota(A("Gi", 0, 128, 1, 0, 8), [[1, 8], [0, 16]], 0, -1)
+    iota(A("Pm", 0, 128), [[-16, 8], [0, 16]], 0, 1)
+    iota(A("Rw", 0, 64), [[1, 64]], -48, 0)
+    rem(A("snd", 0, 240), [(A("lnd", 240 * (t - 1), 240 * t), HOP * t) for t in (1, 2, 3)], 3 * 61440)
+    iota(A("Em", 0, 144, 1, 0, 8), [[1, 144]], 0, -16)
+    iota(A("ptr", 64, 192), [[16, 128]], 0, 0)
+    iota(A("pval", 0, 256), [[16, 256]], 2048, 0)
+
+    def col(j, p1=128):
+        return A("col", j, j + 1, 1, 0, p1)
+    LANE, PF, C3681, CE, C15, CZ, CZ8, CW, CS0, CS1, SM = 0, 1, 2, 3, 4, 5, 6, 7, 8, 9, 12
+    D128 = A("Dm", 0, 128)
+    ts(A("pi", 1, 2), A("pi", 0, 1), 15, None, ALU.bitwise_and)
+    cp(A("col", PF, PF + 1), A("pi", 0, 1))
+    cp(col(LANE), A("pi", 1, 2))
+    ident = A("Sh", 0, 128)
+    ts(ident, D128, 0.0, None, ALU.is_equal)
+    ts(col(CW, 8), col(PF, 8), 7.0, -8.0, ALU.is_ge, ALU.mult)
+    sprev, srep = A("Sr", 0, 128, 1, 0, 8), A("Sr", 128, 256, 1, 0, 8)
+    ts(sprev, A("Gi", 0, 128, 1, 0, 8), col(CW, 8), 1.0, ALU.subtract, ALU.is_equal)
+    ts(srep, A("Gi", 0, 128, 1, 0, 8), 0.0, None, ALU.is_equal)
+    tt(A("mn", 0, 128), A("Pm", 0, 128), D128, ALU.min)
+    ts(A("kli", 0, 2), A("kl", 0, 2), 0xFF00, None, ALU.bitwise_and)
+    ts(A("kli", 2, 4), A("kl", 0, 2), 0xFF, None, ALU.bitwise_and)
+    cp(A("klf", 0, 4), A("kli", 0, 4))
+    for j in (0, 2):
+        ts(A("KL", 128 * j, 128 * j + 128), A("mn", 0, 128), 0.0, A("klf", j, j + 1), ALU.is_ge, ALU.mult)
+    for j in (1, 3):
+        ts(A("KL", 128 * j, 128 * j + 128), D128, 0.0, A("klf", j, j + 1), ALU.is_equal, ALU.mult)
+    ts(col(C3681), col(LANE), 3681.0, None, ALU.mult)
+    ts(col(CE), col(LANE), 8.0 / 4096, 1.0 / 4096, ALU.mult, ALU.max)
+    ts(col(C15), col(LANE), -1.0, 15.0, ALU.mult, ALU.add)
+    ts(col(CZ), col(LANE), 0.0, 4096.0, ALU.is_equal, ALU.mult)
+    ts(col(CZ8), col(LANE), 0.0, -32768.0, ALU.is_equal, ALU.mult)
+    ts(col(CS0), col(PF), 112.0, -128.0, ALU.is_ge, ALU.mult)
+    ts(col(CS1), col(CS0), 16.0, None, ALU.add)
+    ts(A("col", SM, SM + 4), A("Rw", 48, 52), col(LANE), 15.0, ALU.add, ALU.is_le)
+    ts(A("Y37", 0, 144), A("Dm", 0, 144), col(C15), 37.0, ALU.is_equal, ALU.mult)
+    ts(A("B37", 0, 128), A("Pm", 0, 128), col(LANE), 37.0, ALU.is_equal, ALU.mult)
+    ts(A("Y1", 0, 144), A("Dm", 0, 144), col(C15), None, ALU.is_equal)
+    ts(A("B1", 0, 128), A("Pm", 0, 128), col(LANE), None, ALU.is_equal)
+    ts(A("ut", 0, 128), A("mn", 0, 128), 0.0, 4096.0, ALU.is_ge, ALU.mult)
+    ts(A("ut", 128, 256), A("Pm", 0, 128), col(LANE), -4096.0, ALU.is_equal, ALU.mult)
+    ts(A("ut", 256, 384), D128, 0.0, 4096.0, ALU.is_equal, ALU.mult)
+    tt(A("ut", 0, 128), A("ut", 0, 128), A("ut", 128, 256), ALU.add)
+    tt(A("Um", 0, 128), A("ut", 0, 128), A("ut", 256, 384), ALU.add)
+    cp(A("Um", 128, 256), A("Um", 0, 128))
+    mset(A("Um", 128, 256, 16), 0.0)
+    ts(A("S0", 0, 128), D128, 0.0, col(CZ), ALU.is_equal, ALU.mult)
+    ts(A("S0", 128, 256), D128, 0.0, col(CZ8), ALU.is_equal, ALU.mult)
+    ts(A("Mk", 0, 64), A("Rw", 0, 64), col(LANE), 4096.0, ALU.is_ge, ALU.mult)
+    negI, halfI, negS = A("F32", 0, 128), A("F32", 128, 256), A("F32", 256, 384)
+    ts(negI, D128, 0.0, -1.0, ALU.is_equal, ALU.mult)
+    ts(halfI, D128, 0.0, 0.5, ALU.is_equal, ALU.mult)
+    ts(negS, D128, col(CS1), -1.0 / 32, ALU.is_equal, ALU.mult)
+    for t in (1, 2, 3):
+        ts(A("Sh", 128 * t, 128 * t + 128), D128, float(t), col(SM + t), ALU.is_equal, ALU.mult)
+    ts(A("Zw", 0, 144, 1, 0, 8), A("Em", 0, 144, 1, 0, 8), 2.0, None, ALU.is_equal)
+    mset(A("Cs", 0, 8 * SEG), 0.0)
+    mset(A("Cs", 0, 8 * SEG, SEG), BIG)
+    for k in (0, 1):
+        ts(A("Cs", 4 * SEG * k + SEG - 1, 4 * SEG * (k + 1), SEG), A("Rw", 48, 52), 16.0, col(LANE), ALU.mult, ALU.add)
+    mset(A("tb", 0, 8 * SEG), BIG)
+    for t in (1, 2, 3):
+        l_com = dma("sync", A("com", 768 * t, 768 * t + 768, 1, 0, 8), A("lnd", 240 * (t - 1) + 192, 240 * t), 12288)
+    dma("g", A("Wt", 0, 2048), A("W0", 0, 2048), 1048576, (l_com,))
+
+    def lane_in(i):
+        return A("Zw", 2 - i, 130 - i, 1, 0, 8)
+
+    def comc(t, tt_, u0, n):
+        return A("com", 768 * t + 192 * tt_ + u0, 768 * t + 192 * tt_ + u0 + n, 1, 0, 8)
+
+    def phase_a(t):
+        ph[0] += 1
+        rot, par = U * (t % 3), t % 2
+        pieces = [(0, rot, S - rot)] + ([(S - rot, 0, rot)] if rot else [])
+        pb, pc = ("snd", 0) if t == 0 else ("lnd", 240 * (t - 1))
+        for (p, u, n) in pieces:
+            mm(A("p0", p, p + n), [(A("Sh", 128 * t, 128 * t + 128), A(pb, pc + u, pc + u + n))]
+               + [(lane_in(t - 1 - s), comc(t, s, u, n)) for s in range(t)])
+            mm(A("p0", 192 + p, 192 + p + n), [(sprev, comc(t, t, u, n))])
+        x, sp = A("xs", 384 * par, 384 * par + 192), A("xs", 384 * par + 192, 384 * par + 384)
+        act(A("xs", 384 * par, 384 * par + 384), A("p0", 0, 384), ACT.Copy)
+        act(A("ge", 192 * par, 192 * par + 192), x, ACT.Sigmoid, -1920.0, 256.0)
+        mm(A("p0", 192, 384), [(A("KL", 0, 128), x), (A("KL", 256, 384), x), (A("KL", 128, 256), sp), (A("KL", 384, 512), sp)])
+        for (p, u, n) in pieces:
+            mm(A("p0", p, p + n), [(srep, comc(t, t, u, n))])
+        cp(A("ci", 0, 192), A("p0", 192, 384))
+        if t in cfg["oh_s"]:
+            act(A("oa", 0, 192), A("p0", 0, 192), ACT.Abs, col(LANE), -1.0)
+            act(A("oh", 192 * t, 192 * t + 192), A("oa", 0, 192), ACT.Relu, 1.0, -1.0)
+        else:
+            ts(A("oh", 192 * t, 192 * t + 192), A("p0", 0, 192), col(LANE), None, ALU.is_equal)
+        ts(A("cj", 192 * par, 192 * par + 192), A("ci", 0, 192), 5, 2047, ALU.logical_shift_right, ALU.bitwise_and)
+        cp(A("coff", 192 * par, 192 * par + 192), A("cj", 192 * par, 192 * par + 192))
+
+    def phase_h(t, a, b):
+        ph[0] += 1
+        par = t % 2
+        if a == 0:
+            mm(A("p1", 0, 192), [(ident, A("xs", 384 * par, 384 * par + 192))])
+        h0 = 3072 * par
+        for c in range(a, b, 64):
+            gather("v" if (t, c) in cfg["hg_v"] else "s", A("hp", h0 + 16 * c, h0 + 16 * c + 1024), A("Hs", 64, 64 + CH),
+                   A("coff", 192 * par + c, 192 * par + c + 64))
+        n = b - a
+        for k in range(16):
+            tt(A("ph", 16 * a + n * k, 16 * a + n * k + n), A("hp", h0 + 16 * a + k, h0 + 16 * b, 16), A("p1", a, b), ALU.mult)
+        mm(A("p3", 192 + a, 192 + b), [(A("B37", 0, 128), A("ph", 16 * a, 16 * a + n))])
+        mm(A("p3", a, b), [(A("Y37", 15 - k, 143 - k), A("ph", 16 * a + n * k, 16 * a + n * k + n)) for k in range(16)])
+        ts(A("ai", a, b), A("p3", a, b), col(C3681), None, ALU.add)
+        tt(A("di", a, b), A("ai", a, b), A("p3", 192 + a, 192 + b), ALU.subtract)
+        ts(A("am", a, b), A("ai", a, b), 4095, None, ALU.bitwise_and)
+        ts(A("dj", a, b), A("di", a, b), 15, None, ALU.bitwise_and)
+        cp(A("aoff", 192 * par + a, 192 * par + b), A("am", a, b))
+        ts(A("eq", a, b), A("dj", a, b), col(LANE), None, ALU.is_equal)
+
+    def phase_m(t, a, b):
+        ph[0] += 1
+        par, n = t % 2, b - a
+        hu = a == 0 and t < STEPS - 1
+        vp = A("p0", 384, 384 + n)
+        if hu:
+            mm(A("p4", 320, 384), [(A("Um", 0, 128), A("eq", 0, 64))])
+        mm(vp, [(A("S0", 0, 128), A("xs", 384 * par + a, 384 * par + b)), (A("S0", 128, 256), A("ge", 192 * par + a, 192 * par + b)),
+                (A("Um", 128, 256), A("eq", a, b))])
+        if hu:
+            tt(A("tmp", 0, 64), A("p4", 320, 384), A("cj", 192 * par, 192 * par + 64), ALU.min)
+        ts(A("src", 64 + a, 64 + b), vp, 0.0, col(CE), ALU.max, ALU.mult)
+        if hu:
+            ts(A("src", 0, 64), A("tmp", 0, 64), 0.0, None, ALU.max)
+        s0 = 0 if hu else 64 + a
+        d0, d1 = s0 // 16, (64 + b) // 16
+        mm(A("p4", 448 + d0, 448 + d1), [(A("Y1", 15 - c, 143 - c), A("src", s0 + c, 64 + b, 16)) for c in range(16)])
+        kinds = ((0, 1) if hu else (1,)) if a == 0 else ()
+        for k in kinds:
+            for j in range(4):
+                r0 = 160 * k + 8 * j * (j + 1)
+                mm(A("p4", r0, r0 + 16 * j + 16), [(ident, A("Mk", 48 - 16 * j, 64)), (A("B1", 0, 128), A("src", 64 * k, 64 * k + 16 * j + 16))])
+        cp(A("doff", d0, d1), A("p4", 448 + d0, 448 + d1))
+        ts(A("woff", 192 * par + a, 192 * par + b), IND(A("ptr", 64, 192), A("doff", 4 + a // 16, 4 + b // 16)), col(LANE), None, ALU.add)
+        if a == 0:
+            act(A("vdb", d0, 8), A("p4", 448 + d0, 456), ACT.Identity, None, 4096.0)
+            act(A("tb", SEG * d0, 8 * SEG, SEG), A("p4", 448 + d0, 456), ACT.Identity, 64.0, None)
+            for k in kinds:
+                for j in range(4):
+                    r0, q = 160 * k + 8 * j * (j + 1), 4 * k + j
+                    act(A("tb", SEG * q + 1, SEG * q + 17 + 16 * j), A("p4", r0, r0 + 16 * j + 16), ACT.Abs, A("vdb", q, q + 1), -4096.0)
+            o, c, d = A("so", SEG * d0, 8 * SEG), A("Cs", SEG * d0, 8 * SEG), A("tb", SEG * d0, 8 * SEG)
+            add("v", ("tensor_tensor_scan", o, c, d, 0.0, ALU.max, ALU.min), [c, d], [o], vcost(o, [c]))
+            cp(A("soff", d0, 8), A("so", SEG * d0 + SEG - 1, 8 * SEG, SEG))
+        if hu:
+            gather("s", A("hold", 0, 64), A("Hs", 64, 64 + CH), A("doff", 0, 4))
+            mm(A("p4", 384, 448), [(lane_in(0), comc(t, t, U * (t % 3), 64)), (A("Sh", 128, 256), A("hold", 0, 64))])
+            act(A("hnew", 0, 64), A("p4", 384, 448), ACT.Copy)
+
+    def phase_u(t):
+        ph[0] += 1
+        if t < STEPS - 1:
+            cp(IND(A("Hs", 0, 64 + CH), A("soff", 0, 4)), A("hnew", 0, 64))
+        cp(IND(A("ptr", 0, 192), A("soff", 4, 8)), A("pval", 64 * t, 64 * t + 64))
+
+    def phase_r(t):
+        par = t % 2
+        g0 = 3072 * par
+        win = A("Wt", 0, 2048 + 1024 * t) if t else A("W0", 0, 2048)
+        bi = 192 * (t - 1)
+        qs = []
+        for (a, b) in cfg["rch"][t]:
+            ph[0] += 1
+            lg = A("p5", 0, 64) if a == 0 else A("p7", a - 64, b - 64)
+            for c in range(a, b, 64):
+                gather("v" if (t, c) in cfg["pg_v"] else "s", A("pg", g0 + 16 * c, g0 + 16 * c + 1024), A("Ps", 0, CP),
+                       A("aoff", 192 * par + c, 192 * par + c + 64), 1.0 / 32)
+                tt(A("pw", g0 + 16 * c, g0 + 16 * c + 1024), IND(win, A("woff", 192 * par + c, 192 * par + c + 64)),
+                   A("pg", g0 + 16 * c, g0 + 16 * c + 1024), ALU.mult)
+            for c in range(a, b, 64):
+                l2 = A(lg["b"], lg["c0"] + c - a, lg["c0"] + c - a + 64)
+                mm(l2, [(negI, A("pw", g0 + 16 * c + k, g0 + 16 * c + 1024, 16)) for k in range(16)]
+                   + ([(negS, A("Bi", bi + c, bi + c + 64))] if t else []))
+            act(A("ys", a, b), lg, ACT.Sigmoid, None, -32.0)
+            if a == 0:
+                mm(A("p5", 64, 128), [(ident, A("oh", 192 * t, 192 * t + 64)), (negI, A("ys", 0, 64))])
+                gather("s", A("wg", 0, 1024), win, A("woff", 192 * par, 192 * par + 64))
+                for k in range(16):
+                    tt(A("pd", k, 1024, 16), A("pg", g0 + k, g0 + 1024, 16), A("p5", 64, 128), ALU.mult)
+                tt(A("Wt", 2048 + 1024 * t, 3072 + 1024 * t), A("wg", 0, 1024), A("pd", 0, 1024), ALU.add)
+                qs.append((a, b))
+                continue
+            qs = [(a, b)] + qs
+            for (qa, qb) in qs:
+                mm(A("p7", 128 + qa, 128 + qb), [(ident, A("oh", 192 * t + qa, 192 * t + qb))]
+                   + ([(halfI, A("Bi", bi + qa, bi + qb))] if t else []) + [(negI, A("ys", qa, qb))])
+            last = t == STEPS - 1
+            if last and len(qs) == 2 and qs[1][1] == qs[0][0]:
+                qs = [(qs[1][0], qs[0][1])]
+            lo, hi = min(q[0] for q in qs), max(q[1] for q in qs)
+            if hi - lo == sum(q[1] - q[0] for q in qs):
+                act(A("Bo", 192 * t + lo, 192 * t + hi), A("p7", 128 + lo, 128 + hi), ACT.Copy)
+            else:
+                for (qa, qb) in qs:
+                    act(A("Bo", 192 * t + qa, 192 * t + qb), A("p7", 128 + qa, 128 + qb), ACT.Copy)
+            for (qa, qb) in qs:
+                da = qa if last else (qa - U) % S
+                hop = -HOP * (STEPS - 1) if last else HOP
+                rem(A("Bo", 192 * t + qa, 192 * t + qb), [(A("Bi", 192 * t + da, 192 * t + da + qb - qa), hop)], 512 * (qb - qa))
+                if last:
+                    dma("sync", EXT("yb", qa, qb), A("Bi", 192 * t + qa, 192 * t + qb), 512 * (qb - qa))
+            qs = []
+
+    phase_a(0)
+    for t in range(STEPS):
+        ch = cfg["ich"][t]
+        for (a, b) in ch:
+            phase_h(t, a, b)
+        if t + 1 < STEPS and t not in cfg["a_late"]:
+            phase_a(t + 1)
+        for (a, b) in ch:
+            phase_m(t, a, b)
+        if t + 1 < STEPS and t in cfg["a_late"]:
+            phase_a(t + 1)
+        phase_u(t)
+        phase_r(t)
+    ts(A("foff", 0, 128), A("ptr", 64, 192), col(LANE), None, ALU.add)
+    for n, (e, a, b) in enumerate(cfg["fin"]):
+        gather(e, A("wo", 16 * a, 16 * b), A("Wt", 0, 6144), A("foff", a, b))
+        dma("sync" if e == "v" else "s", EXT("yw", 16 * a, 16 * b), A("wo", 16 * a, 16 * b), 8192 * (b - a))
+    return ops
+
+
+def replay(ops, order, cfg):
+    free, done, pipe, end, wk = {}, {}, 0.0, 0.0, cfg["WK"]
+    for i in order:
+        o = ops[i]
+        t = free.get(o["eng"], 0.0)
+        for j in o["sem"]:
+            if done[j] + wk > t:
+                t = done[j] + wk
+        d = free[o["eng"]] = t + o["dur"]
+        if o["kind"] != "c":
+            pipe = max(pipe, d + (cfg["RF"] if o["kind"] == "rem" else cfg["DF"]) - 500.0) + o["bytes"] / cfg["BW"]
+            d = pipe + 500.0
+        done[i] = d
+        end = max(end, d)
+    return end
+
+
+def search(cfg, rounds, seed=0):
+    cfgs = [dict(cfg, **v) for v in VARIANTS]
+    opss = [build(c) for c in cfgs]
+    base = priorities(opss[0], cfgs[0])
+    keys = sorted({o["key"] for o in opss[0]})
+    rnd = np.random.RandomState(seed)
+
+    def score(b):
+        order = schedule(opss[0], cfgs[0], base, b)[0]
+        return [replay(o, order, c) for o, c in zip(opss, cfgs)]
+    cur = dict(cfg["bias"])
+    v0 = score({})
+    cv = score(cur)
+    for r in range(rounds):
+        b = dict(cur)
+        for s in range(1 + int(rnd.randint(3))):
+            k0, d = keys[int(rnd.randint(len(keys)))], round(float(rnd.normal()) * 2500.0, -1)
+            for k in ([k for k in keys if k[1] == k0[1]] if rnd.rand() < 0.3 else [k0]):
+                b[k] = b.get(k, 0.0) + d
+        v = score(b)
+        if sum(x / y for x, y in zip(v, v0)) <= sum(x / y for x, y in zip(cv, v0)):
+            cur, cv = b, v
+    return cur, cv, v0
+
+
+def priorities(ops, cfg):
+    n = len(ops)
+    succ = [[] for o in ops]
+    for o in ops:
+        for j in o["sem"] | o["ord"]:
+            succ[j].append(o["i"])
+
+    def lat(o):
+        if o["kind"] == "c":
+            return 0.0
+        return (cfg["RF"] if o["kind"] == "rem" else cfg["DF"]) + o["bytes"] / cfg["BW"]
+    prio = [0.0] * n
+    for o in reversed(ops):
+        best = 0.0
+        for j in succ[o["i"]]:
+            best = max(best, prio[j] + (cfg["WK"] + lat(o) if o["i"] in ops[j]["sem"] else 0.0))
+        prio[o["i"]] = max(best, lat(o)) + o["dur"]
+    return succ, prio
+
+
+def schedule(ops, cfg, base, bias):
+    succ = base[0]
+    prio = [p + bias.get(o["key"], 0.0) for p, o in zip(base[1], ops)]
+    left = [len(o["sem"] | o["ord"]) for o in ops]
+    ready = {e: [] for e in ("pe", "v", "s", "g", "sync")}
+    for o in ops:
+        if left[o["i"]] == 0:
+            ready[o["eng"]].append(o["i"])
+    rt = [0.0] * len(ops)
+    free = {e: 0.0 for e in ready}
+    pipe = [0.0]
+    order = []
+    end = 0.0
+    for step in range(len(ops)):
+        t, e = min((max(free[q], min(rt[j] for j in r)), q) for q, r in ready.items() if r)
+        lim = t + cfg["look"]
+        i = max((j for j in ready[e] if rt[j] <= lim), key=lambda j: (prio[j], -j))
+        o = ops[i]
+        o["t0"] = max(t, rt[i])
+        free[e] = o["t0"] + o["dur"]
+        done = free[e]
+        if o["kind"] != "c":
+            fixed = cfg["RF"] if o["kind"] == "rem" else cfg["DF"]
+            pipe[0] = max(pipe[0], done + fixed - 500.0) + o["bytes"] / cfg["BW"]
+            done = pipe[0] + 500.0
+        o["t1"] = done
+        end = max(end, done)
+        ready[e].remove(i)
+        order.append(i)
+        for j in succ[i]:
+            rt[j] = max(rt[j], done + cfg["WK"] if i in ops[j]["sem"] else free[e])
+            left[j] -= 1
+            if left[j] == 0:
+                ready[ops[j]["eng"]].append(j)
+    return order, end
+
+
+def plan(cfg):
+    bias = search(cfg, cfg["rounds"])[0]
+    ops = build(cfg)
+    order, end = schedule(ops, cfg, priorities(ops, cfg), bias)
+    need = set()
+    for o in ops:
+        need |= o["sem"]
+    count = {}
+    know = {}
+    for i in order:
+        o = ops[i]
+        k = know.setdefault(o["eng"], {})
+        want = {}
+        for j in sorted(o["sem"], key=lambda j: -ops[j]["t1"]):
+            p = ops[j]
+            name, val = p["sig"]
+            if k.get(name, 0) >= val:
+                continue
+            want[name] = max(want.get(name, 0), val)
+            if p["kind"] != "rem":
+                for a, b in p["clock"].items():
+                    k[a] = max(k.get(a, 0), b)
+            k[name] = max(k.get(name, 0), val)
+        o["waits"] = sorted(want.items())
+        o["clock"] = dict(k)
+        if o["kind"] == "c":
+            o["inc"] = i in need
+            name = "e_" + o["eng"]
+            if o["inc"]:
+                count[name] = count.get(name, 0) + 1
+            o["sig"] = (name, count.get(name, 0))
+        else:
+            o["sig"] = (o["tok"], 1)
+    return ops, order, end
+
+
+PLAN = []
+
+
+def rank_program(g, core, T, topo):
+    rank = T.rank_of(core)
+    if rank is None:
+        return
+    if not PLAN:
+        PLAN.append(plan(CFG))
+    ops, order, end = PLAN[0]
+    cores = list(T.cores)
+    queue = {"pe": g.tensor, "v": g.vector, "s": g.scalar, "g": g, "sync": g.sync}
+
+    def mask_of(src, hops):
+        m = -1
+        for h in hops:
+            m &= topo.mask(src, cores[(cores.index(src) + h) % NR])
+        return m
+
+    def bits(m):
+        return bin(m).count("1")
+    full = {}
+    for o in ops:
+        if o["kind"] == "dma":
+            full[o["tok"]] = 16
+        elif o["kind"] == "rem":
+            hops = [d[1] for d in o["call"][2]]
+            full[o["tok"]] = sum(bits(mask_of(cores[(rank - h) % NR], hops)) for h in hops)
+    sent = 0
+    outs = []
+    for i in order:
+        o = ops[i]
+        q = queue[o["eng"]]
+        for name, val in o["waits"]:
+            q.wait_ge(T.sem[name], full.get(name, val))
+        c = o["call"]
+        x = [real(T, a) if isinstance(a, dict) else a for a in c[1:]]
+        if c[0] == "remote":
+            hops = [d[1] for d in c[2]]
+            m = mask_of(core, hops)
+            to = [topo.addr(cores[(rank + h) % NR]) for h in hops]
+            if len(hops) == 1:
+                g.remote_dma(real(T, c[2][0][0]), x[0], T.sem[o["tok"]], T.sem.loc, to[0][1], to[0][0], m)
+            else:
+                g.remote_dma_fused([RemoteDMATransfer(dst_ids=[DstId(rid=a[0], pnc=a[1]) for a in to], dma_engine_mask=m,
+                                                      remote_sem=T.sem[o["tok"]], srcs=[x[0]], dsts=[real(T, d[0]) for d in c[2]])],
+                                   local_sem=T.sem.loc)
+            sent += bits(m)
+            continue
+        if c[0] == "dma_start":
+            q.dma_start(x[0], x[1]).then_inc(T.sem[o["tok"]], 16)
+            if "ext" in c[1]:
+                outs.append(o)
+            continue
+        if c[0] == "activation":
+            kw = {}
+            if x[3] is not None:
+                kw["bias"] = x[3]
+            if x[4] is not None:
+                kw["scale"] = x[4]
+            ins = q.activation(x[0], x[1], x[2], **kw)
+        elif c[0] == "iota":
+            if SCRATCH[c[1]["b"]][2] == "int32":
+                ins = q.iota(*x)
+            else:
+                ins = q.iota(*x, allow_small_or_imprecise_dtypes=True)
+        elif c[0] == "matmul":
+            ins = q.matmul(*x)
+        elif c[0] == "tensor_copy":
+            ins = q.tensor_copy(*x)
+        elif c[0] == "tensor_scalar":
+            ins = q.tensor_scalar(*x)
+        elif c[0] == "tensor_tensor":
+            ins = q.tensor_tensor(*x)
+        elif c[0] == "tensor_tensor_scan":
+            ins = q.tensor_tensor_scan(*x)
+        else:
+            ins = q.memset(*x)
+        if o["inc"]:
+            ins.then_inc(T.sem["e_" + o["eng"]], 1)
+    g.wait_ge(T.sem.loc, sent)
+    for o in outs:
+        queue[o["eng"]].wait_ge(T.sem[o["tok"]], 16)

@@ -3,8 +3,9 @@ from concourse.bass import DstId, RemoteDMATransfer
 from concourse.mybir import AluOpType, ActivationFunctionType
 
 S, U, CH, CP, STEPS, HOP, NR = 192, 64, 2048, 4096, 4, 3, 8
-SEG = 66
+SEG = 65
 BIG = 1.0e6
+ZC = 1800.0
 
 SCRATCH = {
     "snd": ("sbuf", [128, 240], "bfloat16"),
@@ -24,38 +25,53 @@ SCRATCH = {
     "Em": ("sbuf", [128, 144], "bfloat16"),
     "Gi": ("sbuf", [128, 128], "bfloat16"),
     "Rw": ("sbuf", [128, 64], "float32"),
+    "Ix": ("sbuf", [128, 4 * SEG], "float32"),
     "pi": ("sbuf", [128, 2], "int32"),
     "col": ("sbuf", [128, 16], "float32"),
+    "pk": ("sbuf", [128, 16], "bfloat16"),
+    "pf": ("sbuf", [128, 8], "float32"),
     "mn": ("sbuf", [128, 128], "bfloat16"),
     "KL": ("sbuf", [128, 4 * 128], "bfloat16"),
+    "Lr": ("sbuf", [128, 256], "bfloat16"),
     "Sh": ("sbuf", [128, 4 * 128], "bfloat16"),
+    "Iy": ("sbuf", [128, 128], "bfloat16"),
+    "Mk": ("sbuf", [128, 128], "bfloat16"),
+    "Us": ("sbuf", [128, 128], "bfloat16"),
+    "Cr": ("sbuf", [128, 128], "float32"),
+    "sd": ("sbuf", [128, 256], "float32"),
+    "zf": ("sbuf", [128, 192], "float16"),
     "Zw": ("sbuf", [128, 144], "bfloat16"),
-    "Sr": ("sbuf", [128, 2 * 128], "bfloat16"),
-    "Y37": ("sbuf", [128, 144], "bfloat16"),
+    "Sr": ("sbuf", [128, 128], "bfloat16"),
+    "Yy": ("sbuf", [128, 144], "float16"),
+    "Yd": ("sbuf", [128, 144], "float16"),
     "Y1": ("sbuf", [128, 144], "float16"),
-    "B37": ("sbuf", [128, 128], "bfloat16"),
     "B1": ("sbuf", [128, 128], "float16"),
     "ut": ("sbuf", [128, 3 * 128], "bfloat16"),
     "Um": ("sbuf", [128, 2 * 128], "bfloat16"),
     "S0": ("sbuf", [128, 2 * 128], "bfloat16"),
-    "Mk": ("sbuf", [128, 64], "bfloat16"),
     "F32": ("sbuf", [128, 3 * 128], "float32"),
-    "Cs": ("sbuf", [128, 8 * SEG], "float32"),
+    "Cs": ("sbuf", [128, 4 * SEG], "float32"),
     "tb": ("sbuf", [128, 8 * SEG], "float32"),
     "so": ("sbuf", [128, 8 * SEG], "float32"),
-    "xs": ("sbuf", [128, 2 * 384], "bfloat16"),
-    "ge": ("sbuf", [128, 2 * 192], "bfloat16"),
+    "xs": ("sbuf", [128, 4 * 192], "bfloat16"),
+    "xm": ("sbuf", [128, 2 * 1536], "bfloat16"),
+    "ge": ("sbuf", [128, 4 * 192], "bfloat16"),
     "oh": ("sbuf", [128, 4 * 192], "bfloat16"),
-    "oa": ("sbuf", [128, 192], "bfloat16"),
     "ci": ("sbuf", [128, 192], "int32"),
-    "cj": ("sbuf", [128, 2 * 192], "int32"),
-    "coff": ("sbuf", [128, 2 * 192], "uint16"),
+    "cj": ("sbuf", [128, 4 * 192], "int32"),
+    "ct": ("sbuf", [128, 192], "bfloat16"),
+    "mg": ("sbuf", [128, 8], "float32"),
+    "df": ("sbuf", [128, 192], "float32"),
+    "Cz": ("sbuf", [128, 1024], "bfloat16"),
+    "nI": ("sbuf", [128, 128], "bfloat16"),
+    "Y37": ("sbuf", [128, 128], "float16"),
+    "coff": ("sbuf", [128, 4 * 192], "uint16"),
     "hp": ("sbuf", [128, 2 * 3072], "bfloat16"),
-    "ph": ("sbuf", [128, 3072], "bfloat16"),
+    "zc": ("sbuf", [128, 384], "float16"),
+    "at": ("sbuf", [128, 192], "bfloat16"),
     "ai": ("sbuf", [128, 192], "int32"),
     "am": ("sbuf", [128, 192], "int32"),
-    "di": ("sbuf", [128, 192], "int32"),
-    "dj": ("sbuf", [128, 192], "int32"),
+    "dr": ("sbuf", [128, 192], "bfloat16"),
     "aoff": ("sbuf", [128, 2 * 192], "uint16"),
     "eq": ("sbuf", [128, 192], "bfloat16"),
     "tmp": ("sbuf", [128, 64], "float32"),
@@ -68,36 +84,39 @@ SCRATCH = {
     "hold": ("sbuf", [128, 64], "bfloat16"),
     "hnew": ("sbuf", [128, 64], "bfloat16"),
     "pg": ("sbuf", [128, 2 * 3072], "bfloat16"),
-    "wg": ("sbuf", [128, 1024], "float32"),
     "pw": ("sbuf", [128, 2 * 3072], "float32"),
+    "pd": ("sbuf", [128, 1024], "float32"),
     "ys": ("sbuf", [128, 192], "float32"),
     "Bo": ("sbuf", [128, 4 * 192], "float32"),
     "Bi": ("sbuf", [128, 4 * 192], "float32"),
     "wo": ("sbuf", [128, 2048], "float32"),
-    "p0": ("psum", [128, 512], "float32"),
-    "p1": ("psum", [128, 512], "float32"),
-    "p3": ("psum", [128, 512], "float32"),
-    "p4": ("psum", [128, 512], "float32"),
-    "p5": ("psum", [128, 512], "float32"),
-    "p7": ("psum", [128, 512], "float32"),
-    "pd": ("psum", [128, 1024], "float32"),
+    "pa": ("psum", [128, 512], "float32"),
+    "pz0": ("psum", [128, 512], "float32"),
+    "pz1": ("psum", [128, 512], "float32"),
+    "py": ("psum", [128, 512], "float32"),
+    "pl0": ("psum", [128, 512], "float32"),
+    "pl1": ("psum", [128, 512], "float32"),
+    "pl2": ("psum", [128, 512], "float32"),
+    "pq": ("psum", [128, 512], "float32"),
 }
 NDMA = 40
 SEMAPHORES = ["e_pe", "e_v", "e_s", "e_g", "loc"] + ["d%d" % i for i in range(NDMA)]
 
 CFG = {
-    "ich": [[(0, 64), (64, 128), (128, 192)], [(0, 64), (64, 192)], [(0, 64), (64, 192)], [(0, 64), (64, 192)]],
-    "hg_v": {(0, 64)},
-    "pg_v": {(0, 64)},
-    "rch": [[(0, 64), (64, 128), (128, 192)]] * 4,
-    "a_late": {0},
-    "oh_s": set(),
+    "ich": [[(0, 64), (64, 192)]] * 4,
+    "hg_v": {(0, 32), (0, 128), (0, 160)},
+    "hcut": [[0, 32, 64, 96, 128, 160, 192]] * 4,
+    "pg_v": set(),
+    "a_at": {1: (0, 1), 2: (0, 2), 3: (1, 2)},
+    "ge_s": {0}, "oh_s": set(), "dr_s": set(), "am_s": set(), "rscan": {(3, 128)}, "xm_s": 4, "DI": 200.0,
+    "zc_s": {(t, a) for t in range(4) for a in (0, 64)}, "zf_s": {(t, a) for t in range(4) for a in (0, 64)}, "src_s": set(),
+    "rep_b": "pz0", "pcut": 32, "wcut": 32, "dscan": set(), "half": True, "ai_zf": True,
     "fin": [("v", 0, 32), ("s", 32, 64), ("v", 64, 96), ("s", 96, 128)],
-    "G": 1.5, "SC": 3.8, "CY": 1.0, "OV": 50.0, "PE": 0.42, "WK": 120.0, "look": 100.0,
-    "OV2": 0.0, "DF": 2000.0, "BW": 200.0, "RF": 2500.0, "rounds": 2500, "bias": {},
+    "G": 1.5, "SC": 3.8, "CY": 1.0, "OV": 50.0, "PE": 0.42, "WK": 170.0, "look": 100.0,
+    "OV2": 10.0, "DF": 1700.0, "BW": 300.0, "RF": 2300.0, "rounds": 100, "shuttle": 4000, "polish": 100000, "bias": {}, "mix": 0.3, "heat": 0.0003, "heat2": 0.003,
 }
-VARIANTS = [{}, {"G": 1.15, "SC": 2.5, "CY": 1.3, "BW": 300.0}, {"G": 1.95, "SC": 5.0, "CY": 1.1, "WK": 200.0},
-            {"CY": 1.25, "OV2": 30.0, "BW": 150.0, "RF": 3500.0}]
+VARIANTS = [{}, {"G": 1.15, "SC": 2.5, "CY": 1.3, "BW": 380.0, "WK": 120.0, "OV2": 0.0, "DI": 100.0},
+            {"G": 1.95, "SC": 5.0, "CY": 1.25, "WK": 250.0, "OV2": 25.0, "BW": 200.0, "RF": 3200.0, "DI": 400.0}]
 ALU = AluOpType
 ACT = ActivationFunctionType
 
@@ -140,60 +159,51 @@ def build(cfg):
     ndma = [0]
     ph = [0]
 
-    def flat(aps):
-        out = []
-        for a in aps:
-            if not isinstance(a, dict) or "ext" in a:
-                continue
-            if "win" in a:
-                out.append(a["win"])
-                out.append(a["off"])
-            else:
-                out.append(a)
-        return out
-
-    def add(eng, call, reads, writes, dur, kind="c", after=(), nbytes=0):
+    def add(eng, calls, dur, kind="c", after=(), nbytes=0, grp=None):
         i = len(ops)
-        o = {"i": i, "eng": eng, "call": call, "dur": dur, "kind": kind, "sem": set(after), "ord": set(), "bytes": nbytes, "key": (call[1]["b"], ph[0])}
-        rd = flat(reads)
-        wr = []
-        for a in writes:
-            if "ext" in a:
-                continue
-            if "win" in a:
-                wr.append(a["win"])
-                rd.append(a["off"])
+        o = {"i": i, "eng": eng, "calls": calls, "dur": dur, "kind": kind, "sem": set(after), "ord": set(), "bytes": nbytes, "grp": grp}
+        rd, wr = [], []
+        for c in calls:
+            if c[0] == "remote":
+                ins, outs = [c[1]], [d[0] for d in c[2]]
             else:
-                wr.append(a)
+                ins, outs = list(c[2:]), [c[1]]
+            for a in ins:
+                if isinstance(a, dict) and "ext" not in a:
+                    rd += [a["win"], a["off"]] if "win" in a else [a]
+            for a in outs:
+                if "win" in a:
+                    wr.append(a["win"])
+                    rd.append(a["off"])
+                elif "ext" not in a:
+                    wr.append(a)
+        o["key"] = (wr[0]["b"] if wr else calls[0][1]["b"], ph[0])
 
-        def dep(j, raw):
-            if j == i:
-                return
-            p = ops[j]
-            if eng == "pe" and p["eng"] == "pe" and call[1] is p["call"][1]:
-                o["ord"].add(j)
-            else:
-                o["sem"].add(j)
+        def dep(j):
+            if j != i:
+                o["ord" if grp is not None and ops[j]["grp"] == grp else "sem"].add(j)
 
-        def meet(a, lo, hi, st):
-            if not (lo < a["c1"] and a["c0"] < hi):
+        def meet(a, e):
+            if not (e["c0"] < a["c1"] and a["c0"] < e["c1"] and e["p0"] < a["p1"] and a["p0"] < e["p1"]):
                 return False
-            return st == 1 or st != a["st"] or (lo - a["c0"]) % st == 0
+            return e["st"] == 1 or e["st"] != a["st"] or (e["c0"] - a["c0"]) % e["st"] == 0
+
+        def covers(a, e):
+            return a["p0"] <= e["p0"] and e["p1"] <= a["p1"] and a["c0"] <= e["c0"] and e["c1"] <= a["c1"] and (a["st"] == 1 or (e["st"] == a["st"] and meet(a, e)))
         for a in rd:
-            for (j, w, lo, hi, st) in hist.get(a["b"], []):
-                if w and meet(a, lo, hi, st):
-                    dep(j, True)
+            for (j, w, e) in hist.get(a["b"], []):
+                if w and meet(a, e):
+                    dep(j)
         for a in wr:
-            for (j, w, lo, hi, st) in hist.get(a["b"], []):
-                if meet(a, lo, hi, st):
-                    dep(j, False)
+            for (j, w, e) in hist.get(a["b"], []):
+                if meet(a, e):
+                    dep(j)
         for a in wr:
             h = hist.setdefault(a["b"], [])
-            if a["p0"] == 0 and a["p1"] == 128:
-                h[:] = [e for e in h if e[0] == i or not (a["c0"] <= e[2] and e[3] <= a["c1"] and (a["st"] == 1 or (e[4] == a["st"] and meet(a, e[2], e[3], e[4]))))]
-            h.append((i, True, a["c0"], a["c1"], a["st"]))
+            h[:] = [x for x in h if x[0] == i or not covers(a, x[2])]
+            h.append((i, True, a))
         for a in rd:
-            hist.setdefault(a["b"], []).append((i, False, a["c0"], a["c1"], a["st"]))
+            hist.setdefault(a["b"], []).append((i, False, a))
         for name in sorted({a["b"] for a in rd + wr if in_psum(a)}):
             st = bank.setdefault(name, {"eng": None, "cur": [], "prev": []})
             if st["eng"] != eng:
@@ -227,36 +237,55 @@ def build(cfg):
         return cfg["OV2"] + max(n * f, 64) * cy
 
     def cp(out, a):
-        return add("v", ("tensor_copy", out, a), [a], [out], vcost(out, [a]))
+        return add("v", [("tensor_copy", out, a)], vcost(out, [a]))
+
+    def tsc(out, a, s1, s2, o0, o1=None):
+        return ("tensor_scalar", out, a, s1, s2, o0) + (() if o1 is None else (o1,))
 
     def ts(out, a, s1, s2, o0, o1=None):
-        c = ("tensor_scalar", out, a, s1, s2, o0) + (() if o1 is None else (o1,))
-        return add("v", c, [a, s1, s2], [out], vcost(out, [a]))
+        return add("v", [tsc(out, a, s1, s2, o0, o1)], vcost(out, [a]))
 
     def tt(out, a, b, o):
-        return add("v", ("tensor_tensor", out, a, b, o), [a, b], [out], vcost(out, [a, b], True))
+        return add("v", [("tensor_tensor", out, a, b, o)], vcost(out, [a, b], True))
 
     def mset(out, val):
-        return add("v", ("memset", out, val), [], [out], vcost(out, []))
+        return add("v", [("memset", out, val)], vcost(out, []))
 
     def act(out, a, f, bias=None, scale=None):
-        return add("s", ("activation", out, a, f, bias, scale), [a, bias, scale], [out], 15 + vcost(out, [a, A("tb", 0, 1)]))
+        return add("s", [("activation", out, a, f, bias, scale)], 15 + vcost(out, [a, A("tb", 0, 1)]))
+
+    def mcost(c):
+        f = 4 if SCRATCH[c[3]["b"]][2] == "float32" else 1
+        return max(min(64, c[2]["n"]), c[3]["n"]) * f * cfg["PE"] * cfg["CY"]
+
+    def mrun(calls, grp=None, cut=500.0):
+        grp = ("g", len(ops)) if grp is None else grp
+        run = []
+        for c in calls:
+            run.append(c)
+            if sum(mcost(x) for x in run) >= cut * cfg["CY"] * cfg["PE"] / 0.42 or c is calls[-1]:
+                i = add("pe", run, sum(mcost(x) for x in run), grp=grp)
+                if run[0] is not calls[0]:
+                    ops[i]["ord"].add(i - 1)
+                run = []
+        return grp
+
+    def group(items, start=True, stop=True):
+        return [("matmul", o, l, r, start and n == 0, stop and n == len(items) - 1) for n, (o, l, r) in enumerate(items)]
 
     def mm(out, pairs):
-        for n, (l, r) in enumerate(pairs):
-            f = 4 if SCRATCH[r["b"]][2] == "float32" else 1
-            add("pe", ("matmul", out, l, r, n == 0, n == len(pairs) - 1), [l, r], [out], max(64, r["n"]) * f * cfg["PE"] * cfg["CY"])
+        return mrun(group([(out, l, r) for (l, r) in pairs]))
 
     def iota(out, pat, base, cm):
-        return add("g", ("iota", out, pat, base, cm), [], [out], 130 + 2 * out["n"] * cy)
+        return add("g", [("iota", out, pat, base, cm)], 130 + 2 * out["n"] * cy)
 
-    def dma(q, out, a, nbytes, after=(), behind=()):
-        i = add(q, ("dma_start", out, a), [a], [out], 100.0 if q != "g" else 1000.0, "dma", after, nbytes)
+    def dma(q, pairs, nbytes, after=(), behind=()):
+        i = add(q, [("dma_start", o, a) for (o, a) in pairs], len(pairs) * (cfg["DI"] if q != "g" else 1000.0), "dma", after, nbytes)
         ops[i]["ord"] |= set(behind)
         return i
 
     def rem(srcap, dsts, nbytes):
-        return add("g", ("remote", srcap, dsts), [srcap], [d[0] for d in dsts], 500.0, "rem", (), nbytes)
+        return add("g", [("remote", srcap, dsts)], 500.0, "rem", (), nbytes)
 
     def gather(eng, out, win, off, scale=None):
         if eng == "s":
@@ -265,36 +294,44 @@ def build(cfg):
             return cp(out, IND(win, off))
         return ts(out, IND(win, off), scale, None, ALU.mult)
 
-    l_past = dma("sync", A("snd", 0, 192), EXT("past"), 49152)
-    dma("s", A("com", 0, 768, 1, 0, 8), EXT("coming"), 12288)
-    l_kap = dma("sync", A("kl", 0, 1), EXT("kap"), 8192, (), (l_past,))
-    dma("s", A("kl", 1, 2), EXT("lam"), 8192)
-    l_snd = dma("sync", A("snd", 192, 240), EXT("coming"), 12288, (), (l_kap,))
-    l_hist = dma("sync", A("Hs", 64, 64 + CH), EXT("hist"), 524288, (), (l_snd,))
-    l_score = dma("sync", A("Ps", 0, CP), EXT("score"), 1048576, (), (l_hist,))
-    dma("sync", A("W0", 0, 2048), EXT("weight"), 524288, (l_hist,), (l_score,))
+    l_past = dma("sync", [(A("snd", 0, 192), EXT("past"))], 49152)
+    dma("s", [(A("com", 0, 768, 1, 0, 8), EXT("coming"))], 12288)
+    l_kap = dma("sync", [(A("kl", 0, 1), EXT("kap"))], 8192, (), (l_past,))
+    dma("s", [(A("kl", 1, 2), EXT("lam"))], 8192)
+    l_snd = dma("sync", [(A("snd", 192, 240), EXT("coming"))], 12288, (), (l_kap,))
+    l_hist = dma("sync", [(A("Hs", 64, 64 + CH), EXT("hist"))], 524288, (), (l_snd,))
+    l_score = dma("sync", [(A("Ps", 0, CP), EXT("score"))], 1048576, (), (l_hist,))
+    dma("sync", [(A("W0", 0, 2048), EXT("weight"))], 524288, (l_hist,), (l_score,))
     iota(A("Dm", 0, 144), [[1, 144]], 0, -1)
     iota(A("pi", 0, 1), [[1, 1]], 0, 1)
-    iota(A("Gi", 0, 128, 1, 0, 8), [[1, 8], [0, 16]], 0, -1)
     iota(A("Pm", 0, 128), [[-16, 8], [0, 16]], 0, 1)
-    iota(A("Rw", 0, 64), [[1, 64]], -48, 0)
+    iota(A("Gi", 0, 128, 1, 0, 8), [[1, 8], [0, 16]], 0, -1)
+    iota(A("Rw", 0, 64), [[1, 64]], -16, 0)
+    iota(A("Ix", 0, 4 * SEG), [[-16, 4], [1, SEG]], 0, 0)
     rem(A("snd", 0, 240), [(A("lnd", 240 * (t - 1), 240 * t), HOP * t) for t in (1, 2, 3)], 3 * 61440)
+    iota(A("Iy", 0, 128), [[0, 8], [1, 16]], 0, 0)
     iota(A("Em", 0, 144, 1, 0, 8), [[1, 144]], 0, -16)
+    iota(A("tb", 0, 8 * SEG), [[0, 8 * SEG]], int(BIG), 0)
+    for j in range(3):
+        iota(A("xm", 1536 + 512 * j, 2048 + 512 * j), [[0, 512]], 0, 0)
     iota(A("ptr", 64, 192), [[16, 128]], 0, 0)
     iota(A("pval", 0, 256), [[16, 256]], 2048, 0)
+    if cfg["rscan"]:
+        iota(A("Cz", 0, 1024), [[0, 1024]], 1, 0)
+    first = [o["i"] for o in ops if o["eng"] == "g"]
+    for i, j in zip(first, first[1:]):
+        ops[j]["ord"].add(i)
 
     def col(j, p1=128):
         return A("col", j, j + 1, 1, 0, p1)
-    LANE, PF, C3681, CE, C15, CZ, CZ8, CW, CS0, CS1, SM = 0, 1, 2, 3, 4, 5, 6, 7, 8, 9, 12
+    LANE, PF, CA, CE, C15, CZ, CZ8, CB, CS0, CS1, CN, CC, SM = 0, 1, 2, 3, 4, 5, 6, 7, 8, 9, 10, 11, 12
     D128 = A("Dm", 0, 128)
     ts(A("pi", 1, 2), A("pi", 0, 1), 15, None, ALU.bitwise_and)
     cp(A("col", PF, PF + 1), A("pi", 0, 1))
     cp(col(LANE), A("pi", 1, 2))
     ident = A("Sh", 0, 128)
     ts(ident, D128, 0.0, None, ALU.is_equal)
-    ts(col(CW, 8), col(PF, 8), 7.0, -8.0, ALU.is_ge, ALU.mult)
-    sprev, srep = A("Sr", 0, 128, 1, 0, 8), A("Sr", 128, 256, 1, 0, 8)
-    ts(sprev, A("Gi", 0, 128, 1, 0, 8), col(CW, 8), 1.0, ALU.subtract, ALU.is_equal)
+    srep = A("Sr", 0, 128, 1, 0, 8)
     ts(srep, A("Gi", 0, 128, 1, 0, 8), 0.0, None, ALU.is_equal)
     tt(A("mn", 0, 128), A("Pm", 0, 128), D128, ALU.min)
     ts(A("kli", 0, 2), A("kl", 0, 2), 0xFF00, None, ALU.bitwise_and)
@@ -304,43 +341,69 @@ def build(cfg):
         ts(A("KL", 128 * j, 128 * j + 128), A("mn", 0, 128), 0.0, A("klf", j, j + 1), ALU.is_ge, ALU.mult)
     for j in (1, 3):
         ts(A("KL", 128 * j, 128 * j + 128), D128, 0.0, A("klf", j, j + 1), ALU.is_equal, ALU.mult)
-    ts(col(C3681), col(LANE), 3681.0, None, ALU.mult)
+    ts(A("pf", 0, 8), A("Pm", 0, 128, 16), col(LANE), None, ALU.is_equal)
+    act(A("pk", 0, 8), A("pf", 0, 8), ACT.Copy)
+    act(A("pk", 8, 9), A("pf", 0, 1), ACT.Copy)
+    for j in (0, 1):
+        mm(A("py", 128 * j, 128 * j + 128, 1, 0, 8), [(A("pk", 1, 9), A("KL", 128 + 256 * j, 256 + 256 * j))])
+    act(A("Lr", 0, 256, 1, 0, 8), A("py", 0, 256, 1, 0, 8), ACT.Copy)
+    mset(col(CC), ZC)
+    for (pz, c) in (("pz0", 0), ("pz1", 0), ("pz1", 128)):
+        act(A(pz, c, c + 128), D128, ACT.Identity, col(CC), 0.0)
+    ts(col(CB), col(LANE), 3681.0, 37 * ZC, ALU.mult, ALU.add)
+    if cfg["zc_s"]:
+        mset(col(CA), -ZC)
+    if cfg["dr_s"]:
+        mset(A("mg", 0, 1), 1.5 * 2.0 ** 27)
+        mset(A("mg", 1, 2), -1.5 * 2.0 ** 27)
+    if cfg["am_s"]:
+        ts(A("mg", 2, 3), col(CB), 786432.0 - 2047.5, None, ALU.add)
+        ts(A("mg", 3, 4), col(CB), 786432.0, None, ALU.add)
     ts(col(CE), col(LANE), 8.0 / 4096, 1.0 / 4096, ALU.mult, ALU.max)
     ts(col(C15), col(LANE), -1.0, 15.0, ALU.mult, ALU.add)
     ts(col(CZ), col(LANE), 0.0, 4096.0, ALU.is_equal, ALU.mult)
     ts(col(CZ8), col(LANE), 0.0, -32768.0, ALU.is_equal, ALU.mult)
+    ts(col(CN), col(LANE), 0.0, -1.0, ALU.is_equal, ALU.mult)
     ts(col(CS0), col(PF), 112.0, -128.0, ALU.is_ge, ALU.mult)
     ts(col(CS1), col(CS0), 16.0, None, ALU.add)
-    ts(A("col", SM, SM + 4), A("Rw", 48, 52), col(LANE), 15.0, ALU.add, ALU.is_le)
-    ts(A("Y37", 0, 144), A("Dm", 0, 144), col(C15), 37.0, ALU.is_equal, ALU.mult)
-    ts(A("B37", 0, 128), A("Pm", 0, 128), col(LANE), 37.0, ALU.is_equal, ALU.mult)
+    ts(A("col", SM, SM + 4), A("Rw", 16, 20), col(LANE), 15.0, ALU.add, ALU.is_le)
+    ts(A("Yy", 0, 144), A("Dm", 0, 144), 16.0, None, ALU.is_equal)
+    ts(A("Yd", 0, 128), A("Pm", 0, 128), col(LANE), col(CN), ALU.is_equal, ALU.mult)
     ts(A("Y1", 0, 144), A("Dm", 0, 144), col(C15), None, ALU.is_equal)
-    ts(A("B1", 0, 128), A("Pm", 0, 128), col(LANE), None, ALU.is_equal)
+    ts(A("B1", 0, 128), A("Pm", 0, 128), col(LANE), 4096.0, ALU.is_equal, ALU.mult)
+    ts(A("mg", 4, 5), col(LANE), -1.0, 0.0, ALU.add, ALU.max)
+    ts(A("mg", 5, 6), A("mg", 4, 5), 4096.0, None, ALU.mult)
+    act(A("Us", 0, 128), A("B1", 0, 128), ACT.Identity, None, A("mg", 5, 6))
+    ts(A("Mk", 0, 128), A("Iy", 0, 128), col(LANE), -2.0 ** 24, ALU.not_equal, ALU.mult)
+    act(A("Cr", 0, 128), A("Iy", 0, 128), ACT.Identity, -1.0e8, 2.0e8)
     ts(A("ut", 0, 128), A("mn", 0, 128), 0.0, 4096.0, ALU.is_ge, ALU.mult)
     ts(A("ut", 128, 256), A("Pm", 0, 128), col(LANE), -4096.0, ALU.is_equal, ALU.mult)
     ts(A("ut", 256, 384), D128, 0.0, 4096.0, ALU.is_equal, ALU.mult)
     tt(A("ut", 0, 128), A("ut", 0, 128), A("ut", 128, 256), ALU.add)
     tt(A("Um", 0, 128), A("ut", 0, 128), A("ut", 256, 384), ALU.add)
-    cp(A("Um", 128, 256), A("Um", 0, 128))
-    mset(A("Um", 128, 256, 16), 0.0)
-    ts(A("S0", 0, 128), D128, 0.0, col(CZ), ALU.is_equal, ALU.mult)
-    ts(A("S0", 128, 256), D128, 0.0, col(CZ8), ALU.is_equal, ALU.mult)
-    ts(A("Mk", 0, 64), A("Rw", 0, 64), col(LANE), 4096.0, ALU.is_ge, ALU.mult)
+    act(A("Um", 128, 256), A("Um", 0, 128), ACT.Copy)
+    act(A("Um", 128, 256, 16), A("Dm", 0, 8), ACT.Identity, None, 0.0)
+    act(A("S0", 0, 128), ident, ACT.Identity, None, col(CZ))
+    act(A("S0", 128, 256), ident, ACT.Identity, None, col(CZ8))
     negI, halfI, negS = A("F32", 0, 128), A("F32", 128, 256), A("F32", 256, 384)
-    ts(negI, D128, 0.0, -1.0, ALU.is_equal, ALU.mult)
-    ts(halfI, D128, 0.0, 0.5, ALU.is_equal, ALU.mult)
+    if cfg["am_s"]:
+        act(A("nI", 0, 128), ident, ACT.Identity, None, -1.0)
+        act(A("Y37", 0, 128), ident, ACT.Identity, None, 37.0)
+    act(negI, ident, ACT.Identity, None, -1.0)
+    act(halfI, ident, ACT.Identity, None, 0.5)
     ts(negS, D128, col(CS1), -1.0 / 32, ALU.is_equal, ALU.mult)
     for t in (1, 2, 3):
         ts(A("Sh", 128 * t, 128 * t + 128), D128, float(t), col(SM + t), ALU.is_equal, ALU.mult)
     ts(A("Zw", 0, 144, 1, 0, 8), A("Em", 0, 144, 1, 0, 8), 2.0, None, ALU.is_equal)
-    mset(A("Cs", 0, 8 * SEG), 0.0)
-    mset(A("Cs", 0, 8 * SEG, SEG), BIG)
-    for k in (0, 1):
-        ts(A("Cs", 4 * SEG * k + SEG - 1, 4 * SEG * (k + 1), SEG), A("Rw", 48, 52), 16.0, col(LANE), ALU.mult, ALU.add)
-    mset(A("tb", 0, 8 * SEG), BIG)
+    ts(A("Cs", 0, 4 * SEG), A("Ix", 0, 4 * SEG), col(LANE), -3000.0, ALU.is_equal, ALU.mult)
+    ts(A("Cs", 0, 4 * SEG, SEG), A("Cs", 0, 4 * SEG, SEG), BIG, None, ALU.add)
+    ts(A("tmp", 0, 4), A("Rw", 16, 20), 16.0, 3000.0, ALU.mult, ALU.add)
+    ts(A("Cs", SEG - 1, 4 * SEG, SEG), A("tmp", 0, 4), col(LANE), None, ALU.add)
+    if cfg["rscan"]:
+        mset(A("Cz", 0, 1024, 16), 0.0)
     for t in (1, 2, 3):
-        l_com = dma("sync", A("com", 768 * t, 768 * t + 768, 1, 0, 8), A("lnd", 240 * (t - 1) + 192, 240 * t), 12288)
-    dma("g", A("Wt", 0, 2048), A("W0", 0, 2048), 1048576, (l_com,))
+        l_com = dma("sync", [(A("com", 768 * t, 768 * t + 768, 1, 0, 8), A("lnd", 240 * (t - 1) + 192, 240 * t))], 12288)
+    dma("g", [(A("Wt", 0, 2048), A("W0", 0, 2048))], 1048576, (l_com,))
 
     def lane_in(i):
         return A("Zw", 2 - i, 130 - i, 1, 0, 8)
@@ -350,87 +413,145 @@ def build(cfg):
 
     def phase_a(t):
         ph[0] += 1
-        rot, par = U * (t % 3), t % 2
+        rot, s0, m0 = U * (t % 3), 192 * t, 1536 * (t % 2)
         pieces = [(0, rot, S - rot)] + ([(S - rot, 0, rot)] if rot else [])
         pb, pc = ("snd", 0) if t == 0 else ("lnd", 240 * (t - 1))
+        x = A("xs", s0, s0 + 192) if t else A("snd", 0, 192)
+        if t:
+            for (p, u, n) in pieces:
+                mm(A("pa", p, p + n), [(A("Sh", 128 * t, 128 * t + 128), A(pb, pc + u, pc + u + n))]
+                   + [(lane_in(t - 1 - s), comc(t, s, u, n)) for s in range(t)])
+            act(x, A("pa", 0, 192), ACT.Copy)
+            dma("sync", [(A("xm", m0 + 192 * g, m0 + 192 * g + 192, 1, 16 * g, 16 * g + 16), A("xs", s0, s0 + 192, 1, 16 * g, 16 * g + 16))
+                         for g in range(8)], 49152)
+        cs = A("pa", 192, 384)
+
+        def lrows(j):
+            return [(A("pa", 192 + p, 192 + p + n), A("Lr", 128 * j, 128 * j + 128, 1, 0, 8), comc(t, t, u, n)) for (p, u, n) in pieces]
+        mrun(group([(cs, A("KL", 0, 128), x)] + lrows(0) + lrows(1) + [(cs, A("KL", 256, 384), x)]))
+        cp(A("ci", 0, 192), cs)
+        ts(A("cj", s0, s0 + 192), A("ci", 0, 192), 5, 2047, ALU.logical_shift_right, ALU.bitwise_and)
+        cp(A("coff", s0, s0 + 192), A("cj", s0, s0 + 192))
+        if t == 0:
+            for g in range(8):
+                if g < cfg["xm_s"]:
+                    act(A("xm", 192 * g, 192 * g + 192), x, ACT.Identity, None, A("pf", g, g + 1))
+                else:
+                    ts(A("xm", 192 * g, 192 * g + 192), x, A("pf", g, g + 1), None, ALU.mult)
         for (p, u, n) in pieces:
-            mm(A("p0", p, p + n), [(A("Sh", 128 * t, 128 * t + 128), A(pb, pc + u, pc + u + n))]
-               + [(lane_in(t - 1 - s), comc(t, s, u, n)) for s in range(t)])
-            mm(A("p0", 192 + p, 192 + p + n), [(sprev, comc(t, t, u, n))])
-        x, sp = A("xs", 384 * par, 384 * par + 192), A("xs", 384 * par + 192, 384 * par + 384)
-        act(A("xs", 384 * par, 384 * par + 384), A("p0", 0, 384), ACT.Copy)
-        act(A("ge", 192 * par, 192 * par + 192), x, ACT.Sigmoid, -1920.0, 256.0)
-        mm(A("p0", 192, 384), [(A("KL", 0, 128), x), (A("KL", 256, 384), x), (A("KL", 128, 256), sp), (A("KL", 384, 512), sp)])
-        for (p, u, n) in pieces:
-            mm(A("p0", p, p + n), [(srep, comc(t, t, u, n))])
-        cp(A("ci", 0, 192), A("p0", 192, 384))
+            mm(A("pa", p, p + n), [(srep, comc(t, t, u, n))])
         if t in cfg["oh_s"]:
-            act(A("oa", 0, 192), A("p0", 0, 192), ACT.Abs, col(LANE), -1.0)
-            act(A("oh", 192 * t, 192 * t + 192), A("oa", 0, 192), ACT.Relu, 1.0, -1.0)
+            act(A("ct", 0, 192), A("pa", 0, 192), ACT.Abs, col(LANE), -1.0)
+            act(A("oh", s0, s0 + 192), A("ct", 0, 192), ACT.Relu, 1.0, -1.0)
         else:
-            ts(A("oh", 192 * t, 192 * t + 192), A("p0", 0, 192), col(LANE), None, ALU.is_equal)
-        ts(A("cj", 192 * par, 192 * par + 192), A("ci", 0, 192), 5, 2047, ALU.logical_shift_right, ALU.bitwise_and)
-        cp(A("coff", 192 * par, 192 * par + 192), A("cj", 192 * par, 192 * par + 192))
+            ts(A("oh", s0, s0 + 192), A("pa", 0, 192), col(LANE), None, ALU.is_equal)
+        if t in cfg["ge_s"]:
+            i = act(A("ge", s0, s0 + 192), x, ACT.Sigmoid, -1920.0, 256.0)
+            ops[i]["dur"] += 1300.0 if t == 0 else 0.0
+        else:
+            ts(A("ge", s0, s0 + 192), x, 8.0, None, ALU.is_ge)
 
-    def phase_h(t, a, b):
+    def phase_h(t, a, b, pz):
         ph[0] += 1
-        par = t % 2
-        if a == 0:
-            mm(A("p1", 0, 192), [(ident, A("xs", 384 * par, 384 * par + 192))])
-        h0 = 3072 * par
-        for c in range(a, b, 64):
-            gather("v" if (t, c) in cfg["hg_v"] else "s", A("hp", h0 + 16 * c, h0 + 16 * c + 1024), A("Hs", 64, 64 + CH),
-                   A("coff", 192 * par + c, 192 * par + c + 64))
-        n = b - a
-        for k in range(16):
-            tt(A("ph", 16 * a + n * k, 16 * a + n * k + n), A("hp", h0 + 16 * a + k, h0 + 16 * b, 16), A("p1", a, b), ALU.mult)
-        mm(A("p3", 192 + a, 192 + b), [(A("B37", 0, 128), A("ph", 16 * a, 16 * a + n))])
-        mm(A("p3", a, b), [(A("Y37", 15 - k, 143 - k), A("ph", 16 * a + n * k, 16 * a + n * k + n)) for k in range(16)])
-        ts(A("ai", a, b), A("p3", a, b), col(C3681), None, ALU.add)
-        tt(A("di", a, b), A("ai", a, b), A("p3", 192 + a, 192 + b), ALU.subtract)
-        ts(A("am", a, b), A("ai", a, b), 4095, None, ALU.bitwise_and)
-        ts(A("dj", a, b), A("di", a, b), 15, None, ALU.bitwise_and)
-        cp(A("aoff", 192 * par + a, 192 * par + b), A("am", a, b))
-        ts(A("eq", a, b), A("dj", a, b), col(LANE), None, ALU.is_equal)
+        par, n, s0 = t % 2, b - a, 192 * t
+        h0, m0, nb = 3072 * par, 1536 * par, n // 4
+        cut = [c for c in cfg["hcut"][t] if a <= c <= b]
+        for c, d in zip(cut, cut[1:]):
+            gather("v" if (t, c) in cfg["hg_v"] else "s", A("hp", h0 + 16 * c, h0 + 16 * d), A("Hs", 64, 64 + CH), A("coff", s0 + c, s0 + d))
+        for q in range(4):
+            mrun([("matmul", A(pz, 8 * j, 8 * j + 8, 1, 32 * q, 32 * q + 16), A("hp", h0 + 16 * u, h0 + 16 * u + 16),
+                   A("xm", m0 + u, m0 + 1536, 192), True, True) for j, u in enumerate(range(a + q * nb, a + q * nb + nb))])
+        if (t, a) in cfg["zc_s"]:
+            act(A("zc", 2 * a, 2 * b), A(pz, 0, 2 * n), ACT.Identity, col(CA), None)
+        else:
+            ts(A("zc", 2 * a, 2 * b), A(pz, 0, 2 * n), -ZC, None, ALU.add)
+        d, y = A(pz, 2 * n, 3 * n), A("py", a, b)
+        back = []
+        for q in range(4):
+            for g in range(8):
+                h, m = 1 - g % 2, 32 - 16 * (g % 2)
+                back.append(("matmul", A("py", a + q * nb, a + q * nb + nb, 1, 32 * (g // 2), 32 * (g // 2) + (m if cfg["half"] else 32)),
+                             A("Yy", 32 * q + 16 - 16 * h, 32 * q + 16 - 16 * h + (m if cfg["half"] else 32)),
+                             A("zc", 2 * a + (g ^ 1), 2 * b, 8), h == 1, h == 0))
+        mrun(back)
+        if (t, a) in cfg["zf_s"]:
+            act(A("zf", a, b), y, ACT.Copy)
+        else:
+            cp(A("zf", a, b), y)
+        mm(d, [(A("Yy", 16, 144), A("zf", a, b)), (A("Yd", 0, 128), A("zf", a, b))])
+        if (t, a) in cfg["dr_s"]:
+            act(A("df", a, b), d, ACT.Identity, A("mg", 0, 1), None)
+            act(A("dr", a, b), A("df", a, b), ACT.Identity, A("mg", 1, 2), None)
+        else:
+            ts(A("dr", a, b), d, 1.5 * 2.0 ** 27, 1.5 * 2.0 ** 27, ALU.add, ALU.subtract)
+        tt(A("eq", a, b), d, A("dr", a, b), ALU.is_equal)
+        ao = A("aoff", 192 * par + a, 192 * par + b)
+        if (t, a) in cfg["am_s"]:
+            act(A("at", a, b), y, ACT.Identity, A("mg", 2, 3), 37.0)
+            r = A("py", 256 + a, 256 + b)
+            mm(r, [(A("Y37", 0, 128), A("zf", a, b)), (A("nI", 0, 128), A("at", a, b))])
+            ts(ao, r, A("mg", 3, 4), None, ALU.add)
+        else:
+            ts(A("ai", a, b), A("zf", a, b) if cfg["ai_zf"] else y, 37.0, col(CB), ALU.mult, ALU.add)
+            ts(A("am", a, b), A("ai", a, b), 4095, None, ALU.bitwise_and)
+            cp(ao, A("am", a, b))
 
-    def phase_m(t, a, b):
+    def phase_m(t, a, b, pz):
         ph[0] += 1
-        par, n = t % 2, b - a
+        par, n, s0 = t % 2, b - a, 192 * t
         hu = a == 0 and t < STEPS - 1
-        vp = A("p0", 384, 384 + n)
+        xb = "xs" if t else "snd"
+        vp, sel, dq = A(pz, 3 * n, 4 * n), A(pz, 256, 320), (320 if n == 64 else 256)
         if hu:
-            mm(A("p4", 320, 384), [(A("Um", 0, 128), A("eq", 0, 64))])
-        mm(vp, [(A("S0", 0, 128), A("xs", 384 * par + a, 384 * par + b)), (A("S0", 128, 256), A("ge", 192 * par + a, 192 * par + b)),
-                (A("Um", 128, 256), A("eq", a, b))])
+            mm(sel, [(A("Um", 0, 128), A("eq", 0, 64))])
+        mm(vp, [(A("S0", 0, 128), A(xb, s0 + a, s0 + b)), (A("S0", 128, 256), A("ge", s0 + a, s0 + b)), (A("Um", 128, 256), A("eq", a, b))])
         if hu:
-            tt(A("tmp", 0, 64), A("p4", 320, 384), A("cj", 192 * par, 192 * par + 64), ALU.min)
-        ts(A("src", 64 + a, 64 + b), vp, 0.0, col(CE), ALU.max, ALU.mult)
-        if hu:
-            ts(A("src", 0, 64), A("tmp", 0, 64), 0.0, None, ALU.max)
-        s0 = 0 if hu else 64 + a
-        d0, d1 = s0 // 16, (64 + b) // 16
-        mm(A("p4", 448 + d0, 448 + d1), [(A("Y1", 15 - c, 143 - c), A("src", s0 + c, 64 + b, 16)) for c in range(16)])
-        kinds = ((0, 1) if hu else (1,)) if a == 0 else ()
-        for k in kinds:
-            for j in range(4):
-                r0 = 160 * k + 8 * j * (j + 1)
-                mm(A("p4", r0, r0 + 16 * j + 16), [(ident, A("Mk", 48 - 16 * j, 64)), (A("B1", 0, 128), A("src", 64 * k, 64 * k + 16 * j + 16))])
-        cp(A("doff", d0, d1), A("p4", 448 + d0, 448 + d1))
-        ts(A("woff", 192 * par + a, 192 * par + b), IND(A("ptr", 64, 192), A("doff", 4 + a // 16, 4 + b // 16)), col(LANE), None, ALU.add)
+            tt(A("src", 0, 64), sel, A("cj", s0, s0 + 64), ALU.min)
+        if (t, a) in cfg["src_s"]:
+            act(A("src", 64 + a, 64 + b), vp, ACT.Relu, None, col(CE))
+        else:
+            ts(A("src", 64 + a, 64 + b), vp, 0.0, col(CE), ALU.max, ALU.mult)
+        r0 = 0 if hu else 64 + a
+        d0, d1 = r0 // 16, (64 + b) // 16
+        w = 64 + b - r0
+        wo = A("woff", 192 * par + a, 192 * par + b)
+        rp = 384 if a == 0 else 2 * n - r0
+
+        def lanes(name, c0):
+            return [(A(name, c0, c0 + w), A("B1", 0, 128), A("src", r0, 64 + b))] + ([(A(name, c0, c0 + 64), A("Us", 0, 128), A("eq", 0, 64))] if hu else [])
+        rb = cfg["rep_b"] if a == 0 else pz
+        if a == 0 or t == 0:
+            mrun(group(lanes(rb, rp + r0)))
+        if a == 0 or (t, a) in cfg["dscan"]:
+            m0 = 128 if a == 0 else 2 * n
+            mk = A(pz, m0, m0 + w)
+            mrun(group(lanes(pz, m0) + [(mk, ident, A("Mk", 0, w))]))
+            o, c = A("sd", r0, r0 + w), A("Cr", 0, w)
+            add("v", [("tensor_tensor_scan", o, c, mk, 0.0, ALU.min, ALU.max)], vcost(o, [mk]))
+            dp = A("sd", r0 + 15, r0 + w, 16)
+            ts(A("doff", d0, d1), dp, 1.0 / 4096, None, ALU.mult)
+        elif t > 0:
+            dp = A(pz, dq, dq + d1 - d0)
+            mm(dp, [(A("Y1", 15 - c, 143 - c), A("src", r0 + c, 64 + b, 16)) for c in range(16)])
+            cp(A("doff", d0, d1), dp)
+        if t == 0:
+            ts(wo, A(rb, rp + 64 + a, rp + 64 + b), 16.0 / 4096, col(LANE), ALU.mult, ALU.add)
+        else:
+            ts(wo, IND(A("ptr", 64, 192), A("doff", 4 + a // 16, 4 + b // 16)), col(LANE), None, ALU.add)
         if a == 0:
-            act(A("vdb", d0, 8), A("p4", 448 + d0, 456), ACT.Identity, None, 4096.0)
-            act(A("tb", SEG * d0, 8 * SEG, SEG), A("p4", 448 + d0, 456), ACT.Identity, 64.0, None)
-            for k in kinds:
+            act(A("tb", SEG * d0 + SEG - 1, 8 * SEG, SEG), dp, ACT.Identity, 64.0, 1.0 / 4096)
+            for k in ((0, 1) if hu else (1,)):
                 for j in range(4):
-                    r0, q = 160 * k + 8 * j * (j + 1), 4 * k + j
-                    act(A("tb", SEG * q + 1, SEG * q + 17 + 16 * j), A("p4", r0, r0 + 16 * j + 16), ACT.Abs, A("vdb", q, q + 1), -4096.0)
-            o, c, d = A("so", SEG * d0, 8 * SEG), A("Cs", SEG * d0, 8 * SEG), A("tb", SEG * d0, 8 * SEG)
-            add("v", ("tensor_tensor_scan", o, c, d, 0.0, ALU.max, ALU.min), [c, d], [o], vcost(o, [c]))
-            cp(A("soff", d0, 8), A("so", SEG * d0 + SEG - 1, 8 * SEG, SEG))
+                    q = 4 * k + j
+                    act(A("tb", SEG * q, SEG * q + 16 + 16 * j), A(rb, 384 + 64 * k, 400 + 64 * k + 16 * j), ACT.Abs,
+                        A("sd", 16 * q + 15, 16 * q + 16), -1.0)
+                o, c, d = A("so", 4 * SEG * k, 4 * SEG * (k + 1)), A("Cs", 0, 4 * SEG), A("tb", 4 * SEG * k, 4 * SEG * (k + 1))
+                add("v", [("tensor_tensor_scan", o, c, d, 0.0, ALU.add, ALU.min)], vcost(o, [c]))
+                cp(A("soff", 4 * k, 4 * k + 4), A("so", 4 * SEG * k + SEG - 1, 4 * SEG * (k + 1), SEG))
         if hu:
             gather("s", A("hold", 0, 64), A("Hs", 64, 64 + CH), A("doff", 0, 4))
-            mm(A("p4", 384, 448), [(lane_in(0), comc(t, t, U * (t % 3), 64)), (A("Sh", 128, 256), A("hold", 0, 64))])
-            act(A("hnew", 0, 64), A("p4", 384, 448), ACT.Copy)
+            mm(A("py", 192, 256), [(lane_in(0), comc(t, t, U * (t % 3), 64)), (A("Sh", 128, 256), A("hold", 0, 64))])
+            act(A("hnew", 0, 64), A("py", 192, 256), ACT.Copy)
 
     def phase_u(t):
         ph[0] += 1
@@ -439,71 +560,74 @@ def build(cfg):
         cp(IND(A("ptr", 0, 192), A("soff", 4, 8)), A("pval", 64 * t, 64 * t + 64))
 
     def phase_r(t):
-        par = t % 2
+        par, s0 = t % 2, 192 * t
         g0 = 3072 * par
         win = A("Wt", 0, 2048 + 1024 * t) if t else A("W0", 0, 2048)
-        bi = 192 * (t - 1)
-        qs = []
-        for (a, b) in cfg["rch"][t]:
+        last = t == STEPS - 1
+
+        def carry(a, b):
+            return A("Bi", 192 * (t - 1) + (a + U) % S, 192 * (t - 1) + (a + U) % S + b - a)
+        for n, c in enumerate((0, 64, 128)):
             ph[0] += 1
-            lg = A("p5", 0, 64) if a == 0 else A("p7", a - 64, b - 64)
-            for c in range(a, b, 64):
-                gather("v" if (t, c) in cfg["pg_v"] else "s", A("pg", g0 + 16 * c, g0 + 16 * c + 1024), A("Ps", 0, CP),
-                       A("aoff", 192 * par + c, 192 * par + c + 64), 1.0 / 32)
-                tt(A("pw", g0 + 16 * c, g0 + 16 * c + 1024), IND(win, A("woff", 192 * par + c, 192 * par + c + 64)),
-                   A("pg", g0 + 16 * c, g0 + 16 * c + 1024), ALU.mult)
-            for c in range(a, b, 64):
-                l2 = A(lg["b"], lg["c0"] + c - a, lg["c0"] + c - a + 64)
-                mm(l2, [(negI, A("pw", g0 + 16 * c + k, g0 + 16 * c + 1024, 16)) for k in range(16)]
-                   + ([(negS, A("Bi", bi + c, bi + c + 64))] if t else []))
-            act(A("ys", a, b), lg, ACT.Sigmoid, None, -32.0)
-            if a == 0:
-                mm(A("p5", 64, 128), [(ident, A("oh", 192 * t, 192 * t + 64)), (negI, A("ys", 0, 64))])
-                gather("s", A("wg", 0, 1024), win, A("woff", 192 * par, 192 * par + 64))
-                for k in range(16):
-                    tt(A("pd", k, 1024, 16), A("pg", g0 + k, g0 + 1024, 16), A("p5", 64, 128), ALU.mult)
-                tt(A("Wt", 2048 + 1024 * t, 3072 + 1024 * t), A("wg", 0, 1024), A("pd", 0, 1024), ALU.add)
-                qs.append((a, b))
-                continue
-            qs = [(a, b)] + qs
-            for (qa, qb) in qs:
-                mm(A("p7", 128 + qa, 128 + qb), [(ident, A("oh", 192 * t + qa, 192 * t + qb))]
-                   + ([(halfI, A("Bi", bi + qa, bi + qb))] if t else []) + [(negI, A("ys", qa, qb))])
-            last = t == STEPS - 1
-            if last and len(qs) == 2 and qs[1][1] == qs[0][0]:
-                qs = [(qs[1][0], qs[0][1])]
-            lo, hi = min(q[0] for q in qs), max(q[1] for q in qs)
-            if hi - lo == sum(q[1] - q[0] for q in qs):
-                act(A("Bo", 192 * t + lo, 192 * t + hi), A("p7", 128 + lo, 128 + hi), ACT.Copy)
+            pl = "pl%d" % n
+            lg = A(pl, 0, 64)
+            wof = A("woff", 192 * par + c, 192 * par + c + 64)
+            for u in range(c, c + 64, cfg["pcut"]):
+                gather("v" if (t, u) in cfg["pg_v"] else "s", A("pg", g0 + 16 * u, g0 + 16 * (u + cfg["pcut"])), A("Ps", 0, CP),
+                       A("aoff", 192 * par + u, 192 * par + u + cfg["pcut"]), 1.0 / 32)
+            for u in range(c, c + 64, cfg["wcut"]):
+                tt(A("pw", g0 + 16 * u, g0 + 16 * (u + cfg["wcut"])), IND(win, A("woff", 192 * par + u, 192 * par + u + cfg["wcut"])),
+                   A("pg", g0 + 16 * u, g0 + 16 * (u + cfg["wcut"])), ALU.mult)
+            if (t, c) in cfg["rscan"]:
+                o, z, w = A("wo", 0, 1024), A("Cz", 0, 1024), A("pw", g0 + 16 * c, g0 + 16 * c + 1024)
+                add("v", [("tensor_tensor_scan", o, z, w, 0.0, ALU.mult, ALU.add)], vcost(o, [w]))
+                mm(lg, ([(negS, carry(c, c + 64))] if t else []) + [(negI, A("wo", 15, 1024, 16))])
             else:
-                for (qa, qb) in qs:
-                    act(A("Bo", 192 * t + qa, 192 * t + qb), A("p7", 128 + qa, 128 + qb), ACT.Copy)
-            for (qa, qb) in qs:
-                da = qa if last else (qa - U) % S
-                hop = -HOP * (STEPS - 1) if last else HOP
-                rem(A("Bo", 192 * t + qa, 192 * t + qb), [(A("Bi", 192 * t + da, 192 * t + da + qb - qa), hop)], 512 * (qb - qa))
-                if last:
-                    dma("sync", EXT("yb", qa, qb), A("Bi", 192 * t + qa, 192 * t + qb), 512 * (qb - qa))
-            qs = []
+                mm(lg, [(negI, A("pw", g0 + 16 * c + k, g0 + 16 * c + 1024, 16)) for k in range(16)] + ([(negS, carry(c, c + 64))] if t else []))
+            act(A("ys", c, c + 64), lg, ACT.Sigmoid, None, -32.0)
+            if c == 0:
+                er = A(pl, 64, 128)
+                mm(er, [(ident, A("oh", s0, s0 + 64)), (negI, A("ys", 0, 64))])
+                for k0 in range(0, 16, 4):
+                    cs = [("tensor_tensor", A("pd", k, 1024, 16), A("pg", g0 + k, g0 + 1024, 16), er, ALU.mult) for k in range(k0, k0 + 4)]
+                    add("v", cs, sum(vcost(x[1], [x[2], x[3]], True) for x in cs))
+                tt(A("Wt", 2048 + 1024 * t, 3072 + 1024 * t), IND(win, wof), A("pd", 0, 1024), ALU.add)
+                continue
+            a, b = (0, 128) if c == 64 else (128, 192)
+            mm(A("pq", a, b), [(ident, A("oh", s0 + a, s0 + b))] + ([(halfI, carry(a, b))] if t else []))
+            tt(A("Bo", s0 + a, s0 + b), A("pq", a, b), A("ys", a, b), ALU.subtract)
+            rem(A("Bo", s0 + a, s0 + b), [(A("Bi", s0 + a, s0 + b), -HOP * (STEPS - 1) if last else HOP)], 512 * (b - a))
+            if last:
+                dma("sync", [(EXT("yb", a, b), A("Bi", s0 + a, s0 + b))], 512 * (b - a))
 
     phase_a(0)
     for t in range(STEPS):
-        ch = cfg["ich"][t]
-        for (a, b) in ch:
-            phase_h(t, a, b)
-        if t + 1 < STEPS and t not in cfg["a_late"]:
-            phase_a(t + 1)
-        for (a, b) in ch:
-            phase_m(t, a, b)
-        if t + 1 < STEPS and t in cfg["a_late"]:
-            phase_a(t + 1)
+        ch = list(zip(cfg["ich"][t], ("pz0", "pz1")))
+
+        def ahead(place):
+            for s in range(1, STEPS):
+                if cfg["a_at"][s] == (t, place):
+                    phase_a(s)
+        ahead(0)
+        for ((a, b), pz) in ch:
+            phase_h(t, a, b, pz)
+        ahead(1)
+        for ((a, b), pz) in ch:
+            phase_m(t, a, b, pz)
+        ahead(2)
         phase_u(t)
         phase_r(t)
     ts(A("foff", 0, 128), A("ptr", 64, 192), col(LANE), None, ALU.add)
     for n, (e, a, b) in enumerate(cfg["fin"]):
         gather(e, A("wo", 16 * a, 16 * b), A("Wt", 0, 6144), A("foff", a, b))
-        dma("sync" if e == "v" else "s", EXT("yw", 16 * a, 16 * b), A("wo", 16 * a, 16 * b), 8192 * (b - a))
+        dma("sync" if e == "v" else "s", [(EXT("yw", 16 * a, 16 * b), A("wo", 16 * a, 16 * b))], 8192 * (b - a))
     return ops
+
+
+def landing(o, issued, pipe, cfg):
+    first, own = issued + (cfg["RF"] if o["kind"] == "rem" else cfg["DF"]) - 500.0, o["bytes"] / cfg["BW"]
+    after = max(pipe, first) + own
+    return (min(after, first + 2 * own) if o["bytes"] < 200000 else after) + 500.0, after
 
 
 def replay(ops, order, cfg):
@@ -516,9 +640,9 @@ def replay(ops, order, cfg):
                 t = done[j] + wk
         d = free[o["eng"]] = t + o["dur"]
         if o["kind"] != "c":
-            pipe = max(pipe, d + (cfg["RF"] if o["kind"] == "rem" else cfg["DF"]) - 500.0) + o["bytes"] / cfg["BW"]
-            d = pipe + 500.0
-        done[i] = d
+            d, pipe = landing(o, d, pipe, cfg)
+        done[i] = o["t1"] = d
+        o["t0"] = t
         end = max(end, d)
     return end
 
@@ -546,6 +670,131 @@ def search(cfg, rounds, seed=0):
         if sum(x / y for x, y in zip(v, v0)) <= sum(x / y for x, y in zip(cv, v0)):
             cur, cv = b, v
     return cur, cv, v0
+
+
+def shuttle(opss, cfgs, order, rounds, seed=0):
+    n = len(opss[0])
+    rnd = np.random.RandomState(seed)
+    keys = sorted({o["key"] for o in opss[0]})
+    norm = [replay(o, order, c) for o, c in zip(opss, cfgs)]
+    succ = [[] for i in range(n)]
+    for o in opss[0]:
+        for j in o["sem"] | o["ord"]:
+            succ[j].append(o["i"])
+    pred = [sorted(o["sem"] | o["ord"]) for o in opss[0]]
+
+    def pack(ops, prio, before, after, gap):
+        left = [len(x) for x in before]
+        heap = [(prio[i], i) for i in range(n) if not left[i]]
+        busy = {}
+        start = [0.0] * n
+        while heap:
+            heap.sort(reverse=True)
+            i = heap.pop()[1]
+            t, dur = 0.0, ops[i]["dur"]
+            for j in before[i]:
+                t = max(t, start[j] + ops[j]["dur"] + gap(j, i))
+            line = busy.setdefault(ops[i]["eng"], [])
+            p = len(line)
+            while p and line[p - 1][1] > t:
+                p -= 1
+            while p < len(line) and line[p][0] < t + dur:
+                t = max(t, line[p][1])
+                p += 1
+            line.insert(p, (t, t + dur))
+            start[i] = t
+            for j in after[i]:
+                left[j] -= 1
+                if not left[j]:
+                    heap.append((prio[j], j))
+        return start
+
+    def value(od):
+        return sum(replay(o, od, c) / x for o, c, x in zip(opss, cfgs, norm)) / len(cfgs)
+    cur = best = value(order)
+    keep = order
+    for r in range(rounds):
+        v = int(rnd.randint(len(cfgs)))
+        ops, wk = opss[v], cfgs[v]["WK"]
+        replay(ops, order, cfgs[v])
+        lat = [o["t1"] - o["t0"] - o["dur"] for o in ops]
+        push = {keys[int(rnd.randint(len(keys)))]: float(rnd.normal()) * 1500.0 for s in range(1 + int(rnd.randint(6)))}
+        ends = [-(o["t1"] + push.get(o["key"], 0.0)) for o in ops]
+        tail = [0.0 if succ[i] else lat[i] for i in range(n)]
+        back = pack([dict(eng=o["eng"], dur=o["dur"] + tail[o["i"]]) for o in ops], ends, succ, pred,
+                    lambda j, i: wk + lat[i] if i in ops[j]["sem"] else 0.0)
+        fore = pack(ops, [-(back[i] + ops[i]["dur"] + tail[i]) for i in range(n)], pred, succ,
+                    lambda j, i: wk + lat[j] if j in ops[i]["sem"] else 0.0)
+        od = sorted(range(n), key=lambda i: (fore[i], i))
+        x = value(od)
+        if x <= cur + cfgs[0]["heat2"] * (1 - r / rounds) * rnd.exponential():
+            order, cur = od, x
+            if x < best:
+                best, keep = x, od
+    return keep, [replay(o, keep, c) for o, c in zip(opss, cfgs)]
+
+
+def polish(opss, cfgs, order, rounds, seed=0):
+    ops = opss[0]
+    n = len(ops)
+    pred = [sorted(o["sem"] | o["ord"]) for o in ops]
+    succ = [[] for o in ops]
+    for i in range(n):
+        for j in pred[i]:
+            succ[j].append(i)
+    engs = sorted({o["eng"] for o in ops})
+    eng = [engs.index(o["eng"]) for o in ops]
+    sems = [sorted(o["sem"]) for o in ops]
+    durs = [[o["dur"] for o in x] for x in opss]
+    moving = [o["kind"] != "c" for o in ops]
+    rnd = np.random.RandomState(seed)
+
+    def run(od, v):
+        free, done, start, pipe, wk, dur = [0.0] * len(engs), [0.0] * n, [0.0] * n, 0.0, cfgs[v]["WK"], durs[v]
+        for i in od:
+            t = free[eng[i]]
+            for j in sems[i]:
+                if done[j] + wk > t:
+                    t = done[j] + wk
+            start[i] = t
+            d = free[eng[i]] = t + dur[i]
+            if moving[i]:
+                d, pipe = landing(ops[i], d, pipe, cfgs[v])
+            done[i] = d
+        return max(done), start, sum(done) / n
+    norm = [run(order, v)[0] for v in range(len(cfgs))]
+    mix, heat = cfgs[0]["mix"], cfgs[0]["heat"]
+
+    def value(od):
+        x = [run(od, v) for v in range(len(cfgs))]
+        return sum((a[0] + mix * a[2]) / b for a, b in zip(x, norm)) / len(cfgs)
+    cur = best = value(order)
+    keep = order
+    for r in range(rounds):
+        if r % 200 == 0:
+            start = run(order, (r // 200) % len(cfgs))[1]
+            rank = {i: p for p, i in enumerate(order)}
+            order = sorted(order, key=lambda i: (start[i], rank[i]))
+            cur = value(order)
+        p = int(rnd.randint(n))
+        i = order[p]
+        step, hops, q, stop = (1 if rnd.rand() < 0.5 else -1), 1 + int(rnd.geometric(0.4)) - 1, p, False
+        bar = set(succ[i] if step > 0 else pred[i])
+        while hops and not stop:
+            q += step
+            stop = q < 0 or q >= n or order[q] in bar
+            if not stop and eng[order[q]] == eng[i]:
+                hops -= 1
+        if stop:
+            continue
+        od = order[:p] + order[p + 1:]
+        od.insert(q, i)
+        v = value(od)
+        if v <= cur + heat * (1 - r / rounds) * rnd.exponential():
+            order, cur = od, v
+            if v < best:
+                best, keep = v, od
+    return keep, [run(keep, v)[0] for v in range(len(cfgs))]
 
 
 def priorities(ops, cfg):
@@ -590,9 +839,7 @@ def schedule(ops, cfg, base, bias):
         free[e] = o["t0"] + o["dur"]
         done = free[e]
         if o["kind"] != "c":
-            fixed = cfg["RF"] if o["kind"] == "rem" else cfg["DF"]
-            pipe[0] = max(pipe[0], done + fixed - 500.0) + o["bytes"] / cfg["BW"]
-            done = pipe[0] + 500.0
+            done, pipe[0] = landing(o, done, pipe[0], cfg)
         o["t1"] = done
         end = max(end, done)
         ready[e].remove(i)
@@ -607,8 +854,13 @@ def schedule(ops, cfg, base, bias):
 
 def plan(cfg):
     bias = search(cfg, cfg["rounds"])[0]
-    ops = build(cfg)
-    order, end = schedule(ops, cfg, priorities(ops, cfg), bias)
+    cfgs = [dict(cfg, **v) for v in VARIANTS]
+    opss = [build(c) for c in cfgs]
+    ops = opss[0]
+    order = schedule(ops, cfg, priorities(ops, cfg), bias)[0]
+    order = shuttle(opss, cfgs, order, cfg["shuttle"])[0]
+    order, end = polish(opss, cfgs, order, cfg["polish"])
+    replay(ops, order, cfg)
     need = set()
     for o in ops:
         need |= o["sem"]
@@ -634,7 +886,7 @@ def plan(cfg):
             o["inc"] = i in need
             name = "e_" + o["eng"]
             if o["inc"]:
-                count[name] = count.get(name, 0) + 1
+                count[name] = count.get(name, 0) + (1 if o["eng"] == "pe" else len(o["calls"]))
             o["sig"] = (name, count.get(name, 0))
         else:
             o["sig"] = (o["tok"], 1)
@@ -665,9 +917,9 @@ def rank_program(g, core, T, topo):
     full = {}
     for o in ops:
         if o["kind"] == "dma":
-            full[o["tok"]] = 16
+            full[o["tok"]] = 16 * len(o["calls"])
         elif o["kind"] == "rem":
-            hops = [d[1] for d in o["call"][2]]
+            hops = [d[1] for d in o["calls"][0][2]]
             full[o["tok"]] = sum(bits(mask_of(cores[(rank - h) % NR], hops)) for h in hops)
     sent = 0
     outs = []
@@ -676,51 +928,51 @@ def rank_program(g, core, T, topo):
         q = queue[o["eng"]]
         for name, val in o["waits"]:
             q.wait_ge(T.sem[name], full.get(name, val))
-        c = o["call"]
-        x = [real(T, a) if isinstance(a, dict) else a for a in c[1:]]
-        if c[0] == "remote":
-            hops = [d[1] for d in c[2]]
-            m = mask_of(core, hops)
-            to = [topo.addr(cores[(rank + h) % NR]) for h in hops]
-            if len(hops) == 1:
-                g.remote_dma(real(T, c[2][0][0]), x[0], T.sem[o["tok"]], T.sem.loc, to[0][1], to[0][0], m)
+        for c in o["calls"]:
+            x = [real(T, a) if isinstance(a, dict) else a for a in c[1:]]
+            if c[0] == "remote":
+                hops = [d[1] for d in c[2]]
+                m = mask_of(core, hops)
+                to = [topo.addr(cores[(rank + h) % NR]) for h in hops]
+                if len(hops) == 1:
+                    g.remote_dma(real(T, c[2][0][0]), x[0], T.sem[o["tok"]], T.sem.loc, to[0][1], to[0][0], m)
+                else:
+                    g.remote_dma_fused([RemoteDMATransfer(dst_ids=[DstId(rid=a[0], pnc=a[1]) for a in to], dma_engine_mask=m,
+                                                          remote_sem=T.sem[o["tok"]], srcs=[x[0]], dsts=[real(T, d[0]) for d in c[2]])],
+                                       local_sem=T.sem.loc)
+                sent += bits(m)
+                continue
+            if c[0] == "dma_start":
+                q.dma_start(x[0], x[1]).then_inc(T.sem[o["tok"]], 16)
+                if "ext" in c[1]:
+                    outs.append(o)
+                continue
+            if c[0] == "activation":
+                kw = {}
+                if x[3] is not None:
+                    kw["bias"] = x[3]
+                if x[4] is not None:
+                    kw["scale"] = x[4]
+                ins = q.activation(x[0], x[1], x[2], **kw)
+            elif c[0] == "iota":
+                if SCRATCH[c[1]["b"]][2] == "int32":
+                    ins = q.iota(*x)
+                else:
+                    ins = q.iota(*x, allow_small_or_imprecise_dtypes=True)
+            elif c[0] == "matmul":
+                ins = q.matmul(*x)
+            elif c[0] == "tensor_copy":
+                ins = q.tensor_copy(*x)
+            elif c[0] == "tensor_scalar":
+                ins = q.tensor_scalar(*x)
+            elif c[0] == "tensor_tensor":
+                ins = q.tensor_tensor(*x)
+            elif c[0] == "tensor_tensor_scan":
+                ins = q.tensor_tensor_scan(*x)
             else:
-                g.remote_dma_fused([RemoteDMATransfer(dst_ids=[DstId(rid=a[0], pnc=a[1]) for a in to], dma_engine_mask=m,
-                                                      remote_sem=T.sem[o["tok"]], srcs=[x[0]], dsts=[real(T, d[0]) for d in c[2]])],
-                                   local_sem=T.sem.loc)
-            sent += bits(m)
-            continue
-        if c[0] == "dma_start":
-            q.dma_start(x[0], x[1]).then_inc(T.sem[o["tok"]], 16)
-            if "ext" in c[1]:
-                outs.append(o)
-            continue
-        if c[0] == "activation":
-            kw = {}
-            if x[3] is not None:
-                kw["bias"] = x[3]
-            if x[4] is not None:
-                kw["scale"] = x[4]
-            ins = q.activation(x[0], x[1], x[2], **kw)
-        elif c[0] == "iota":
-            if SCRATCH[c[1]["b"]][2] == "int32":
-                ins = q.iota(*x)
-            else:
-                ins = q.iota(*x, allow_small_or_imprecise_dtypes=True)
-        elif c[0] == "matmul":
-            ins = q.matmul(*x)
-        elif c[0] == "tensor_copy":
-            ins = q.tensor_copy(*x)
-        elif c[0] == "tensor_scalar":
-            ins = q.tensor_scalar(*x)
-        elif c[0] == "tensor_tensor":
-            ins = q.tensor_tensor(*x)
-        elif c[0] == "tensor_tensor_scan":
-            ins = q.tensor_tensor_scan(*x)
-        else:
-            ins = q.memset(*x)
-        if o["inc"]:
-            ins.then_inc(T.sem["e_" + o["eng"]], 1)
+                ins = q.memset(*x)
+            if o["inc"] and (o["eng"] != "pe" or c is o["calls"][-1]):
+                ins.then_inc(T.sem["e_" + o["eng"]], 1)
     g.wait_ge(T.sem.loc, sent)
     for o in outs:
         queue[o["eng"]].wait_ge(T.sem[o["tok"]], 16)

@@ -4,119 +4,57 @@ from concourse.mybir import AluOpType, ActivationFunctionType
 
 S, U, CH, CP, STEPS, HOP, NR = 192, 64, 2048, 4096, 4, 3, 8
 SEG = 65
-BIG = 1.0e6
+BIG = 30000.0
 ZC = 1800.0
+TOP = 786432.0
 
+
+def sb(n, dtype):
+    return ("sbuf", [128, n], dtype)
+
+
+BF, HF, FL, IN, UI = "bfloat16", "float16", "float32", "int32", "uint16"
 SCRATCH = {
-    "snd": ("sbuf", [128, 240], "bfloat16"),
-    "lnd": ("sbuf", [128, 3 * 240], "bfloat16"),
-    "com": ("sbuf", [128, 4 * 768], "bfloat16"),
-    "kl": ("sbuf", [128, 8], "int32"),
-    "kli": ("sbuf", [128, 4], "int32"),
-    "klf": ("sbuf", [128, 4], "float32"),
-    "Hs": ("sbuf", [128, 64 + CH], "bfloat16"),
-    "Ps": ("sbuf", [128, CP], "bfloat16"),
-    "W0": ("sbuf", [128, 2048], "bfloat16"),
-    "Wt": ("sbuf", [128, 2048 + 4096], "float32"),
-    "ptr": ("sbuf", [128, 64 + 128], "float32"),
-    "pval": ("sbuf", [128, 256], "float32"),
-    "Dm": ("sbuf", [128, 144], "bfloat16"),
-    "Pm": ("sbuf", [128, 128], "bfloat16"),
-    "Em": ("sbuf", [128, 144], "bfloat16"),
-    "Gi": ("sbuf", [128, 128], "bfloat16"),
-    "Rw": ("sbuf", [128, 64], "float32"),
-    "Ix": ("sbuf", [128, 4 * SEG], "float32"),
-    "pi": ("sbuf", [128, 2], "int32"),
-    "col": ("sbuf", [128, 16], "float32"),
-    "pk": ("sbuf", [128, 16], "bfloat16"),
-    "pf": ("sbuf", [128, 8], "float32"),
-    "mn": ("sbuf", [128, 128], "bfloat16"),
-    "KL": ("sbuf", [128, 4 * 128], "bfloat16"),
-    "Lr": ("sbuf", [128, 256], "bfloat16"),
-    "Sh": ("sbuf", [128, 4 * 128], "bfloat16"),
-    "Iy": ("sbuf", [128, 128], "bfloat16"),
-    "Mk": ("sbuf", [128, 128], "bfloat16"),
-    "Us": ("sbuf", [128, 128], "bfloat16"),
-    "Cr": ("sbuf", [128, 128], "float32"),
-    "sd": ("sbuf", [128, 256], "float32"),
-    "zf": ("sbuf", [128, 192], "float16"),
-    "Zw": ("sbuf", [128, 144], "bfloat16"),
-    "Sr": ("sbuf", [128, 128], "bfloat16"),
-    "Yy": ("sbuf", [128, 144], "float16"),
-    "Yd": ("sbuf", [128, 144], "float16"),
-    "Y1": ("sbuf", [128, 144], "float16"),
-    "B1": ("sbuf", [128, 128], "float16"),
-    "ut": ("sbuf", [128, 3 * 128], "bfloat16"),
-    "Um": ("sbuf", [128, 2 * 128], "bfloat16"),
-    "S0": ("sbuf", [128, 2 * 128], "bfloat16"),
-    "F32": ("sbuf", [128, 3 * 128], "float32"),
-    "Cs": ("sbuf", [128, 4 * SEG], "float32"),
-    "tb": ("sbuf", [128, 8 * SEG], "float32"),
-    "so": ("sbuf", [128, 8 * SEG], "float32"),
-    "xs": ("sbuf", [128, 4 * 192], "bfloat16"),
-    "xm": ("sbuf", [128, 2 * 1536], "bfloat16"),
-    "ge": ("sbuf", [128, 4 * 192], "bfloat16"),
-    "oh": ("sbuf", [128, 4 * 192], "bfloat16"),
-    "ci": ("sbuf", [128, 192], "int32"),
-    "cj": ("sbuf", [128, 4 * 192], "int32"),
-    "ct": ("sbuf", [128, 192], "bfloat16"),
-    "mg": ("sbuf", [128, 8], "float32"),
-    "df": ("sbuf", [128, 192], "float32"),
-    "Cz": ("sbuf", [128, 1024], "bfloat16"),
-    "nI": ("sbuf", [128, 128], "bfloat16"),
-    "Y37": ("sbuf", [128, 128], "float16"),
-    "coff": ("sbuf", [128, 4 * 192], "uint16"),
-    "hp": ("sbuf", [128, 2 * 3072], "bfloat16"),
-    "zc": ("sbuf", [128, 384], "float16"),
-    "at": ("sbuf", [128, 192], "bfloat16"),
-    "ai": ("sbuf", [128, 192], "int32"),
-    "am": ("sbuf", [128, 192], "int32"),
-    "dr": ("sbuf", [128, 192], "bfloat16"),
-    "aoff": ("sbuf", [128, 2 * 192], "uint16"),
-    "eq": ("sbuf", [128, 192], "bfloat16"),
-    "tmp": ("sbuf", [128, 64], "float32"),
-    "src": ("sbuf", [128, 256], "float16"),
-    "vdb": ("sbuf", [128, 8], "float32"),
-    "doff": ("sbuf", [128, 16], "uint16"),
-    "soff": ("sbuf", [128, 8], "uint16"),
-    "woff": ("sbuf", [128, 2 * 192], "uint16"),
-    "foff": ("sbuf", [128, 128], "uint16"),
-    "hold": ("sbuf", [128, 64], "bfloat16"),
-    "hnew": ("sbuf", [128, 64], "bfloat16"),
-    "pg": ("sbuf", [128, 2 * 3072], "bfloat16"),
-    "pw": ("sbuf", [128, 2 * 3072], "float32"),
-    "pd": ("sbuf", [128, 1024], "float32"),
-    "ys": ("sbuf", [128, 192], "float32"),
-    "Bo": ("sbuf", [128, 4 * 192], "float32"),
-    "Bi": ("sbuf", [128, 4 * 192], "float32"),
-    "wo": ("sbuf", [128, 2048], "float32"),
-    "pa": ("psum", [128, 512], "float32"),
-    "pz0": ("psum", [128, 512], "float32"),
-    "pz1": ("psum", [128, 512], "float32"),
-    "py": ("psum", [128, 512], "float32"),
-    "pl0": ("psum", [128, 512], "float32"),
-    "pl1": ("psum", [128, 512], "float32"),
-    "pl2": ("psum", [128, 512], "float32"),
-    "pq": ("psum", [128, 512], "float32"),
+    "snd": sb(240, BF), "lnd": sb(3 * 240, BF), "com": sb(4 * 768, BF),
+    "kl": sb(8, IN), "kli": sb(4, IN), "klf": sb(4, FL),
+    "Hs": sb(CH + 128, BF), "Ps": sb(CP, BF), "W0": sb(2048, BF), "Wt": sb(2048 + 3072, FL),
+    "ptr": sb(CH + 128, FL), "pts": sb(CH + 128, FL), "pval": sb(256, FL),
+    "Dm": sb(144, BF), "Pm": sb(128, BF), "Em": sb(144, BF), "Gi": sb(128, BF), "Rw": sb(4, FL), "Ix": sb(4 * SEG, BF), "Iy": sb(128, BF),
+    "pi": sb(2, IN), "col": sb(16, FL), "Sm": sb(144, BF), "pf": sb(8, FL), "mn": sb(128, BF),
+    "KL": sb(4 * 128, BF), "Lr": sb(256, BF), "Sh": sb(4 * 128, BF), "Mk": sb(128, BF), "Us": sb(128, BF), "Cr": sb(128, FL),
+    "Zw": sb(144, BF), "Sr": sb(256, BF), "Yy": sb(144, HF), "Yd": sb(3 * 128, HF), "B1": sb(128, HF), "Y37": sb(128, HF), "nI": sb(128, BF),
+    "ut": sb(3 * 128, BF), "Um": sb(2 * 128, BF), "S0": sb(2 * 128, BF), "F32": sb(3 * 128, FL), "Cs": sb(4 * SEG, HF), "Cz": sb(1024, BF),
+    "xs": sb(4 * 192, BF), "xm": sb(2 * 1536, BF), "ge": sb(4 * 192, BF), "of": sb(4 * 192, FL),
+    "ci": sb(192, IN), "cj": sb(4 * 192, IN), "coff": sb(4 * 192, UI), "hp": sb(2 * 3072, BF),
+    "zc": sb(384, HF), "zf": sb(192, HF), "zq": sb(192, HF), "at": sb(192, BF), "ai": sb(192, IN), "am": sb(192, IN),
+    "aoff": sb(2 * 192, UI), "eq": sb(192, BF), "src": sb(256, HF), "sd": sb(256, FL), "tb": sb(8 * SEG, HF), "so": sb(8 * SEG, HF),
+    "doff": sb(16, UI), "soff": sb(8, UI), "woff": sb(2 * 192, UI), "foff": sb(256, UI), "hold": sb(64, BF), "hnew": sb(64, BF),
+    "pg": sb(2 * 3072, BF), "pw": sb(2 * 3072, FL), "ps": sb(1024, FL), "pd": sb(1040, FL), "wb": sb(2048, FL),
+    "ys": sb(4 * 192, FL), "Bo": sb(4 * 192, FL), "Bi": sb(4 * 192, FL), "wo": sb(2048, FL),
 }
+for _b in ("pa", "pz0", "pz1", "py", "pl0", "pl1", "pl2", "pq"):
+    SCRATCH[_b] = ("psum", [128, 512], "float32")
 NDMA = 40
 SEMAPHORES = ["e_pe", "e_v", "e_s", "e_g", "loc"] + ["d%d" % i for i in range(NDMA)]
 
+CUT = [0, 32, 64, 96, 128, 160, 192]
 CFG = {
-    "ich": [[(0, 64), (64, 192)]] * 4,
-    "hg_v": {(0, 32), (0, 128), (0, 160)},
-    "hcut": [[0, 32, 64, 96, 128, 160, 192]] * 4,
-    "pg_v": set(),
+    "hcut": [CUT] * 4, "pcut": [CUT] * 4, "wcut": [CUT] * 4,
+    "rch": [[(0, 64), (64, 128), (128, 192)]] * 4,
     "a_at": {1: (0, 1), 2: (0, 2), 3: (1, 2)},
-    "ge_s": {0}, "oh_s": set(), "dr_s": set(), "am_s": set(), "rscan": {(3, 128)}, "xm_s": 4, "DI": 200.0,
-    "zc_s": {(t, a) for t in range(4) for a in (0, 64)}, "zf_s": {(t, a) for t in range(4) for a in (0, 64)}, "src_s": set(),
-    "rep_b": "pz0", "pcut": 32, "wcut": 32, "dscan": set(), "half": True, "ai_zf": True,
-    "fin": [("v", 0, 32), ("s", 32, 64), ("v", 64, 96), ("s", 96, 128)],
-    "G": 1.5, "SC": 3.8, "CY": 1.0, "OV": 50.0, "PE": 0.42, "WK": 170.0, "look": 100.0,
-    "OV2": 10.0, "DF": 1700.0, "BW": 300.0, "RF": 2300.0, "rounds": 100, "shuttle": 4000, "polish": 100000, "bias": {}, "mix": 0.3, "heat": 0.0003, "heat2": 0.003,
+    "am_s": {(t, a) for t in range(4) for a in (0, 64)},
+    "xm_c": {0},
+    "rscan": {(1, 128), (3, 128)}, "gate": True, "early": [0, 0, 0, 0], "share": 40,
+    "fin": [0, 24, 56, 92, 128],
+    "G": 1.55, "SC": 4.2, "CY": 1.1, "OV": 50.0, "OS": 35.0, "MS": 40, "PE": 0.42, "WK": 140.0, "OV2": 0.0, "DI": 150.0, "DF": 1500.0, "BW": 370.0, "RF": 2000.0, "RC": 25.0, "RI": 500.0, "R1": 1000.0,
+    "tries": 5, "shuttle": 1200, "trim": 4000, "polish": 72000, "far": 1000.0, "pick": 0.02, "even": 0.0, "aim": 0.25, "mix": 0.25, "heat": 0.0003, "heat2": 0.001,
 }
-VARIANTS = [{}, {"G": 1.15, "SC": 2.5, "CY": 1.3, "BW": 380.0, "WK": 120.0, "OV2": 0.0, "DI": 100.0},
-            {"G": 1.95, "SC": 5.0, "CY": 1.25, "WK": 250.0, "OV2": 25.0, "BW": 200.0, "RF": 3200.0, "DI": 400.0}]
+VARIANTS = [{}, {"G": 1.3, "SC": 2.8, "CY": 1.2, "BW": 420.0, "WK": 110.0, "DI": 100.0, "RC": 15.0},
+            {"G": 2.7, "SC": 7.0, "CY": 1.35, "WK": 200.0, "BW": 300.0, "RF": 2800.0, "DI": 250.0, "RC": 40.0},
+            {"G": 1.4, "SC": 3.5, "CY": 1.05, "BW": 240.0, "RC": 35.0, "DF": 1900.0, "RF": 2800.0, "DI": 250.0, "RI": 1000.0, "R1": 2500.0},
+            {"G": 1.45, "CY": 1.0, "WK": 250.0, "OS": 80.0, "OV2": 15.0, "BW": 280.0},
+            {"G": 1.4, "CY": 1.05, "PE": 0.5, "RF": 3500.0, "RI": 700.0},
+            {"G": 2.0, "SC": 3.0, "CY": 1.2, "WK": 180.0, "OS": 15.0, "MS": 64, "OV2": 20.0, "BW": 260.0, "DF": 1200.0, "RF": 1500.0, "R1": 3000.0, "DI": 60.0}]
 ALU = AluOpType
 ACT = ActivationFunctionType
 
@@ -149,7 +87,7 @@ def in_psum(a):
 
 
 def width(a):
-    return 2 if SCRATCH[a["b"]][2] in ("bfloat16", "float16", "uint16") else 4
+    return 2 if SCRATCH[a["b"]][2] in (BF, HF, UI) else 4
 
 
 def build(cfg):
@@ -159,13 +97,13 @@ def build(cfg):
     ndma = [0]
     ph = [0]
 
-    def add(eng, calls, dur, kind="c", after=(), nbytes=0, grp=None):
+    def add(eng, calls, dur, kind="c", after=(), nbytes=0, grp=None, free=False):
         i = len(ops)
-        o = {"i": i, "eng": eng, "calls": calls, "dur": dur, "kind": kind, "sem": set(after), "ord": set(), "bytes": nbytes, "grp": grp}
+        o = {"i": i, "eng": eng, "calls": calls, "dur": dur, "kind": kind, "sem": set(after), "ord": set(), "bank": set(), "bytes": nbytes, "grp": grp}
         rd, wr = [], []
         for c in calls:
             if c[0] == "remote":
-                ins, outs = [c[1]], [d[0] for d in c[2]]
+                ins, outs = c[1], [d[0] for d in c[2]]
             else:
                 ins, outs = list(c[2:]), [c[1]]
             for a in ins:
@@ -206,15 +144,15 @@ def build(cfg):
             hist.setdefault(a["b"], []).append((i, False, a))
         for name in sorted({a["b"] for a in rd + wr if in_psum(a)}):
             st = bank.setdefault(name, {"eng": None, "cur": [], "prev": []})
-            if st["eng"] != eng:
+            if st["eng"] != eng or free:
                 st["prev"] = st["cur"]
                 st["cur"] = []
-                st["eng"] = eng
+                st["eng"] = None if free else eng
             elif eng == "pe" and st["cur"]:
                 o["ord"].add(st["cur"][-1])
-            for j in st["prev"]:
-                o["sem"].add(j)
+            o["bank"] |= set(st["prev"]) - o["sem"]
             st["cur"].append(i)
+        o["sem"] |= o["bank"]
         o["ord"] -= o["sem"]
         if kind != "c":
             o["tok"] = "d%d" % ndma[0]
@@ -227,9 +165,9 @@ def build(cfg):
     def vcost(out, ins, two=False):
         n = out["n"]
         if "win" in out:
-            return ov + n * cfg["SC"] * cy
+            return ov + n * cfg["SC"] * 0.83
         if any("win" in a for a in ins):
-            return ov + n * cfg["G"] * cy
+            return ov + n * cfg["G"] * 0.83
         if two:
             f = 1.0 if any(in_psum(a) for a in ins) else 2.0
         else:
@@ -248,162 +186,186 @@ def build(cfg):
     def tt(out, a, b, o):
         return add("v", [("tensor_tensor", out, a, b, o)], vcost(out, [a, b], True))
 
+    def scan(out, a, b, o0, o1):
+        return add("v", [("tensor_tensor_scan", out, a, b, 0.0, o0, o1)], vcost(out, [a, b]))
+
     def mset(out, val):
         return add("v", [("memset", out, val)], vcost(out, []))
 
-    def act(out, a, f, bias=None, scale=None):
-        return add("s", [("activation", out, a, f, bias, scale)], 15 + vcost(out, [a, A("tb", 0, 1)]))
+    def acts(items, eng="s"):
+        other = []
+        for (out, a, f, bias, scale) in items:
+            if f == ACT.Copy:
+                other.append(("tensor_copy", out, a))
+            elif f == ACT.Identity and (bias is None or scale is None):
+                other.append(tsc(out, a, scale if bias is None else bias, None, ALU.mult if bias is None else ALU.add))
+            elif f == ACT.Identity:
+                other.append(tsc(out, a, scale, bias, ALU.mult, ALU.add))
+            elif f == ACT.Relu:
+                other.append(tsc(out, a, 0.0, scale, ALU.max, ALU.mult))
+            elif f == ACT.Abs:
+                other.append(tsc(out, a, bias, 4096.0, ALU.not_equal, ALU.mult))
+        both = {"s": ([("activation",) + x for x in items],
+                      sum(15 + vcost(x[0], [x[1]]) if "win" in x[1] else cfg["OS"] + max(x[0]["n"], cfg["MS"]) * cy for x in items))}
+        if other:
+            both["v"] = (other, sum(vcost(x[0], [x[1]]) for x in items))
+        i = add(eng, both[eng][0], both[eng][1], free=len(both) > 1)
+        if len(both) > 1:
+            ops[i]["both"] = both
+        return i
+
+    def act(out, a, f, bias=None, scale=None, eng="s"):
+        return acts([(out, a, f, bias, scale)], eng)
 
     def mcost(c):
-        f = 4 if SCRATCH[c[3]["b"]][2] == "float32" else 1
+        f = 4 if SCRATCH[c[3]["b"]][2] == FL else 1
         return max(min(64, c[2]["n"]), c[3]["n"]) * f * cfg["PE"] * cfg["CY"]
 
-    def mrun(calls, grp=None, cut=500.0):
-        grp = ("g", len(ops)) if grp is None else grp
-        run = []
+    def mrun(calls, cycles=1200):
+        grp, run = ("g", len(ops)), []
         for c in calls:
             run.append(c)
-            if sum(mcost(x) for x in run) >= cut * cfg["CY"] * cfg["PE"] / 0.42 or c is calls[-1]:
+            if sum(mcost(x) for x in run) >= cycles * cfg["CY"] * cfg["PE"] - 0.01 or c is calls[-1]:
                 i = add("pe", run, sum(mcost(x) for x in run), grp=grp)
                 if run[0] is not calls[0]:
                     ops[i]["ord"].add(i - 1)
                 run = []
-        return grp
 
-    def group(items, start=True, stop=True):
-        return [("matmul", o, l, r, start and n == 0, stop and n == len(items) - 1) for n, (o, l, r) in enumerate(items)]
+    def group(items):
+        mrun([("matmul", o, l, r, n == 0, n == len(items) - 1) for n, (o, l, r) in enumerate(items)])
 
     def mm(out, pairs):
-        return mrun(group([(out, l, r) for (l, r) in pairs]))
+        group([(out, l, r) for (l, r) in pairs])
 
     def iota(out, pat, base, cm):
         return add("g", [("iota", out, pat, base, cm)], 130 + 2 * out["n"] * cy)
 
+    def keep(out, a, pat, op, fill, base, cm):
+        return add("g", [("affine_select", out, a, pat, op, fill, base, cm)], 170 + 2 * out["n"] * cy)
+
     def dma(q, pairs, nbytes, after=(), behind=()):
         i = add(q, [("dma_start", o, a) for (o, a) in pairs], len(pairs) * (cfg["DI"] if q != "g" else 1000.0), "dma", after, nbytes)
         ops[i]["ord"] |= set(behind)
+        ops[i]["rows"] = 8
         return i
 
-    def rem(srcap, dsts, nbytes):
-        return add("g", [("remote", srcap, dsts)], 500.0, "rem", (), nbytes)
+    def rem(srcs, dsts, nbytes):
+        i = add("g", [("remote", srcs, dsts)], cfg["RI"], "rem", (), nbytes)
+        ops[i]["once"] = cfg["R1"] if len(dsts) > 1 else 0.0
+        ops[i]["rows"] = 8 * len(srcs) * len(dsts)
+        return i
 
-    def gather(eng, out, win, off, scale=None):
-        if eng == "s":
-            return act(out, IND(win, off), ACT.Copy if scale is None else ACT.Identity, None, scale)
-        if scale is None:
-            return cp(out, IND(win, off))
-        return ts(out, IND(win, off), scale, None, ALU.mult)
+    def gather(out, win, off, scale=None, eng="s"):
+        i = act(out, IND(win, off), ACT.Copy if scale is None else ACT.Identity, None, scale, eng)
+        if out["n"] >= 512 and ph[0] > cfg["share"]:
+            del ops[i]["both"]
+        return i
 
-    l_past = dma("sync", [(A("snd", 0, 192), EXT("past"))], 49152)
-    dma("s", [(A("com", 0, 768, 1, 0, 8), EXT("coming"))], 12288)
-    l_kap = dma("sync", [(A("kl", 0, 1), EXT("kap"))], 8192, (), (l_past,))
-    dma("s", [(A("kl", 1, 2), EXT("lam"))], 8192)
-    l_snd = dma("sync", [(A("snd", 192, 240), EXT("coming"))], 12288, (), (l_kap,))
-    l_hist = dma("sync", [(A("Hs", 64, 64 + CH), EXT("hist"))], 524288, (), (l_snd,))
-    l_score = dma("sync", [(A("Ps", 0, CP), EXT("score"))], 1048576, (), (l_hist,))
-    dma("sync", [(A("W0", 0, 2048), EXT("weight"))], 524288, (l_hist,), (l_score,))
+    l_kap = dma("sync", [(A("kl", 0, 1), EXT("kap"))], 8192)
+    l_lam = dma("s", [(A("kl", 1, 2), EXT("lam"))], 8192)
+    l_past = dma("sync", [(A("snd", 0, 192), EXT("past"))], 49152, (), (l_kap,))
+    l_com = dma("s", [(A("com", 0, 768, 1, 0, 8), EXT("coming"))], 12288, (), (l_lam,))
+    dma("s", [(A("snd", 192, 240), EXT("coming"))], 12288, (), (l_com,))
+    l_hist = dma("sync", [(A("Hs", 0, CH), EXT("hist"))], 524288, (), (l_past,))
     iota(A("Dm", 0, 144), [[1, 144]], 0, -1)
     iota(A("pi", 0, 1), [[1, 1]], 0, 1)
     iota(A("Pm", 0, 128), [[-16, 8], [0, 16]], 0, 1)
     iota(A("Gi", 0, 128, 1, 0, 8), [[1, 8], [0, 16]], 0, -1)
-    iota(A("Rw", 0, 64), [[1, 64]], -16, 0)
-    iota(A("Ix", 0, 4 * SEG), [[-16, 4], [1, SEG]], 0, 0)
-    rem(A("snd", 0, 240), [(A("lnd", 240 * (t - 1), 240 * t), HOP * t) for t in (1, 2, 3)], 3 * 61440)
+    iota(A("Rw", 0, 4), [[1, 4]], 0, 0)
     iota(A("Iy", 0, 128), [[0, 8], [1, 16]], 0, 0)
-    iota(A("Em", 0, 144, 1, 0, 8), [[1, 144]], 0, -16)
-    iota(A("tb", 0, 8 * SEG), [[0, 8 * SEG]], int(BIG), 0)
-    for j in range(3):
-        iota(A("xm", 1536 + 512 * j, 2048 + 512 * j), [[0, 512]], 0, 0)
-    iota(A("ptr", 64, 192), [[16, 128]], 0, 0)
-    iota(A("pval", 0, 256), [[16, 256]], 2048, 0)
-    if cfg["rscan"]:
-        iota(A("Cz", 0, 1024), [[0, 1024]], 1, 0)
+    iota(A("Ix", 0, 4 * SEG), [[-16, 4], [1, SEG]], 0, 0)
+    rem([A("snd", 0, 240)], [(A("lnd", 240 * (t - 1), 240 * t), HOP * t) for t in (1, 2, 3)], 3 * 61440)
     first = [o["i"] for o in ops if o["eng"] == "g"]
     for i, j in zip(first, first[1:]):
         ops[j]["ord"].add(i)
+    iota(A("Em", 0, 144, 1, 0, 8), [[1, 144]], 0, -16)
+    for j in range(0 if 1 in cfg["xm_c"] else 3):
+        iota(A("xm", 1536 + 512 * j, 2048 + 512 * j), [[0, 512]], 0, 0)
+    iota(A("ptr", 0, 128), [[16, 128]], 0, 0)
+    iota(A("pval", 0, 192), [[16, 192]], 2048, 0)
+    iota(A("pval", 192, 256), [[16, 64]], 0, 0)
+    iota(A("pts", 0, 128), [[0, 128]], 1024, 0)
+    iota(A("pd", 1024, 1040), [[0, 16]], 0, 0)
+    for j in range(2 if cfg["rscan"] else 0):
+        iota(A("Cz", 512 * j, 512 * j + 512), [[0, 512]], 1, 0)
 
     def col(j, p1=128):
         return A("col", j, j + 1, 1, 0, p1)
-    LANE, PF, CA, CE, C15, CZ, CZ8, CB, CS0, CS1, CN, CC, SM = 0, 1, 2, 3, 4, 5, 6, 7, 8, 9, 10, 11, 12
+    LANE, PF, CE, CW, CZ, CB, CT, CV, CD = range(9)
     D128 = A("Dm", 0, 128)
     ts(A("pi", 1, 2), A("pi", 0, 1), 15, None, ALU.bitwise_and)
-    cp(A("col", PF, PF + 1), A("pi", 0, 1))
+    cp(col(PF), A("pi", 0, 1))
     cp(col(LANE), A("pi", 1, 2))
     ident = A("Sh", 0, 128)
     ts(ident, D128, 0.0, None, ALU.is_equal)
-    srep = A("Sr", 0, 128, 1, 0, 8)
+    srep, sprev = A("Sr", 0, 128, 1, 0, 8), A("Sr", 128, 256, 1, 0, 8)
     ts(srep, A("Gi", 0, 128, 1, 0, 8), 0.0, None, ALU.is_equal)
+    ts(col(CW, 8), col(PF, 8), 7.0, -8.0, ALU.is_ge, ALU.mult)
+    ts(sprev, A("Gi", 0, 128, 1, 0, 8), col(CW, 8), 1.0, ALU.subtract, ALU.is_equal)
     tt(A("mn", 0, 128), A("Pm", 0, 128), D128, ALU.min)
     ts(A("kli", 0, 2), A("kl", 0, 2), 0xFF00, None, ALU.bitwise_and)
     ts(A("kli", 2, 4), A("kl", 0, 2), 0xFF, None, ALU.bitwise_and)
     cp(A("klf", 0, 4), A("kli", 0, 4))
     for j in (0, 2):
-        ts(A("KL", 128 * j, 128 * j + 128), A("mn", 0, 128), 0.0, A("klf", j, j + 1), ALU.is_ge, ALU.mult)
+        split = ts(A("KL", 128 * j, 128 * j + 128), A("mn", 0, 128), 0.0, A("klf", j, j + 1), ALU.is_ge, ALU.mult)
+    l_score = dma("sync", [(A("Ps", 0, CP), EXT("score"))], 1048576, (split,) if cfg["gate"] else (), (l_hist,))
+    l_w = dma("sync", [(A("W0", 0, 2048), EXT("weight"))], 524288, () if cfg["gate"] else (l_hist,), (l_score,))
     for j in (1, 3):
-        ts(A("KL", 128 * j, 128 * j + 128), D128, 0.0, A("klf", j, j + 1), ALU.is_equal, ALU.mult)
-    ts(A("pf", 0, 8), A("Pm", 0, 128, 16), col(LANE), None, ALU.is_equal)
-    act(A("pk", 0, 8), A("pf", 0, 8), ACT.Copy)
-    act(A("pk", 8, 9), A("pf", 0, 1), ACT.Copy)
+        act(A("KL", 128 * j, 128 * j + 128), ident, ACT.Identity, None, A("klf", j, j + 1), "v")
+    same = A("Sm", 0, 128)
+    ts(same, A("Pm", 0, 128), col(LANE), None, ALU.is_equal)
+    act(A("Sm", 128, 129), A("Sm", 0, 1), ACT.Copy)
+    table = act(col(CZ), col(LANE), ACT.Sigmoid, 128.0, -256.0)
+    ops[table]["dur"] += 1300.0
+    i = act(A("pf", 0, 8), A("Sm", 0, 128, 16), ACT.Copy)
+    del ops[i]["both"]
+    ops[i]["ord"].add(table)
     for j in (0, 1):
-        mm(A("py", 128 * j, 128 * j + 128, 1, 0, 8), [(A("pk", 1, 9), A("KL", 128 + 256 * j, 256 + 256 * j))])
+        mm(A("py", 128 * j, 128 * j + 128, 1, 0, 8), [(A("Sm", 16, 129, 16), A("KL", 128 + 256 * j, 256 + 256 * j))])
     act(A("Lr", 0, 256, 1, 0, 8), A("py", 0, 256, 1, 0, 8), ACT.Copy)
-    mset(col(CC), ZC)
-    for (pz, c) in (("pz0", 0), ("pz1", 0), ("pz1", 128)):
-        act(A(pz, c, c + 128), D128, ACT.Identity, col(CC), 0.0)
-    ts(col(CB), col(LANE), 3681.0, 37 * ZC, ALU.mult, ALU.add)
-    if cfg["zc_s"]:
-        mset(col(CA), -ZC)
-    if cfg["dr_s"]:
-        mset(A("mg", 0, 1), 1.5 * 2.0 ** 27)
-        mset(A("mg", 1, 2), -1.5 * 2.0 ** 27)
-    if cfg["am_s"]:
-        ts(A("mg", 2, 3), col(CB), 786432.0 - 2047.5, None, ALU.add)
-        ts(A("mg", 3, 4), col(CB), 786432.0, None, ALU.add)
+    mset(A("ut", 128, 384), ZC)
+    for (pz, n) in (("pz0", 128), ("pz1", 256)):
+        mm(A(pz, 0, n), [(ident, A("ut", 128, 128 + n))])
+    if len(cfg["am_s"]) < 2 * STEPS:
+        ts(col(CB), col(LANE), 3681.0, 37 * ZC, ALU.mult, ALU.add)
+    act(col(CT), col(LANE), ACT.Identity, 37 * ZC + TOP - 2047.5, 3681.0)
     ts(col(CE), col(LANE), 8.0 / 4096, 1.0 / 4096, ALU.mult, ALU.max)
-    ts(col(C15), col(LANE), -1.0, 15.0, ALU.mult, ALU.add)
-    ts(col(CZ), col(LANE), 0.0, 4096.0, ALU.is_equal, ALU.mult)
-    ts(col(CZ8), col(LANE), 0.0, -32768.0, ALU.is_equal, ALU.mult)
-    ts(col(CN), col(LANE), 0.0, -1.0, ALU.is_equal, ALU.mult)
-    ts(col(CS0), col(PF), 112.0, -128.0, ALU.is_ge, ALU.mult)
-    ts(col(CS1), col(CS0), 16.0, None, ALU.add)
-    ts(A("col", SM, SM + 4), A("Rw", 16, 20), col(LANE), 15.0, ALU.add, ALU.is_le)
     ts(A("Yy", 0, 144), A("Dm", 0, 144), 16.0, None, ALU.is_equal)
-    ts(A("Yd", 0, 128), A("Pm", 0, 128), col(LANE), col(CN), ALU.is_equal, ALU.mult)
-    ts(A("Y1", 0, 144), A("Dm", 0, 144), col(C15), None, ALU.is_equal)
-    ts(A("B1", 0, 128), A("Pm", 0, 128), col(LANE), 4096.0, ALU.is_equal, ALU.mult)
-    ts(A("mg", 4, 5), col(LANE), -1.0, 0.0, ALU.add, ALU.max)
-    ts(A("mg", 5, 6), A("mg", 4, 5), 4096.0, None, ALU.mult)
-    act(A("Us", 0, 128), A("B1", 0, 128), ACT.Identity, None, A("mg", 5, 6))
+    act(A("Yd", 256, 384), same, ACT.Identity, None, col(CZ))
+    tt(A("Yd", 0, 128), ident, A("Yd", 256, 384), ALU.subtract)
+    act(A("Yd", 128, 256), A("Yd", 0, 128), ACT.Identity, None, -16.0)
+    act(A("B1", 0, 128), same, ACT.Identity, None, 16.0)
+    add("s", [("activation", col(CV), col(LANE), ACT.Relu, -65536.0, 65536.0)], 15 + 64 * cy)
+    act(A("Us", 0, 128), same, ACT.Identity, None, col(CV))
     ts(A("Mk", 0, 128), A("Iy", 0, 128), col(LANE), -2.0 ** 24, ALU.not_equal, ALU.mult)
     act(A("Cr", 0, 128), A("Iy", 0, 128), ACT.Identity, -1.0e8, 2.0e8)
-    ts(A("ut", 0, 128), A("mn", 0, 128), 0.0, 4096.0, ALU.is_ge, ALU.mult)
-    ts(A("ut", 128, 256), A("Pm", 0, 128), col(LANE), -4096.0, ALU.is_equal, ALU.mult)
-    ts(A("ut", 256, 384), D128, 0.0, 4096.0, ALU.is_equal, ALU.mult)
-    tt(A("ut", 0, 128), A("ut", 0, 128), A("ut", 128, 256), ALU.add)
-    tt(A("Um", 0, 128), A("ut", 0, 128), A("ut", 256, 384), ALU.add)
-    act(A("Um", 128, 256), A("Um", 0, 128), ACT.Copy)
-    act(A("Um", 128, 256, 16), A("Dm", 0, 8), ACT.Identity, None, 0.0)
-    act(A("S0", 0, 128), ident, ACT.Identity, None, col(CZ))
-    act(A("S0", 128, 256), ident, ACT.Identity, None, col(CZ8))
-    negI, halfI, negS = A("F32", 0, 128), A("F32", 128, 256), A("F32", 256, 384)
-    if cfg["am_s"]:
-        act(A("nI", 0, 128), ident, ACT.Identity, None, -1.0)
-        act(A("Y37", 0, 128), ident, ACT.Identity, None, 37.0)
-    act(negI, ident, ACT.Identity, None, -1.0)
-    act(halfI, ident, ACT.Identity, None, 0.5)
-    ts(negS, D128, col(CS1), -1.0 / 32, ALU.is_equal, ALU.mult)
+    act(A("ut", 0, 128), same, ACT.Identity, None, -4096.0)
+    keep(A("ut", 0, 128), A("ut", 0, 128), [[-1, 128]], ALU.is_gt, 0.0, 0, 1)
+    keep(A("Um", 0, 128), A("ut", 0, 128), [[-1, 128]], ALU.not_equal, 4096.0, 0, 1)
+    keep(A("Um", 128, 256), A("Um", 0, 128), [[0, 8], [1, 16]], ALU.not_equal, 0.0, 0, 0)
+    ts(A("S0", 0, 128), ident, col(CZ), 4096.0, ALU.mult, ALU.mult)
+    act(A("S0", 128, 256), A("S0", 0, 128), ACT.Identity, None, -8.0)
+    posI, posS = A("F32", 0, 128), A("F32", 128, 256)
+    act(A("nI", 0, 128), ident, ACT.Identity, None, -1.0)
+    act(A("Y37", 0, 128), ident, ACT.Identity, None, 37.0)
+    act(posI, ident, ACT.Copy)
+    act(A("F32", 128, 144), A("Yy", 128, 144), ACT.Identity, None, 1.0 / 32)
+    act(A("F32", 144, 256), A("Yy", 16, 128), ACT.Identity, None, 1.0 / 32)
     for t in (1, 2, 3):
-        ts(A("Sh", 128 * t, 128 * t + 128), D128, float(t), col(SM + t), ALU.is_equal, ALU.mult)
+        keep(A("Sh", 128 * t, 128 * t + 128), same, [[1, 128]], ALU.is_equal, 0.0, -t, -1)
     ts(A("Zw", 0, 144, 1, 0, 8), A("Em", 0, 144, 1, 0, 8), 2.0, None, ALU.is_equal)
-    ts(A("Cs", 0, 4 * SEG), A("Ix", 0, 4 * SEG), col(LANE), -3000.0, ALU.is_equal, ALU.mult)
+    ts(A("Cs", 0, 4 * SEG), A("Ix", 0, 4 * SEG), col(LANE), -12.0, ALU.is_equal, ALU.mult)
     ts(A("Cs", 0, 4 * SEG, SEG), A("Cs", 0, 4 * SEG, SEG), BIG, None, ALU.add)
-    ts(A("tmp", 0, 4), A("Rw", 16, 20), 16.0, 3000.0, ALU.mult, ALU.add)
-    ts(A("Cs", SEG - 1, 4 * SEG, SEG), A("tmp", 0, 4), col(LANE), None, ALU.add)
+    ts(A("col", CD, CD + 4), A("Rw", 0, 4), 16.0, col(LANE), ALU.mult, ALU.add)
+    act(A("Cs", SEG - 1, 4 * SEG, SEG), A("col", CD, CD + 4), ACT.Identity, 12.0, -1.0 / 128)
+    for k in (0, 1):
+        act(A("tb", 4 * SEG * k, 4 * SEG * (k + 1)), A("Ix", 0, 4 * SEG), ACT.Identity, BIG, 0.0)
     if cfg["rscan"]:
         mset(A("Cz", 0, 1024, 16), 0.0)
     for t in (1, 2, 3):
-        l_com = dma("sync", [(A("com", 768 * t, 768 * t + 768, 1, 0, 8), A("lnd", 240 * (t - 1) + 192, 240 * t))], 12288)
-    dma("g", [(A("Wt", 0, 2048), A("W0", 0, 2048))], 1048576, (l_com,))
+        dma("sync", [(A("com", 768 * t, 768 * t + 768, 1, 0, 8), A("lnd", 240 * (t - 1) + 192, 240 * t))], 12288, (), (l_w,))
+    for j in range(0, 2048, 512):
+        keep(A("Wt", j, j + 512), A("W0", j, j + 512), [[0, 512]], ALU.is_gt, 0.0, 1, 0)
 
     def lane_in(i):
         return A("Zw", 2 - i, 130 - i, 1, 0, 8)
@@ -415,84 +377,73 @@ def build(cfg):
         ph[0] += 1
         rot, s0, m0 = U * (t % 3), 192 * t, 1536 * (t % 2)
         pieces = [(0, rot, S - rot)] + ([(S - rot, 0, rot)] if rot else [])
-        pb, pc = ("snd", 0) if t == 0 else ("lnd", 240 * (t - 1))
         x = A("xs", s0, s0 + 192) if t else A("snd", 0, 192)
         if t:
             for (p, u, n) in pieces:
-                mm(A("pa", p, p + n), [(A("Sh", 128 * t, 128 * t + 128), A(pb, pc + u, pc + u + n))]
+                mm(A("pa", p, p + n), [(A("Sh", 128 * t, 128 * t + 128), A("lnd", 240 * (t - 1) + u, 240 * (t - 1) + u + n))]
                    + [(lane_in(t - 1 - s), comc(t, s, u, n)) for s in range(t)])
             act(x, A("pa", 0, 192), ACT.Copy)
-            dma("sync", [(A("xm", m0 + 192 * g, m0 + 192 * g + 192, 1, 16 * g, 16 * g + 16), A("xs", s0, s0 + 192, 1, 16 * g, 16 * g + 16))
-                         for g in range(8)], 49152)
-        cs = A("pa", 192, 384)
+
+        def columns(cs, a, b):
+            cp(A("ci", a, b), cs)
+            ts(A("cj", s0 + a, s0 + b), A("ci", a, b), 5, 2047, ALU.logical_shift_right, ALU.bitwise_and)
+            cp(A("coff", s0 + a, s0 + b), A("cj", s0 + a, s0 + b))
 
         def lrows(j):
             return [(A("pa", 192 + p, 192 + p + n), A("Lr", 128 * j, 128 * j + 128, 1, 0, 8), comc(t, t, u, n)) for (p, u, n) in pieces]
-        mrun(group([(cs, A("KL", 0, 128), x)] + lrows(0) + lrows(1) + [(cs, A("KL", 256, 384), x)]))
-        cp(A("ci", 0, 192), cs)
-        ts(A("cj", s0, s0 + 192), A("ci", 0, 192), 5, 2047, ALU.logical_shift_right, ALU.bitwise_and)
-        cp(A("coff", s0, s0 + 192), A("cj", s0, s0 + 192))
-        if t == 0:
+        if t:
+            cs = A("pa", 192, 384)
+            group([(cs, A("KL", 0, 128), x)] + lrows(0) + lrows(1) + [(cs, A("KL", 256, 384), x)])
+            columns(cs, 0, 192)
+        else:
+            mm(A("pl0", 0, 192), [(sprev, comc(0, 0, 0, 192))])
+            act(A("xs", 0, 192), A("pl0", 0, 192), ACT.Copy)
+            for (name, a, b) in (("pa", 0, 64), ("pl1", 64, 192)):
+                cs = A(name, 192 + a, 192 + b)
+                mm(cs, [(A("KL", 128 * j, 128 * j + 128), A("xs" if j % 2 else "snd", a, b)) for j in range(4)])
+                columns(cs, a, b)
+        if t in cfg["xm_c"]:
             for g in range(8):
-                if g < cfg["xm_s"]:
-                    act(A("xm", 192 * g, 192 * g + 192), x, ACT.Identity, None, A("pf", g, g + 1))
-                else:
-                    ts(A("xm", 192 * g, 192 * g + 192), x, A("pf", g, g + 1), None, ALU.mult)
+                act(A("xm", m0 + 192 * g, m0 + 192 * g + 192), x, ACT.Identity, None, A("pf", g, g + 1), "s" if g < 4 - 4 * t else "v")
         for (p, u, n) in pieces:
             mm(A("pa", p, p + n), [(srep, comc(t, t, u, n))])
-        if t in cfg["oh_s"]:
-            act(A("ct", 0, 192), A("pa", 0, 192), ACT.Abs, col(LANE), -1.0)
-            act(A("oh", s0, s0 + 192), A("ct", 0, 192), ACT.Relu, 1.0, -1.0)
-        else:
-            ts(A("oh", s0, s0 + 192), A("pa", 0, 192), col(LANE), None, ALU.is_equal)
-        if t in cfg["ge_s"]:
-            i = act(A("ge", s0, s0 + 192), x, ACT.Sigmoid, -1920.0, 256.0)
-            ops[i]["dur"] += 1300.0 if t == 0 else 0.0
-        else:
-            ts(A("ge", s0, s0 + 192), x, 8.0, None, ALU.is_ge)
+        ts(A("of", s0, s0 + 192), A("pa", 0, 192), col(LANE), -1.0, ALU.not_equal, ALU.mult)
+        ts(A("ge", s0, s0 + 192), x, 8.0, None, ALU.is_ge)
 
     def phase_h(t, a, b, pz):
         ph[0] += 1
         par, n, s0 = t % 2, b - a, 192 * t
         h0, m0, nb = 3072 * par, 1536 * par, n // 4
+        if a == 0 and t not in cfg["xm_c"]:
+            dma("sync", [(A("xm", m0 + 192 * g, m0 + 192 * g + 192, 1, 16 * g, 16 * g + 16), A("xs", s0, s0 + 192, 1, 16 * g, 16 * g + 16))
+                         for g in range(8)], 49152)
         cut = [c for c in cfg["hcut"][t] if a <= c <= b]
         for c, d in zip(cut, cut[1:]):
-            gather("v" if (t, c) in cfg["hg_v"] else "s", A("hp", h0 + 16 * c, h0 + 16 * d), A("Hs", 64, 64 + CH), A("coff", s0 + c, s0 + d))
+            gather(A("hp", h0 + 16 * c, h0 + 16 * d), A("Hs", 0, CH), A("coff", s0 + c, s0 + d), None, "v" if t == 0 and c % 64 else "s")
         for q in range(4):
             mrun([("matmul", A(pz, 8 * j, 8 * j + 8, 1, 32 * q, 32 * q + 16), A("hp", h0 + 16 * u, h0 + 16 * u + 16),
                    A("xm", m0 + u, m0 + 1536, 192), True, True) for j, u in enumerate(range(a + q * nb, a + q * nb + nb))])
-        if (t, a) in cfg["zc_s"]:
-            act(A("zc", 2 * a, 2 * b), A(pz, 0, 2 * n), ACT.Identity, col(CA), None)
-        else:
-            ts(A("zc", 2 * a, 2 * b), A(pz, 0, 2 * n), -ZC, None, ALU.add)
-        d, y = A(pz, 2 * n, 3 * n), A("py", a, b)
+        act(A("zc", 2 * a, 2 * b), A(pz, 0, 2 * n), ACT.Identity, -ZC, None)
+        py = "pq" if a else "py"
+        d, z = A(pz, 2 * n, 3 * n), A(py, a, b)
         back = []
         for q in range(4):
             for g in range(8):
                 h, m = 1 - g % 2, 32 - 16 * (g % 2)
-                back.append(("matmul", A("py", a + q * nb, a + q * nb + nb, 1, 32 * (g // 2), 32 * (g // 2) + (m if cfg["half"] else 32)),
-                             A("Yy", 32 * q + 16 - 16 * h, 32 * q + 16 - 16 * h + (m if cfg["half"] else 32)),
-                             A("zc", 2 * a + (g ^ 1), 2 * b, 8), h == 1, h == 0))
+                back.append(("matmul", A(py, a + q * nb, a + q * nb + nb, 1, 32 * (g // 2), 32 * (g // 2) + m),
+                             A("Yy", 32 * q + 16 - 16 * h, 32 * q + 16 - 16 * h + m), A("zc", 2 * a + (g ^ 1), 2 * b, 8), h == 1, h == 0))
         mrun(back)
-        if (t, a) in cfg["zf_s"]:
-            act(A("zf", a, b), y, ACT.Copy)
-        else:
-            cp(A("zf", a, b), y)
-        mm(d, [(A("Yy", 16, 144), A("zf", a, b)), (A("Yd", 0, 128), A("zf", a, b))])
-        if (t, a) in cfg["dr_s"]:
-            act(A("df", a, b), d, ACT.Identity, A("mg", 0, 1), None)
-            act(A("dr", a, b), A("df", a, b), ACT.Identity, A("mg", 1, 2), None)
-        else:
-            ts(A("dr", a, b), d, 1.5 * 2.0 ** 27, 1.5 * 2.0 ** 27, ALU.add, ALU.subtract)
-        tt(A("eq", a, b), d, A("dr", a, b), ALU.is_equal)
+        acts([(A("zf", a, b), z, ACT.Copy, None, None), (A("zq", a, b), z, ACT.Identity, 1536.0 + 1.0 / 32, 1.0 / 16)])
+        mm(d, [(A("Yd", 0, 128), A("zf", a, b)), (A("Yd", 128, 256), A("zq", a, b))])
+        ts(A("eq", a, b), d, 0.0, None, ALU.is_equal)
         ao = A("aoff", 192 * par + a, 192 * par + b)
         if (t, a) in cfg["am_s"]:
-            act(A("at", a, b), y, ACT.Identity, A("mg", 2, 3), 37.0)
-            r = A("py", 256 + a, 256 + b)
+            act(A("at", a, b), A("zf", a, b), ACT.Identity, col(CT), 37.0)
+            r = A(py, 256 + a, 256 + b)
             mm(r, [(A("Y37", 0, 128), A("zf", a, b)), (A("nI", 0, 128), A("at", a, b))])
-            ts(ao, r, A("mg", 3, 4), None, ALU.add)
+            ts(ao, r, col(CT), 2047.5, ALU.add, ALU.add)
         else:
-            ts(A("ai", a, b), A("zf", a, b) if cfg["ai_zf"] else y, 37.0, col(CB), ALU.mult, ALU.add)
+            ts(A("ai", a, b), A("zf", a, b), 37.0, col(CB), ALU.mult, ALU.add)
             ts(A("am", a, b), A("ai", a, b), 4095, None, ALU.bitwise_and)
             cp(ao, A("am", a, b))
 
@@ -501,108 +452,111 @@ def build(cfg):
         par, n, s0 = t % 2, b - a, 192 * t
         hu = a == 0 and t < STEPS - 1
         xb = "xs" if t else "snd"
-        vp, sel, dq = A(pz, 3 * n, 4 * n), A(pz, 256, 320), (320 if n == 64 else 256)
+        vp, sel = A(pz, 3 * n, 4 * n), A(pz, 256, 320)
         if hu:
             mm(sel, [(A("Um", 0, 128), A("eq", 0, 64))])
         mm(vp, [(A("S0", 0, 128), A(xb, s0 + a, s0 + b)), (A("S0", 128, 256), A("ge", s0 + a, s0 + b)), (A("Um", 128, 256), A("eq", a, b))])
         if hu:
             tt(A("src", 0, 64), sel, A("cj", s0, s0 + 64), ALU.min)
-        if (t, a) in cfg["src_s"]:
-            act(A("src", 64 + a, 64 + b), vp, ACT.Relu, None, col(CE))
-        else:
-            ts(A("src", 64 + a, 64 + b), vp, 0.0, col(CE), ALU.max, ALU.mult)
+        act(A("src", 64 + a, 64 + b), vp, ACT.Relu, None, col(CE), "v")
         r0 = 0 if hu else 64 + a
         d0, d1 = r0 // 16, (64 + b) // 16
         w = 64 + b - r0
         wo = A("woff", 192 * par + a, 192 * par + b)
         rp = 384 if a == 0 else 2 * n - r0
 
+        pr = pz if a else "py"
+
         def lanes(name, c0):
             return [(A(name, c0, c0 + w), A("B1", 0, 128), A("src", r0, 64 + b))] + ([(A(name, c0, c0 + 64), A("Us", 0, 128), A("eq", 0, 64))] if hu else [])
-        rb = cfg["rep_b"] if a == 0 else pz
         if a == 0 or t == 0:
-            mrun(group(lanes(rb, rp + r0)))
-        if a == 0 or (t, a) in cfg["dscan"]:
+            group(lanes(pr, rp + r0))
+        if a == 0 or t > 0:
             m0 = 128 if a == 0 else 2 * n
             mk = A(pz, m0, m0 + w)
-            mrun(group(lanes(pz, m0) + [(mk, ident, A("Mk", 0, w))]))
-            o, c = A("sd", r0, r0 + w), A("Cr", 0, w)
-            add("v", [("tensor_tensor_scan", o, c, mk, 0.0, ALU.min, ALU.max)], vcost(o, [mk]))
+            group(lanes(pz, m0) + [(mk, ident, A("Mk", 0, w))])
+            scan(A("sd", r0, r0 + w), A("Cr", 0, w), mk, ALU.min, ALU.max)
             dp = A("sd", r0 + 15, r0 + w, 16)
-            ts(A("doff", d0, d1), dp, 1.0 / 4096, None, ALU.mult)
-        elif t > 0:
-            dp = A(pz, dq, dq + d1 - d0)
-            mm(dp, [(A("Y1", 15 - c, 143 - c), A("src", r0 + c, 64 + b, 16)) for c in range(16)])
-            cp(A("doff", d0, d1), dp)
+            ts(A("doff", d0, d1), dp, 1.0 / 16, None, ALU.mult)
         if t == 0:
-            ts(wo, A(rb, rp + 64 + a, rp + 64 + b), 16.0 / 4096, col(LANE), ALU.mult, ALU.add)
+            ts(wo, A(pr, rp + 64 + a, rp + 64 + b), col(LANE), None, ALU.add)
         else:
-            ts(wo, IND(A("ptr", 64, 192), A("doff", 4 + a // 16, 4 + b // 16)), col(LANE), None, ALU.add)
+            ts(wo, IND(A("ptr", 0, 128), A("doff", 4 + a // 16, 4 + b // 16)), col(LANE), None, ALU.add)
         if a == 0:
-            act(A("tb", SEG * d0 + SEG - 1, 8 * SEG, SEG), dp, ACT.Identity, 64.0, 1.0 / 4096)
+            act(A("tb", SEG * d0 + SEG - 1, 8 * SEG, SEG), dp, ACT.Identity, 8.0, -1.0 / 4096)
             for k in ((0, 1) if hu else (1,)):
-                for j in range(4):
-                    q = 4 * k + j
-                    act(A("tb", SEG * q, SEG * q + 16 + 16 * j), A(rb, 384 + 64 * k, 400 + 64 * k + 16 * j), ACT.Abs,
-                        A("sd", 16 * q + 15, 16 * q + 16), -1.0)
-                o, c, d = A("so", 4 * SEG * k, 4 * SEG * (k + 1)), A("Cs", 0, 4 * SEG), A("tb", 4 * SEG * k, 4 * SEG * (k + 1))
-                add("v", [("tensor_tensor_scan", o, c, d, 0.0, ALU.add, ALU.min)], vcost(o, [c]))
-                cp(A("soff", 4 * k, 4 * k + 4), A("so", 4 * SEG * k + SEG - 1, 4 * SEG * (k + 1), SEG))
+                acts([(A("tb", SEG * q, SEG * q + 16 + 16 * (q % 4)), A(pr, 384 + 64 * k, 400 + 64 * k + 16 * (q % 4)), ACT.Abs,
+                       A("sd", 16 * q + 15, 16 * q + 16), -1.0) for q in range(4 * k, 4 * k + 4)])
+                scan(A("so", 4 * SEG * k, 4 * SEG * (k + 1)), A("Cs", 0, 4 * SEG), A("tb", 4 * SEG * k, 4 * SEG * (k + 1)), ALU.add, ALU.min)
+                ts(A("soff", 4 * k, 4 * k + 4), A("so", 4 * SEG * k + SEG - 1, 4 * SEG * (k + 1), SEG), -256.0, 2048.0, ALU.mult, ALU.add)
         if hu:
-            gather("s", A("hold", 0, 64), A("Hs", 64, 64 + CH), A("doff", 0, 4))
-            mm(A("py", 192, 256), [(lane_in(0), comc(t, t, U * (t % 3), 64)), (A("Sh", 128, 256), A("hold", 0, 64))])
-            act(A("hnew", 0, 64), A("py", 192, 256), ACT.Copy)
+            gather(A("hold", 0, 64), A("Hs", 0, CH), A("doff", 0, 4))
+            mm(A(pz, 320, 384), [(lane_in(0), comc(t, t, U * (t % 3), 64)), (A("Sh", 128, 256), A("hold", 0, 64))])
+            act(A("hnew", 0, 64), A(pz, 320, 384), ACT.Copy)
 
     def phase_u(t):
         ph[0] += 1
         if t < STEPS - 1:
-            cp(IND(A("Hs", 0, 64 + CH), A("soff", 0, 4)), A("hnew", 0, 64))
-        cp(IND(A("ptr", 0, 192), A("soff", 4, 8)), A("pval", 64 * t, 64 * t + 64))
+            cp(IND(A("Hs", 0, CH + 128), A("soff", 0, 4)), A("hnew", 0, 64))
+        cp(IND(A("ptr" if t < STEPS - 1 else "pts", 0, CH + 128), A("soff", 4, 8)), A("pval", 64 * t, 64 * t + 64))
 
     def phase_r(t):
         par, s0 = t % 2, 192 * t
         g0 = 3072 * par
         win = A("Wt", 0, 2048 + 1024 * t) if t else A("W0", 0, 2048)
         last = t == STEPS - 1
+        early = set()
+        if last:
+            early.add(ts(A("foff", 128, 256), A("pts", 0, 128), col(LANE), None, ALU.add))
+            ts(A("foff", 0, 128), A("ptr", 0, 128), col(LANE), None, ALU.add)
+            for a in range(0, 128, 32):
+                gather(A("wb", 16 * a, 16 * a + 512), win, A("foff", a, a + 32))
 
-        def carry(a, b):
-            return A("Bi", 192 * (t - 1) + (a + U) % S, 192 * (t - 1) + (a + U) % S + b - a)
-        for n, c in enumerate((0, 64, 128)):
+        def landed(a, b):
+            return [(u, v, A("Bi", 192 * (t - 1) + (u + U) % S, 192 * (t - 1) + (u + U) % S + v - u))
+                    for (u, v) in ((a, min(b, S - U)), (max(a, S - U), b)) if u < v and t]
+
+        def carry(name, c0, const, a, b):
+            return [(A(name, c0 + u - a, c0 + v - a), const, x) for (u, v, x) in landed(a, b)]
+        for n, (c, e) in enumerate(cfg["rch"][t]):
             ph[0] += 1
             pl = "pl%d" % n
-            lg = A(pl, 0, 64)
-            wof = A("woff", 192 * par + c, 192 * par + c + 64)
-            for u in range(c, c + 64, cfg["pcut"]):
-                gather("v" if (t, u) in cfg["pg_v"] else "s", A("pg", g0 + 16 * u, g0 + 16 * (u + cfg["pcut"])), A("Ps", 0, CP),
-                       A("aoff", 192 * par + u, 192 * par + u + cfg["pcut"]), 1.0 / 32)
-            for u in range(c, c + 64, cfg["wcut"]):
-                tt(A("pw", g0 + 16 * u, g0 + 16 * (u + cfg["wcut"])), IND(win, A("woff", 192 * par + u, 192 * par + u + cfg["wcut"])),
-                   A("pg", g0 + 16 * u, g0 + 16 * (u + cfg["wcut"])), ALU.mult)
+            lg, ys = A(pl, 0, e - c), A("ys", s0 + c, s0 + e)
+            cut = [u for u in cfg["pcut"][t] if c <= u <= e]
+            for u, v in zip(cut, cut[1:]):
+                gather(A("pg", g0 + 16 * u, g0 + 16 * v), A("Ps", 0, CP), A("aoff", 192 * par + u, 192 * par + v), 1.0 / 32)
+            cut = [u for u in cfg["wcut"][t] if c <= u <= e]
+            for u, v in zip(cut, cut[1:]):
+                i = tt(A("pw", g0 + 16 * u, g0 + 16 * v), IND(win, A("woff", 192 * par + u, 192 * par + v)), A("pg", g0 + 16 * u, g0 + 16 * v), ALU.mult)
+                if u < cfg["early"][t]:
+                    early.add(i)
             if (t, c) in cfg["rscan"]:
-                o, z, w = A("wo", 0, 1024), A("Cz", 0, 1024), A("pw", g0 + 16 * c, g0 + 16 * c + 1024)
-                add("v", [("tensor_tensor_scan", o, z, w, 0.0, ALU.mult, ALU.add)], vcost(o, [w]))
-                mm(lg, ([(negS, carry(c, c + 64))] if t else []) + [(negI, A("wo", 15, 1024, 16))])
+                scan(A("ps", 0, 16 * (e - c)), A("Cz", 0, 16 * (e - c)), A("pw", g0 + 16 * c, g0 + 16 * e), ALU.mult, ALU.add)
+                group(carry(pl, 0, posS, c, e) + [(lg, posI, A("ps", 15, 16 * (e - c), 16))])
             else:
-                mm(lg, [(negI, A("pw", g0 + 16 * c + k, g0 + 16 * c + 1024, 16)) for k in range(16)] + ([(negS, carry(c, c + 64))] if t else []))
-            act(A("ys", c, c + 64), lg, ACT.Sigmoid, None, -32.0)
+                group([(lg, posI, A("pw", g0 + 16 * c + k, g0 + 16 * e, 16)) for k in range(16)] + carry(pl, 0, posS, c, e))
+            act(ys, lg, ACT.Sigmoid, None, -32.0)
             if c == 0:
                 er = A(pl, 64, 128)
-                mm(er, [(ident, A("oh", s0, s0 + 64)), (negI, A("ys", 0, 64))])
-                for k0 in range(0, 16, 4):
-                    cs = [("tensor_tensor", A("pd", k, 1024, 16), A("pg", g0 + k, g0 + 1024, 16), er, ALU.mult) for k in range(k0, k0 + 4)]
-                    add("v", cs, sum(vcost(x[1], [x[2], x[3]], True) for x in cs))
-                tt(A("Wt", 2048 + 1024 * t, 3072 + 1024 * t), IND(win, wof), A("pd", 0, 1024), ALU.add)
+                mm(er, [(posI, A("of", s0, s0 + 64)), (posI, ys)])
                 continue
-            a, b = (0, 128) if c == 64 else (128, 192)
-            mm(A("pq", a, b), [(ident, A("oh", s0 + a, s0 + b))] + ([(halfI, carry(a, b))] if t else []))
-            tt(A("Bo", s0 + a, s0 + b), A("pq", a, b), A("ys", a, b), ALU.subtract)
-            rem(A("Bo", s0 + a, s0 + b), [(A("Bi", s0 + a, s0 + b), -HOP * (STEPS - 1) if last else HOP)], 512 * (b - a))
+            a, b = (0, e) if c == 64 else (c, e)
+            for (u, v, x) in landed(a, b):
+                act(A("Bo", s0 + u, s0 + v), x, ACT.Identity, None, 0.5)
+            srcs = [A(x, s0 + a, s0 + b) for x in (("Bo", "of", "ys") if t else ("of", "ys"))]
+            rem(srcs, [(A("Bi", s0 + a, s0 + b), -HOP * (STEPS - 1) if last else HOP)], 512 * (b - a) * len(srcs))
             if last:
-                dma("sync", [(EXT("yb", a, b), A("Bi", s0 + a, s0 + b))], 512 * (b - a))
+                dma("s", [(EXT("yb", a, b), A("Bi", s0 + a, s0 + b))], 512 * (b - a))
+        ph[0] += 1
+        for k0 in range(0, 16, 4):
+            cs = [("tensor_tensor", A("pd", k, 1024, 16), A("pg", g0 + k, g0 + 1024, 16), er, ALU.mult) for k in range(k0, k0 + 4)]
+            ops[add("v", cs, sum(vcost(x[1], [x[2], x[3]], True) for x in cs))]["ord"] |= early
+        if not last:
+            tt(A("Wt", 2048 + 1024 * t, 3072 + 1024 * t), IND(win, A("woff", 192 * par, 192 * par + 64)), A("pd", 0, 1024), ALU.add)
 
     phase_a(0)
     for t in range(STEPS):
-        ch = list(zip(cfg["ich"][t], ("pz0", "pz1")))
+        ch = (((0, U), "pz0"), ((U, S), "pz1"))
 
         def ahead(place):
             for s in range(1, STEPS):
@@ -617,17 +571,18 @@ def build(cfg):
         ahead(2)
         phase_u(t)
         phase_r(t)
-    ts(A("foff", 0, 128), A("ptr", 64, 192), col(LANE), None, ALU.add)
-    for n, (e, a, b) in enumerate(cfg["fin"]):
-        gather(e, A("wo", 16 * a, 16 * b), A("Wt", 0, 6144), A("foff", a, b))
-        dma("sync" if e == "v" else "s", [(EXT("yw", 16 * a, 16 * b), A("wo", 16 * a, 16 * b))], 8192 * (b - a))
+    ph[0] += 1
+    for a, b in zip(cfg["fin"], cfg["fin"][1:]):
+        tt(A("wo", 16 * a, 16 * b), IND(A("pd", 0, 1040), A("foff", 128 + a, 128 + b)), A("wb", 16 * a, 16 * b), ALU.add)
+        dma("sync", [(EXT("yw", 16 * a, 16 * b), A("wo", 16 * a, 16 * b))], 8192 * (b - a))
     return ops
 
 
 def landing(o, issued, pipe, cfg):
-    first, own = issued + (cfg["RF"] if o["kind"] == "rem" else cfg["DF"]) - 500.0, o["bytes"] / cfg["BW"]
+    first, own = issued + (cfg["RF"] if o["kind"] == "rem" else cfg["DF"]) - 500.0, o["bytes"] / cfg["BW"] + o["rows"] * cfg["RC"]
+    first += o.get("once", 0.0)
     after = max(pipe, first) + own
-    return (min(after, first + 2 * own) if o["bytes"] < 200000 else after) + 500.0, after
+    return (min(after, first + 2 * own) if o["bytes"] < 100000 else after) + 500.0, max(pipe, issued + cfg["DF"] - 500.0) + own
 
 
 def replay(ops, order, cfg):
@@ -647,220 +602,270 @@ def replay(ops, order, cfg):
     return end
 
 
-def search(cfg, rounds, seed=0):
-    cfgs = [dict(cfg, **v) for v in VARIANTS]
-    opss = [build(c) for c in cfgs]
-    base = priorities(opss[0], cfgs[0])
-    keys = sorted({o["key"] for o in opss[0]})
-    rnd = np.random.RandomState(seed)
-
-    def score(b):
-        order = schedule(opss[0], cfgs[0], base, b)[0]
-        return [replay(o, order, c) for o, c in zip(opss, cfgs)]
-    cur = dict(cfg["bias"])
-    v0 = score({})
-    cv = score(cur)
-    for r in range(rounds):
-        b = dict(cur)
-        for s in range(1 + int(rnd.randint(3))):
-            k0, d = keys[int(rnd.randint(len(keys)))], round(float(rnd.normal()) * 2500.0, -1)
-            for k in ([k for k in keys if k[1] == k0[1]] if rnd.rand() < 0.3 else [k0]):
-                b[k] = b.get(k, 0.0) + d
-        v = score(b)
-        if sum(x / y for x, y in zip(v, v0)) <= sum(x / y for x, y in zip(cv, v0)):
-            cur, cv = b, v
-    return cur, cv, v0
+def assign(opss, i, eng):
+    for ops in opss:
+        ops[i].update(eng=eng, calls=ops[i]["both"][eng][0], dur=ops[i]["both"][eng][1])
 
 
 def shuttle(opss, cfgs, order, rounds, seed=0):
     n = len(opss[0])
     rnd = np.random.RandomState(seed)
     keys = sorted({o["key"] for o in opss[0]})
-    norm = [replay(o, order, c) for o, c in zip(opss, cfgs)]
+    pred = [[(j, j in o["sem"]) for j in sorted(o["sem"] | o["ord"])] for o in opss[0]]
     succ = [[] for i in range(n)]
-    for o in opss[0]:
-        for j in o["sem"] | o["ord"]:
-            succ[j].append(o["i"])
-    pred = [sorted(o["sem"] | o["ord"]) for o in opss[0]]
+    for i in range(n):
+        for (j, w) in pred[i]:
+            succ[j].append((i, w))
 
-    def pack(ops, prio, before, after, gap):
-        left = [len(x) for x in before]
-        heap = [(prio[i], i) for i in range(n) if not left[i]]
-        busy = {}
-        start = [0.0] * n
-        while heap:
-            heap.sort(reverse=True)
-            i = heap.pop()[1]
-            t, dur = 0.0, ops[i]["dur"]
-            for j in before[i]:
-                t = max(t, start[j] + ops[j]["dur"] + gap(j, i))
-            line = busy.setdefault(ops[i]["eng"], [])
-            p = len(line)
-            while p and line[p - 1][1] > t:
-                p -= 1
-            while p < len(line) and line[p][0] < t + dur:
-                t = max(t, line[p][1])
-                p += 1
-            line.insert(p, (t, t + dur))
-            start[i] = t
-            for j in after[i]:
-                left[j] -= 1
-                if not left[j]:
-                    heap.append((prio[j], j))
-        return start
+    def fit(line, t, dur):
+        p = len(line)
+        while p and line[p - 1][1] > t:
+            p -= 1
+        while p < len(line) and line[p][0] < t + dur:
+            if line[p][1] > t:
+                t = line[p][1]
+            p += 1
+        return t, p
+
+    def pack(ops, prio, walk, before, first, out, into, choose):
+        for i in walk:
+            for (j, w) in before[i]:
+                if prio[i] <= prio[j]:
+                    prio[i] = prio[j] + 0.001
+        busy = {e: [] for e in ("pe", "v", "s", "g", "sync")}
+        end = [0.0] * n
+        for i in sorted(walk, key=lambda i: prio[i]):
+            t, o = first[i], ops[i]
+            for (j, w) in before[i]:
+                x = end[j] + out[j] + into[i] if w else end[j]
+                if x > t:
+                    t = x
+            if choose and "both" in o:
+                e = min("vs", key=lambda e: fit(busy[e], t, o["both"][e][1])[0] + o["both"][e][1] + (choose if e != o["eng"] else 0.0))
+                if e != o["eng"]:
+                    assign(opss, i, e)
+            t, p = fit(busy[o["eng"]], t, o["dur"])
+            end[i] = t + o["dur"]
+            busy[o["eng"]].insert(p, (t, end[i]))
+        return end
 
     def value(od):
-        return sum(replay(o, od, c) / x for o, c, x in zip(opss, cfgs, norm)) / len(cfgs)
+        return sum(np.log(replay(o, od, c) + c["even"] * max(sum(x["dur"] for x in o if x["eng"] == e) for e in "vs"))
+                   for o, c in zip(opss, cfgs)) / len(cfgs)
+    zero = [0.0] * n
+    if order is None:
+        replay(opss[0], range(n), cfgs[0])
+        wait = [cfgs[0]["WK"] + min(o["t1"] - o["t0"] - o["dur"], cfgs[0]["DF"] + o["bytes"] / cfgs[0]["BW"]) for o in opss[0]]
+        way = [0.0] * n
+        for i in range(n - 1, -1, -1):
+            way[i] = opss[0][i]["dur"] + max([wait[i]] + [way[j] + (wait[i] if w else 0.0) for (j, w) in succ[i]])
+        fore = pack(opss[0], [-x for x in way], range(n), pred, zero, wait, zero, 0.0)
+        order = sorted(range(n), key=lambda i: (fore[i] - opss[0][i]["dur"], i))
     cur = best = value(order)
-    keep = order
+    keep = (order, [o["eng"] for o in opss[0]])
+    either = [o["i"] for o in opss[0] if "both" in o]
     for r in range(rounds):
         v = int(rnd.randint(len(cfgs)))
         ops, wk = opss[v], cfgs[v]["WK"]
+        was = [ops[i]["eng"] for i in either]
         replay(ops, order, cfgs[v])
         lat = [o["t1"] - o["t0"] - o["dur"] for o in ops]
         push = {keys[int(rnd.randint(len(keys)))]: float(rnd.normal()) * 1500.0 for s in range(1 + int(rnd.randint(6)))}
-        ends = [-(o["t1"] + push.get(o["key"], 0.0)) for o in ops]
-        tail = [0.0 if succ[i] else lat[i] for i in range(n)]
-        back = pack([dict(eng=o["eng"], dur=o["dur"] + tail[o["i"]]) for o in ops], ends, succ, pred,
-                    lambda j, i: wk + lat[i] if i in ops[j]["sem"] else 0.0)
-        fore = pack(ops, [-(back[i] + ops[i]["dur"] + tail[i]) for i in range(n)], pred, succ,
-                    lambda j, i: wk + lat[j] if j in ops[i]["sem"] else 0.0)
-        od = sorted(range(n), key=lambda i: (fore[i], i))
+        whole = {int(rnd.randint(ops[-1]["key"][1] + 1)): float(rnd.normal()) * cfgs[0]["far"] for s in range(int(rnd.randint(4)))}
+        ends = [-(o["t1"] + push.get(o["key"], 0.0) + whole.get(o["key"][1], 0.0)) for o in ops]
+        for i in rnd.choice(either, int(rnd.randint(3)), False):
+            assign(opss, int(i), "v" if ops[i]["eng"] == "s" else "s")
+        pick, wait = rnd.rand(), [x + wk for x in lat]
+        back = pack(ops, ends, range(n - 1, -1, -1), succ, lat, zero, wait, 600.0 * rnd.rand() + 300.0 if pick < cfgs[0]["pick"] else 0.0)
+        whole = {int(rnd.randint(ops[-1]["key"][1] + 1)): float(rnd.normal()) * cfgs[0]["far"] for s in range(int(rnd.randint(2)))}
+        fore = pack(ops, [whole.get(o["key"][1], 0.0) - x for o, x in zip(ops, back)], range(n), pred, zero, wait, zero, 600.0 * rnd.rand() + 300.0 if pick > 1 - cfgs[0]["pick"] else 0.0)
+        od = sorted(range(n), key=lambda i: (fore[i] - ops[i]["dur"], i))
         x = value(od)
         if x <= cur + cfgs[0]["heat2"] * (1 - r / rounds) * rnd.exponential():
             order, cur = od, x
             if x < best:
-                best, keep = x, od
-    return keep, [replay(o, keep, c) for o, c in zip(opss, cfgs)]
+                best, keep = x, (od, [o["eng"] for o in ops])
+        else:
+            for i, e in zip(either, was):
+                if ops[i]["eng"] != e:
+                    assign(opss, i, e)
+    for i in either:
+        assign(opss, i, keep[1][i])
+    return keep[0], [replay(o, keep[0], c) for o, c in zip(opss, cfgs)]
 
 
 def polish(opss, cfgs, order, rounds, seed=0):
-    ops = opss[0]
+    ops, nv = opss[0], len(cfgs)
     n = len(ops)
     pred = [sorted(o["sem"] | o["ord"]) for o in ops]
     succ = [[] for o in ops]
-    for i in range(n):
+    above = [0] * n
+    sems = []
+    for i, o in enumerate(ops):
         for j in pred[i]:
             succ[j].append(i)
+            above[i] |= above[j]
+        sems.append([j for j in sorted(o["sem"]) if not above[i] >> j & 1])
+        for j in o["sem"]:
+            above[i] |= 1 << j
     engs = sorted({o["eng"] for o in ops})
     eng = [engs.index(o["eng"]) for o in ops]
-    sems = [sorted(o["sem"]) for o in ops]
     durs = [[o["dur"] for o in x] for x in opss]
     moving = [o["kind"] != "c" for o in ops]
     rnd = np.random.RandomState(seed)
+    mix, heat, aim = cfgs[0]["mix"] / n, cfgs[0]["heat"], cfgs[0]["aim"]
 
-    def run(od, v):
-        free, done, start, pipe, wk, dur = [0.0] * len(engs), [0.0] * n, [0.0] * n, 0.0, cfgs[v]["WK"], durs[v]
-        for i in od:
-            t = free[eng[i]]
+    def run(od, v, p0, old):
+        wk, dur, free, pipe = cfgs[v]["WK"], durs[v], [0.0] * len(engs), 0.0
+        fin, ready, load = old[0][:], old[1][:], old[2][:]
+        seen = set()
+        for i in od[p0 - 1::-1] if p0 else []:
+            if eng[i] not in seen:
+                seen.add(eng[i])
+                free[eng[i]] = fin[i]
+            if moving[i] and -1 not in seen:
+                seen.add(-1)
+                pipe = load[i]
+            if len(seen) > len(engs):
+                break
+        for i in od[p0:]:
+            e = eng[i]
+            t = free[e]
             for j in sems[i]:
-                if done[j] + wk > t:
-                    t = done[j] + wk
-            start[i] = t
-            d = free[eng[i]] = t + dur[i]
+                if ready[j] > t:
+                    t = ready[j]
+            fin[i] = free[e] = t = t + dur[i]
             if moving[i]:
-                d, pipe = landing(ops[i], d, pipe, cfgs[v])
-            done[i] = d
-        return max(done), start, sum(done) / n
-    norm = [run(order, v)[0] for v in range(len(cfgs))]
-    mix, heat = cfgs[0]["mix"], cfgs[0]["heat"]
+                t, pipe = landing(ops[i], t, pipe, cfgs[v])
+                load[i] = pipe
+            ready[i] = t + wk
+        return fin, ready, load
+    blank = ([0.0] * n, [0.0] * n, [0.0] * n)
+    state = [run(order, v, 0, blank) for v in range(nv)]
+    norm = [nv * max(s[1]) for s in state]
 
-    def value(od):
-        x = [run(od, v) for v in range(len(cfgs))]
-        return sum((a[0] + mix * a[2]) / b for a, b in zip(x, norm)) / len(cfgs)
-    cur = best = value(order)
-    keep = order
+    def worth(s, v):
+        return (max(s[1]) + mix * sum(s[1])) / norm[v]
+    part = [worth(s, v) for v, s in enumerate(state)]
+
+    def better(od, p0, room):
+        new, val = [], []
+        for v in range(nv):
+            new.append(run(od, v, p0, state[v]))
+            val.append(worth(new[v], v))
+            if sum(val) - sum(part[:v + 1]) > room + 0.001 * (nv - 1 - v):
+                return False
+        state[:], part[:] = new, val
+        return True
+
+    def tight(od, v):
+        fin, ready = state[v][0], state[v][1]
+        before, last = {}, {}
+        for i in od:
+            before[i] = last.get(eng[i])
+            last[eng[i]] = i
+        i, pairs = ready.index(max(ready)), []
+        while fin[i] - durs[v][i] > 0.01:
+            a = before[i]
+            if a is not None and fin[a] >= fin[i] - durs[v][i] - 0.01:
+                if a not in pred[i]:
+                    pairs.append((a, i))
+                i = a
+            else:
+                i = max(sems[i], key=lambda j: ready[j])
+        return pairs
+
+    def turn(i):
+        assign(opss, i, "v" if ops[i]["eng"] == "s" else "s")
+        eng[i] = engs.index(ops[i]["eng"])
+        for x, d in zip(opss, durs):
+            d[i] = x[i]["dur"]
+    best, keep, held = sum(part), (order, list(eng)), [None] * nv
     for r in range(rounds):
         if r % 200 == 0:
-            start = run(order, (r // 200) % len(cfgs))[1]
+            v = (r // 200) % nv
             rank = {i: p for p, i in enumerate(order)}
-            order = sorted(order, key=lambda i: (start[i], rank[i]))
-            cur = value(order)
-        p = int(rnd.randint(n))
-        i = order[p]
-        step, hops, q, stop = (1 if rnd.rand() < 0.5 else -1), 1 + int(rnd.geometric(0.4)) - 1, p, False
-        bar = set(succ[i] if step > 0 else pred[i])
-        while hops and not stop:
-            q += step
-            stop = q < 0 or q >= n or order[q] in bar
-            if not stop and eng[order[q]] == eng[i]:
-                hops -= 1
-        if stop:
-            continue
-        od = order[:p] + order[p + 1:]
-        od.insert(q, i)
-        v = value(od)
-        if v <= cur + heat * (1 - r / rounds) * rnd.exponential():
-            order, cur = od, v
-            if v < best:
-                best, keep = v, od
-    return keep, [run(keep, v)[0] for v in range(len(cfgs))]
+            order = sorted(order, key=lambda i: (state[v][0][i] - durs[v][i], rank[i]))
+            state[:] = [run(order, v, 0, blank) for v in range(nv)]
+            part[:] = [worth(s, v) for v, s in enumerate(state)]
+        x = rnd.rand(5)
+        room = -heat * (1 - r / rounds) * np.log(1 - x[0])
+        od = None
+        if x[1] < aim:
+            v = int(x[2] * nv)
+            if held[v] is None:
+                held[v] = tight(order, v)
+            if not held[v]:
+                continue
+            a, b = held[v][int(x[3] * len(held[v]))]
+            i = a if x[4] < 0.15 else b
+            p0 = order.index(i)
+            if "both" not in ops[i] or x[4] > 0.3:
+                p0, pb = order.index(a), p0 if i == b else order.index(b)
+                move, need, queues = [b], set(pred[b]), set()
+                for y in order[pb - 1:p0:-1]:
+                    if y in need or eng[y] in queues:
+                        move.append(y)
+                        need.update(pred[y])
+                        queues.add(eng[y])
+                if a in need or eng[a] in queues:
+                    continue
+                od = order[:p0] + move[::-1] + [y for y in order[p0:pb] if y not in move] + order[pb + 1:]
+        else:
+            p0 = int(x[2] * n)
+            i = order[p0]
+            if "both" not in ops[i] or x[4] > 0.15:
+                step, hops, q, stop = (1 if x[3] < 0.5 else -1), int(rnd.geometric(0.4)), p0, False
+                bar = set(succ[i] if step > 0 else pred[i])
+                while hops and not stop:
+                    q += step
+                    stop = q < 0 or q >= n or order[q] in bar
+                    if not stop and eng[order[q]] == eng[i]:
+                        hops -= 1
+                if stop:
+                    continue
+                od = order[:p0] + order[p0 + 1:]
+                od.insert(q, i)
+                p0 = min(p0, q)
+        if od is None:
+            turn(i)
+        if better(od or order, p0, room):
+            order, held = od or order, [None] * nv
+            if sum(part) < best:
+                best, keep = sum(part), (order, list(eng))
+        elif od is None:
+            turn(i)
+    for i in range(n):
+        if eng[i] != keep[1][i]:
+            turn(i)
+    return keep[0], [max(run(keep[0], v, 0, blank)[1]) - cfgs[v]["WK"] for v in range(nv)]
 
 
-def priorities(ops, cfg):
-    n = len(ops)
-    succ = [[] for o in ops]
-    for o in ops:
-        for j in o["sem"] | o["ord"]:
-            succ[j].append(o["i"])
-
-    def lat(o):
-        if o["kind"] == "c":
-            return 0.0
-        return (cfg["RF"] if o["kind"] == "rem" else cfg["DF"]) + o["bytes"] / cfg["BW"]
-    prio = [0.0] * n
-    for o in reversed(ops):
-        best = 0.0
-        for j in succ[o["i"]]:
-            best = max(best, prio[j] + (cfg["WK"] + lat(o) if o["i"] in ops[j]["sem"] else 0.0))
-        prio[o["i"]] = max(best, lat(o)) + o["dur"]
-    return succ, prio
-
-
-def schedule(ops, cfg, base, bias):
-    succ = base[0]
-    prio = [p + bias.get(o["key"], 0.0) for p, o in zip(base[1], ops)]
-    left = [len(o["sem"] | o["ord"]) for o in ops]
-    ready = {e: [] for e in ("pe", "v", "s", "g", "sync")}
-    for o in ops:
-        if left[o["i"]] == 0:
-            ready[o["eng"]].append(o["i"])
-    rt = [0.0] * len(ops)
-    free = {e: 0.0 for e in ready}
-    pipe = [0.0]
-    order = []
-    end = 0.0
-    for step in range(len(ops)):
-        t, e = min((max(free[q], min(rt[j] for j in r)), q) for q, r in ready.items() if r)
-        lim = t + cfg["look"]
-        i = max((j for j in ready[e] if rt[j] <= lim), key=lambda j: (prio[j], -j))
-        o = ops[i]
-        o["t0"] = max(t, rt[i])
-        free[e] = o["t0"] + o["dur"]
-        done = free[e]
-        if o["kind"] != "c":
-            done, pipe[0] = landing(o, done, pipe[0], cfg)
-        o["t1"] = done
-        end = max(end, done)
-        ready[e].remove(i)
-        order.append(i)
-        for j in succ[i]:
-            rt[j] = max(rt[j], done + cfg["WK"] if i in ops[j]["sem"] else free[e])
-            left[j] -= 1
-            if left[j] == 0:
-                ready[ops[j]["eng"]].append(j)
-    return order, end
+def arrange(cfg):
+    cfgs = [dict(cfg, **v) for v in VARIANTS]
+    found = []
+    for seed in range(cfg["tries"]):
+        opss = [build(c) for c in cfgs]
+        order = shuttle(opss, cfgs, None, cfg["shuttle"], seed)[0]
+        order, ends = polish(opss, cfgs, order, cfg["trim"], seed)
+        found.append((float(np.sum(np.log(ends))), seed, opss, order))
+    opss, order = min(found)[2:]
+    order, ends = polish(opss, cfgs, order, cfg["polish"])
+    for ops in opss:
+        for o in ops:
+            near = {j for j in o["bank"] if ops[j]["eng"] == o["eng"] != "pe"}
+            for j in near:
+                ops[j].pop("both", None)
+                o.pop("both", None)
+                o["sem"] = (o["sem"] - {j}) | (ops[j]["bank"] & ops[j]["sem"])
+            o["ord"] |= near
+    order, ends = polish(opss, cfgs, order, cfg["polish"] // 4, 1)
+    replay(opss[0], order, cfg)
+    return opss[0], order, ends
 
 
 def plan(cfg):
-    bias = search(cfg, cfg["rounds"])[0]
-    cfgs = [dict(cfg, **v) for v in VARIANTS]
-    opss = [build(c) for c in cfgs]
-    ops = opss[0]
-    order = schedule(ops, cfg, priorities(ops, cfg), bias)[0]
-    order = shuttle(opss, cfgs, order, cfg["shuttle"])[0]
-    order, end = polish(opss, cfgs, order, cfg["polish"])
-    replay(ops, order, cfg)
+    ops, order, ends = arrange(cfg)
     need = set()
     for o in ops:
         need |= o["sem"]
@@ -890,7 +895,7 @@ def plan(cfg):
             o["sig"] = (name, count.get(name, 0))
         else:
             o["sig"] = (o["tok"], 1)
-    return ops, order, end
+    return ops, order
 
 
 PLAN = []
@@ -902,7 +907,7 @@ def rank_program(g, core, T, topo):
         return
     if not PLAN:
         PLAN.append(plan(CFG))
-    ops, order, end = PLAN[0]
+    ops, order = PLAN[0]
     cores = list(T.cores)
     queue = {"pe": g.tensor, "v": g.vector, "s": g.scalar, "g": g, "sync": g.sync}
 
@@ -929,19 +934,20 @@ def rank_program(g, core, T, topo):
         for name, val in o["waits"]:
             q.wait_ge(T.sem[name], full.get(name, val))
         for c in o["calls"]:
-            x = [real(T, a) if isinstance(a, dict) else a for a in c[1:]]
             if c[0] == "remote":
                 hops = [d[1] for d in c[2]]
                 m = mask_of(core, hops)
                 to = [topo.addr(cores[(rank + h) % NR]) for h in hops]
-                if len(hops) == 1:
-                    g.remote_dma(real(T, c[2][0][0]), x[0], T.sem[o["tok"]], T.sem.loc, to[0][1], to[0][0], m)
+                srcs = [real(T, a) for a in c[1]]
+                if len(hops) == 1 and len(srcs) == 1:
+                    g.remote_dma(real(T, c[2][0][0]), srcs[0], T.sem[o["tok"]], T.sem.loc, to[0][1], to[0][0], m)
                 else:
                     g.remote_dma_fused([RemoteDMATransfer(dst_ids=[DstId(rid=a[0], pnc=a[1]) for a in to], dma_engine_mask=m,
-                                                          remote_sem=T.sem[o["tok"]], srcs=[x[0]], dsts=[real(T, d[0]) for d in c[2]])],
-                                       local_sem=T.sem.loc)
+                                                          remote_sem=T.sem[o["tok"]], srcs=srcs, dsts=[real(T, d[0]) for d in c[2]],
+                                                          alu_op=1 if len(srcs) > 1 else 0)], local_sem=T.sem.loc)
                 sent += bits(m)
                 continue
+            x = [real(T, a) if isinstance(a, dict) else a for a in c[1:]]
             if c[0] == "dma_start":
                 q.dma_start(x[0], x[1]).then_inc(T.sem[o["tok"]], 16)
                 if "ext" in c[1]:
@@ -955,10 +961,12 @@ def rank_program(g, core, T, topo):
                     kw["scale"] = x[4]
                 ins = q.activation(x[0], x[1], x[2], **kw)
             elif c[0] == "iota":
-                if SCRATCH[c[1]["b"]][2] == "int32":
+                if SCRATCH[c[1]["b"]][2] == IN:
                     ins = q.iota(*x)
                 else:
                     ins = q.iota(*x, allow_small_or_imprecise_dtypes=True)
+            elif c[0] == "affine_select":
+                ins = q.affine_select(*x)
             elif c[0] == "matmul":
                 ins = q.matmul(*x)
             elif c[0] == "tensor_copy":

@@ -1,3 +1,4 @@
+import math
 import numpy as np
 from concourse.bass import DstId, RemoteDMATransfer
 from concourse.mybir import AluOpType, ActivationFunctionType
@@ -5,7 +6,7 @@ from concourse.mybir import AluOpType, ActivationFunctionType
 S, U, CH, CP, STEPS, HOP, NR = 192, 64, 2048, 4096, 4, 3, 8
 SEG = 65
 BIG = 30000.0
-ZC = 1800.0
+ZC = 2048.0
 TOP = 786432.0
 
 
@@ -17,44 +18,50 @@ BF, HF, FL, IN, UI = "bfloat16", "float16", "float32", "int32", "uint16"
 SCRATCH = {
     "snd": sb(240, BF), "lnd": sb(3 * 240, BF), "com": sb(4 * 768, BF),
     "kl": sb(8, IN), "kli": sb(4, IN), "klf": sb(4, FL),
-    "Hs": sb(CH + 128, BF), "Ps": sb(CP, BF), "W0": sb(2048, BF), "Wt": sb(2048 + 3072, FL),
-    "ptr": sb(CH + 128, FL), "pts": sb(CH + 128, FL), "pval": sb(256, FL),
-    "Dm": sb(144, BF), "Pm": sb(128, BF), "Em": sb(144, BF), "Gi": sb(128, BF), "Rw": sb(4, FL), "Ix": sb(4 * SEG, BF), "Iy": sb(128, BF),
-    "pi": sb(2, IN), "col": sb(16, FL), "Sm": sb(144, BF), "pf": sb(8, FL), "mn": sb(128, BF),
-    "KL": sb(4 * 128, BF), "Lr": sb(256, BF), "Sh": sb(4 * 128, BF), "Mk": sb(128, BF), "Us": sb(128, BF), "Cr": sb(128, FL),
-    "Zw": sb(144, BF), "Sr": sb(256, BF), "Yy": sb(144, HF), "Yd": sb(3 * 128, HF), "B1": sb(128, HF), "Y37": sb(128, HF), "nI": sb(128, BF),
-    "ut": sb(3 * 128, BF), "Um": sb(2 * 128, BF), "S0": sb(2 * 128, BF), "F32": sb(3 * 128, FL), "Cs": sb(4 * SEG, HF), "Cz": sb(1024, BF),
-    "xs": sb(4 * 192, BF), "xm": sb(2 * 1536, BF), "ge": sb(4 * 192, BF), "of": sb(4 * 192, FL),
+    "Hs": sb(CH + 128, BF), "Ps": sb(CP, BF), "W0": sb(2048, BF), "Wt": sb(2048 + 4096, FL),
+    "ptr": sb(CH + 128, FL), "pts": sb(CH + 128, FL), "pval": sb(320, FL),
+    "Dm": sb(128, BF), "Pm": sb(128, BF), "Gi": sb(192, BF), "Ix": sb(4 * SEG, BF), "Iy": sb(128, BF),
+    "pi": sb(2, IN), "col": sb(16, FL), "Sm": sb(144, BF), "mn": sb(128, BF), "I16": sb(128, BF), "sw": sb(192, BF),
+    "KL": sb(4 * 128, BF), "Lr": sb(256, BF), "Sh": sb(4 * 128, BF), "Mk": sb(64, BF), "dm": sb(128, BF), "Oh": sb(2 * 128, BF),
+    "Zw": sb(144, BF), "Sr": sb(320, BF), "B1": sb(128, HF), "I4": sb(128, HF), "Bq": sb(256, BF), "nI": sb(128, BF), "zr": sb(144, BF),
+    "kk": sb(64, BF), "My": sb(2 * 64, FL), "MA": sb(64, HF), "MF": sb(64, HF), "cm": sb(4, FL),
+    "F32": sb(2 * 128, FL), "Cs": sb(4 * SEG, HF), "Cz": sb(128, BF),
+    "xs": sb(4 * 192, BF), "xm": sb(1536, BF), "bz": sb(4 * 128, BF), "gz": sb(4 * 128, BF), "of": sb(4 * 192, FL),
     "ci": sb(192, IN), "cj": sb(4 * 192, IN), "coff": sb(4 * 192, UI), "hp": sb(2 * 3072, BF),
-    "zc": sb(384, HF), "zf": sb(192, HF), "zq": sb(192, HF), "at": sb(192, BF), "ai": sb(192, IN), "am": sb(192, IN),
-    "aoff": sb(2 * 192, UI), "eq": sb(192, BF), "src": sb(256, HF), "sd": sb(256, FL), "tb": sb(8 * SEG, HF), "so": sb(8 * SEG, HF),
-    "doff": sb(16, UI), "soff": sb(8, UI), "woff": sb(2 * 192, UI), "foff": sb(256, UI), "hold": sb(64, BF), "hnew": sb(64, BF),
-    "pg": sb(2 * 3072, BF), "pw": sb(2 * 3072, FL), "ps": sb(1024, FL), "pd": sb(1040, FL), "wb": sb(2048, FL),
+    "zc": sb(384, HF), "dq": sb(192, HF), "at": sb(192, BF), "se": sb(4 * 192, BF), "ea": sb(64, BF), "tv": sb(192, BF), "sv": sb(256, BF),
+    "aoff": sb(4 * 192, UI), "src": sb(64, HF), "sd": sb(64, FL), "tb": sb(8 * SEG, HF), "so": sb(8 * SEG, HF),
+    "doff": sb(4 * 16, UI), "soff": sb(8, UI), "woff": sb(4 * 192, UI), "wold": sb(4 * 64, UI), "foff": sb(256, UI), "hold": sb(64, BF), "hnew": sb(64, BF),
+    "pg": sb(4 * 3072, BF), "pw": sb(4 * 3072, FL), "pd": sb(1040, FL), "wb": sb(2048, FL),
     "ys": sb(4 * 192, FL), "Bo": sb(4 * 192, FL), "Bi": sb(4 * 192, FL), "wo": sb(2048, FL),
 }
 for _b in ("pa", "pz0", "pz1", "py", "pl0", "pl1", "pl2", "pq"):
     SCRATCH[_b] = ("psum", [128, 512], "float32")
-NDMA = 40
+NDMA = 72
 SEMAPHORES = ["e_pe", "e_v", "e_s", "e_g", "loc"] + ["d%d" % i for i in range(NDMA)]
 
 CUT = [0, 32, 64, 96, 128, 160, 192]
 CFG = {
-    "hcut": [CUT] * 4, "pcut": [CUT] * 4, "wcut": [CUT] * 4,
-    "rch": [[(0, 64), (64, 128), (128, 192)]] * 4,
+    "hcut": [CUT] * 4,
+    "pcut": [[[0, 8, 16]] * 3] * 4, "wcut": [[[0, 8, 16]] * 3] * 4,
     "a_at": {1: (0, 1), 2: (0, 2), 3: (1, 2)},
-    "am_s": {(t, a) for t in range(4) for a in (0, 64)},
-    "xm_c": {0},
-    "rscan": {(1, 128), (3, 128)}, "gate": True, "early": [0, 0, 0, 0], "share": 40,
+    "turn": {(1, 64), (2, 64), (3, 64)},
+    "late": set(), "bcut": [0, 32, 64, 96, 128],
+    "fold": {(0, 2): 1, (1, 2): 1, (2, 2): 1},
+    "send": [[(0, 128), (128, 192)]] * 4,
+    "sym": [(1,), (2, 3)],
+    "log": False,
     "fin": [0, 24, 56, 92, 128],
+    "g_l": {1, 2}, "g_c": {1, 2, 3}, "g_e": {(t, a) for t in (1, 2, 3) for a in (0, 64)}, "short": False, "chain": set(), "early": set(), "ybq": "s", "npw": 4, "SH": 100000, "gate": False, "GD": 1000.0, "GD1": 1000.0, "AD": 2.0,
     "G": 1.55, "SC": 4.2, "CY": 1.1, "OV": 50.0, "OS": 35.0, "MS": 40, "PE": 0.42, "WK": 140.0, "OV2": 0.0, "DI": 150.0, "DF": 1500.0, "BW": 370.0, "RF": 2000.0, "RC": 25.0, "RI": 500.0, "R1": 1000.0,
-    "tries": 5, "shuttle": 1200, "trim": 4000, "polish": 72000, "far": 1000.0, "pick": 0.02, "even": 0.0, "aim": 0.25, "mix": 0.25, "heat": 0.0003, "heat2": 0.001,
+    "seed": 0, "tries": 1, "shuttle": 600, "trim": 9000, "polish": 75000, "passes": 2, "far": 1000.0, "pick": 0.02, "swap": 0.5, "packs": (3, 4, 5), "slack": 0.0, "aim": 0.25, "mix": 1.0, "heat": 0.0003, "heat2": 0.002,
 }
 VARIANTS = [{}, {"G": 1.3, "SC": 2.8, "CY": 1.2, "BW": 420.0, "WK": 110.0, "DI": 100.0, "RC": 15.0},
             {"G": 2.7, "SC": 7.0, "CY": 1.35, "WK": 200.0, "BW": 300.0, "RF": 2800.0, "DI": 250.0, "RC": 40.0},
-            {"G": 1.4, "SC": 3.5, "CY": 1.05, "BW": 240.0, "RC": 35.0, "DF": 1900.0, "RF": 2800.0, "DI": 250.0, "RI": 1000.0, "R1": 2500.0},
-            {"G": 1.45, "CY": 1.0, "WK": 250.0, "OS": 80.0, "OV2": 15.0, "BW": 280.0},
-            {"G": 1.4, "CY": 1.05, "PE": 0.5, "RF": 3500.0, "RI": 700.0},
+            {"G": 1.4, "SC": 3.5, "CY": 1.05, "BW": 280.0, "RC": 30.0, "DF": 1900.0, "RF": 2800.0, "DI": 200.0, "RI": 1000.0, "R1": 2500.0},
+            {"G": 1.45, "CY": 1.0, "WK": 250.0, "OS": 80.0, "OV2": 15.0, "BW": 300.0},
+            {"G": 1.4, "CY": 1.05, "PE": 0.5, "RF": 3500.0, "RI": 700.0, "GD": 1500.0, "AD": 2.5},
             {"G": 2.0, "SC": 3.0, "CY": 1.2, "WK": 180.0, "OS": 15.0, "MS": 64, "OV2": 20.0, "BW": 260.0, "DF": 1200.0, "RF": 1500.0, "R1": 3000.0, "DI": 60.0}]
+QUEUES = ("pe", "v", "s", "g", "sync")
 ALU = AluOpType
 ACT = ActivationFunctionType
 
@@ -72,14 +79,16 @@ def real(T, a):
     if "win" in a:
         return real(T, a["win"]).indirect(real(T, a["off"]))
     if "ext" in a:
+        if a["ext"] == "rows":
+            return T[a["b"]][a["p0"]:a["p1"], a["c0"]:a["c1"]]
         return T[a["b"]][:, a["c0"]:a["c1"]] if a["ext"] == "cols" else T[a["b"]][:]
     if a["st"] == 1:
         return T[a["b"]][a["p0"]:a["p1"], a["c0"]:a["c1"]]
     return T[a["b"]][a["p0"]:a["p1"], a["c0"]:a["c1"]:a["st"]]
 
 
-def EXT(name, c0=None, c1=None):
-    return {"b": name, "ext": "all" if c0 is None else "cols", "c0": c0, "c1": c1}
+def EXT(name, c0=None, c1=None, p0=None, p1=None):
+    return {"b": name, "ext": "all" if c0 is None else "cols" if p0 is None else "rows", "c0": c0, "c1": c1, "p0": p0, "p1": p1}
 
 
 def in_psum(a):
@@ -105,7 +114,7 @@ def build(cfg):
             if c[0] == "remote":
                 ins, outs = c[1], [d[0] for d in c[2]]
             else:
-                ins, outs = list(c[2:]), [c[1]]
+                ins, outs = list(c[1 if c[0] == "dma_add" else 2:]), [c[1]]
             for a in ins:
                 if isinstance(a, dict) and "ext" not in a:
                     rd += [a["win"], a["off"]] if "win" in a else [a]
@@ -243,6 +252,9 @@ def build(cfg):
     def keep(out, a, pat, op, fill, base, cm):
         return add("g", [("affine_select", out, a, pat, op, fill, base, cm)], 170 + 2 * out["n"] * cy)
 
+    def plain(out, a):
+        return keep(out, a, [[0, out["n"]]], ALU.is_gt, 0.0, 1, 0)
+
     def dma(q, pairs, nbytes, after=(), behind=()):
         i = add(q, [("dma_start", o, a) for (o, a) in pairs], len(pairs) * (cfg["DI"] if q != "g" else 1000.0), "dma", after, nbytes)
         ops[i]["ord"] |= set(behind)
@@ -251,55 +263,65 @@ def build(cfg):
 
     def rem(srcs, dsts, nbytes):
         i = add("g", [("remote", srcs, dsts)], cfg["RI"], "rem", (), nbytes)
-        ops[i]["once"] = cfg["R1"] if len(dsts) > 1 else 0.0
         ops[i]["rows"] = 8 * len(srcs) * len(dsts)
         return i
 
     def gather(out, win, off, scale=None, eng="s"):
-        i = act(out, IND(win, off), ACT.Copy if scale is None else ACT.Identity, None, scale, eng)
-        if out["n"] >= 512 and ph[0] > cfg["share"]:
-            del ops[i]["both"]
+        return act(out, IND(win, off), ACT.Copy if scale is None else ACT.Identity, None, scale, eng)
+
+    adds = []
+
+    def dma_add(out, a):
+        i = add("g", [("dma_add", out, a)], cfg["GD"] + (0.0 if adds else cfg["GD1"]), "dma", (), int(512 * a["n"] * cfg["AD"]))
+        ops[i]["rows"] = 8
+        if adds:
+            ops[i]["ord"].add(adds[0])
+        adds.append(i)
         return i
 
     l_kap = dma("sync", [(A("kl", 0, 1), EXT("kap"))], 8192)
     l_lam = dma("s", [(A("kl", 1, 2), EXT("lam"))], 8192)
     l_past = dma("sync", [(A("snd", 0, 192), EXT("past"))], 49152, (), (l_kap,))
     l_com = dma("s", [(A("com", 0, 768, 1, 0, 8), EXT("coming"))], 12288, (), (l_lam,))
-    dma("s", [(A("snd", 192, 240), EXT("coming"))], 12288, (), (l_com,))
+    l_snd = dma("s", [(A("snd", 192, 240), EXT("coming"))], 12288, (), (l_com,))
     l_hist = dma("sync", [(A("Hs", 0, CH), EXT("hist"))], 524288, (), (l_past,))
-    iota(A("Dm", 0, 144), [[1, 144]], 0, -1)
+    mset(A("xm", 0, 1536), 0.0)
+    mset(A("zr", 0, 144), 0.0)
+    loads = {
+        "x": ([(A("xm", 192 * g, 192 * g + 192, 1, 16 * g, 16 * g + 16), EXT("past", 0, S, 16 * g, 16 * g + 16)) for g in range(8)], 49152),
+        "b": ([(A("bz", 16 * g, 16 * g + 16, 1, 0, 12), EXT("past", 0, S, 16 * g, 16 * g + 1)) for g in range(8)], 4096),
+        "s": ([(A("Ps", 0, CP), EXT("score"))], 1048576), "w": ([(A("W0", 0, 2048), EXT("weight"))], 524288)}
+    l_x = dma("sync", loads["x"][0], loads["x"][1], (), (l_hist,))
+    dma("s", loads["b"][0], loads["b"][1], (), (l_snd,))
+    iota(A("Dm", 0, 128), [[1, 128]], 0, -1)
     iota(A("pi", 0, 1), [[1, 1]], 0, 1)
     iota(A("Pm", 0, 128), [[-16, 8], [0, 16]], 0, 1)
-    iota(A("Gi", 0, 128, 1, 0, 8), [[1, 8], [0, 16]], 0, -1)
-    iota(A("Rw", 0, 4), [[1, 4]], 0, 0)
+    iota(A("Gi", 0, 192, 1, 0, 12), [[1, 12], [0, 16]], 0, -1)
     iota(A("Iy", 0, 128), [[0, 8], [1, 16]], 0, 0)
     iota(A("Ix", 0, 4 * SEG), [[-16, 4], [1, SEG]], 0, 0)
-    rem([A("snd", 0, 240)], [(A("lnd", 240 * (t - 1), 240 * t), HOP * t) for t in (1, 2, 3)], 3 * 61440)
+
+    def line(out, fill, base, cm):
+        return keep(out, A("zr", 0, out["n"], 1, 0, out["p1"]), [[1, out["n"]]], ALU.not_equal, fill, base, cm)
+
+    def symbols(steps):
+        return rem([A("snd", 0, 240)], [(A("lnd", 240 * (t - 1), 240 * t), HOP * t) for t in steps], len(steps) * 61440)
+    ops[symbols(cfg["sym"][0])].update(once=cfg["R1"], step=1)
+    iota(A("kk", 0, 64), [[1, 16], [0, 4]], 0, 0)
     first = [o["i"] for o in ops if o["eng"] == "g"]
     for i, j in zip(first, first[1:]):
         ops[j]["ord"].add(i)
-    iota(A("Em", 0, 144, 1, 0, 8), [[1, 144]], 0, -16)
-    for j in range(0 if 1 in cfg["xm_c"] else 3):
-        iota(A("xm", 1536 + 512 * j, 2048 + 512 * j), [[0, 512]], 0, 0)
-    iota(A("ptr", 0, 128), [[16, 128]], 0, 0)
-    iota(A("pval", 0, 192), [[16, 192]], 2048, 0)
-    iota(A("pval", 192, 256), [[16, 64]], 0, 0)
-    iota(A("pts", 0, 128), [[0, 128]], 1024, 0)
-    iota(A("pd", 1024, 1040), [[0, 16]], 0, 0)
-    for j in range(2 if cfg["rscan"] else 0):
-        iota(A("Cz", 512 * j, 512 * j + 512), [[0, 512]], 1, 0)
 
     def col(j, p1=128):
         return A("col", j, j + 1, 1, 0, p1)
-    LANE, PF, CE, CW, CZ, CB, CT, CV, CD = range(9)
+    LANE, PF, CW, L2, CD = range(5)
     D128 = A("Dm", 0, 128)
     ts(A("pi", 1, 2), A("pi", 0, 1), 15, None, ALU.bitwise_and)
     cp(col(PF), A("pi", 0, 1))
     cp(col(LANE), A("pi", 1, 2))
     ident = A("Sh", 0, 128)
     ts(ident, D128, 0.0, None, ALU.is_equal)
-    srep, sprev = A("Sr", 0, 128, 1, 0, 8), A("Sr", 128, 256, 1, 0, 8)
-    ts(srep, A("Gi", 0, 128, 1, 0, 8), 0.0, None, ALU.is_equal)
+    srep, sprev = A("Sr", 0, 128, 1, 0, 8), A("Sr", 192, 320, 1, 0, 8)
+    ts(A("Sr", 0, 192, 1, 0, 12), A("Gi", 0, 192, 1, 0, 12), 0.0, None, ALU.is_equal)
     ts(col(CW, 8), col(PF, 8), 7.0, -8.0, ALU.is_ge, ALU.mult)
     ts(sprev, A("Gi", 0, 128, 1, 0, 8), col(CW, 8), 1.0, ALU.subtract, ALU.is_equal)
     tt(A("mn", 0, 128), A("Pm", 0, 128), D128, ALU.min)
@@ -308,64 +330,79 @@ def build(cfg):
     cp(A("klf", 0, 4), A("kli", 0, 4))
     for j in (0, 2):
         split = ts(A("KL", 128 * j, 128 * j + 128), A("mn", 0, 128), 0.0, A("klf", j, j + 1), ALU.is_ge, ALU.mult)
-    l_score = dma("sync", [(A("Ps", 0, CP), EXT("score"))], 1048576, (split,) if cfg["gate"] else (), (l_hist,))
-    l_w = dma("sync", [(A("W0", 0, 2048), EXT("weight"))], 524288, () if cfg["gate"] else (l_hist,), (l_score,))
+    l_score = dma("sync", loads["s"][0], loads["s"][1], (split,) if cfg["gate"] else (), (l_x,))
+    l_w = dma("sync", loads["w"][0], loads["w"][1], (), (l_score,))
+    for steps in cfg["sym"][1:]:
+        i = symbols(steps)
+        ops[i]["ord"].add(first[-1])
+        ops[i]["sem"].add(l_score)
     for j in (1, 3):
         act(A("KL", 128 * j, 128 * j + 128), ident, ACT.Identity, None, A("klf", j, j + 1), "v")
     same = A("Sm", 0, 128)
     ts(same, A("Pm", 0, 128), col(LANE), None, ALU.is_equal)
     act(A("Sm", 128, 129), A("Sm", 0, 1), ACT.Copy)
-    table = act(col(CZ), col(LANE), ACT.Sigmoid, 128.0, -256.0)
+    table = act(A("Cz", 0, 128), A("Iy", 0, 128), ACT.Sigmoid, -128.0, 256.0)
     ops[table]["dur"] += 1300.0
-    i = act(A("pf", 0, 8), A("Sm", 0, 128, 16), ACT.Copy)
-    del ops[i]["both"]
-    ops[i]["ord"].add(table)
     for j in (0, 1):
         mm(A("py", 128 * j, 128 * j + 128, 1, 0, 8), [(A("Sm", 16, 129, 16), A("KL", 128 + 256 * j, 256 + 256 * j))])
     act(A("Lr", 0, 256, 1, 0, 8), A("py", 0, 256, 1, 0, 8), ACT.Copy)
-    mset(A("ut", 128, 384), ZC)
-    for (pz, n) in (("pz0", 128), ("pz1", 256)):
-        mm(A(pz, 0, n), [(ident, A("ut", 128, 128 + n))])
-    if len(cfg["am_s"]) < 2 * STEPS:
-        ts(col(CB), col(LANE), 3681.0, 37 * ZC, ALU.mult, ALU.add)
-    act(col(CT), col(LANE), ACT.Identity, 37 * ZC + TOP - 2047.5, 3681.0)
-    ts(col(CE), col(LANE), 8.0 / 4096, 1.0 / 4096, ALU.mult, ALU.max)
-    ts(A("Yy", 0, 144), A("Dm", 0, 144), 16.0, None, ALU.is_equal)
-    act(A("Yd", 256, 384), same, ACT.Identity, None, col(CZ))
-    tt(A("Yd", 0, 128), ident, A("Yd", 256, 384), ALU.subtract)
-    act(A("Yd", 128, 256), A("Yd", 0, 128), ACT.Identity, None, -16.0)
-    act(A("B1", 0, 128), same, ACT.Identity, None, 16.0)
-    add("s", [("activation", col(CV), col(LANE), ACT.Relu, -65536.0, 65536.0)], 15 + 64 * cy)
-    act(A("Us", 0, 128), same, ACT.Identity, None, col(CV))
-    ts(A("Mk", 0, 128), A("Iy", 0, 128), col(LANE), -2.0 ** 24, ALU.not_equal, ALU.mult)
-    act(A("Cr", 0, 128), A("Iy", 0, 128), ACT.Identity, -1.0e8, 2.0e8)
-    act(A("ut", 0, 128), same, ACT.Identity, None, -4096.0)
-    keep(A("ut", 0, 128), A("ut", 0, 128), [[-1, 128]], ALU.is_gt, 0.0, 0, 1)
-    keep(A("Um", 0, 128), A("ut", 0, 128), [[-1, 128]], ALU.not_equal, 4096.0, 0, 1)
-    keep(A("Um", 128, 256), A("Um", 0, 128), [[0, 8], [1, 16]], ALU.not_equal, 0.0, 0, 0)
-    ts(A("S0", 0, 128), ident, col(CZ), 4096.0, ALU.mult, ALU.mult)
-    act(A("S0", 128, 256), A("S0", 0, 128), ACT.Identity, None, -8.0)
+    for (pz, c) in (("pz0", 0), ("pz1", 0), ("pz1", 128)):
+        mm(A(pz, c, c + 128), [(A("zr", 0, 128), D128)])
+    act(A("cm", 3, 4), A("Sh", 17, 18), ACT.Identity, None, -3584.0 / ZC)
+    act(A("cm", 0, 1), A("Sh", 16, 17), ACT.Identity, A("cm", 3, 4), -97.0 / ZC)
+    act(A("cm", 1, 2), A("Sh", 17, 18), ACT.Identity, None, -8.0 / ZC)
+    act(A("cm", 2, 3), A("Sh", 16, 17), ACT.Identity, None, 4096.0 * 1536 / ZC)
+    ma, mf = A("My", 0, 64), A("My", 64, 128)
+    act(ma, A("kk", 0, 64), ACT.Identity, None, A("cm", 0, 1))
+    soon = [first[-1], keep(A("MA", 0, 64), ma, [[-1, 16], [-32, 4]], ALU.not_equal, 37.0, 0, 1)]
+    act(mf, A("Iy", 0, 64), ACT.Identity, A("cm", 2, 3), A("cm", 1, 2))
+    soon.append(keep(mf, mf, [[-32, 4], [-1, 16]], ALU.not_equal, -256.0, 0, 1))
+    keep(mf, mf, [[-32, 4], [0, 16]], ALU.not_equal, 256.0, 0, 1)
+    soon.append(keep(A("MF", 0, 64), mf, [[-32, 4], [1000, 16]], ALU.not_equal, 0.0, 0, 1))
+    soon.append(line(A("nI", 0, 128), -1.0, 0, -1))
+    later = len(ops)
+    iota(A("Oh", 128, 256), [[1, 16], [0, 8]], 0, 0)
+    iota(A("ptr", 0, 128), [[1, 128]], -128, 0)
+    iota(A("pval", 0, 256), [[1, 256]], 0, 0)
+    if not cfg["log"]:
+        iota(A("pval", 256, 320), [[16, 64]], 0, 0)
+        iota(A("pts", 0, 128), [[0, 128]], 1024, 0)
+        iota(A("pd", 1024, 1040), [[0, 16]], 0, 0)
+    plain(A("B1", 0, 128), same)
+    ts(A("dm", 0, 128), A("Iy", 0, 128), col(LANE), None, ALU.is_equal)
+    act(A("Mk", 0, 64), A("dm", 0, 64), ACT.Identity, -4096.0, 4096.0)
+    ts(A("Oh", 0, 128), A("Oh", 128, 256), col(LANE), None, ALU.is_equal)
+    act(col(L2), col(LANE), ACT.Identity, 2048.0, None)
     posI, posS = A("F32", 0, 128), A("F32", 128, 256)
-    act(A("nI", 0, 128), ident, ACT.Identity, None, -1.0)
-    act(A("Y37", 0, 128), ident, ACT.Identity, None, 37.0)
-    act(posI, ident, ACT.Copy)
-    act(A("F32", 128, 144), A("Yy", 128, 144), ACT.Identity, None, 1.0 / 32)
-    act(A("F32", 144, 256), A("Yy", 16, 128), ACT.Identity, None, 1.0 / 32)
+    act(A("I4", 0, 128), ident, ACT.Identity, None, 4096.0, "v")
+    if len(cfg["turn"]) < 2 * STEPS:
+        line(A("I16", 0, 128), 16.0, 0, -1)
+    if cfg["turn"]:
+        iota(A("Bq", 128, 256), [[-64, 2], [0, 16], [-16, 4]], 0, 1)
+        ts(A("Bq", 0, 128), A("Bq", 128, 256), col(LANE), 16.0, ALU.is_equal, ALU.mult)
+    line(posI, 1.0, 0, -1)
+    line(A("F32", 128, 144), 1.0 / 32, 112, -1)
+    line(A("F32", 144, 256), 1.0 / 32, 0, -1)
     for t in (1, 2, 3):
         keep(A("Sh", 128 * t, 128 * t + 128), same, [[1, 128]], ALU.is_equal, 0.0, -t, -1)
-    ts(A("Zw", 0, 144, 1, 0, 8), A("Em", 0, 144, 1, 0, 8), 2.0, None, ALU.is_equal)
-    ts(A("Cs", 0, 4 * SEG), A("Ix", 0, 4 * SEG), col(LANE), -12.0, ALU.is_equal, ALU.mult)
+    line(A("Zw", 0, 144, 1, 0, 8), 1.0, -2, -16)
+    ts(A("Cs", 0, 4 * SEG), A("Ix", 0, 4 * SEG), col(LANE), -0.75, ALU.is_equal, ALU.mult)
     ts(A("Cs", 0, 4 * SEG, SEG), A("Cs", 0, 4 * SEG, SEG), BIG, None, ALU.add)
-    ts(A("col", CD, CD + 4), A("Rw", 0, 4), 16.0, col(LANE), ALU.mult, ALU.add)
-    act(A("Cs", SEG - 1, 4 * SEG, SEG), A("col", CD, CD + 4), ACT.Identity, 12.0, -1.0 / 128)
-    for k in (0, 1):
+    act(col(CD), col(LANE), ACT.Identity, 0.75, -1.0 / 2048)
+    act(A("Cs", SEG - 1, 4 * SEG, SEG), A("Ix", 0, 4 * SEG, SEG), ACT.Identity, col(CD), 1.0 / 2048)
+    for k in (0, 1) if cfg["short"] else ():
         act(A("tb", 4 * SEG * k, 4 * SEG * (k + 1)), A("Ix", 0, 4 * SEG), ACT.Identity, BIG, 0.0)
-    if cfg["rscan"]:
-        mset(A("Cz", 0, 1024, 16), 0.0)
     for t in (1, 2, 3):
         dma("sync", [(A("com", 768 * t, 768 * t + 768, 1, 0, 8), A("lnd", 240 * (t - 1) + 192, 240 * t))], 12288, (), (l_w,))
+        dma("sync", [(A("bz", 128 * t + 16 * g, 128 * t + 16 * g + 16, 1, 0, 12),
+                      A("lnd", 240 * (t - 1) + 192, 240 * t, 1, 16 * g + 4 * t - 4, 16 * g + 4 * t)) for g in range(8)], 4096, (), (l_w,))
     for j in range(0, 2048, 512):
-        keep(A("Wt", j, j + 512), A("W0", j, j + 512), [[0, 512]], ALU.is_gt, 0.0, 1, 0)
+        plain(A("Wt", j, j + 512), A("W0", j, j + 512))
+    for i, j in zip(soon, soon[1:]):
+        ops[j]["ord"].add(i)
+    for o in ops[later:]:
+        if o["eng"] == "g":
+            o["ord"].add(soon[-1])
 
     def lane_in(i):
         return A("Zw", 2 - i, 130 - i, 1, 0, 8)
@@ -375,7 +412,7 @@ def build(cfg):
 
     def phase_a(t):
         ph[0] += 1
-        rot, s0, m0 = U * (t % 3), 192 * t, 1536 * (t % 2)
+        rot, s0 = U * (t % 3), 192 * t
         pieces = [(0, rot, S - rot)] + ([(S - rot, 0, rot)] if rot else [])
         x = A("xs", s0, s0 + 192) if t else A("snd", 0, 192)
         if t:
@@ -385,9 +422,12 @@ def build(cfg):
             act(x, A("pa", 0, 192), ACT.Copy)
 
         def columns(cs, a, b):
-            cp(A("ci", a, b), cs)
+            act(A("ci", a, b), cs, ACT.Copy, None, None, "s" if t else "v")
             ts(A("cj", s0 + a, s0 + b), A("ci", a, b), 5, 2047, ALU.logical_shift_right, ALU.bitwise_and)
-            cp(A("coff", s0 + a, s0 + b), A("cj", s0 + a, s0 + b))
+            if t in cfg["g_c"]:
+                plain(A("coff", s0 + a, s0 + b), A("cj", s0 + a, s0 + b))
+            else:
+                act(A("coff", s0 + a, s0 + b), A("cj", s0 + a, s0 + b), ACT.Copy, None, None, "s" if t else "v")
 
         def lrows(j):
             return [(A("pa", 192 + p, 192 + p + n), A("Lr", 128 * j, 128 * j + 128, 1, 0, 8), comc(t, t, u, n)) for (p, u, n) in pieces]
@@ -402,115 +442,134 @@ def build(cfg):
                 cs = A(name, 192 + a, 192 + b)
                 mm(cs, [(A("KL", 128 * j, 128 * j + 128), A("xs" if j % 2 else "snd", a, b)) for j in range(4)])
                 columns(cs, a, b)
-        if t in cfg["xm_c"]:
-            for g in range(8):
-                act(A("xm", m0 + 192 * g, m0 + 192 * g + 192), x, ACT.Identity, None, A("pf", g, g + 1), "s" if g < 4 - 4 * t else "v")
         for (p, u, n) in pieces:
             mm(A("pa", p, p + n), [(srep, comc(t, t, u, n))])
         ts(A("of", s0, s0 + 192), A("pa", 0, 192), col(LANE), -1.0, ALU.not_equal, ALU.mult)
-        ts(A("ge", s0, s0 + 192), x, 8.0, None, ALU.is_ge)
+        ts(A("gz", 128 * t, 128 * t + 128, 1, 0, 12), A("bz", 128 * t, 128 * t + 128, 1, 0, 12), 8.0, -8.0, ALU.is_ge, ALU.mult)
 
     def phase_h(t, a, b, pz):
         ph[0] += 1
         par, n, s0 = t % 2, b - a, 192 * t
-        h0, m0, nb = 3072 * par, 1536 * par, n // 4
-        if a == 0 and t not in cfg["xm_c"]:
+        h0, m0 = 3072 * par, 0
+        if a == 0 and t:
             dma("sync", [(A("xm", m0 + 192 * g, m0 + 192 * g + 192, 1, 16 * g, 16 * g + 16), A("xs", s0, s0 + 192, 1, 16 * g, 16 * g + 16))
                          for g in range(8)], 49152)
         cut = [c for c in cfg["hcut"][t] if a <= c <= b]
         for c, d in zip(cut, cut[1:]):
             gather(A("hp", h0 + 16 * c, h0 + 16 * d), A("Hs", 0, CH), A("coff", s0 + c, s0 + d), None, "v" if t == 0 and c % 64 else "s")
-        for q in range(4):
-            mrun([("matmul", A(pz, 8 * j, 8 * j + 8, 1, 32 * q, 32 * q + 16), A("hp", h0 + 16 * u, h0 + 16 * u + 16),
-                   A("xm", m0 + u, m0 + 1536, 192), True, True) for j, u in enumerate(range(a + q * nb, a + q * nb + nb))])
+        for u0 in range(a, b, 16):
+            q, c = u0 // 16 % 4, 2 * ((u0 - a) // 64 * 64)
+            mrun([("matmul", A(pz, c + r, c + 128, 16, 32 * q, 32 * q + 16), A("hp", h0 + 16 * (u0 + r), h0 + 16 * (u0 + r) + 16),
+                   A("xm", m0 + u0 + r, m0 + 1536, 192), True, True) for r in range(16)])
         act(A("zc", 2 * a, 2 * b), A(pz, 0, 2 * n), ACT.Identity, -ZC, None)
-        py = "pq" if a else "py"
-        d, z = A(pz, 2 * n, 3 * n), A(py, a, b)
-        back = []
-        for q in range(4):
-            for g in range(8):
-                h, m = 1 - g % 2, 32 - 16 * (g % 2)
-                back.append(("matmul", A(py, a + q * nb, a + q * nb + nb, 1, 32 * (g // 2), 32 * (g // 2) + m),
-                             A("Yy", 32 * q + 16 - 16 * h, 32 * q + 16 - 16 * h + m), A("zc", 2 * a + (g ^ 1), 2 * b, 8), h == 1, h == 0))
-        mrun(back)
-        acts([(A("zf", a, b), z, ACT.Copy, None, None), (A("zq", a, b), z, ACT.Identity, 1536.0 + 1.0 / 32, 1.0 / 16)])
-        mm(d, [(A("Yd", 0, 128), A("zf", a, b)), (A("Yd", 128, 256), A("zq", a, b))])
-        ts(A("eq", a, b), d, 0.0, None, ALU.is_equal)
-        ao = A("aoff", 192 * par + a, 192 * par + b)
-        if (t, a) in cfg["am_s"]:
-            act(A("at", a, b), A("zf", a, b), ACT.Identity, col(CT), 37.0)
-            r = A(py, 256 + a, 256 + b)
-            mm(r, [(A("Y37", 0, 128), A("zf", a, b)), (A("nI", 0, 128), A("at", a, b))])
-            ts(ao, r, col(CT), 2047.5, ALU.add, ALU.add)
-        else:
-            ts(A("ai", a, b), A("zf", a, b), 37.0, col(CB), ALU.mult, ALU.add)
-            ts(A("am", a, b), A("ai", a, b), 4095, None, ALU.bitwise_and)
-            cp(ao, A("am", a, b))
 
-    def phase_m(t, a, b, pz):
+    def turned(bank, c0, a, b, const):
+        return [(A(bank, c0 + u - a, c0 + u - a + 64), A("zc", 2 * u, 2 * u + 128), A(const, 0, 64)) for u in range(a, b, 64)]
+
+    def elist(t, a, b):
+        return A("doff", 16 * t + 4 + a // 16, 16 * t + 4 + b // 16)
+
+    def phase_e(t, a, b):
         ph[0] += 1
-        par, n, s0 = t % 2, b - a, 192 * t
-        hu = a == 0 and t < STEPS - 1
-        xb = "xs" if t else "snd"
-        vp, sel = A(pz, 3 * n, 4 * n), A(pz, 256, 320)
-        if hu:
-            mm(sel, [(A("Um", 0, 128), A("eq", 0, 64))])
-        mm(vp, [(A("S0", 0, 128), A(xb, s0 + a, s0 + b)), (A("S0", 128, 256), A("ge", s0 + a, s0 + b)), (A("Um", 128, 256), A("eq", a, b))])
-        if hu:
-            tt(A("src", 0, 64), sel, A("cj", s0, s0 + 64), ALU.min)
-        act(A("src", 64 + a, 64 + b), vp, ACT.Relu, None, col(CE), "v")
-        r0 = 0 if hu else 64 + a
-        d0, d1 = r0 // 16, (64 + b) // 16
-        w = 64 + b - r0
-        wo = A("woff", 192 * par + a, 192 * par + b)
-        rp = 384 if a == 0 else 2 * n - r0
+        n, py, e0 = b - a, "pq" if a else "py", 192 * t
+        group(turned(py, 0, a, b, "MF"))
+        act(A("dq", a, b), A(py, 0, n), ACT.Identity, 1.0 / 64 - 15.0 / 32, -1.0 / 4096)
+        new = [(A(py, n + u - a, n + u - a + 64), A(x, 128 * t, 128 * t + 128, 1, 0, 12), A("Sr", (u + U * t) % S, (u + U * t) % S + 64, 1, 0, 12))
+               for u in range(a, b, 64) for x in ("bz", "gz")]
+        group(turned(py, n, a, b, "MF") + new + [(A(py, n, 2 * n), A("I4", 0, 128), A("dq", a, b))])
+        scan(A("se", e0 + a, e0 + b), A("Cz", 0, n), A(py, n, 2 * n), ALU.mult, ALU.max)
+        if (t, a) in cfg["g_e"]:
+            plain(elist(t, a, b), A("se", e0 + a + 15, e0 + b, 16))
+        elif t or a == 0 or (t, a) in cfg["turn"]:
+            act(elist(t, a, b), A("se", e0 + a + 15, e0 + b, 16), ACT.Copy, None, None, "v")
 
-        pr = pz if a else "py"
+    def phase_s(t, a, b, pz):
+        ph[0] += 1
+        n = b - a
+        group(turned(pz, 2 * n, a, b, "MA"))
+        act(A("at", a, b), A(pz, 2 * n, 3 * n), ACT.Identity, 37 * ZC + TOP - 2047.5, None)
+        group(turned(pz, 3 * n, a, b, "MA") + [(A(pz, 3 * n, 4 * n), A("nI", 0, 128), A("at", a, b))])
+        act(A("aoff", 192 * t + a, 192 * t + b), A(pz, 3 * n, 4 * n), ACT.Identity, 37 * ZC + TOP, None, "v")
 
-        def lanes(name, c0):
-            return [(A(name, c0, c0 + w), A("B1", 0, 128), A("src", r0, 64 + b))] + ([(A(name, c0, c0 + 64), A("Us", 0, 128), A("eq", 0, 64))] if hu else [])
-        if a == 0 or t == 0:
-            group(lanes(pr, rp + r0))
-        if a == 0 or t > 0:
-            m0 = 128 if a == 0 else 2 * n
-            mk = A(pz, m0, m0 + w)
-            group(lanes(pz, m0) + [(mk, ident, A("Mk", 0, w))])
-            scan(A("sd", r0, r0 + w), A("Cr", 0, w), mk, ALU.min, ALU.max)
-            dp = A("sd", r0 + 15, r0 + w, 16)
-            ts(A("doff", d0, d1), dp, 1.0 / 16, None, ALU.mult)
-        if t == 0:
-            ts(wo, A(pr, rp + 64 + a, rp + 64 + b), col(LANE), None, ALU.add)
+    def phase_w(t, a, b):
+        ph[0] += 1
+        n, py, nk = b - a, "pq" if a else "py", 8 if t else 16
+        turn = (t, a) in cfg["turn"]
+        if t or turn:
+            tt(A("tv", a, b), IND(A("ptr", 0, 128), elist(t, a, b)), A("dm", 0, n), ALU.mult)
+        if turn:
+            mm(A(py, 384, 512, 1, 0, n), [(A("tv", a, b), ident)])
+            sv = A("sv", 2 * a, 2 * a + 128, 1, 0, n)
+            act(sv, A(py, 384, 512, 1, 0, n), ACT.Copy)
+        elif t:
+            scan(A("sw", a, b), A("Cz", 0, n), A("tv", a, b), ALU.mult, ALU.add)
+        items = []
+        for u in range(0, n, 64):
+            c = 2 * n + u // 16 * nk
+            items += [(A(py, c, c + 4 * nk), ident, A("kk", 0, 4 * nk))]
+            if turn:
+                items += [(A(py, c, c + 4 * nk), sv, A("Bq", u, u + 4 * nk, 1, 0, n))]
+            else:
+                items += [(A(py, c + 4 * k, c + 4 * k + 4), A("I16", 0, 128), A("sw" if t else "se", a + u + 15, a + u + 64, 16)) for k in range(nk)]
+        group(items)
+        act(A("woff", 192 * t + a // 16 * nk, 192 * t + b // 16 * nk), A(py, 2 * n, 2 * n + n // 16 * nk), ACT.Identity, 2048.0 if t or turn else 0.0, None, "v")
+
+    def repeats(k, lanes, own, target):
+        act(A("tb", 4 * SEG * k + SEG - 1, 4 * SEG * (k + 1), SEG), A(target[0], target[1] + 15, target[1] + 64, 16), ACT.Identity, 0.5, -1.0 / 4096)
+        w = [16 + 16 * q if cfg["short"] else 64 for q in range(4)]
+        acts([(A("tb", SEG * (4 * k + q), SEG * (4 * k + q) + w[q]), A(lanes[0], lanes[1], lanes[1] + w[q]), ACT.Abs,
+               A(own[0], own[1] + 16 * q + 15, own[1] + 16 * q + 16), -1.0) for q in range(4)])
+        scan(A("so", 4 * SEG * k, 4 * SEG * (k + 1)), A("Cs", 0, 4 * SEG), A("tb", 4 * SEG * k, 4 * SEG * (k + 1)), ALU.add, ALU.min)
+        act(A("soff", 4 * k, 4 * k + 4), A("so", 4 * SEG * k + SEG - 1, 4 * SEG * (k + 1), SEG), ACT.Identity, 2048.0, -4096.0, "v")
+
+    def phase_c(t):
+        ph[0] += 1
+        s0, cl = 192 * t, A("doff", 16 * t, 16 * t + 4)
+        tt(A("src", 0, 64), IND(A("Oh", 0, 128), elist(t, 0, U)), A("cj", s0, s0 + 64), ALU.mult)
+        mk = A("py", 256, 320)
+        mm(mk, [(ident, A("Mk", 0, 64)), (A("B1", 0, 128), A("src", 0, 64))])
+        mm(A("py", 192, 256), [(A("B1", 0, 128), A("src", 0, 64))])
+        scan(A("sd", 0, 64), A("Cz", 0, 64), mk, ALU.mult, ALU.max)
+        if t in cfg["g_l"]:
+            plain(cl, A("sd", 15, 64, 16))
         else:
-            ts(wo, IND(A("ptr", 0, 128), A("doff", 4 + a // 16, 4 + b // 16)), col(LANE), None, ALU.add)
-        if a == 0:
-            act(A("tb", SEG * d0 + SEG - 1, 8 * SEG, SEG), dp, ACT.Identity, 8.0, -1.0 / 4096)
-            for k in ((0, 1) if hu else (1,)):
-                acts([(A("tb", SEG * q, SEG * q + 16 + 16 * (q % 4)), A(pr, 384 + 64 * k, 400 + 64 * k + 16 * (q % 4)), ACT.Abs,
-                       A("sd", 16 * q + 15, 16 * q + 16), -1.0) for q in range(4 * k, 4 * k + 4)])
-                scan(A("so", 4 * SEG * k, 4 * SEG * (k + 1)), A("Cs", 0, 4 * SEG), A("tb", 4 * SEG * k, 4 * SEG * (k + 1)), ALU.add, ALU.min)
-                ts(A("soff", 4 * k, 4 * k + 4), A("so", 4 * SEG * k + SEG - 1, 4 * SEG * (k + 1), SEG), -256.0, 2048.0, ALU.mult, ALU.add)
-        if hu:
-            gather(A("hold", 0, 64), A("Hs", 0, CH), A("doff", 0, 4))
-            mm(A(pz, 320, 384), [(lane_in(0), comc(t, t, U * (t % 3), 64)), (A("Sh", 128, 256), A("hold", 0, 64))])
-            act(A("hnew", 0, 64), A(pz, 320, 384), ACT.Copy)
+            act(cl, A("sd", 15, 64, 16), ACT.Copy, None, None, "v")
+        repeats(0, ("py", 192), ("sd", 0), ("sd", 0))
+        gather(A("hold", 0, 64), A("Hs", 0, CH), cl)
+        mm(A("py", 320, 384), [(lane_in(0), comc(t, t, U * (t % 3), 64)), (A("Sh", 128, 256), A("hold", 0, 64))])
+        act(A("hnew", 0, 64), A("py", 320, 384), ACT.Copy)
+
+    def phase_m(t):
+        ph[0] += 1
+        if t == 0:
+            act(A("ea", 0, 64), IND(D128, elist(t, 0, U)), ACT.Identity, col(PF), None)
+            repeats(1, ("ea", 0), ("se", 0), ("se", 0))
+            act(A("wold", 0, 64), A("ea", 0, 64), ACT.Identity, col(LANE), 16.0)
+            return
+        mm(A("py", 384, 448), [(same, A("tv", 0, 64))])
+        if t < STEPS - 1 or cfg["log"]:
+            act(A("wold", 64 * t, 64 * t + 64), A("py", 384, 448), ACT.Identity, col(L2), 16.0)
+        repeats(1, ("py", 384), ("sw", 0), ("se", 192 * t))
 
     def phase_u(t):
         ph[0] += 1
         if t < STEPS - 1:
             cp(IND(A("Hs", 0, CH + 128), A("soff", 0, 4)), A("hnew", 0, 64))
-        cp(IND(A("ptr" if t < STEPS - 1 else "pts", 0, CH + 128), A("soff", 4, 8)), A("pval", 64 * t, 64 * t + 64))
+        if t < STEPS - 1 or cfg["log"]:
+            cp(IND(A("ptr", 0, CH + 128), A("soff", 4, 8)), A("pval", 64 * t, 64 * t + 64))
+        else:
+            cp(IND(A("pts", 0, CH + 128), A("soff", 4, 8)), A("pval", 256, 320))
 
     def phase_r(t):
-        par, s0 = t % 2, 192 * t
-        g0 = 3072 * par
+        s0, g0, f0 = 192 * t, 3072 * t, 3072 * (t % cfg["npw"])
         win = A("Wt", 0, 2048 + 1024 * t) if t else A("W0", 0, 2048)
         last = t == STEPS - 1
-        early = set()
         if last:
-            early.add(ts(A("foff", 128, 256), A("pts", 0, 128), col(LANE), None, ALU.add))
-            ts(A("foff", 0, 128), A("ptr", 0, 128), col(LANE), None, ALU.add)
-            for a in range(0, 128, 32):
-                gather(A("wb", 16 * a, 16 * a + 512), win, A("foff", a, a + 32))
+            act(A("foff", 0, 128), A("ptr", 0, 128), ACT.Identity, col(L2), 16.0)
+        if last and not cfg["log"]:
+            act(A("foff", 128, 256), A("pts", 0, 128), ACT.Identity, col(LANE), None)
+            for a, b in zip(cfg["bcut"], cfg["bcut"][1:]):
+                gather(A("wb", 16 * a, 16 * b), win, A("foff", a, b))
 
         def landed(a, b):
             return [(u, v, A("Bi", 192 * (t - 1) + (u + U) % S, 192 * (t - 1) + (u + U) % S + v - u))
@@ -518,41 +577,51 @@ def build(cfg):
 
         def carry(name, c0, const, a, b):
             return [(A(name, c0 + u - a, c0 + v - a), const, x) for (u, v, x) in landed(a, b)]
-        for n, (c, e) in enumerate(cfg["rch"][t]):
+        prods = []
+
+        def update():
             ph[0] += 1
-            pl = "pl%d" % n
-            lg, ys = A(pl, 0, e - c), A("ys", s0 + c, s0 + e)
-            cut = [u for u in cfg["pcut"][t] if c <= u <= e]
-            for u, v in zip(cut, cut[1:]):
-                gather(A("pg", g0 + 16 * u, g0 + 16 * v), A("Ps", 0, CP), A("aoff", 192 * par + u, 192 * par + v), 1.0 / 32)
-            cut = [u for u in cfg["wcut"][t] if c <= u <= e]
-            for u, v in zip(cut, cut[1:]):
-                i = tt(A("pw", g0 + 16 * u, g0 + 16 * v), IND(win, A("woff", 192 * par + u, 192 * par + v)), A("pg", g0 + 16 * u, g0 + 16 * v), ALU.mult)
-                if u < cfg["early"][t]:
-                    early.add(i)
-            if (t, c) in cfg["rscan"]:
-                scan(A("ps", 0, 16 * (e - c)), A("Cz", 0, 16 * (e - c)), A("pw", g0 + 16 * c, g0 + 16 * e), ALU.mult, ALU.add)
-                group(carry(pl, 0, posS, c, e) + [(lg, posI, A("ps", 15, 16 * (e - c), 16))])
-            else:
-                group([(lg, posI, A("pw", g0 + 16 * c + k, g0 + 16 * e, 16)) for k in range(16)] + carry(pl, 0, posS, c, e))
+            for k0 in range(0, 16, 4):
+                cs = [("tensor_tensor", A("pd", k, 1024, 16), A("pg", g0 + 64 * k, g0 + 64 * k + 64), A("pl0", 64, 128), ALU.mult) for k in range(k0, k0 + 4)]
+                i = add("v", cs, sum(vcost(x[1], [x[2], x[3]], True) for x in cs))
+                if t in cfg["early"]:
+                    prods.append(i)
+            if not last or cfg["log"]:
+                tt(A("Wt", 2048 + 1024 * t, 3072 + 1024 * t), IND(win, A("wold", 64 * t, 64 * t + 64)), A("pd", 0, 1024), ALU.add)
+        for n in range(3):
+            if n == 2:
+                update()
+            ph[0] += 1
+            c, e, pl, b0 = 64 * n, 64 * n + 64, "pl%d" % n, g0 + 1024 * n
+            lg, ys = A(pl, 0, 64), A("ys", s0 + c, s0 + e)
+            cut = cfg["pcut"][t][n]
+            for k, l in zip(cut, cut[1:]):
+                gather(A("pg", b0 + 64 * k, b0 + 64 * l), A("Ps", 0, CP), A("aoff", s0 + c + 4 * k, s0 + c + 4 * l), 1.0 / 32)
+            cut, f = cfg["wcut"][t][n], f0 + 1024 * n
+            for k, l in zip(cut, cut[1:]):
+                h = 8 * (k // 8) if t else 0
+                w0 = s0 + (c // 2 if t else c) - 4 * h
+                i = tt(A("pw", f + 64 * k, f + 64 * l), IND(A(win["b"], h, win["c1"]), A("woff", w0 + 4 * k, w0 + 4 * l)), A("pg", b0 + 64 * k, b0 + 64 * l), ALU.mult)
+                if t in cfg["chain"] and prods:
+                    ops[i]["ord"].add(prods[-1])
+                prods.append(i)
+            nk = 16
+            for j in range(cfg["fold"].get((t, n), 0)):
+                nk //= 2
+                dma_add(A("pw", f, f + 64 * nk), A("pw", f + 64 * nk, f + 128 * nk))
+            group([(lg, posI, A("pw", f + 64 * k, f + 64 * k + 64)) for k in range(nk)] + carry(pl, 0, posS, c, e))
             act(ys, lg, ACT.Sigmoid, None, -32.0)
             if c == 0:
-                er = A(pl, 64, 128)
-                mm(er, [(posI, A("of", s0, s0 + 64)), (posI, ys)])
-                continue
-            a, b = (0, e) if c == 64 else (c, e)
-            for (u, v, x) in landed(a, b):
-                act(A("Bo", s0 + u, s0 + v), x, ACT.Identity, None, 0.5)
-            srcs = [A(x, s0 + a, s0 + b) for x in (("Bo", "of", "ys") if t else ("of", "ys"))]
-            rem(srcs, [(A("Bi", s0 + a, s0 + b), -HOP * (STEPS - 1) if last else HOP)], 512 * (b - a) * len(srcs))
-            if last:
-                dma("s", [(EXT("yb", a, b), A("Bi", s0 + a, s0 + b))], 512 * (b - a))
-        ph[0] += 1
-        for k0 in range(0, 16, 4):
-            cs = [("tensor_tensor", A("pd", k, 1024, 16), A("pg", g0 + k, g0 + 1024, 16), er, ALU.mult) for k in range(k0, k0 + 4)]
-            ops[add("v", cs, sum(vcost(x[1], [x[2], x[3]], True) for x in cs))]["ord"] |= early
-        if not last:
-            tt(A("Wt", 2048 + 1024 * t, 3072 + 1024 * t), IND(win, A("woff", 192 * par, 192 * par + 64)), A("pd", 0, 1024), ALU.add)
+                mm(A(pl, 64, 128), [(posI, A("of", s0, s0 + 64)), (posI, ys)])
+            for (a, b) in cfg["send"][t]:
+                if b != e:
+                    continue
+                for (u, v, x) in landed(a, b):
+                    act(A("Bo", s0 + u, s0 + v), x, ACT.Identity, None, 0.5)
+                srcs = [A(x, s0 + a, s0 + b) for x in (("Bo", "of", "ys") if t else ("of", "ys"))]
+                rem(srcs, [(A("Bi", s0 + a, s0 + b), -HOP * (STEPS - 1) if last else HOP)], 512 * (b - a) * len(srcs))
+                if last:
+                    dma(cfg["ybq"], [(EXT("yb", a, b), A("Bi", s0 + a, s0 + b))], 512 * (b - a))
 
     phase_a(0)
     for t in range(STEPS):
@@ -565,15 +634,27 @@ def build(cfg):
         ahead(0)
         for ((a, b), pz) in ch:
             phase_h(t, a, b, pz)
+            phase_e(t, a, b)
+            phase_s(t, a, b, pz)
+            if a == 0 and t < STEPS - 1:
+                phase_c(t)
+            phase_w(t, a, b)
         ahead(1)
-        for ((a, b), pz) in ch:
-            phase_m(t, a, b, pz)
+        phase_m(t)
         ahead(2)
         phase_u(t)
         phase_r(t)
     ph[0] += 1
     for a, b in zip(cfg["fin"], cfg["fin"][1:]):
-        tt(A("wo", 16 * a, 16 * b), IND(A("pd", 0, 1040), A("foff", 128 + a, 128 + b)), A("wb", 16 * a, 16 * b), ALU.add)
+        if cfg["log"]:
+            gather(A("wo", 16 * a, 16 * b), A("Wt", 0, 2048 + 1024 * STEPS), A("foff", a, b))
+        elif a in cfg["late"]:
+            old = dma("sync", [(EXT("yw", 16 * a, 16 * b), A("wb", 16 * a, 16 * b))], 8192 * (b - a))
+            gather(A("wo", 16 * a, 16 * b), A("pd", 0, 1040), A("foff", 128 + a, 128 + b))
+            ops[dma_add(EXT("yw", 16 * a, 16 * b), A("wo", 16 * a, 16 * b))]["sem"].add(old)
+            continue
+        else:
+            tt(A("wo", 16 * a, 16 * b), IND(A("pd", 0, 1040), A("foff", 128 + a, 128 + b)), A("wb", 16 * a, 16 * b), ALU.add)
         dma("sync", [(EXT("yw", 16 * a, 16 * b), A("wo", 16 * a, 16 * b))], 8192 * (b - a))
     return ops
 
@@ -582,7 +663,7 @@ def landing(o, issued, pipe, cfg):
     first, own = issued + (cfg["RF"] if o["kind"] == "rem" else cfg["DF"]) - 500.0, o["bytes"] / cfg["BW"] + o["rows"] * cfg["RC"]
     first += o.get("once", 0.0)
     after = max(pipe, first) + own
-    return (min(after, first + 2 * own) if o["bytes"] < 100000 else after) + 500.0, max(pipe, issued + cfg["DF"] - 500.0) + own
+    return (min(after, first + 2 * own) if o["bytes"] < cfg["SH"] else after) + 500.0, max(pipe, issued + cfg["DF"] - 500.0) + own
 
 
 def replay(ops, order, cfg):
@@ -605,6 +686,19 @@ def replay(ops, order, cfg):
 def assign(opss, i, eng):
     for ops in opss:
         ops[i].update(eng=eng, calls=ops[i]["both"][eng][0], dur=ops[i]["both"][eng][1])
+
+
+def direct(ops):
+    above, sems, soft = [0] * len(ops), [], []
+    for i, o in enumerate(ops):
+        for j in o["sem"] | o["ord"]:
+            above[i] |= above[j]
+        near = {j for j in o["bank"] & o["sem"] if "pe" not in (ops[j]["eng"], o["eng"])}
+        sems.append([j for j in sorted(o["sem"] - near) if not above[i] >> j & 1])
+        soft.append([j for j in sorted(near) if not above[i] >> j & 1])
+        for j in o["sem"] - near:
+            above[i] |= 1 << j
+    return sems, soft
 
 
 def shuttle(opss, cfgs, order, rounds, seed=0):
@@ -632,7 +726,7 @@ def shuttle(opss, cfgs, order, rounds, seed=0):
             for (j, w) in before[i]:
                 if prio[i] <= prio[j]:
                     prio[i] = prio[j] + 0.001
-        busy = {e: [] for e in ("pe", "v", "s", "g", "sync")}
+        busy = {e: [] for e in QUEUES}
         end = [0.0] * n
         for i in sorted(walk, key=lambda i: prio[i]):
             t, o = first[i], ops[i]
@@ -649,9 +743,30 @@ def shuttle(opss, cfgs, order, rounds, seed=0):
             busy[o["eng"]].insert(p, (t, end[i]))
         return end
 
-    def value(od):
-        return sum(np.log(replay(o, od, c) + c["even"] * max(sum(x["dur"] for x in o if x["eng"] == e) for e in "vs"))
-                   for o, c in zip(opss, cfgs)) / len(cfgs)
+    sems, soft = direct(opss[0])
+    part = [0.0] * len(cfgs)
+
+    def value(od, bar=None):
+        got = []
+        for ops, c in zip(opss, cfgs):
+            free, ready, pipe, wk = {e: 0.0 for e in QUEUES}, [0.0] * n, 0.0, c["WK"]
+            for i in od:
+                o = ops[i]
+                t = free[o["eng"]]
+                for j in sems[i]:
+                    if ready[j] > t:
+                        t = ready[j]
+                for j in soft[i]:
+                    if ready[j] > t and ops[j]["eng"] != o["eng"]:
+                        t = ready[j]
+                free[o["eng"]] = t = t + o["dur"]
+                if o["kind"] != "c":
+                    t, pipe = landing(o, t, pipe, c)
+                ready[i] = t + wk
+            got.append(math.log(max(ready) - wk))
+            if bar is not None and sum(got) - sum(part[:len(got)]) > len(cfgs) * bar + 0.02:
+                return 1e9, got
+        return sum(got) / len(cfgs), got
     zero = [0.0] * n
     if order is None:
         replay(opss[0], range(n), cfgs[0])
@@ -661,12 +776,13 @@ def shuttle(opss, cfgs, order, rounds, seed=0):
             way[i] = opss[0][i]["dur"] + max([wait[i]] + [way[j] + (wait[i] if w else 0.0) for (j, w) in succ[i]])
         fore = pack(opss[0], [-x for x in way], range(n), pred, zero, wait, zero, 0.0)
         order = sorted(range(n), key=lambda i: (fore[i] - opss[0][i]["dur"], i))
-    cur = best = value(order)
+    cur, part[:] = value(order)
+    best = cur
     keep = (order, [o["eng"] for o in opss[0]])
     either = [o["i"] for o in opss[0] if "both" in o]
     for r in range(rounds):
-        v = int(rnd.randint(len(cfgs)))
-        ops, wk = opss[v], cfgs[v]["WK"]
+        v = cfgs[0]["packs"][int(rnd.randint(len(cfgs[0]["packs"])))] % len(cfgs)
+        ops, wk = opss[v], cfgs[v]["WK"] + cfgs[0]["slack"]
         was = [ops[i]["eng"] for i in either]
         replay(ops, order, cfgs[v])
         lat = [o["t1"] - o["t0"] - o["dur"] for o in ops]
@@ -680,9 +796,10 @@ def shuttle(opss, cfgs, order, rounds, seed=0):
         whole = {int(rnd.randint(ops[-1]["key"][1] + 1)): float(rnd.normal()) * cfgs[0]["far"] for s in range(int(rnd.randint(2)))}
         fore = pack(ops, [whole.get(o["key"][1], 0.0) - x for o, x in zip(ops, back)], range(n), pred, zero, wait, zero, 600.0 * rnd.rand() + 300.0 if pick > 1 - cfgs[0]["pick"] else 0.0)
         od = sorted(range(n), key=lambda i: (fore[i] - ops[i]["dur"], i))
-        x = value(od)
-        if x <= cur + cfgs[0]["heat2"] * (1 - r / rounds) * rnd.exponential():
-            order, cur = od, x
+        room = cfgs[0]["heat2"] * (1 - r / rounds) * rnd.exponential()
+        x, got = value(od, room)
+        if x <= cur + room:
+            order, cur, part[:] = od, x, got
             if x < best:
                 best, keep = x, (od, [o["eng"] for o in ops])
         else:
@@ -699,15 +816,10 @@ def polish(opss, cfgs, order, rounds, seed=0):
     n = len(ops)
     pred = [sorted(o["sem"] | o["ord"]) for o in ops]
     succ = [[] for o in ops]
-    above = [0] * n
-    sems = []
-    for i, o in enumerate(ops):
+    sems, soft = direct(ops)
+    for i in range(n):
         for j in pred[i]:
             succ[j].append(i)
-            above[i] |= above[j]
-        sems.append([j for j in sorted(o["sem"]) if not above[i] >> j & 1])
-        for j in o["sem"]:
-            above[i] |= 1 << j
     engs = sorted({o["eng"] for o in ops})
     eng = [engs.index(o["eng"]) for o in ops]
     durs = [[o["dur"] for o in x] for x in opss]
@@ -734,9 +846,12 @@ def polish(opss, cfgs, order, rounds, seed=0):
             for j in sems[i]:
                 if ready[j] > t:
                     t = ready[j]
+            for j in soft[i]:
+                if ready[j] > t and eng[j] != e:
+                    t = ready[j]
             fin[i] = free[e] = t = t + dur[i]
             if moving[i]:
-                t, pipe = landing(ops[i], t, pipe, cfgs[v])
+                t, pipe = landing(opss[v][i], t, pipe, cfgs[v])
                 load[i] = pipe
             ready[i] = t + wk
         return fin, ready, load
@@ -772,7 +887,7 @@ def polish(opss, cfgs, order, rounds, seed=0):
                     pairs.append((a, i))
                 i = a
             else:
-                i = max(sems[i], key=lambda j: ready[j])
+                i = max(sems[i] + soft[i], key=lambda j: ready[j])
         return pairs
 
     def turn(i):
@@ -827,14 +942,24 @@ def polish(opss, cfgs, order, rounds, seed=0):
                 od = order[:p0] + order[p0 + 1:]
                 od.insert(q, i)
                 p0 = min(p0, q)
+        turned = []
         if od is None:
-            turn(i)
+            turned = [i]
+            if rnd.rand() < cfgs[0]["swap"]:
+                near = [q for q in range(max(0, p0 - 40), min(n, p0 + 40)) if "both" in ops[order[q]] and eng[order[q]] != eng[i]]
+                if near:
+                    q = near[int(rnd.randint(len(near)))]
+                    turned.append(order[q])
+                    p0 = min(p0, q)
+        for y in turned:
+            turn(y)
         if better(od or order, p0, room):
             order, held = od or order, [None] * nv
             if sum(part) < best:
                 best, keep = sum(part), (order, list(eng))
-        elif od is None:
-            turn(i)
+        else:
+            for y in turned:
+                turn(y)
     for i in range(n):
         if eng[i] != keep[1][i]:
             turn(i)
@@ -844,23 +969,21 @@ def polish(opss, cfgs, order, rounds, seed=0):
 def arrange(cfg):
     cfgs = [dict(cfg, **v) for v in VARIANTS]
     found = []
-    for seed in range(cfg["tries"]):
+    for seed in range(cfg["seed"], cfg["seed"] + cfg["tries"]):
         opss = [build(c) for c in cfgs]
         order = shuttle(opss, cfgs, None, cfg["shuttle"], seed)[0]
         order, ends = polish(opss, cfgs, order, cfg["trim"], seed)
         found.append((float(np.sum(np.log(ends))), seed, opss, order))
     opss, order = min(found)[2:]
-    order, ends = polish(opss, cfgs, order, cfg["polish"])
+    for seed in range(cfg["passes"]):
+        order, ends = polish(opss, cfgs, order, cfg["polish"], seed)
     for ops in opss:
         for o in ops:
             near = {j for j in o["bank"] if ops[j]["eng"] == o["eng"] != "pe"}
             for j in near:
-                ops[j].pop("both", None)
-                o.pop("both", None)
                 o["sem"] = (o["sem"] - {j}) | (ops[j]["bank"] & ops[j]["sem"])
             o["ord"] |= near
-    order, ends = polish(opss, cfgs, order, cfg["polish"] // 4, 1)
-    replay(opss[0], order, cfg)
+    ends = [replay(x, order, c) for x, c in zip(opss, cfgs)]
     return opss[0], order, ends
 
 
@@ -911,11 +1034,10 @@ def rank_program(g, core, T, topo):
     cores = list(T.cores)
     queue = {"pe": g.tensor, "v": g.vector, "s": g.scalar, "g": g, "sync": g.sync}
 
-    def mask_of(src, hops):
-        m = -1
-        for h in hops:
-            m &= topo.mask(src, cores[(cores.index(src) + h) % NR])
-        return m
+    def mask_of(src, hops, step):
+        to = [cores[(cores.index(src) + h) % NR] for h in hops]
+        both = [e for e in topo.engines(src, to[0]) if all(e in topo.engines(src, c) for c in to)]
+        return sum(1 << e for e in both[::step])
 
     def bits(m):
         return bin(m).count("1")
@@ -925,7 +1047,7 @@ def rank_program(g, core, T, topo):
             full[o["tok"]] = 16 * len(o["calls"])
         elif o["kind"] == "rem":
             hops = [d[1] for d in o["calls"][0][2]]
-            full[o["tok"]] = sum(bits(mask_of(cores[(rank - h) % NR], hops)) for h in hops)
+            full[o["tok"]] = sum(bits(mask_of(cores[(rank - h) % NR], hops, o.get("step", 1))) for h in hops)
     sent = 0
     outs = []
     for i in order:
@@ -936,7 +1058,7 @@ def rank_program(g, core, T, topo):
         for c in o["calls"]:
             if c[0] == "remote":
                 hops = [d[1] for d in c[2]]
-                m = mask_of(core, hops)
+                m = mask_of(core, hops, o.get("step", 1))
                 to = [topo.addr(cores[(rank + h) % NR]) for h in hops]
                 srcs = [real(T, a) for a in c[1]]
                 if len(hops) == 1 and len(srcs) == 1:
@@ -950,6 +1072,11 @@ def rank_program(g, core, T, topo):
             x = [real(T, a) if isinstance(a, dict) else a for a in c[1:]]
             if c[0] == "dma_start":
                 q.dma_start(x[0], x[1]).then_inc(T.sem[o["tok"]], 16)
+                if "ext" in c[1]:
+                    outs.append(o)
+                continue
+            if c[0] == "dma_add":
+                q.dma_start(x[0], x[1], accum_op=ALU.add).then_inc(T.sem[o["tok"]], 16)
                 if "ext" in c[1]:
                     outs.append(o)
                 continue

@@ -1,13 +1,11 @@
 import math
 import numpy as np
 from concourse.bass import DstId, RemoteDMATransfer
-from concourse.mybir import AluOpType, ActivationFunctionType
+from concourse.mybir import AluOpType, ActivationFunctionType, AxisListType
 
 S, U, CH, CP, STEPS, HOP, NR = 192, 64, 2048, 4096, 4, 3, 8
-SEG = 65
-BIG = 30000.0
 ZC = 2048.0
-TOP = 786432.0
+TOP = 1.5 * 2.0 ** 35
 
 
 def sb(n, dtype):
@@ -16,51 +14,54 @@ def sb(n, dtype):
 
 BF, HF, FL, IN, UI = "bfloat16", "float16", "float32", "int32", "uint16"
 SCRATCH = {
-    "snd": sb(240, BF), "lnd": sb(3 * 240, BF), "com": sb(4 * 768, BF),
+    "snd": sb(192, BF), "com": sb(768, BF), "Xh": sb(768, BF), "Xl": sb(3 * 384, BF), "oh": sb(768, FL), "ol": sb(3 * 384, FL),
     "kl": sb(8, IN), "kli": sb(4, IN), "klf": sb(4, FL),
-    "Hs": sb(CH + 128, BF), "Ps": sb(CP, BF), "W0": sb(2048, BF), "Wt": sb(2048 + 4096, FL),
-    "ptr": sb(CH + 128, FL), "pts": sb(CH + 128, FL), "pval": sb(320, FL),
-    "Dm": sb(128, BF), "Pm": sb(128, BF), "Gi": sb(192, BF), "Ix": sb(4 * SEG, BF), "Iy": sb(128, BF),
-    "pi": sb(2, IN), "col": sb(16, FL), "Sm": sb(144, BF), "mn": sb(128, BF), "I16": sb(128, BF), "sw": sb(192, BF),
-    "KL": sb(4 * 128, BF), "Lr": sb(256, BF), "Sh": sb(4 * 128, BF), "Mk": sb(64, BF), "dm": sb(128, BF), "Oh": sb(2 * 128, BF),
-    "Zw": sb(144, BF), "Sr": sb(320, BF), "B1": sb(128, HF), "I4": sb(128, HF), "Bq": sb(256, BF), "nI": sb(128, BF), "zr": sb(144, BF),
-    "kk": sb(64, BF), "My": sb(2 * 64, FL), "MA": sb(64, HF), "MF": sb(64, HF), "cm": sb(4, FL),
-    "F32": sb(2 * 128, FL), "Cs": sb(4 * SEG, HF), "Cz": sb(128, BF),
-    "xs": sb(4 * 192, BF), "xm": sb(1536, BF), "bz": sb(4 * 128, BF), "gz": sb(4 * 128, BF), "of": sb(4 * 192, FL),
+    "Hs": sb(U + CH, BF), "Ps": sb(CP, BF), "W0": sb(2048, BF), "Wt": sb(2048 + 4096, FL),
+    "ptr": sb(192, FL), "pts": sb(192, FL), "pval": sb(320, FL),
+    "Dm": sb(128, BF), "Pm": sb(128, BF), "Gi": sb(192, BF), "Ix": sb(388, BF), "Iy": sb(128, BF),
+    "pi": sb(2, IN), "col": sb(16, FL), "Sm": sb(144, BF), "mn": sb(128, BF), "I1": sb(128, HF), "B8": sb(128, HF), "Dq": sb(260, HF),
+    "KL": sb(4 * 128, BF), "Lr": sb(256, BF), "Sh": sb(5 * 128, BF), "E0": sb(256, BF), "KF": sb(256, FL), "xf": sb(384, FL), "dm": sb(128, BF), "Oh": sb(384, BF),
+    "Zw": sb(144, BF), "Sr": sb(320, BF), "B1": sb(256, HF), "Bq": sb(128, HF), "nI": sb(128, BF), "zr": sb(144, BF),
+    "kk": sb(64, BF), "My": sb(2 * 64, FL), "MA": sb(128, HF), "MF": sb(128, HF), "cm": sb(8, FL), "top": sb(128, BF), "vc": sb(16, FL),
+    "F32": sb(3 * 128, FL), "Cz": sb(128, BF),
+    "xs": sb(192, BF), "xm": sb(1536, BF), "bz": sb(4 * 128, BF), "gz": sb(4 * 128, BF),
     "ci": sb(192, IN), "cj": sb(4 * 192, IN), "coff": sb(4 * 192, UI), "hp": sb(2 * 3072, BF),
-    "zc": sb(384, HF), "dq": sb(192, HF), "at": sb(192, BF), "se": sb(4 * 192, BF), "ea": sb(64, BF), "tv": sb(192, BF), "sv": sb(256, BF),
-    "aoff": sb(4 * 192, UI), "src": sb(64, HF), "sd": sb(64, FL), "tb": sb(8 * SEG, HF), "so": sb(8 * SEG, HF),
+    "zc": sb(384, HF), "se": sb(4 * 192, BF), "tv": sb(192, HF), "sv": sb(384, HF),
+    "aoff": sb(4 * 192, UI), "src": sb(64, HF), "so": sb(8, FL),
     "doff": sb(4 * 16, UI), "soff": sb(8, UI), "woff": sb(4 * 192, UI), "wold": sb(4 * 64, UI), "foff": sb(256, UI), "hold": sb(64, BF), "hnew": sb(64, BF),
     "pg": sb(4 * 3072, BF), "pw": sb(4 * 3072, FL), "pd": sb(1040, FL), "wb": sb(2048, FL),
-    "ys": sb(4 * 192, FL), "Bo": sb(4 * 192, FL), "Bi": sb(4 * 192, FL), "wo": sb(2048, FL),
+    "ys": sb(12 * 64, FL), "Bo": sb(12 * 64, FL), "Bi": sb(12 * 64, FL), "wo": sb(2048, FL), "sp": sb(8 * 256, FL),
 }
 for _b in ("pa", "pz0", "pz1", "py", "pl0", "pl1", "pl2", "pq"):
     SCRATCH[_b] = ("psum", [128, 512], "float32")
 NDMA = 72
 SEMAPHORES = ["e_pe", "e_v", "e_s", "e_g", "loc"] + ["d%d" % i for i in range(NDMA)]
 
-CUT = [0, 32, 64, 96, 128, 160, 192]
+CUT, ONE, TWO = [0, 32, 64, 96, 128, 160, 192], [0, 16], [0, 8, 16]
 CFG = {
-    "hcut": [CUT] * 4,
-    "pcut": [[[0, 8, 16]] * 3] * 4, "wcut": [[[0, 8, 16]] * 3] * 4,
+    "hcut": [CUT] + [[0, 32, 64, 128, 192]] * 3,
+    "pcut": [[TWO, TWO, ONE]] + [[TWO, ONE, ONE]] * 2 + [[TWO] * 3],
+    "wcut": [[TWO] * 3] * 4, "pre": {},
+    "wide": {(0, 0), (0, 64)},
     "a_at": {1: (0, 1), 2: (0, 2), 3: (1, 2)},
     "turn": {(1, 64), (2, 64), (3, 64)},
     "late": set(), "bcut": [0, 32, 64, 96, 128],
-    "fold": {(0, 2): 1, (1, 2): 1, (2, 2): 1},
-    "send": [[(0, 128), (128, 192)]] * 4,
-    "sym": [(1,), (2, 3)],
+    "parts": [[None, [(0, 16, 4)], [(0, 16, 4)]]] * 3 + [[None, [(0, 8, 4), (8, 16, 4)], None]],
+    "place": [[0, 3, 3, 3], [1, 1, 0, 0], [2, 2, 2, 3]], "fold": {},
+    "on": True, "widen": 0, "f32": 64,
     "log": False,
     "fin": [0, 24, 56, 92, 128],
-    "g_l": {1, 2}, "g_c": {1, 2, 3}, "g_e": {(t, a) for t in (1, 2, 3) for a in (0, 64)}, "short": False, "chain": set(), "early": set(), "ybq": "s", "npw": 4, "SH": 100000, "gate": False, "GD": 1000.0, "GD1": 1000.0, "AD": 2.0,
-    "G": 1.55, "SC": 4.2, "CY": 1.1, "OV": 50.0, "OS": 35.0, "MS": 40, "PE": 0.42, "WK": 140.0, "OV2": 0.0, "DI": 150.0, "DF": 1500.0, "BW": 370.0, "RF": 2000.0, "RC": 25.0, "RI": 500.0, "R1": 1000.0,
-    "seed": 0, "tries": 1, "shuttle": 600, "trim": 9000, "polish": 75000, "passes": 2, "far": 1000.0, "pick": 0.02, "swap": 0.5, "packs": (3, 4, 5), "slack": 0.0, "aim": 0.25, "mix": 1.0, "heat": 0.0003, "heat2": 0.002,
+    "g_l": {(t, k) for t in range(4) for k in (0, 1)} - {(0, 0)}, "g_c": {1, 2, 3}, "g_e": {(t, a) for t in (1, 2, 3) for a in (0, 64)}, "short": False, "chain": {0, 1, 2, 3}, "after": {0, 1, 2}, "pair": {}, "blocks": [(0, 1, 2)] * 4, "ybq": "s", "npw": 4, "SH": 100000, "gate": False, "GD": 1000.0, "GD1": 1000.0, "AD": 2.0,
+    "G": 1.6, "SC": 4.2, "CY": 1.12, "OV": 50.0, "OS": 35.0, "MS": 40, "PE": 0.4, "WK": 150.0, "OV2": 0.0, "DI": 150.0, "DF": 1200.0, "BW": 370.0, "RF": 1500.0, "RC": 25.0, "RI": 600.0, "R1": 1500.0, "RR": 1.2, "RB": 1.4, "GF": 1.25,
+    "seed": 0, "tries": 1, "shuttle": 100, "trim": 1000, "polish": 600000, "passes": 1, "far": 1000.0, "pick": 0.02, "swap": 0.5, "packs": (0, 3, 4), "slack": 0.0, "aim": 0.25, "mix": 0.3, "ahead": 0.0002, "spare": 0.0003, "every": 200, "leap": 0.2, "heavy": 3.0, "heat": 0.001, "heat2": 0.002,
 }
-VARIANTS = [{}, {"G": 1.3, "SC": 2.8, "CY": 1.2, "BW": 420.0, "WK": 110.0, "DI": 100.0, "RC": 15.0},
-            {"G": 2.7, "SC": 7.0, "CY": 1.35, "WK": 200.0, "BW": 300.0, "RF": 2800.0, "DI": 250.0, "RC": 40.0},
-            {"G": 1.4, "SC": 3.5, "CY": 1.05, "BW": 280.0, "RC": 30.0, "DF": 1900.0, "RF": 2800.0, "DI": 200.0, "RI": 1000.0, "R1": 2500.0},
-            {"G": 1.45, "CY": 1.0, "WK": 250.0, "OS": 80.0, "OV2": 15.0, "BW": 300.0},
-            {"G": 1.4, "CY": 1.05, "PE": 0.5, "RF": 3500.0, "RI": 700.0, "GD": 1500.0, "AD": 2.5},
+VARIANTS = [{}, {"G": 1.35, "SC": 2.5, "CY": 1.15, "BW": 420.0, "WK": 110.0, "DI": 100.0, "RC": 15.0, "RB": 1.6, "RR": 2.0, "DF": 900.0, "RF": 1100.0},
+            {"G": 2.7, "SC": 7.0, "CY": 1.35, "WK": 200.0, "BW": 300.0, "RF": 2000.0, "DI": 250.0, "RC": 40.0, "GF": 1.4},
+            {"G": 1.4, "CY": 1.05, "PE": 0.46, "WK": 180.0, "RF": 2500.0, "RI": 900.0, "GD": 1500.0, "RB": 1.5, "RR": 1.2, "GF": 1.4, "DF": 1700.0, "R1": 2500.0, "BW": 300.0, "DI": 200.0},
+            {"G": 1.3, "SC": 3.0, "CY": 1.4, "PE": 0.42, "GF": 1.45, "DF": 1500.0, "RF": 2000.0},
+            {"G": 2.5, "SC": 5.5, "CY": 1.25, "WK": 230.0, "OS": 60.0, "OV2": 10.0, "RB": 1.0, "RR": 1.0, "GF": 1.5, "RI": 1000.0},
             {"G": 2.0, "SC": 3.0, "CY": 1.2, "WK": 180.0, "OS": 15.0, "MS": 64, "OV2": 20.0, "BW": 260.0, "DF": 1200.0, "RF": 1500.0, "R1": 3000.0, "DI": 60.0}]
+SHARE = {1: (1,), 2: (2, 2), 3: (2, 4, 4)}
 QUEUES = ("pe", "v", "s", "g", "sync")
 ALU = AluOpType
 ACT = ActivationFunctionType
@@ -100,6 +101,10 @@ def width(a):
 
 
 def build(cfg):
+    PLACE = cfg["place"]
+    HOT = sorted(((gr, t) for gr in range(3) for t in range(STEPS)), key=lambda x: PLACE[x[0]][x[1]])
+    HW = max([PLACE[gr][t] for gr, t in HOT].count(h) for h in (1, 2, 3))
+    FROM = {h: min(12 - HW, [PLACE[gr][t] for gr, t in HOT].index(h)) for h in (1, 2, 3)}
     ops = []
     hist = {}
     bank = {}
@@ -112,7 +117,7 @@ def build(cfg):
         rd, wr = [], []
         for c in calls:
             if c[0] == "remote":
-                ins, outs = c[1], [d[0] for d in c[2]]
+                ins, outs = [a for x in c[1] for a in x[0]], [x[1] for x in c[1]]
             else:
                 ins, outs = list(c[1 if c[0] == "dma_add" else 2:]), [c[1]]
             for a in ins:
@@ -240,20 +245,27 @@ def build(cfg):
                     ops[i]["ord"].add(i - 1)
                 run = []
 
-    def group(items):
-        mrun([("matmul", o, l, r, n == 0, n == len(items) - 1) for n, (o, l, r) in enumerate(items)])
+    def group(items, close=True):
+        mrun([("matmul", o, l, r, n == 0, close and n == len(items) - 1) for n, (o, l, r) in enumerate(items)])
 
     def mm(out, pairs):
         group([(out, l, r) for (l, r) in pairs])
 
-    def iota(out, pat, base, cm):
-        return add("g", [("iota", out, pat, base, cm)], 130 + 2 * out["n"] * cy)
+    def pool(call, fixed, other):
+        dur = cfg["GF"] * (fixed + 2 * call[1]["n"] * cy)
+        i = add("g", [call] + ([other] if other else []), dur)
+        if other:
+            ops[i].update(calls=[call], both={"g": ([call], dur), "v": ([other], vcost(other[1], [x for x in other[2:3] if isinstance(x, dict)]))})
+        return i
 
-    def keep(out, a, pat, op, fill, base, cm):
-        return add("g", [("affine_select", out, a, pat, op, fill, base, cm)], 170 + 2 * out["n"] * cy)
+    def iota(out, pat, base, cm, other=None):
+        return pool(("iota", out, pat, base, cm), 130, other)
+
+    def keep(out, a, pat, op, fill, base, cm, other=None):
+        return pool(("affine_select", out, a, pat, op, fill, base, cm), 170, other)
 
     def plain(out, a):
-        return keep(out, a, [[0, out["n"]]], ALU.is_gt, 0.0, 1, 0)
+        return keep(out, a, [[0, out["n"]]], ALU.is_gt, 0.0, 1, 0, ("tensor_copy", out, a))
 
     def dma(q, pairs, nbytes, after=(), behind=()):
         i = add(q, [("dma_start", o, a) for (o, a) in pairs], len(pairs) * (cfg["DI"] if q != "g" else 1000.0), "dma", after, nbytes)
@@ -261,9 +273,11 @@ def build(cfg):
         ops[i]["rows"] = 8
         return i
 
-    def rem(srcs, dsts, nbytes):
-        i = add("g", [("remote", srcs, dsts)], cfg["RI"], "rem", (), nbytes)
-        ops[i]["rows"] = 8 * len(srcs) * len(dsts)
+    def rem(moves):
+        part = SHARE[len(moves)]
+        i = add("g", [("remote", moves)], cfg["RI"], "rem", (), max(128 * len(m[0]) * m[1]["n"] * width(m[1]) * p for m, p in zip(moves, part)))
+        ops[i]["rows"] = max(8 * len(m[0]) * p for m, p in zip(moves, part)) * cfg["RR"]
+        ops[i].update(raw=ops[i]["bytes"], bytes=ops[i]["bytes"] * cfg["RB"])
         return i
 
     def gather(out, win, off, scale=None, eng="s"):
@@ -283,8 +297,7 @@ def build(cfg):
     l_lam = dma("s", [(A("kl", 1, 2), EXT("lam"))], 8192)
     l_past = dma("sync", [(A("snd", 0, 192), EXT("past"))], 49152, (), (l_kap,))
     l_com = dma("s", [(A("com", 0, 768, 1, 0, 8), EXT("coming"))], 12288, (), (l_lam,))
-    l_snd = dma("s", [(A("snd", 192, 240), EXT("coming"))], 12288, (), (l_com,))
-    l_hist = dma("sync", [(A("Hs", 0, CH), EXT("hist"))], 524288, (), (l_past,))
+    l_hist = dma("sync", [(A("Hs", U, U + CH), EXT("hist"))], 524288, (), (l_past,))
     mset(A("xm", 0, 1536), 0.0)
     mset(A("zr", 0, 144), 0.0)
     loads = {
@@ -292,24 +305,18 @@ def build(cfg):
         "b": ([(A("bz", 16 * g, 16 * g + 16, 1, 0, 12), EXT("past", 0, S, 16 * g, 16 * g + 1)) for g in range(8)], 4096),
         "s": ([(A("Ps", 0, CP), EXT("score"))], 1048576), "w": ([(A("W0", 0, 2048), EXT("weight"))], 524288)}
     l_x = dma("sync", loads["x"][0], loads["x"][1], (), (l_hist,))
-    dma("s", loads["b"][0], loads["b"][1], (), (l_snd,))
+    dma("s", loads["b"][0], loads["b"][1], (), (l_com,))
     iota(A("Dm", 0, 128), [[1, 128]], 0, -1)
     iota(A("pi", 0, 1), [[1, 1]], 0, 1)
     iota(A("Pm", 0, 128), [[-16, 8], [0, 16]], 0, 1)
-    iota(A("Gi", 0, 192, 1, 0, 12), [[1, 12], [0, 16]], 0, -1)
     iota(A("Iy", 0, 128), [[0, 8], [1, 16]], 0, 0)
-    iota(A("Ix", 0, 4 * SEG), [[-16, 4], [1, SEG]], 0, 0)
+    iota(A("Gi", 0, 192, 1, 0, 12), [[1, 12], [0, 16]], 0, -1)
 
-    def line(out, fill, base, cm):
-        return keep(out, A("zr", 0, out["n"], 1, 0, out["p1"]), [[1, out["n"]]], ALU.not_equal, fill, base, cm)
+    def line(out, fill, base, cm, other=None):
+        return keep(out, A("zr", 0, out["n"], 1, 0, out["p1"]), [[1, out["n"]]], ALU.not_equal, fill, base, cm, other)
 
-    def symbols(steps):
-        return rem([A("snd", 0, 240)], [(A("lnd", 240 * (t - 1), 240 * t), HOP * t) for t in steps], len(steps) * 61440)
-    ops[symbols(cfg["sym"][0])].update(once=cfg["R1"], step=1)
-    iota(A("kk", 0, 64), [[1, 16], [0, 4]], 0, 0)
-    first = [o["i"] for o in ops if o["eng"] == "g"]
-    for i, j in zip(first, first[1:]):
-        ops[j]["ord"].add(i)
+    def diagonal(out, fill, c0, d):
+        return line(out, fill, c0 - d, -1, tsc(out, A("Dm", c0, c0 + out["n"]), 1.0 * d, fill, ALU.is_equal, ALU.mult))
 
     def col(j, p1=128):
         return A("col", j, j + 1, 1, 0, p1)
@@ -318,6 +325,36 @@ def build(cfg):
     ts(A("pi", 1, 2), A("pi", 0, 1), 15, None, ALU.bitwise_and)
     cp(col(PF), A("pi", 0, 1))
     cp(col(LANE), A("pi", 1, 2))
+    same = A("Sm", 0, 128)
+    ts(same, A("Pm", 0, 128), col(LANE), None, ALU.is_equal)
+
+    ts(A("vc", 0, 16), A("Iy", 0, 16), col(LANE), None, ALU.is_ge)
+
+    def shift(t):
+        out = A("Sh", 128 * t, 128 * t + 128)
+        return keep(out, same, [[1, 128]], ALU.is_equal, 0.0, -t, -1, tsc(out, D128, 1.0 * t, A("vc", 15 - t, 16 - t), ALU.is_equal, ALU.mult))
+
+    def lane_in(i):
+        return A("Zw", 3 - i, 131 - i, 1, 0, 8)
+
+    def comc(t, u0, n):
+        return A("com", 192 * t + u0, 192 * t + u0 + n, 1, 0, 8)
+
+    def symbols(t0, bank):
+        for t in (t0, t0 + 1):
+            c = 192 * (t - t0)
+            mm(A(bank, c, c + 192), [(A("Sh", 128 * t, 128 * t + 128), A("snd", 0, 192))] + [(lane_in(t - 1 - s), comc(s, 0, 192)) for s in range(t)])
+        act(A("Xh", 192 * t0 - 192, 192 * t0 + 192), A(bank, 0, 384), ACT.Copy)
+
+    def moved(t):
+        return ([A("Xh", 192 * t - 192, 192 * t + 192)], A("Xl", 384 * t - 384, 384 * t), HOP * t)
+    line(A("Zw", 0, 144, 1, 0, 8), 1.0, -3, -16)
+    shift(1)
+    shift(2)
+    iota(A("kk", 0, 64), [[1, 16], [0, 4]], 0, 0)
+    symbols(1, "pl2")
+    first = rem([moved(1)])
+    ops[first].update(once=cfg["R1"])
     ident = A("Sh", 0, 128)
     ts(ident, D128, 0.0, None, ALU.is_equal)
     srep, sprev = A("Sr", 0, 128, 1, 0, 8), A("Sr", 192, 320, 1, 0, 8)
@@ -325,6 +362,11 @@ def build(cfg):
     ts(col(CW, 8), col(PF, 8), 7.0, -8.0, ALU.is_ge, ALU.mult)
     ts(sprev, A("Gi", 0, 128, 1, 0, 8), col(CW, 8), 1.0, ALU.subtract, ALU.is_equal)
     tt(A("mn", 0, 128), A("Pm", 0, 128), D128, ALU.min)
+    if cfg["f32"]:
+        cp(A("col", 8, 10), A("kl", 0, 2))
+        ts(A("KF", 0, 128), A("mn", 0, 128), 0.0, col(8), ALU.is_ge, ALU.mult)
+        act(A("KF", 128, 256), ident, ACT.Identity, None, col(9))
+        act(A("xf", 0, cfg["f32"]), A("snd", 0, cfg["f32"]), ACT.Copy)
     ts(A("kli", 0, 2), A("kl", 0, 2), 0xFF00, None, ALU.bitwise_and)
     ts(A("kli", 2, 4), A("kl", 0, 2), 0xFF, None, ALU.bitwise_and)
     cp(A("klf", 0, 4), A("kli", 0, 4))
@@ -332,94 +374,96 @@ def build(cfg):
         split = ts(A("KL", 128 * j, 128 * j + 128), A("mn", 0, 128), 0.0, A("klf", j, j + 1), ALU.is_ge, ALU.mult)
     l_score = dma("sync", loads["s"][0], loads["s"][1], (split,) if cfg["gate"] else (), (l_x,))
     l_w = dma("sync", loads["w"][0], loads["w"][1], (), (l_score,))
-    for steps in cfg["sym"][1:]:
-        i = symbols(steps)
-        ops[i]["ord"].add(first[-1])
-        ops[i]["sem"].add(l_score)
     for j in (1, 3):
         act(A("KL", 128 * j, 128 * j + 128), ident, ACT.Identity, None, A("klf", j, j + 1), "v")
-    same = A("Sm", 0, 128)
-    ts(same, A("Pm", 0, 128), col(LANE), None, ALU.is_equal)
-    act(A("Sm", 128, 129), A("Sm", 0, 1), ACT.Copy)
+    act(A("Sm", 128, 144), A("Sm", 0, 16), ACT.Copy)
     table = act(A("Cz", 0, 128), A("Iy", 0, 128), ACT.Sigmoid, -128.0, 256.0)
     ops[table]["dur"] += 1300.0
-    for j in (0, 1):
-        mm(A("py", 128 * j, 128 * j + 128, 1, 0, 8), [(A("Sm", 16, 129, 16), A("KL", 128 + 256 * j, 256 + 256 * j))])
-    act(A("Lr", 0, 256, 1, 0, 8), A("py", 0, 256, 1, 0, 8), ACT.Copy)
     for (pz, c) in (("pz0", 0), ("pz1", 0), ("pz1", 128)):
         mm(A(pz, c, c + 128), [(A("zr", 0, 128), D128)])
     act(A("cm", 3, 4), A("Sh", 17, 18), ACT.Identity, None, -3584.0 / ZC)
     act(A("cm", 0, 1), A("Sh", 16, 17), ACT.Identity, A("cm", 3, 4), -97.0 / ZC)
     act(A("cm", 1, 2), A("Sh", 17, 18), ACT.Identity, None, -8.0 / ZC)
-    act(A("cm", 2, 3), A("Sh", 16, 17), ACT.Identity, None, 4096.0 * 1536 / ZC)
+    act(A("cm", 2, 3), A("Sh", 16, 17), ACT.Identity, None, (1856.0 - U) / ZC)
+    act(A("cm", 5, 6), A("Sh", 16, 17), ACT.Identity, None, -1.0 * U / ZC)
+    act(A("cm", 4, 5), A("Sh", 18, 19), ACT.Identity, None, 0.5 / ZC)
+    mset(A("top", 0, 128), TOP)
     ma, mf = A("My", 0, 64), A("My", 64, 128)
     act(ma, A("kk", 0, 64), ACT.Identity, None, A("cm", 0, 1))
-    soon = [first[-1], keep(A("MA", 0, 64), ma, [[-1, 16], [-32, 4]], ALU.not_equal, 37.0, 0, 1)]
-    act(mf, A("Iy", 0, 64), ACT.Identity, A("cm", 2, 3), A("cm", 1, 2))
-    soon.append(keep(mf, mf, [[-32, 4], [-1, 16]], ALU.not_equal, -256.0, 0, 1))
+    keep(A("MA", 0, 64), ma, [[-1, 16], [-32, 4]], ALU.not_equal, 37.0, 0, 1)
+    act(A("MA", 64, 128), A("MA", 0, 64), ACT.Identity, A("cm", 4, 5), -1.0)
+    act(mf, A("Iy", 0, 64), ACT.Identity, A("cm", 5, 6), A("cm", 1, 2))
+    keep(mf, mf, [[-32, 4], [-1, 16]], ALU.not_equal, -256.0, 0, 1)
     keep(mf, mf, [[-32, 4], [0, 16]], ALU.not_equal, 256.0, 0, 1)
-    soon.append(keep(A("MF", 0, 64), mf, [[-32, 4], [1000, 16]], ALU.not_equal, 0.0, 0, 1))
-    soon.append(line(A("nI", 0, 128), -1.0, 0, -1))
-    later = len(ops)
-    iota(A("Oh", 128, 256), [[1, 16], [0, 8]], 0, 0)
-    iota(A("ptr", 0, 128), [[1, 128]], -128, 0)
+    keep(A("MF", 0, 64), mf, [[-32, 4], [1000, 16]], ALU.not_equal, 0.0, 0, 1)
+    act(A("MF", 64, 128), A("MF", 0, 64), ACT.Identity, A("cm", 2, 3), -1.0)
+    diagonal(A("nI", 0, 128), -1.0, 0, 0)
+    iota(A("Oh", 192, 384), [[1, 24], [0, 8]], -8, 0)
+    iota(A("ptr", 0, 192), [[1, 192]], -192, 0)
     iota(A("pval", 0, 256), [[1, 256]], 0, 0)
     if not cfg["log"]:
         iota(A("pval", 256, 320), [[16, 64]], 0, 0)
-        iota(A("pts", 0, 128), [[0, 128]], 1024, 0)
-        iota(A("pd", 1024, 1040), [[0, 16]], 0, 0)
-    plain(A("B1", 0, 128), same)
+        iota(A("pts", 0, 192), [[0, 192]], 1024, 0, ("memset", A("pts", 0, 192), 1024.0))
+        iota(A("pd", 1024, 1040), [[0, 16]], 0, 0, ("memset", A("pd", 1024, 1040), 0.0))
+    act(A("B1", 0, 128), same, ACT.Copy)
+    act(A("B1", 128, 256), same, ACT.Identity, None, 8192.0)
     ts(A("dm", 0, 128), A("Iy", 0, 128), col(LANE), None, ALU.is_equal)
-    act(A("Mk", 0, 64), A("dm", 0, 64), ACT.Identity, -4096.0, 4096.0)
-    ts(A("Oh", 0, 128), A("Oh", 128, 256), col(LANE), None, ALU.is_equal)
+    ts(A("Oh", 0, 192), A("Oh", 192, 384), col(LANE), None, ALU.is_equal)
     act(col(L2), col(LANE), ACT.Identity, 2048.0, None)
     posI, posS = A("F32", 0, 128), A("F32", 128, 256)
-    act(A("I4", 0, 128), ident, ACT.Identity, None, 4096.0, "v")
-    if len(cfg["turn"]) < 2 * STEPS:
-        line(A("I16", 0, 128), 16.0, 0, -1)
-    if cfg["turn"]:
-        iota(A("Bq", 128, 256), [[-64, 2], [0, 16], [-16, 4]], 0, 1)
-        ts(A("Bq", 0, 128), A("Bq", 128, 256), col(LANE), 16.0, ALU.is_equal, ALU.mult)
-    line(posI, 1.0, 0, -1)
-    line(A("F32", 128, 144), 1.0 / 32, 112, -1)
-    line(A("F32", 144, 256), 1.0 / 32, 0, -1)
-    for t in (1, 2, 3):
-        keep(A("Sh", 128 * t, 128 * t + 128), same, [[1, 128]], ALU.is_equal, 0.0, -t, -1)
-    line(A("Zw", 0, 144, 1, 0, 8), 1.0, -2, -16)
-    ts(A("Cs", 0, 4 * SEG), A("Ix", 0, 4 * SEG), col(LANE), -0.75, ALU.is_equal, ALU.mult)
-    ts(A("Cs", 0, 4 * SEG, SEG), A("Cs", 0, 4 * SEG, SEG), BIG, None, ALU.add)
-    act(col(CD), col(LANE), ACT.Identity, 0.75, -1.0 / 2048)
-    act(A("Cs", SEG - 1, 4 * SEG, SEG), A("Ix", 0, 4 * SEG, SEG), ACT.Identity, col(CD), 1.0 / 2048)
-    for k in (0, 1) if cfg["short"] else ():
-        act(A("tb", 4 * SEG * k, 4 * SEG * (k + 1)), A("Ix", 0, 4 * SEG), ACT.Identity, BIG, 0.0)
-    for t in (1, 2, 3):
-        dma("sync", [(A("com", 768 * t, 768 * t + 768, 1, 0, 8), A("lnd", 240 * (t - 1) + 192, 240 * t))], 12288, (), (l_w,))
-        dma("sync", [(A("bz", 128 * t + 16 * g, 128 * t + 16 * g + 16, 1, 0, 12),
-                      A("lnd", 240 * (t - 1) + 192, 240 * t, 1, 16 * g + 4 * t - 4, 16 * g + 4 * t)) for g in range(8)], 4096, (), (l_w,))
-    for j in range(0, 2048, 512):
+    act(A("I1", 0, 128), ident, ACT.Copy)
+    iota(A("Ix", 0, 128), [[-64, 2], [0, 16], [-16, 4]], 0, 1)
+    ts(A("Bq", 0, 128), A("Ix", 0, 128), col(LANE), 16.0, ALU.is_equal, ALU.mult)
+    keep(A("B8", 0, 128, 1, 0, 8), A("zr", 0, 128, 1, 0, 8), [[-4, 2], [0, 16], [-1, 4]], ALU.not_equal, 16.0, 0, 1)
+    act(A("Dq", 0, 4, 1, 64, 128), A("Bq", 64, 68, 1, 64, 128), ACT.Identity, None, 1.0 / 16)
+    acts([(A("Dq", 4 + 64 * j, 68 + 64 * j, 1, 64, 128), A("Bq", 64, 128, 1, 64, 128), ACT.Identity, None, -512.0) for j in range(4)])
+    ts(A("Dq", 0, 128, 1, 0, 64), A("zr", 0, 128, 1, 0, 64), 0.0, None, ALU.add)
+    ts(A("Dq", 128, 260, 1, 0, 64), A("zr", 0, 132, 1, 0, 64), 0.0, None, ALU.add)
+    iota(A("Ix", 128, 384, 1, 0, 16), [[0, 64], [16, 4]], 0, 1)
+    keep(A("Dq", 4, 260, 1, 0, 16), A("Ix", 128, 384, 1, 0, 16), [[-1, 64], [16, 4]], ALU.is_gt, 4096.0, 0, 1)
+    ts(A("Dq", 0, 4, 1, 0, 16), A("zr", 0, 4, 1, 0, 16), 1.0 * U, None, ALU.add)
+    acts([(A("sv", 128 * k, 128 * k + 128, 1, 0, 64), A("dm", 0, 128, 1, 0, 64), ACT.Copy, None, None) for k in (0, 1)])
+    diagonal(posI, 1.0, 0, 0)
+    diagonal(A("F32", 128, 144), 1.0 / 32, 0, -112)
+    diagonal(A("F32", 144, 256), 1.0 / 32, 16, 16)
+    halfI = A("F32", 256, 384)
+    diagonal(halfI, 0.5, 0, 0)
+    shift(3)
+    shift(4)
+    lane0 = A("E0", 0, 128)
+    keep(lane0, ident, [[0, 8], [1, 16]], ALU.is_equal, 0.0, 0, 0, tsc(lane0, ident, A("vc", 0, 1), None, ALU.mult))
+    keep(A("E0", 128, 256), A("Sm", 16, 144), [[0, 8], [1, 16]], ALU.is_equal, 0.0, 0, 0)
+
+    def at_home():
+        ph[0] += 1
+        for j in (0, 1):
+            mm(A("pa", 128 * j, 128 * j + 128), [(A("E0", 128, 256), A("KL", 128 + 256 * j, 256 + 256 * j))])
+        act(A("Lr", 0, 256), A("pa", 0, 256), ACT.Copy)
+        ph[0] += 1
+        symbols(3, "pl2")
+        ops[rem([moved(2), moved(3)])]["ord"].add(first)
+        ph[0] += 1
+        for n in range(0, 12, 4):
+            pl = "pl%d" % (1 + n // 4 % 2)
+            group([(A(pl, 64 * j, 64 * j + 64), srep, comc(t, 64 * gr, 64)) for j, (gr, t) in enumerate(HOT[n:n + 4])])
+            ts(A("oh", 64 * n, 64 * n + 256), A(pl, 0, 256), col(LANE), -1.0, ALU.not_equal, ALU.mult)
+        ops[rem([([A("oh", 64 * FROM[h], 64 * (FROM[h] + HW))], A("ol", 64 * HW * (h - 1), 64 * HW * h), HOP * h) for h in (1, 2, 3)])]["ord"].add(first)
+
+    def hot(gr, t):
+        h, n = PLACE[gr][t], HOT.index((gr, t))
+        c = 64 * (HW * (h - 1) + n - FROM[h]) if h else 64 * n
+        return A("ol" if h else "oh", c, c + 64)
+    for j in range(0, cfg["widen"], 512):
         plain(A("Wt", j, j + 512), A("W0", j, j + 512))
-    for i, j in zip(soon, soon[1:]):
-        ops[j]["ord"].add(i)
-    for o in ops[later:]:
-        if o["eng"] == "g":
-            o["ord"].add(soon[-1])
-
-    def lane_in(i):
-        return A("Zw", 2 - i, 130 - i, 1, 0, 8)
-
-    def comc(t, tt_, u0, n):
-        return A("com", 768 * t + 192 * tt_ + u0, 768 * t + 192 * tt_ + u0 + n, 1, 0, 8)
+    if cfg["widen"] < 2048:
+        i = add("g", [("dma_start", A("Wt", cfg["widen"], 2048), A("W0", cfg["widen"], 2048))], cfg["GD"] + cfg["GD1"], "dma", (), 512 * (2048 - cfg["widen"]))
+        ops[i]["rows"] = 8
+        adds.append(i)
 
     def phase_a(t):
         ph[0] += 1
-        rot, s0 = U * (t % 3), 192 * t
+        rot, s0, x0 = U * (t % 3), 192 * t, 384 * t - 384
         pieces = [(0, rot, S - rot)] + ([(S - rot, 0, rot)] if rot else [])
-        x = A("xs", s0, s0 + 192) if t else A("snd", 0, 192)
-        if t:
-            for (p, u, n) in pieces:
-                mm(A("pa", p, p + n), [(A("Sh", 128 * t, 128 * t + 128), A("lnd", 240 * (t - 1) + u, 240 * (t - 1) + u + n))]
-                   + [(lane_in(t - 1 - s), comc(t, s, u, n)) for s in range(t)])
-            act(x, A("pa", 0, 192), ACT.Copy)
 
         def columns(cs, a, b):
             act(A("ci", a, b), cs, ACT.Copy, None, None, "s" if t else "v")
@@ -429,22 +473,22 @@ def build(cfg):
             else:
                 act(A("coff", s0 + a, s0 + b), A("cj", s0 + a, s0 + b), ACT.Copy, None, None, "s" if t else "v")
 
-        def lrows(j):
-            return [(A("pa", 192 + p, 192 + p + n), A("Lr", 128 * j, 128 * j + 128, 1, 0, 8), comc(t, t, u, n)) for (p, u, n) in pieces]
         if t:
-            cs = A("pa", 192, 384)
-            group([(cs, A("KL", 0, 128), x)] + lrows(0) + lrows(1) + [(cs, A("KL", 256, 384), x)])
-            columns(cs, 0, 192)
+            dma("sync", [(A("bz", 128 * t + 16 * g, 128 * t + 16 * g + 16, 1, 0, 12), A("Xl", x0, x0 + 192, 1, 16 * g, 16 * g + 1)) for g in range(8)], 4096, (), (l_w,))
+            group([(A("pa", p, p + n), A(name, c, c + 128), A("Xl", x0 + d + u, x0 + d + u + n))
+                   for (name, c, d) in (("KL", 0, 0), ("KL", 256, 0), ("Lr", 0, 192), ("Lr", 128, 192)) for (p, u, n) in pieces])
+            columns(A("pa", 0, 192), 0, 192)
         else:
-            mm(A("pl0", 0, 192), [(sprev, comc(0, 0, 0, 192))])
-            act(A("xs", 0, 192), A("pl0", 0, 192), ACT.Copy)
+            mm(A("pl0", 0, 192), [(sprev, comc(0, 0, 192))])
+            f = cfg["f32"]
+            acts(([(A("xf", 192, 192 + f), A("pl0", 0, f), ACT.Copy, None, None)] if f else []) + ([(A("xs", f, 192), A("pl0", f, 192), ACT.Copy, None, None)] if f < S else []))
             for (name, a, b) in (("pa", 0, 64), ("pl1", 64, 192)):
                 cs = A(name, 192 + a, 192 + b)
-                mm(cs, [(A("KL", 128 * j, 128 * j + 128), A("xs" if j % 2 else "snd", a, b)) for j in range(4)])
+                if b <= f:
+                    mm(cs, [(A("KF", 128 * j, 128 * j + 128), A("xf", 192 * j + a, 192 * j + b)) for j in range(2)])
+                else:
+                    mm(cs, [(A("KL", 128 * j, 128 * j + 128), A("xs" if j % 2 else "snd", a, b)) for j in range(4)])
                 columns(cs, a, b)
-        for (p, u, n) in pieces:
-            mm(A("pa", p, p + n), [(srep, comc(t, t, u, n))])
-        ts(A("of", s0, s0 + 192), A("pa", 0, 192), col(LANE), -1.0, ALU.not_equal, ALU.mult)
         ts(A("gz", 128 * t, 128 * t + 128, 1, 0, 12), A("bz", 128 * t, 128 * t + 128, 1, 0, 12), 8.0, -8.0, ALU.is_ge, ALU.mult)
 
     def phase_h(t, a, b, pz):
@@ -452,19 +496,22 @@ def build(cfg):
         par, n, s0 = t % 2, b - a, 192 * t
         h0, m0 = 3072 * par, 0
         if a == 0 and t:
-            dma("sync", [(A("xm", m0 + 192 * g, m0 + 192 * g + 192, 1, 16 * g, 16 * g + 16), A("xs", s0, s0 + 192, 1, 16 * g, 16 * g + 16))
+            dma("sync", [(A("xm", m0 + 192 * g, m0 + 192 * g + 192, 1, 16 * g, 16 * g + 16), A("Xl", 384 * t - 384, 384 * t - 192, 1, 16 * g, 16 * g + 16))
                          for g in range(8)], 49152)
         cut = [c for c in cfg["hcut"][t] if a <= c <= b]
         for c, d in zip(cut, cut[1:]):
-            gather(A("hp", h0 + 16 * c, h0 + 16 * d), A("Hs", 0, CH), A("coff", s0 + c, s0 + d), None, "v" if t == 0 and c % 64 else "s")
+            gather(A("hp", h0 + 16 * c, h0 + 16 * d), A("Hs", U, U + CH), A("coff", s0 + c, s0 + d), None, "v" if t == 0 and c % 64 else "s")
         for u0 in range(a, b, 16):
             q, c = u0 // 16 % 4, 2 * ((u0 - a) // 64 * 64)
             mrun([("matmul", A(pz, c + r, c + 128, 16, 32 * q, 32 * q + 16), A("hp", h0 + 16 * (u0 + r), h0 + 16 * (u0 + r) + 16),
-                   A("xm", m0 + u0 + r, m0 + 1536, 192), True, True) for r in range(16)])
+                   A("xm", m0 + (u0 + U * t) % S + r, m0 + 1536, 192), True, True) for r in range(16)])
         act(A("zc", 2 * a, 2 * b), A(pz, 0, 2 * n), ACT.Identity, -ZC, None)
 
-    def turned(bank, c0, a, b, const):
-        return [(A(bank, c0 + u - a, c0 + u - a + 64), A("zc", 2 * u, 2 * u + 128), A(const, 0, 64)) for u in range(a, b, 64)]
+    def turned(bank, c0, a, b, const, m=0):
+        return [(A(bank, c0 + u - a, c0 + u - a + 64), A("zc", 2 * u, 2 * u + 128), A(const, m, m + 64)) for u in range(a, b, 64)]
+
+    def rounded(out):
+        return [(out, ident, A("top", 0, out["n"])), (out, A("nI", 0, 128), A("top", 0, out["n"]))]
 
     def elist(t, a, b):
         return A("doff", 16 * t + 4 + a // 16, 16 * t + 4 + b // 16)
@@ -472,111 +519,92 @@ def build(cfg):
     def phase_e(t, a, b):
         ph[0] += 1
         n, py, e0 = b - a, "pq" if a else "py", 192 * t
-        group(turned(py, 0, a, b, "MF"))
-        act(A("dq", a, b), A(py, 0, n), ACT.Identity, 1.0 / 64 - 15.0 / 32, -1.0 / 4096)
         new = [(A(py, n + u - a, n + u - a + 64), A(x, 128 * t, 128 * t + 128, 1, 0, 12), A("Sr", (u + U * t) % S, (u + U * t) % S + 64, 1, 0, 12))
                for u in range(a, b, 64) for x in ("bz", "gz")]
-        group(turned(py, n, a, b, "MF") + new + [(A(py, n, 2 * n), A("I4", 0, 128), A("dq", a, b))])
+        group(turned(py, n, a, b, "MF", 64) + rounded(A(py, n, 2 * n)) + turned(py, n, a, b, "MF") + new)
         scan(A("se", e0 + a, e0 + b), A("Cz", 0, n), A(py, n, 2 * n), ALU.mult, ALU.max)
         if (t, a) in cfg["g_e"]:
             plain(elist(t, a, b), A("se", e0 + a + 15, e0 + b, 16))
-        elif t or a == 0 or (t, a) in cfg["turn"]:
+        elif t or a == 0:
             act(elist(t, a, b), A("se", e0 + a + 15, e0 + b, 16), ACT.Copy, None, None, "v")
 
     def phase_s(t, a, b, pz):
         ph[0] += 1
         n = b - a
-        group(turned(pz, 2 * n, a, b, "MA"))
-        act(A("at", a, b), A(pz, 2 * n, 3 * n), ACT.Identity, 37 * ZC + TOP - 2047.5, None)
-        group(turned(pz, 3 * n, a, b, "MA") + [(A(pz, 3 * n, 4 * n), A("nI", 0, 128), A("at", a, b))])
-        act(A("aoff", 192 * t + a, 192 * t + b), A(pz, 3 * n, 4 * n), ACT.Identity, 37 * ZC + TOP, None, "v")
+        group(turned(pz, 3 * n, a, b, "MA", 64) + rounded(A(pz, 3 * n, 4 * n)) + turned(pz, 3 * n, a, b, "MA"))
+        act(A("aoff", 192 * t + a, 192 * t + b), A(pz, 3 * n, 4 * n), ACT.Identity, 2048.0, None, "v")
 
     def phase_w(t, a, b):
         ph[0] += 1
-        n, py, nk = b - a, "pq" if a else "py", 8 if t else 16
-        turn = (t, a) in cfg["turn"]
-        if t or turn:
-            tt(A("tv", a, b), IND(A("ptr", 0, 128), elist(t, a, b)), A("dm", 0, n), ALU.mult)
-        if turn:
-            mm(A(py, 384, 512, 1, 0, n), [(A("tv", a, b), ident)])
-            sv = A("sv", 2 * a, 2 * a + 128, 1, 0, n)
-            act(sv, A(py, 384, 512, 1, 0, n), ACT.Copy)
-        elif t:
-            scan(A("sw", a, b), A("Cz", 0, n), A("tv", a, b), ALU.mult, ALU.add)
+        n, py, nk = b - a, "pq" if a else "py", 16 if (t, a) in cfg["wide"] else 8
+        at = 384 if a else 256
+        if t or not a:
+            tt(A("tv", a, b), IND(A("ptr", 0, 192), elist(t, a, b)), A("dm", 0, n), ALU.mult)
+            p0, p1, pick, start = 128 - n, 128, "Bq", 2048.0
+            mm(A(py, at, at + 128, 1, p0, p1), [(A("tv", a, b), A("I1", 0, 128))])
+        else:
+            p0, p1, pick, start = 0, 8, "B8", -16.0 * U
+            mm(A(py, at, at + 128, 1, p0, p1), [(A("se", a + 15, b, 16), ident)])
+        sv = A("sv", 128 + 2 * a, 256 + 2 * a, 1, p0, p1)
+        act(sv, A(py, at, at + 128, 1, p0, p1), ACT.Copy)
         items = []
         for u in range(0, n, 64):
             c = 2 * n + u // 16 * nk
-            items += [(A(py, c, c + 4 * nk), ident, A("kk", 0, 4 * nk))]
-            if turn:
-                items += [(A(py, c, c + 4 * nk), sv, A("Bq", u, u + 4 * nk, 1, 0, n))]
-            else:
-                items += [(A(py, c + 4 * k, c + 4 * k + 4), A("I16", 0, 128), A("sw" if t else "se", a + u + 15, a + u + 64, 16)) for k in range(nk)]
+            items += [(A(py, c, c + 4 * nk), ident, A("kk", 0, 4 * nk)), (A(py, c, c + 4 * nk), sv, A(pick, p0 + u, p0 + u + 4 * nk, 1, p0, p1))]
         group(items)
-        act(A("woff", 192 * t + a // 16 * nk, 192 * t + b // 16 * nk), A(py, 2 * n, 2 * n + n // 16 * nk), ACT.Identity, 2048.0 if t or turn else 0.0, None, "v")
+        act(A("woff", 192 * t + a, 192 * t + a + n // 16 * nk), A(py, 2 * n, 2 * n + n // 16 * nk), ACT.Identity, start, None, "v")
 
-    def repeats(k, lanes, own, target):
-        act(A("tb", 4 * SEG * k + SEG - 1, 4 * SEG * (k + 1), SEG), A(target[0], target[1] + 15, target[1] + 64, 16), ACT.Identity, 0.5, -1.0 / 4096)
-        w = [16 + 16 * q if cfg["short"] else 64 for q in range(4)]
-        acts([(A("tb", SEG * (4 * k + q), SEG * (4 * k + q) + w[q]), A(lanes[0], lanes[1], lanes[1] + w[q]), ACT.Abs,
-               A(own[0], own[1] + 16 * q + 15, own[1] + 16 * q + 16), -1.0) for q in range(4)])
-        scan(A("so", 4 * SEG * k, 4 * SEG * (k + 1)), A("Cs", 0, 4 * SEG), A("tb", 4 * SEG * k, 4 * SEG * (k + 1)), ALU.add, ALU.min)
-        act(A("soff", 4 * k, 4 * k + 4), A("so", 4 * SEG * k + SEG - 1, 4 * SEG * (k + 1), SEG), ACT.Identity, 2048.0, -4096.0, "v")
+    def repeats(t, k, lanes, target):
+        group([(A("py", 252, 256), target[0], target[1]), (A("py", 256, 512), A("sv", 128 * k, 128 * k + 128), A("Dq", 4, 260))]
+              + [(A("py", 256 + q, 512, 4), A("B1", 128, 256), lanes) for q in range(4)])
+        if not k:
+            act(A("doff", 16 * t, 16 * t + 4), A("py", 252, 256), ACT.Identity, -1.0 * U, None, "v")
+        cs = [("tensor_reduce", A("so", 4 * k + q, 4 * k + q + 1), A("py", 252 + q, 320 + 64 * q, 4), ALU.min, True) for q in range(4)]
+        add("v", cs, sum(vcost(x[2], [x[2]]) for x in cs))
+        if (t, k) in cfg["g_l"]:
+            plain(A("soff", 4 * k, 4 * k + 4), A("so", 4 * k, 4 * k + 4))
+        else:
+            act(A("soff", 4 * k, 4 * k + 4), A("so", 4 * k, 4 * k + 4), ACT.Copy, None, None, "v")
 
     def phase_c(t):
         ph[0] += 1
-        s0, cl = 192 * t, A("doff", 16 * t, 16 * t + 4)
-        tt(A("src", 0, 64), IND(A("Oh", 0, 128), elist(t, 0, U)), A("cj", s0, s0 + 64), ALU.mult)
-        mk = A("py", 256, 320)
-        mm(mk, [(ident, A("Mk", 0, 64)), (A("B1", 0, 128), A("src", 0, 64))])
-        mm(A("py", 192, 256), [(A("B1", 0, 128), A("src", 0, 64))])
-        scan(A("sd", 0, 64), A("Cz", 0, 64), mk, ALU.mult, ALU.max)
-        if t in cfg["g_l"]:
-            plain(cl, A("sd", 15, 64, 16))
-        else:
-            act(cl, A("sd", 15, 64, 16), ACT.Copy, None, None, "v")
-        repeats(0, ("py", 192), ("sd", 0), ("sd", 0))
-        gather(A("hold", 0, 64), A("Hs", 0, CH), cl)
-        mm(A("py", 320, 384), [(lane_in(0), comc(t, t, U * (t % 3), 64)), (A("Sh", 128, 256), A("hold", 0, 64))])
-        act(A("hnew", 0, 64), A("py", 320, 384), ACT.Copy)
+        s0 = 192 * t
+        tt(A("src", 0, 64), IND(A("Oh", 0, 192), elist(t, 0, U)), A("cj", s0, s0 + 64), ALU.mult)
+        mm(A("py", 256, 384, 1, 64, 128), [(A("src", 0, 64), A("B1", 0, 128))])
+        tt(A("sv", 0, 128, 1, 64, 128), A("py", 256, 384, 1, 64, 128), A("dm", 0, 128, 1, 64, 128), ALU.mult)
+        repeats(t, 0, A("src", 0, 64), (A("sv", 0, 128), A("Dq", 0, 4)))
+        gather(A("hold", 0, 64), A("Hs", U, U + CH), A("doff", 16 * t, 16 * t + 4))
+        new = (lane0, A("Xl", 384 * t - 192 + U * t, 384 * t - 128 + U * t)) if t else (lane_in(0), comc(0, 0, U))
+        mm(A("py", 0, 64), [new, (A("Sh", 128, 256), A("hold", 0, 64))])
+        act(A("hnew", 0, 64), A("py", 0, 64), ACT.Copy)
 
     def phase_m(t):
         ph[0] += 1
-        if t == 0:
-            act(A("ea", 0, 64), IND(D128, elist(t, 0, U)), ACT.Identity, col(PF), None)
-            repeats(1, ("ea", 0), ("se", 0), ("se", 0))
-            act(A("wold", 0, 64), A("ea", 0, 64), ACT.Identity, col(LANE), 16.0)
-            return
-        mm(A("py", 384, 448), [(same, A("tv", 0, 64))])
         if t < STEPS - 1 or cfg["log"]:
-            act(A("wold", 64 * t, 64 * t + 64), A("py", 384, 448), ACT.Identity, col(L2), 16.0)
-        repeats(1, ("py", 384), ("sw", 0), ("se", 192 * t))
+            mm(A("py", 0, 64), [(A("B1", 0, 128), A("tv", 0, 64))])
+            act(A("wold", 64 * t, 64 * t + 64), A("py", 0, 64), ACT.Identity, col(L2), 16.0)
+        repeats(t, 1, A("tv", 0, 64), (ident, A("se", 192 * t + 15, 192 * t + 64, 16)))
 
     def phase_u(t):
         ph[0] += 1
         if t < STEPS - 1:
-            cp(IND(A("Hs", 0, CH + 128), A("soff", 0, 4)), A("hnew", 0, 64))
+            cp(IND(A("Hs", 0, U + CH), A("soff", 0, 4)), A("hnew", 0, 64))
         if t < STEPS - 1 or cfg["log"]:
-            cp(IND(A("ptr", 0, CH + 128), A("soff", 4, 8)), A("pval", 64 * t, 64 * t + 64))
+            cp(IND(A("ptr", 0, 192), A("soff", 4, 8)), A("pval", 64 * t, 64 * t + 64))
         else:
-            cp(IND(A("pts", 0, CH + 128), A("soff", 4, 8)), A("pval", 256, 320))
+            cp(IND(A("pts", 0, 192), A("soff", 4, 8)), A("pval", 256, 320))
 
     def phase_r(t):
         s0, g0, f0 = 192 * t, 3072 * t, 3072 * (t % cfg["npw"])
         win = A("Wt", 0, 2048 + 1024 * t) if t else A("W0", 0, 2048)
         last = t == STEPS - 1
         if last:
-            act(A("foff", 0, 128), A("ptr", 0, 128), ACT.Identity, col(L2), 16.0)
+            act(A("foff", 0, 128), A("ptr", U, 192), ACT.Identity, col(L2), 16.0)
         if last and not cfg["log"]:
-            act(A("foff", 128, 256), A("pts", 0, 128), ACT.Identity, col(LANE), None)
+            act(A("foff", 128, 256), A("pts", U, 192), ACT.Identity, col(LANE), None)
             for a, b in zip(cfg["bcut"], cfg["bcut"][1:]):
                 gather(A("wb", 16 * a, 16 * b), win, A("foff", a, b))
 
-        def landed(a, b):
-            return [(u, v, A("Bi", 192 * (t - 1) + (u + U) % S, 192 * (t - 1) + (u + U) % S + v - u))
-                    for (u, v) in ((a, min(b, S - U)), (max(a, S - U), b)) if u < v and t]
-
-        def carry(name, c0, const, a, b):
-            return [(A(name, c0 + u - a, c0 + v - a), const, x) for (u, v, x) in landed(a, b)]
         prods = []
 
         def update():
@@ -584,46 +612,85 @@ def build(cfg):
             for k0 in range(0, 16, 4):
                 cs = [("tensor_tensor", A("pd", k, 1024, 16), A("pg", g0 + 64 * k, g0 + 64 * k + 64), A("pl0", 64, 128), ALU.mult) for k in range(k0, k0 + 4)]
                 i = add("v", cs, sum(vcost(x[1], [x[2], x[3]], True) for x in cs))
-                if t in cfg["early"]:
-                    prods.append(i)
             if not last or cfg["log"]:
-                tt(A("Wt", 2048 + 1024 * t, 3072 + 1024 * t), IND(win, A("wold", 64 * t, 64 * t + 64)), A("pd", 0, 1024), ALU.add)
-        for n in range(3):
-            if n == 2:
+                i = tt(A("Wt", 2048 + 1024 * t, 3072 + 1024 * t), IND(win, A("wold", 64 * t, 64 * t + 64)), A("pd", 0, 1024), ALU.add)
+                if t in cfg["after"]:
+                    ops[i]["ord"].add(prods[-1])
+        for n in cfg["blocks"][t] + (3,):
+            if n == 3:
                 update()
+                break
             ph[0] += 1
-            c, e, pl, b0 = 64 * n, 64 * n + 64, "pl%d" % n, g0 + 1024 * n
-            lg, ys = A(pl, 0, 64), A("ys", s0 + c, s0 + e)
+            c, b0, gr = 64 * n, g0 + 1024 * n, (t + n) % 3
             cut = cfg["pcut"][t][n]
             for k, l in zip(cut, cut[1:]):
                 gather(A("pg", b0 + 64 * k, b0 + 64 * l), A("Ps", 0, CP), A("aoff", s0 + c + 4 * k, s0 + c + 4 * l), 1.0 / 32)
             cut, f = cfg["wcut"][t][n], f0 + 1024 * n
             for k, l in zip(cut, cut[1:]):
-                h = 8 * (k // 8) if t else 0
-                w0 = s0 + (c // 2 if t else c) - 4 * h
+                wide = (t, min(c, U)) in cfg["wide"]
+                h = 0 if wide else 8 * (k // 8)
+                w0 = s0 + (c if wide or n < 2 else 96) - 4 * h
                 i = tt(A("pw", f + 64 * k, f + 64 * l), IND(A(win["b"], h, win["c1"]), A("woff", w0 + 4 * k, w0 + 4 * l)), A("pg", b0 + 64 * k, b0 + 64 * l), ALU.mult)
                 if t in cfg["chain"] and prods:
                     ops[i]["ord"].add(prods[-1])
                 prods.append(i)
-            nk = 16
+            parts = [A("pw", f + 64 * k, f + 64 * k + 64) for k in range(16)]
+            if PLACE[gr][t] != t:
+                parts = []
+                for (k, l, m) in cfg["parts"][t][n]:
+                    c0 = spare[0]
+                    spare[0] += 64 * m
+                    rem([([A("pw", f + 64 * j, f + 64 * (j + m)) for j in range(k, l, m)], A("sp", c0, c0 + 64 * m), HOP * (PLACE[gr][t] - t))])
+                    parts += [A("sp", c0 + 64 * j, c0 + 64 * j + 64) for j in range(m)]
             for j in range(cfg["fold"].get((t, n), 0)):
-                nk //= 2
-                dma_add(A("pw", f, f + 64 * nk), A("pw", f + 64 * nk, f + 128 * nk))
-            group([(lg, posI, A("pw", f + 64 * k, f + 64 * k + 64)) for k in range(nk)] + carry(pl, 0, posS, c, e))
-            act(ys, lg, ACT.Sigmoid, None, -32.0)
-            if c == 0:
-                mm(A(pl, 64, 128), [(posI, A("of", s0, s0 + 64)), (posI, ys)])
-            for (a, b) in cfg["send"][t]:
-                if b != e:
-                    continue
-                for (u, v, x) in landed(a, b):
-                    act(A("Bo", s0 + u, s0 + v), x, ACT.Identity, None, 0.5)
-                srcs = [A(x, s0 + a, s0 + b) for x in (("Bo", "of", "ys") if t else ("of", "ys"))]
-                rem(srcs, [(A("Bi", s0 + a, s0 + b), -HOP * (STEPS - 1) if last else HOP)], 512 * (b - a) * len(srcs))
-                if last:
-                    dma(cfg["ybq"], [(EXT("yb", a, b), A("Bi", s0 + a, s0 + b))], 512 * (b - a))
+                parts = parts[:len(parts) // 2]
+                dma_add(A("pw", f, f + 64 * len(parts)), A("pw", f + 64 * len(parts), f + 128 * len(parts)))
+            m = cfg["pre"].get((t, n), 0)
+            if m:
+                low = A("pw", f + 1024 - 128 * m, f + 1024 - 64 * m)
+                tt(low, low, A("pw", f + 1024 - 64 * m, f + 1024), ALU.add)
+                parts = parts[:16 - m]
+            outcome(gr, t, parts, "pl%d" % n)
+
+    spare, held = [0], []
+
+    def tile(name, gr, t):
+        return A(name, 192 * t + 64 * gr, 192 * t + 64 * gr + 64)
+
+    def moves(gr, t):
+        return PLACE[gr][t] != (PLACE[gr] + [0])[t + 1]
+
+    def known(gr, t, pl):
+        mm(A(pl, 128, 192), [(posI, hot(gr, t))] + ([(halfI, tile("Bi", gr, t - 1))] if t else []))
+
+    def outcome(gr, t, parts, pl):
+        ph[0] += 1
+        lg, ys = A(pl, 0, 64), tile("ys", gr, t)
+        if t and not moves(gr, t):
+            known(gr, t, pl)
+        group([(lg, posI, x) for x in parts] + ([(lg, posS, tile("Bi", gr, t - 1))] if t else []))
+        act(ys, lg, ACT.Sigmoid, None, -32.0)
+        if gr == t % 3:
+            mm(A(pl, 64, 128), [(posI, hot(gr, t)), (posI, ys)])
+        if moves(gr, t):
+            if t:
+                act(tile("Bo", gr, t), tile("Bi", gr, t - 1), ACT.Identity, None, 0.5)
+            sides = [tile("Bi", gr, t)] + [tile("Bo", gr, t)] * (t > 0) + [hot(gr, t), ys]
+            d = gr - cfg["pair"].get(t, 9)
+            if d in (0, 1):
+                held.append(gr)
+                if len(held) % 2:
+                    return
+                sides = [A(x["b"], x["c0"] - 64 * d, x["c0"] - 64 * d + 128) for x in sides]
+            rem([(sides[1:], sides[0], HOP * ((PLACE[gr] + [0])[t + 1] - PLACE[gr][t]))])
+        else:
+            sides = [tile("Bi", gr, t)]
+            tt(sides[0], ys, A(pl, 128, 192) if t else hot(gr, t), ALU.add)
+        if t + 1 == STEPS:
+            dma(cfg["ybq"], [(EXT("yb", sides[0]["c0"] - 192 * t, sides[0]["c1"] - 192 * t), sides[0])], 512 * sides[0]["n"])
 
     phase_a(0)
+    at_home()
     for t in range(STEPS):
         ch = (((0, U), "pz0"), ((U, S), "pz1"))
 
@@ -663,7 +730,7 @@ def landing(o, issued, pipe, cfg):
     first, own = issued + (cfg["RF"] if o["kind"] == "rem" else cfg["DF"]) - 500.0, o["bytes"] / cfg["BW"] + o["rows"] * cfg["RC"]
     first += o.get("once", 0.0)
     after = max(pipe, first) + own
-    return (min(after, first + 2 * own) if o["bytes"] < cfg["SH"] else after) + 500.0, max(pipe, issued + cfg["DF"] - 500.0) + own
+    return (min(after, first + 2 * own) if o.get("raw", o["bytes"]) < cfg["SH"] else after) + 500.0, max(pipe, issued + cfg["DF"] - 500.0) + own
 
 
 def replay(ops, order, cfg):
@@ -735,7 +802,7 @@ def shuttle(opss, cfgs, order, rounds, seed=0):
                 if x > t:
                     t = x
             if choose and "both" in o:
-                e = min("vs", key=lambda e: fit(busy[e], t, o["both"][e][1])[0] + o["both"][e][1] + (choose if e != o["eng"] else 0.0))
+                e = min(sorted(o["both"]), key=lambda e: fit(busy[e], t, o["both"][e][1])[0] + o["both"][e][1] + (choose if e != o["eng"] else 0.0))
                 if e != o["eng"]:
                     assign(opss, i, e)
             t, p = fit(busy[o["eng"]], t, o["dur"])
@@ -790,7 +857,7 @@ def shuttle(opss, cfgs, order, rounds, seed=0):
         whole = {int(rnd.randint(ops[-1]["key"][1] + 1)): float(rnd.normal()) * cfgs[0]["far"] for s in range(int(rnd.randint(4)))}
         ends = [-(o["t1"] + push.get(o["key"], 0.0) + whole.get(o["key"][1], 0.0)) for o in ops]
         for i in rnd.choice(either, int(rnd.randint(3)), False):
-            assign(opss, int(i), "v" if ops[i]["eng"] == "s" else "s")
+            assign(opss, int(i), [e for e in ops[i]["both"] if e != ops[i]["eng"]][0])
         pick, wait = rnd.rand(), [x + wk for x in lat]
         back = pack(ops, ends, range(n - 1, -1, -1), succ, lat, zero, wait, 600.0 * rnd.rand() + 300.0 if pick < cfgs[0]["pick"] else 0.0)
         whole = {int(rnd.randint(ops[-1]["key"][1] + 1)): float(rnd.normal()) * cfgs[0]["far"] for s in range(int(rnd.randint(2)))}
@@ -827,51 +894,124 @@ def polish(opss, cfgs, order, rounds, seed=0):
     rnd = np.random.RandomState(seed)
     mix, heat, aim = cfgs[0]["mix"] / n, cfgs[0]["heat"], cfgs[0]["aim"]
 
-    def run(od, v, p0, old):
-        wk, dur, free, pipe = cfgs[v]["WK"], durs[v], [0.0] * len(engs), 0.0
-        fin, ready, load = old[0][:], old[1][:], old[2][:]
-        seen = set()
-        for i in od[p0 - 1::-1] if p0 else []:
+    def prior(od, p0):
+        seen = {}
+        for p in range(p0 - 1, -1, -1):
+            i = od[p]
             if eng[i] not in seen:
-                seen.add(eng[i])
-                free[eng[i]] = fin[i]
+                seen[eng[i]] = i
             if moving[i] and -1 not in seen:
-                seen.add(-1)
-                pipe = load[i]
+                seen[-1] = i
             if len(seen) > len(engs):
                 break
-        for i in od[p0:]:
+        return seen
+
+    def run(rest, v, seen, span, marked, stirred, flow, bar):
+        wk, dur, free, pipe = wks[v], durs[v], [0.0] * len(engs), 0.0
+        fin, ready, load = state[v]
+        for e, i in seen.items():
+            if e < 0:
+                pipe = load[i]
+            else:
+                free[e] = fin[i]
+        way, mark, stir, log, more, left, tail = ways[v], bytearray(marked), stirred[:], [], 0.0, span, tails[v]
+        for i in rest:
             e = eng[i]
+            if mark[i]:
+                left -= 1
+            elif not (stir[e] or (flow and moving[i])):
+                free[e] = fin[i]
+                if moving[i]:
+                    pipe = load[i]
+                continue
             t = free[e]
-            for j in sems[i]:
+            for j in waits[i]:
                 if ready[j] > t:
                     t = ready[j]
-            for j in soft[i]:
-                if ready[j] > t and eng[j] != e:
-                    t = ready[j]
-            fin[i] = free[e] = t = t + dur[i]
-            if moving[i]:
-                t, pipe = landing(opss[v][i], t, pipe, cfgs[v])
-                load[i] = pipe
-            ready[i] = t + wk
-        return fin, ready, load
-    blank = ([0.0] * n, [0.0] * n, [0.0] * n)
-    state = [run(order, v, 0, blank) for v in range(nv)]
-    norm = [nv * max(s[1]) for s in state]
+            free[e] = t = t + dur[i]
+            span -= 1
+            old = fin[i]
+            if t != old or moving[i]:
+                if span < 0 and t + tail[i] > bar:
+                    return log, None
+                stir[e] = span >= 0 or t != old
+                log.append((i, old, ready[i], load[i]))
+                fin[i] = t
+                if moving[i]:
+                    first, own, small, lead = way[i]
+                    first += t
+                    x = (pipe if pipe > first else first) + own
+                    pipe = (pipe if pipe > t + lead else t + lead) + own
+                    flow = span >= 0 or pipe != load[i]
+                    load[i] = pipe
+                    t = (first + 2 * own if small and first + 2 * own < x else x) + 500.0
+                t += wk
+                if t != ready[i]:
+                    more += (t - ready[i]) * weight[i]
+                    ready[i] = t
+                    for k in heed[i]:
+                        if not mark[k]:
+                            mark[k] = 1
+                            left += 1
+            elif span < 0:
+                stir[e] = False
+                if not (left or flow or True in stir):
+                    break
+        return log, more
 
-    def worth(s, v):
-        return (max(s[1]) + mix * sum(s[1])) / norm[v]
-    part = [worth(s, v) for v, s in enumerate(state)]
-
-    def better(od, p0, room):
-        new, val = [], []
+    def anew(od):
         for v in range(nv):
-            new.append(run(od, v, p0, state[v]))
-            val.append(worth(new[v], v))
-            if sum(val) - sum(part[:v + 1]) > room + 0.001 * (nv - 1 - v):
+            state[v] = ([-1.0] * n, [0.0] * n, [0.0] * n)
+            total[v] = run(od, v, {}, n, b"\1" * n, [True] * len(engs), True, 0.0)[1]
+            part[v] = worth(v, total[v])
+            fin, ready, dur, tail, ahead = state[v][0], state[v][1], durs[v], tails[v], [0.0] * len(engs)
+            for i in od[::-1]:
+                t = 0.0
+                for k in waiting[i]:
+                    if dur[k] + tail[k] > t:
+                        t = dur[k] + tail[k]
+                t += ready[i] - fin[i]
+                tail[i] = t = t if t > ahead[eng[i]] else ahead[eng[i]]
+                ahead[eng[i]] = t + dur[i]
+    ways = [{o["i"]: ((c["RF"] if o["kind"] == "rem" else c["DF"]) - 500.0 + o.get("once", 0.0), o["bytes"] / c["BW"] + o["rows"] * c["RC"], o.get("raw", o["bytes"]) < c["SH"],
+                      c["DF"] - 500.0) for o in x if o["kind"] != "c"} for x, c in zip(opss, cfgs)]
+    waits = [sems[i] + [j for j in soft[i] if eng[j] != eng[i]] for i in range(n)]
+    beside = [[i] + [k for k in succ[i] if i in soft[k]] for i in range(n)]
+    heed = [[k for k in succ[i] if i in sems[k] or i in soft[k]] for i in range(n)]
+    wks, ends = [c["WK"] for c in cfgs], [i for i in range(n) if not succ[i] and moving[i]]
+    weight = [cfgs[0]["heavy"] if o["key"][0] in ("ys", "Bi", "Bo", "sp", "pl0", "pl1", "pl2", "pd", "Wt") else 1.0 for o in ops]
+    state, total, part, norm = [None] * nv, [0.0] * nv, [0.0] * nv, [1.0] * nv
+    waiting, tails = [[k for k in succ[i] if i in sems[k]] for i in range(n)], [[0.0] * n for v in range(nv)]
+
+    def worth(v, s):
+        ready = state[v][1]
+        return (max([ready[i] for i in ends]) + mix * s) / norm[v]
+    anew(order)
+    norm = [nv * max(s[1]) for s in state]
+    anew(order)
+
+    def better(od, p0, span, room, both):
+        logs, val, seen, rest, worse = [], [], prior(od, p0), od[p0:], 0.0
+        marked, stirred, flow = bytearray(n), [both and e in ("v", "s", "g") for e in engs], False
+        for i in rest[:span]:
+            marked[i] = stirred[eng[i]] = True
+            flow = flow or moving[i]
+        for v in range(nv):
+            bar = room + ahead * (nv - 1 - v)
+            logs.append(run(rest, v, seen, span, marked, stirred, flow, (part[v] + bar - worse + spare) * norm[v] - mix * total[v]))
+            if logs[v][1] is not None:
+                val.append(worth(v, total[v] + logs[v][1]))
+                worse += val[v] - part[v]
+            if logs[v][1] is None or worse > bar:
+                for (fin, ready, load), (log, more) in zip(state, logs):
+                    for (i, a, b, c) in log:
+                        fin[i], ready[i], load[i] = a, b, c
                 return False
-        state[:], part[:] = new, val
+        for v in range(nv):
+            total[v] += logs[v][1]
+        part[:] = val
         return True
+    ahead, spare, every, leap = cfgs[0]["ahead"], cfgs[0]["spare"], cfgs[0]["every"], cfgs[0]["leap"]
 
     def tight(od, v):
         fin, ready = state[v][0], state[v][1]
@@ -891,18 +1031,21 @@ def polish(opss, cfgs, order, rounds, seed=0):
         return pairs
 
     def turn(i):
-        assign(opss, i, "v" if ops[i]["eng"] == "s" else "s")
+        assign(opss, i, [e for e in ops[i]["both"] if e != ops[i]["eng"]][0])
         eng[i] = engs.index(ops[i]["eng"])
+        for k in beside[i]:
+            waits[k] = sems[k] + [j for j in soft[k] if eng[j] != eng[k]]
         for x, d in zip(opss, durs):
             d[i] = x[i]["dur"]
     best, keep, held = sum(part), (order, list(eng)), [None] * nv
     for r in range(rounds):
-        if r % 200 == 0:
-            v = (r // 200) % nv
+        if r % every == 0:
+            v = (r // every) % nv
             rank = {i: p for p, i in enumerate(order)}
             order = sorted(order, key=lambda i: (state[v][0][i] - durs[v][i], rank[i]))
-            state[:] = [run(order, v, 0, blank) for v in range(nv)]
-            part[:] = [worth(s, v) for v, s in enumerate(state)]
+            anew(order)
+        if r % 40 == 0:
+            held = [None] * nv
         x = rnd.rand(5)
         room = -heat * (1 - r / rounds) * np.log(1 - x[0])
         od = None
@@ -917,6 +1060,8 @@ def polish(opss, cfgs, order, rounds, seed=0):
             p0 = order.index(i)
             if "both" not in ops[i] or x[4] > 0.3:
                 p0, pb = order.index(a), p0 if i == b else order.index(b)
+                if p0 > pb or eng[a] != eng[b]:
+                    continue
                 move, need, queues = [b], set(pred[b]), set()
                 for y in order[pb - 1:p0:-1]:
                     if y in need or eng[y] in queues:
@@ -926,12 +1071,19 @@ def polish(opss, cfgs, order, rounds, seed=0):
                 if a in need or eng[a] in queues:
                     continue
                 od = order[:p0] + move[::-1] + [y for y in order[p0:pb] if y not in move] + order[pb + 1:]
+                span = pb - p0 + 1
         else:
             p0 = int(x[2] * n)
             i = order[p0]
             if "both" not in ops[i] or x[4] > 0.15:
                 step, hops, q, stop = (1 if x[3] < 0.5 else -1), int(rnd.geometric(0.4)), p0, False
                 bar = set(succ[i] if step > 0 else pred[i])
+                if step < 0 and x[4] > 1 - leap:
+                    fin, ready = state[0][0], state[0][1]
+                    t = max([ready[j] for j in waits[i]] + [0.0])
+                    hops = sum(1 for y in order[max(0, p0 - 150):p0] if eng[y] == eng[i] and fin[y] - durs[0][y] >= t)
+                    if not hops:
+                        continue
                 while hops and not stop:
                     q += step
                     stop = q < 0 or q >= n or order[q] in bar
@@ -941,7 +1093,7 @@ def polish(opss, cfgs, order, rounds, seed=0):
                     continue
                 od = order[:p0] + order[p0 + 1:]
                 od.insert(q, i)
-                p0 = min(p0, q)
+                p0, span = min(p0, q), abs(q - p0) + 1
         turned = []
         if od is None:
             turned = [i]
@@ -951,10 +1103,11 @@ def polish(opss, cfgs, order, rounds, seed=0):
                     q = near[int(rnd.randint(len(near)))]
                     turned.append(order[q])
                     p0 = min(p0, q)
+            span = max(order.index(k) for y in turned for k in beside[y]) - p0 + 1
         for y in turned:
             turn(y)
-        if better(od or order, p0, room):
-            order, held = od or order, [None] * nv
+        if better(od or order, p0, span, room, od is None):
+            order = od or order
             if sum(part) < best:
                 best, keep = sum(part), (order, list(eng))
         else:
@@ -963,7 +1116,8 @@ def polish(opss, cfgs, order, rounds, seed=0):
     for i in range(n):
         if eng[i] != keep[1][i]:
             turn(i)
-    return keep[0], [max(run(keep[0], v, 0, blank)[1]) - cfgs[v]["WK"] for v in range(nv)]
+    anew(keep[0])
+    return keep[0], [max(state[v][1]) - wks[v] for v in range(nv)]
 
 
 def arrange(cfg):
@@ -1034,10 +1188,14 @@ def rank_program(g, core, T, topo):
     cores = list(T.cores)
     queue = {"pe": g.tensor, "v": g.vector, "s": g.scalar, "g": g, "sync": g.sync}
 
-    def mask_of(src, hops, step):
+    def masks(src, hops):
         to = [cores[(cores.index(src) + h) % NR] for h in hops]
-        both = [e for e in topo.engines(src, to[0]) if all(e in topo.engines(src, c) for c in to)]
-        return sum(1 << e for e in both[::step])
+        free, out = [e for e in topo.engines(src, to[0]) if all(e in topo.engines(src, c) for c in to)], []
+        total = len(free)
+        for p in SHARE[len(hops)]:
+            out.append(sum(1 << e for e in free[:total // p]))
+            free = free[total // p:]
+        return out
 
     def bits(m):
         return bin(m).count("1")
@@ -1046,8 +1204,8 @@ def rank_program(g, core, T, topo):
         if o["kind"] == "dma":
             full[o["tok"]] = 16 * len(o["calls"])
         elif o["kind"] == "rem":
-            hops = [d[1] for d in o["calls"][0][2]]
-            full[o["tok"]] = sum(bits(mask_of(cores[(rank - h) % NR], hops, o.get("step", 1))) for h in hops)
+            hops = [m[2] for m in o["calls"][0][1]]
+            full[o["tok"]] = sum(bits(masks(cores[(rank - h) % NR], hops)[n]) for n, h in enumerate(hops))
     sent = 0
     outs = []
     for i in order:
@@ -1057,17 +1215,15 @@ def rank_program(g, core, T, topo):
             q.wait_ge(T.sem[name], full.get(name, val))
         for c in o["calls"]:
             if c[0] == "remote":
-                hops = [d[1] for d in c[2]]
-                m = mask_of(core, hops, o.get("step", 1))
-                to = [topo.addr(cores[(rank + h) % NR]) for h in hops]
-                srcs = [real(T, a) for a in c[1]]
-                if len(hops) == 1 and len(srcs) == 1:
-                    g.remote_dma(real(T, c[2][0][0]), srcs[0], T.sem[o["tok"]], T.sem.loc, to[0][1], to[0][0], m)
+                ms = masks(core, [m[2] for m in c[1]])
+                to = [topo.addr(cores[(rank + m[2]) % NR]) for m in c[1]]
+                if len(ms) == 1 and len(c[1][0][0]) == 1:
+                    g.remote_dma(real(T, c[1][0][1]), real(T, c[1][0][0][0]), T.sem[o["tok"]], T.sem.loc, to[0][1], to[0][0], ms[0])
                 else:
-                    g.remote_dma_fused([RemoteDMATransfer(dst_ids=[DstId(rid=a[0], pnc=a[1]) for a in to], dma_engine_mask=m,
-                                                          remote_sem=T.sem[o["tok"]], srcs=srcs, dsts=[real(T, d[0]) for d in c[2]],
-                                                          alu_op=1 if len(srcs) > 1 else 0)], local_sem=T.sem.loc)
-                sent += bits(m)
+                    g.remote_dma_fused([RemoteDMATransfer(dst_ids=[DstId(rid=a[0], pnc=a[1])], dma_engine_mask=e, remote_sem=T.sem[o["tok"]],
+                                                          srcs=[real(T, x) for x in m[0]], dsts=[real(T, m[1])], alu_op=1 if len(m[0]) > 1 else 0)
+                                        for m, a, e in zip(c[1], to, ms)], local_sem=T.sem.loc)
+                sent += sum(bits(e) for e in ms)
                 continue
             x = [real(T, a) if isinstance(a, dict) else a for a in c[1:]]
             if c[0] == "dma_start":
@@ -1102,6 +1258,8 @@ def rank_program(g, core, T, topo):
                 ins = q.tensor_scalar(*x)
             elif c[0] == "tensor_tensor":
                 ins = q.tensor_tensor(*x)
+            elif c[0] == "tensor_reduce":
+                ins = q.tensor_reduce(x[0], x[1], AxisListType.X, x[2], apply_absolute_value=x[3])
             elif c[0] == "tensor_tensor_scan":
                 ins = q.tensor_tensor_scan(*x)
             else:

import math
import numpy as np
from concourse.bass import DstId, RemoteDMATransfer
from concourse.mybir import AluOpType, ActivationFunctionType, AxisListType

S, U, CH, CP, STEPS, HOP, NR = 192, 64, 2048, 4096, 4, 3, 8
ZC = 2048.0
TOP = 1.5 * 2.0 ** 35


def sb(n, dtype):
    return ("sbuf", [128, n], dtype)


BF, HF, FL, IN, UI = "bfloat16", "float16", "float32", "int32", "uint16"
SCRATCH = {
    "snd": sb(192, BF), "com": sb(768, BF), "Xh": sb(768, BF), "Xl": sb(3 * 384, BF), "oh": sb(768, FL), "ol": sb(3 * 384, FL),
    "kl": sb(8, IN), "kli": sb(4, IN), "klf": sb(4, FL),
    "Hs": sb(U + CH, BF), "Ps": sb(CP, BF), "W0": sb(2048, BF), "Wt": sb(2048 + 4096, FL),
    "ptr": sb(192, FL), "pts": sb(192, FL), "pval": sb(320, FL),
    "Dm": sb(128, BF), "Pm": sb(128, BF), "Gi": sb(192, BF), "Ix": sb(388, BF), "Iy": sb(128, BF),
    "pi": sb(2, IN), "col": sb(16, FL), "Sm": sb(144, BF), "mn": sb(128, BF), "I1": sb(128, HF), "B8": sb(128, HF), "Dq": sb(260, HF),
    "KL": sb(4 * 128, BF), "Lr": sb(256, BF), "Sh": sb(5 * 128, BF), "E0": sb(256, BF), "KF": sb(256, FL), "xf": sb(384, FL), "dm": sb(128, BF), "Oh": sb(384, BF),
    "Zw": sb(144, BF), "Sr": sb(320, BF), "B1": sb(256, HF), "Bq": sb(128, HF), "nI": sb(128, BF), "zr": sb(144, BF),
    "kk": sb(64, BF), "My": sb(2 * 64, FL), "MA": sb(128, HF), "MF": sb(128, HF), "cm": sb(8, FL), "top": sb(128, BF), "vc": sb(16, FL),
    "F32": sb(3 * 128, FL), "Cz": sb(128, BF),
    "xs": sb(192, BF), "xm": sb(1536, BF), "bz": sb(4 * 128, BF), "gz": sb(4 * 128, BF),
    "ci": sb(192, IN), "cj": sb(4 * 192, IN), "coff": sb(4 * 192, UI), "hp": sb(2 * 3072, BF),
    "zc": sb(384, HF), "se": sb(4 * 192, BF), "tv": sb(192, HF), "sv": sb(384, HF),
    "aoff": sb(4 * 192, UI), "src": sb(64, HF), "so": sb(8, FL),
    "doff": sb(4 * 16, UI), "soff": sb(8, UI), "woff": sb(4 * 192, UI), "wold": sb(4 * 64, UI), "foff": sb(256, UI), "hold": sb(64, BF), "hnew": sb(64, BF),
    "pg": sb(4 * 3072, BF), "pw": sb(4 * 3072, FL), "pd": sb(1040, FL), "wb": sb(2048, FL),
    "ys": sb(12 * 64, FL), "Bo": sb(12 * 64, FL), "Bi": sb(12 * 64, FL), "wo": sb(2048, FL), "sp": sb(8 * 256, FL),
}
for _b in ("pa", "pz0", "pz1", "py", "pl0", "pl1", "pl2", "pq"):
    SCRATCH[_b] = ("psum", [128, 512], "float32")
NDMA = 72
SEMAPHORES = ["e_pe", "e_v", "e_s", "e_g", "loc"] + ["d%d" % i for i in range(NDMA)]

CUT, ONE, TWO = [0, 32, 64, 96, 128, 160, 192], [0, 16], [0, 8, 16]
CFG = {
    "hcut": [CUT] + [[0, 32, 64, 128, 192]] * 3,
    "pcut": [[TWO, TWO, ONE]] + [[TWO, ONE, ONE]] * 2 + [[TWO] * 3],
    "wcut": [[TWO] * 3] * 4, "pre": {},
    "wide": {(0, 0), (0, 64)},
    "a_at": {1: (0, 1), 2: (0, 2), 3: (1, 2)},
    "turn": {(1, 64), (2, 64), (3, 64)},
    "late": set(), "bcut": [0, 32, 64, 96, 128],
    "parts": [[None, [(0, 16, 4)], [(0, 16, 4)]]] * 3 + [[None, [(0, 8, 4), (8, 16, 4)], None]],
    "place": [[0, 3, 3, 3], [1, 1, 0, 0], [2, 2, 2, 3]], "fold": {},
    "on": True, "widen": 0, "f32": 64,
    "log": False,
    "fin": [0, 24, 56, 92, 128],
    "g_l": {(t, k) for t in range(4) for k in (0, 1)} - {(0, 0)}, "g_c": {1, 2, 3}, "g_e": {(t, a) for t in (1, 2, 3) for a in (0, 64)}, "short": False, "chain": {0, 1, 2, 3}, "after": {0, 1, 2}, "pair": {}, "blocks": [(0, 1, 2)] * 4, "ybq": "s", "npw": 4, "SH": 100000, "gate": False, "GD": 1000.0, "GD1": 1000.0, "AD": 2.0,
    "G": 1.6, "SC": 4.2, "CY": 1.12, "OV": 50.0, "OS": 35.0, "MS": 40, "PE": 0.4, "WK": 150.0, "OV2": 0.0, "DI": 150.0, "DF": 1200.0, "BW": 370.0, "RF": 1500.0, "RC": 25.0, "RI": 600.0, "R1": 1500.0, "RR": 1.2, "RB": 1.4, "GF": 1.25,
    "seed": 0, "tries": 1, "shuttle": 100, "trim": 1000, "polish": 600000, "passes": 1, "far": 1000.0, "pick": 0.02, "swap": 0.5, "packs": (0, 3, 4), "slack": 0.0, "aim": 0.25, "mix": 0.3, "ahead": 0.0002, "spare": 0.0003, "every": 200, "leap": 0.2, "heavy": 3.0, "heat": 0.001, "heat2": 0.002,
}
VARIANTS = [{}, {"G": 1.35, "SC": 2.5, "CY": 1.15, "BW": 420.0, "WK": 110.0, "DI": 100.0, "RC": 15.0, "RB": 1.6, "RR": 2.0, "DF": 900.0, "RF": 1100.0},
            {"G": 2.7, "SC": 7.0, "CY": 1.35, "WK": 200.0, "BW": 300.0, "RF": 2000.0, "DI": 250.0, "RC": 40.0, "GF": 1.4},
            {"G": 1.4, "CY": 1.05, "PE": 0.46, "WK": 180.0, "RF": 2500.0, "RI": 900.0, "GD": 1500.0, "RB": 1.5, "RR": 1.2, "GF": 1.4, "DF": 1700.0, "R1": 2500.0, "BW": 300.0, "DI": 200.0},
            {"G": 1.3, "SC": 3.0, "CY": 1.4, "PE": 0.42, "GF": 1.45, "DF": 1500.0, "RF": 2000.0},
            {"G": 2.5, "SC": 5.5, "CY": 1.25, "WK": 230.0, "OS": 60.0, "OV2": 10.0, "RB": 1.0, "RR": 1.0, "GF": 1.5, "RI": 1000.0},
            {"G": 2.0, "SC": 3.0, "CY": 1.2, "WK": 180.0, "OS": 15.0, "MS": 64, "OV2": 20.0, "BW": 260.0, "DF": 1200.0, "RF": 1500.0, "R1": 3000.0, "DI": 60.0}]
SHARE = {1: (1,), 2: (2, 2), 3: (2, 4, 4)}
QUEUES = ("pe", "v", "s", "g", "sync")
ALU = AluOpType
ACT = ActivationFunctionType


def A(name, c0, c1, step=1, p0=0, p1=128):
    n = (c1 - c0 + step - 1) // step
    return {"b": name, "c0": c0, "c1": c0 + (n - 1) * step + 1, "st": step, "p0": p0, "p1": p1, "n": n}


def IND(win, off):
    return {"b": win["b"], "win": win, "off": off, "n": 16 * off["n"]}


def real(T, a):
    if "win" in a:
        return real(T, a["win"]).indirect(real(T, a["off"]))
    if "ext" in a:
        if a["ext"] == "rows":
            return T[a["b"]][a["p0"]:a["p1"], a["c0"]:a["c1"]]
        return T[a["b"]][:, a["c0"]:a["c1"]] if a["ext"] == "cols" else T[a["b"]][:]
    if a["st"] == 1:
        return T[a["b"]][a["p0"]:a["p1"], a["c0"]:a["c1"]]
    return T[a["b"]][a["p0"]:a["p1"], a["c0"]:a["c1"]:a["st"]]


def EXT(name, c0=None, c1=None, p0=None, p1=None):
    return {"b": name, "ext": "all" if c0 is None else "cols" if p0 is None else "rows", "c0": c0, "c1": c1, "p0": p0, "p1": p1}


def in_psum(a):
    return SCRATCH[a["b"]][0] == "psum"


def width(a):
    return 2 if SCRATCH[a["b"]][2] in (BF, HF, UI) else 4


def build(cfg):
    PLACE = cfg["place"]
    HOT = sorted(((gr, t) for gr in range(3) for t in range(STEPS)), key=lambda x: PLACE[x[0]][x[1]])
    HW = max([PLACE[gr][t] for gr, t in HOT].count(h) for h in (1, 2, 3))
    FROM = {h: min(12 - HW, [PLACE[gr][t] for gr, t in HOT].index(h)) for h in (1, 2, 3)}
    ops = []
    hist = {}
    bank = {}
    ndma = [0]
    ph = [0]

    def add(eng, calls, dur, kind="c", after=(), nbytes=0, grp=None, free=False):
        i = len(ops)
        o = {"i": i, "eng": eng, "calls": calls, "dur": dur, "kind": kind, "sem": set(after), "ord": set(), "bank": set(), "bytes": nbytes, "grp": grp}
        rd, wr = [], []
        for c in calls:
            if c[0] == "remote":
                ins, outs = [a for x in c[1] for a in x[0]], [x[1] for x in c[1]]
            else:
                ins, outs = list(c[1 if c[0] == "dma_add" else 2:]), [c[1]]
            for a in ins:
                if isinstance(a, dict) and "ext" not in a:
                    rd += [a["win"], a["off"]] if "win" in a else [a]
            for a in outs:
                if "win" in a:
                    wr.append(a["win"])
                    rd.append(a["off"])
                elif "ext" not in a:
                    wr.append(a)
        o["key"] = (wr[0]["b"] if wr else calls[0][1]["b"], ph[0])

        def dep(j):
            if j != i:
                o["ord" if grp is not None and ops[j]["grp"] == grp else "sem"].add(j)

        def meet(a, e):
            if not (e["c0"] < a["c1"] and a["c0"] < e["c1"] and e["p0"] < a["p1"] and a["p0"] < e["p1"]):
                return False
            return e["st"] == 1 or e["st"] != a["st"] or (e["c0"] - a["c0"]) % e["st"] == 0

        def covers(a, e):
            return a["p0"] <= e["p0"] and e["p1"] <= a["p1"] and a["c0"] <= e["c0"] and e["c1"] <= a["c1"] and (a["st"] == 1 or (e["st"] == a["st"] and meet(a, e)))
        for a in rd:
            for (j, w, e) in hist.get(a["b"], []):
                if w and meet(a, e):
                    dep(j)
        for a in wr:
            for (j, w, e) in hist.get(a["b"], []):
                if meet(a, e):
                    dep(j)
        for a in wr:
            h = hist.setdefault(a["b"], [])
            h[:] = [x for x in h if x[0] == i or not covers(a, x[2])]
            h.append((i, True, a))
        for a in rd:
            hist.setdefault(a["b"], []).append((i, False, a))
        for name in sorted({a["b"] for a in rd + wr if in_psum(a)}):
            st = bank.setdefault(name, {"eng": None, "cur": [], "prev": []})
            if st["eng"] != eng or free:
                st["prev"] = st["cur"]
                st["cur"] = []
                st["eng"] = None if free else eng
            elif eng == "pe" and st["cur"]:
                o["ord"].add(st["cur"][-1])
            o["bank"] |= set(st["prev"]) - o["sem"]
            st["cur"].append(i)
        o["sem"] |= o["bank"]
        o["ord"] -= o["sem"]
        if kind != "c":
            o["tok"] = "d%d" % ndma[0]
            ndma[0] += 1
        ops.append(o)
        return i

    cy, ov = 0.83 * cfg["CY"], cfg["OV"]

    def vcost(out, ins, two=False):
        n = out["n"]
        if "win" in out:
            return ov + n * cfg["SC"] * 0.83
        if any("win" in a for a in ins):
            return ov + n * cfg["G"] * 0.83
        if two:
            f = 1.0 if any(in_psum(a) for a in ins) else 2.0
        else:
            f = 0.5 if all(width(a) == 2 for a in [out] + ins) else 1.0
        return cfg["OV2"] + max(n * f, 64) * cy

    def cp(out, a):
        return add("v", [("tensor_copy", out, a)], vcost(out, [a]))

    def tsc(out, a, s1, s2, o0, o1=None):
        return ("tensor_scalar", out, a, s1, s2, o0) + (() if o1 is None else (o1,))

    def ts(out, a, s1, s2, o0, o1=None):
        return add("v", [tsc(out, a, s1, s2, o0, o1)], vcost(out, [a]))

    def tt(out, a, b, o):
        return add("v", [("tensor_tensor", out, a, b, o)], vcost(out, [a, b], True))

    def scan(out, a, b, o0, o1):
        return add("v", [("tensor_tensor_scan", out, a, b, 0.0, o0, o1)], vcost(out, [a, b]))

    def mset(out, val):
        return add("v", [("memset", out, val)], vcost(out, []))

    def acts(items, eng="s"):
        other = []
        for (out, a, f, bias, scale) in items:
            if f == ACT.Copy:
                other.append(("tensor_copy", out, a))
            elif f == ACT.Identity and (bias is None or scale is None):
                other.append(tsc(out, a, scale if bias is None else bias, None, ALU.mult if bias is None else ALU.add))
            elif f == ACT.Identity:
                other.append(tsc(out, a, scale, bias, ALU.mult, ALU.add))
            elif f == ACT.Relu:
                other.append(tsc(out, a, 0.0, scale, ALU.max, ALU.mult))
            elif f == ACT.Abs:
                other.append(tsc(out, a, bias, 4096.0, ALU.not_equal, ALU.mult))
        both = {"s": ([("activation",) + x for x in items],
                      sum(15 + vcost(x[0], [x[1]]) if "win" in x[1] else cfg["OS"] + max(x[0]["n"], cfg["MS"]) * cy for x in items))}
        if other:
            both["v"] = (other, sum(vcost(x[0], [x[1]]) for x in items))
        i = add(eng, both[eng][0], both[eng][1], free=len(both) > 1)
        if len(both) > 1:
            ops[i]["both"] = both
        return i

    def act(out, a, f, bias=None, scale=None, eng="s"):
        return acts([(out, a, f, bias, scale)], eng)

    def mcost(c):
        f = 4 if SCRATCH[c[3]["b"]][2] == FL else 1
        return max(min(64, c[2]["n"]), c[3]["n"]) * f * cfg["PE"] * cfg["CY"]

    def mrun(calls, cycles=1200):
        grp, run = ("g", len(ops)), []
        for c in calls:
            run.append(c)
            if sum(mcost(x) for x in run) >= cycles * cfg["CY"] * cfg["PE"] - 0.01 or c is calls[-1]:
                i = add("pe", run, sum(mcost(x) for x in run), grp=grp)
                if run[0] is not calls[0]:
                    ops[i]["ord"].add(i - 1)
                run = []

    def group(items, close=True):
        mrun([("matmul", o, l, r, n == 0, close and n == len(items) - 1) for n, (o, l, r) in enumerate(items)])

    def mm(out, pairs):
        group([(out, l, r) for (l, r) in pairs])

    def pool(call, fixed, other):
        dur = cfg["GF"] * (fixed + 2 * call[1]["n"] * cy)
        i = add("g", [call] + ([other] if other else []), dur)
        if other:
            ops[i].update(calls=[call], both={"g": ([call], dur), "v": ([other], vcost(other[1], [x for x in other[2:3] if isinstance(x, dict)]))})
        return i

    def iota(out, pat, base, cm, other=None):
        return pool(("iota", out, pat, base, cm), 130, other)

    def keep(out, a, pat, op, fill, base, cm, other=None):
        return pool(("affine_select", out, a, pat, op, fill, base, cm), 170, other)

    def plain(out, a):
        return keep(out, a, [[0, out["n"]]], ALU.is_gt, 0.0, 1, 0, ("tensor_copy", out, a))

    def dma(q, pairs, nbytes, after=(), behind=()):
        i = add(q, [("dma_start", o, a) for (o, a) in pairs], len(pairs) * (cfg["DI"] if q != "g" else 1000.0), "dma", after, nbytes)
        ops[i]["ord"] |= set(behind)
        ops[i]["rows"] = 8
        return i

    def rem(moves):
        part = SHARE[len(moves)]
        i = add("g", [("remote", moves)], cfg["RI"], "rem", (), max(128 * len(m[0]) * m[1]["n"] * width(m[1]) * p for m, p in zip(moves, part)))
        ops[i]["rows"] = max(8 * len(m[0]) * p for m, p in zip(moves, part)) * cfg["RR"]
        ops[i].update(raw=ops[i]["bytes"], bytes=ops[i]["bytes"] * cfg["RB"])
        return i

    def gather(out, win, off, scale=None, eng="s"):
        return act(out, IND(win, off), ACT.Copy if scale is None else ACT.Identity, None, scale, eng)

    adds = []

    def dma_add(out, a):
        i = add("g", [("dma_add", out, a)], cfg["GD"] + (0.0 if adds else cfg["GD1"]), "dma", (), int(512 * a["n"] * cfg["AD"]))
        ops[i]["rows"] = 8
        if adds:
            ops[i]["ord"].add(adds[0])
        adds.append(i)
        return i

    l_kap = dma("sync", [(A("kl", 0, 1), EXT("kap"))], 8192)
    l_lam = dma("s", [(A("kl", 1, 2), EXT("lam"))], 8192)
    l_past = dma("sync", [(A("snd", 0, 192), EXT("past"))], 49152, (), (l_kap,))
    l_com = dma("s", [(A("com", 0, 768, 1, 0, 8), EXT("coming"))], 12288, (), (l_lam,))
    l_hist = dma("sync", [(A("Hs", U, U + CH), EXT("hist"))], 524288, (), (l_past,))
    mset(A("xm", 0, 1536), 0.0)
    mset(A("zr", 0, 144), 0.0)
    loads = {
        "x": ([(A("xm", 192 * g, 192 * g + 192, 1, 16 * g, 16 * g + 16), EXT("past", 0, S, 16 * g, 16 * g + 16)) for g in range(8)], 49152),
        "b": ([(A("bz", 16 * g, 16 * g + 16, 1, 0, 12), EXT("past", 0, S, 16 * g, 16 * g + 1)) for g in range(8)], 4096),
        "s": ([(A("Ps", 0, CP), EXT("score"))], 1048576), "w": ([(A("W0", 0, 2048), EXT("weight"))], 524288)}
    l_x = dma("sync", loads["x"][0], loads["x"][1], (), (l_hist,))
    dma("s", loads["b"][0], loads["b"][1], (), (l_com,))
    iota(A("Dm", 0, 128), [[1, 128]], 0, -1)
    iota(A("pi", 0, 1), [[1, 1]], 0, 1)
    iota(A("Pm", 0, 128), [[-16, 8], [0, 16]], 0, 1)
    iota(A("Iy", 0, 128), [[0, 8], [1, 16]], 0, 0)
    iota(A("Gi", 0, 192, 1, 0, 12), [[1, 12], [0, 16]], 0, -1)

    def line(out, fill, base, cm, other=None):
        return keep(out, A("zr", 0, out["n"], 1, 0, out["p1"]), [[1, out["n"]]], ALU.not_equal, fill, base, cm, other)

    def diagonal(out, fill, c0, d):
        return line(out, fill, c0 - d, -1, tsc(out, A("Dm", c0, c0 + out["n"]), 1.0 * d, fill, ALU.is_equal, ALU.mult))

    def col(j, p1=128):
        return A("col", j, j + 1, 1, 0, p1)
    LANE, PF, CW, L2, CD = range(5)
    D128 = A("Dm", 0, 128)
    ts(A("pi", 1, 2), A("pi", 0, 1), 15, None, ALU.bitwise_and)
    cp(col(PF), A("pi", 0, 1))
    cp(col(LANE), A("pi", 1, 2))
    same = A("Sm", 0, 128)
    ts(same, A("Pm", 0, 128), col(LANE), None, ALU.is_equal)

    ts(A("vc", 0, 16), A("Iy", 0, 16), col(LANE), None, ALU.is_ge)

    def shift(t):
        out = A("Sh", 128 * t, 128 * t + 128)
        return keep(out, same, [[1, 128]], ALU.is_equal, 0.0, -t, -1, tsc(out, D128, 1.0 * t, A("vc", 15 - t, 16 - t), ALU.is_equal, ALU.mult))

    def lane_in(i):
        return A("Zw", 3 - i, 131 - i, 1, 0, 8)

    def comc(t, u0, n):
        return A("com", 192 * t + u0, 192 * t + u0 + n, 1, 0, 8)

    def symbols(t0, bank):
        for t in (t0, t0 + 1):
            c = 192 * (t - t0)
            mm(A(bank, c, c + 192), [(A("Sh", 128 * t, 128 * t + 128), A("snd", 0, 192))] + [(lane_in(t - 1 - s), comc(s, 0, 192)) for s in range(t)])
        act(A("Xh", 192 * t0 - 192, 192 * t0 + 192), A(bank, 0, 384), ACT.Copy)

    def moved(t):
        return ([A("Xh", 192 * t - 192, 192 * t + 192)], A("Xl", 384 * t - 384, 384 * t), HOP * t)
    line(A("Zw", 0, 144, 1, 0, 8), 1.0, -3, -16)
    shift(1)
    shift(2)
    iota(A("kk", 0, 64), [[1, 16], [0, 4]], 0, 0)
    symbols(1, "pl2")
    first = rem([moved(1)])
    ops[first].update(once=cfg["R1"])
    ident = A("Sh", 0, 128)
    ts(ident, D128, 0.0, None, ALU.is_equal)
    srep, sprev = A("Sr", 0, 128, 1, 0, 8), A("Sr", 192, 320, 1, 0, 8)
    ts(A("Sr", 0, 192, 1, 0, 12), A("Gi", 0, 192, 1, 0, 12), 0.0, None, ALU.is_equal)
    ts(col(CW, 8), col(PF, 8), 7.0, -8.0, ALU.is_ge, ALU.mult)
    ts(sprev, A("Gi", 0, 128, 1, 0, 8), col(CW, 8), 1.0, ALU.subtract, ALU.is_equal)
    tt(A("mn", 0, 128), A("Pm", 0, 128), D128, ALU.min)
    if cfg["f32"]:
        cp(A("col", 8, 10), A("kl", 0, 2))
        ts(A("KF", 0, 128), A("mn", 0, 128), 0.0, col(8), ALU.is_ge, ALU.mult)
        act(A("KF", 128, 256), ident, ACT.Identity, None, col(9))
        act(A("xf", 0, cfg["f32"]), A("snd", 0, cfg["f32"]), ACT.Copy)
    ts(A("kli", 0, 2), A("kl", 0, 2), 0xFF00, None, ALU.bitwise_and)
    ts(A("kli", 2, 4), A("kl", 0, 2), 0xFF, None, ALU.bitwise_and)
    cp(A("klf", 0, 4), A("kli", 0, 4))
    for j in (0, 2):
        split = ts(A("KL", 128 * j, 128 * j + 128), A("mn", 0, 128), 0.0, A("klf", j, j + 1), ALU.is_ge, ALU.mult)
    l_score = dma("sync", loads["s"][0], loads["s"][1], (split,) if cfg["gate"] else (), (l_x,))
    l_w = dma("sync", loads["w"][0], loads["w"][1], (), (l_score,))
    for j in (1, 3):
        act(A("KL", 128 * j, 128 * j + 128), ident, ACT.Identity, None, A("klf", j, j + 1), "v")
    act(A("Sm", 128, 144), A("Sm", 0, 16), ACT.Copy)
    table = act(A("Cz", 0, 128), A("Iy", 0, 128), ACT.Sigmoid, -128.0, 256.0)
    ops[table]["dur"] += 1300.0
    for (pz, c) in (("pz0", 0), ("pz1", 0), ("pz1", 128)):
        mm(A(pz, c, c + 128), [(A("zr", 0, 128), D128)])
    act(A("cm", 3, 4), A("Sh", 17, 18), ACT.Identity, None, -3584.0 / ZC)
    act(A("cm", 0, 1), A("Sh", 16, 17), ACT.Identity, A("cm", 3, 4), -97.0 / ZC)
    act(A("cm", 1, 2), A("Sh", 17, 18), ACT.Identity, None, -8.0 / ZC)
    act(A("cm", 2, 3), A("Sh", 16, 17), ACT.Identity, None, (1856.0 - U) / ZC)
    act(A("cm", 5, 6), A("Sh", 16, 17), ACT.Identity, None, -1.0 * U / ZC)
    act(A("cm", 4, 5), A("Sh", 18, 19), ACT.Identity, None, 0.5 / ZC)
    mset(A("top", 0, 128), TOP)
    ma, mf = A("My", 0, 64), A("My", 64, 128)
    act(ma, A("kk", 0, 64), ACT.Identity, None, A("cm", 0, 1))
    keep(A("MA", 0, 64), ma, [[-1, 16], [-32, 4]], ALU.not_equal, 37.0, 0, 1)
    act(A("MA", 64, 128), A("MA", 0, 64), ACT.Identity, A("cm", 4, 5), -1.0)
    act(mf, A("Iy", 0, 64), ACT.Identity, A("cm", 5, 6), A("cm", 1, 2))
    keep(mf, mf, [[-32, 4], [-1, 16]], ALU.not_equal, -256.0, 0, 1)
    keep(mf, mf, [[-32, 4], [0, 16]], ALU.not_equal, 256.0, 0, 1)
    keep(A("MF", 0, 64), mf, [[-32, 4], [1000, 16]], ALU.not_equal, 0.0, 0, 1)
    act(A("MF", 64, 128), A("MF", 0, 64), ACT.Identity, A("cm", 2, 3), -1.0)
    diagonal(A("nI", 0, 128), -1.0, 0, 0)
    iota(A("Oh", 192, 384), [[1, 24], [0, 8]], -8, 0)
    iota(A("ptr", 0, 192), [[1, 192]], -192, 0)
    iota(A("pval", 0, 256), [[1, 256]], 0, 0)
    if not cfg["log"]:
        iota(A("pval", 256, 320), [[16, 64]], 0, 0)
        iota(A("pts", 0, 192), [[0, 192]], 1024, 0, ("memset", A("pts", 0, 192), 1024.0))
        iota(A("pd", 1024, 1040), [[0, 16]], 0, 0, ("memset", A("pd", 1024, 1040), 0.0))
    act(A("B1", 0, 128), same, ACT.Copy)
    act(A("B1", 128, 256), same, ACT.Identity, None, 8192.0)
    ts(A("dm", 0, 128), A("Iy", 0, 128), col(LANE), None, ALU.is_equal)
    ts(A("Oh", 0, 192), A("Oh", 192, 384), col(LANE), None, ALU.is_equal)
    act(col(L2), col(LANE), ACT.Identity, 2048.0, None)
    posI, posS = A("F32", 0, 128), A("F32", 128, 256)
    act(A("I1", 0, 128), ident, ACT.Copy)
    iota(A("Ix", 0, 128), [[-64, 2], [0, 16], [-16, 4]], 0, 1)
    ts(A("Bq", 0, 128), A("Ix", 0, 128), col(LANE), 16.0, ALU.is_equal, ALU.mult)
    keep(A("B8", 0, 128, 1, 0, 8), A("zr", 0, 128, 1, 0, 8), [[-4, 2], [0, 16], [-1, 4]], ALU.not_equal, 16.0, 0, 1)
    act(A("Dq", 0, 4, 1, 64, 128), A("Bq", 64, 68, 1, 64, 128), ACT.Identity, None, 1.0 / 16)
    acts([(A("Dq", 4 + 64 * j, 68 + 64 * j, 1, 64, 128), A("Bq", 64, 128, 1, 64, 128), ACT.Identity, None, -512.0) for j in range(4)])
    ts(A("Dq", 0, 128, 1, 0, 64), A("zr", 0, 128, 1, 0, 64), 0.0, None, ALU.add)
    ts(A("Dq", 128, 260, 1, 0, 64), A("zr", 0, 132, 1, 0, 64), 0.0, None, ALU.add)
    iota(A("Ix", 128, 384, 1, 0, 16), [[0, 64], [16, 4]], 0, 1)
    keep(A("Dq", 4, 260, 1, 0, 16), A("Ix", 128, 384, 1, 0, 16), [[-1, 64], [16, 4]], ALU.is_gt, 4096.0, 0, 1)
    ts(A("Dq", 0, 4, 1, 0, 16), A("zr", 0, 4, 1, 0, 16), 1.0 * U, None, ALU.add)
    acts([(A("sv", 128 * k, 128 * k + 128, 1, 0, 64), A("dm", 0, 128, 1, 0, 64), ACT.Copy, None, None) for k in (0, 1)])
    diagonal(posI, 1.0, 0, 0)
    diagonal(A("F32", 128, 144), 1.0 / 32, 0, -112)
    diagonal(A("F32", 144, 256), 1.0 / 32, 16, 16)
    halfI = A("F32", 256, 384)
    diagonal(halfI, 0.5, 0, 0)
    shift(3)
    shift(4)
    lane0 = A("E0", 0, 128)
    keep(lane0, ident, [[0, 8], [1, 16]], ALU.is_equal, 0.0, 0, 0, tsc(lane0, ident, A("vc", 0, 1), None, ALU.mult))
    keep(A("E0", 128, 256), A("Sm", 16, 144), [[0, 8], [1, 16]], ALU.is_equal, 0.0, 0, 0)

    def at_home():
        ph[0] += 1
        for j in (0, 1):
            mm(A("pa", 128 * j, 128 * j + 128), [(A("E0", 128, 256), A("KL", 128 + 256 * j, 256 + 256 * j))])
        act(A("Lr", 0, 256), A("pa", 0, 256), ACT.Copy)
        ph[0] += 1
        symbols(3, "pl2")
        ops[rem([moved(2), moved(3)])]["ord"].add(first)
        ph[0] += 1
        for n in range(0, 12, 4):
            pl = "pl%d" % (1 + n // 4 % 2)
            group([(A(pl, 64 * j, 64 * j + 64), srep, comc(t, 64 * gr, 64)) for j, (gr, t) in enumerate(HOT[n:n + 4])])
            ts(A("oh", 64 * n, 64 * n + 256), A(pl, 0, 256), col(LANE), -1.0, ALU.not_equal, ALU.mult)
        ops[rem([([A("oh", 64 * FROM[h], 64 * (FROM[h] + HW))], A("ol", 64 * HW * (h - 1), 64 * HW * h), HOP * h) for h in (1, 2, 3)])]["ord"].add(first)

    def hot(gr, t):
        h, n = PLACE[gr][t], HOT.index((gr, t))
        c = 64 * (HW * (h - 1) + n - FROM[h]) if h else 64 * n
        return A("ol" if h else "oh", c, c + 64)
    for j in range(0, cfg["widen"], 512):
        plain(A("Wt", j, j + 512), A("W0", j, j + 512))
    if cfg["widen"] < 2048:
        i = add("g", [("dma_start", A("Wt", cfg["widen"], 2048), A("W0", cfg["widen"], 2048))], cfg["GD"] + cfg["GD1"], "dma", (), 512 * (2048 - cfg["widen"]))
        ops[i]["rows"] = 8
        adds.append(i)

    def phase_a(t):
        ph[0] += 1
        rot, s0, x0 = U * (t % 3), 192 * t, 384 * t - 384
        pieces = [(0, rot, S - rot)] + ([(S - rot, 0, rot)] if rot else [])

        def columns(cs, a, b):
            act(A("ci", a, b), cs, ACT.Copy, None, None, "s" if t else "v")
            ts(A("cj", s0 + a, s0 + b), A("ci", a, b), 5, 2047, ALU.logical_shift_right, ALU.bitwise_and)
            if t in cfg["g_c"]:
                plain(A("coff", s0 + a, s0 + b), A("cj", s0 + a, s0 + b))
            else:
                act(A("coff", s0 + a, s0 + b), A("cj", s0 + a, s0 + b), ACT.Copy, None, None, "s" if t else "v")

        if t:
            dma("sync", [(A("bz", 128 * t + 16 * g, 128 * t + 16 * g + 16, 1, 0, 12), A("Xl", x0, x0 + 192, 1, 16 * g, 16 * g + 1)) for g in range(8)], 4096, (), (l_w,))
            group([(A("pa", p, p + n), A(name, c, c + 128), A("Xl", x0 + d + u, x0 + d + u + n))
                   for (name, c, d) in (("KL", 0, 0), ("KL", 256, 0), ("Lr", 0, 192), ("Lr", 128, 192)) for (p, u, n) in pieces])
            columns(A("pa", 0, 192), 0, 192)
        else:
            mm(A("pl0", 0, 192), [(sprev, comc(0, 0, 192))])
            f = cfg["f32"]
            acts(([(A("xf", 192, 192 + f), A("pl0", 0, f), ACT.Copy, None, None)] if f else []) + ([(A("xs", f, 192), A("pl0", f, 192), ACT.Copy, None, None)] if f < S else []))
            for (name, a, b) in (("pa", 0, 64), ("pl1", 64, 192)):
                cs = A(name, 192 + a, 192 + b)
                if b <= f:
                    mm(cs, [(A("KF", 128 * j, 128 * j + 128), A("xf", 192 * j + a, 192 * j + b)) for j in range(2)])
                else:
                    mm(cs, [(A("KL", 128 * j, 128 * j + 128), A("xs" if j % 2 else "snd", a, b)) for j in range(4)])
                columns(cs, a, b)
        ts(A("gz", 128 * t, 128 * t + 128, 1, 0, 12), A("bz", 128 * t, 128 * t + 128, 1, 0, 12), 8.0, -8.0, ALU.is_ge, ALU.mult)

    def phase_h(t, a, b, pz):
        ph[0] += 1
        par, n, s0 = t % 2, b - a, 192 * t
        h0, m0 = 3072 * par, 0
        if a == 0 and t:
            dma("sync", [(A("xm", m0 + 192 * g, m0 + 192 * g + 192, 1, 16 * g, 16 * g + 16), A("Xl", 384 * t - 384, 384 * t - 192, 1, 16 * g, 16 * g + 16))
                         for g in range(8)], 49152)
        cut = [c for c in cfg["hcut"][t] if a <= c <= b]
        for c, d in zip(cut, cut[1:]):
            gather(A("hp", h0 + 16 * c, h0 + 16 * d), A("Hs", U, U + CH), A("coff", s0 + c, s0 + d), None, "v" if t == 0 and c % 64 else "s")
        for u0 in range(a, b, 16):
            q, c = u0 // 16 % 4, 2 * ((u0 - a) // 64 * 64)
            mrun([("matmul", A(pz, c + r, c + 128, 16, 32 * q, 32 * q + 16), A("hp", h0 + 16 * (u0 + r), h0 + 16 * (u0 + r) + 16),
                   A("xm", m0 + (u0 + U * t) % S + r, m0 + 1536, 192), True, True) for r in range(16)])
        act(A("zc", 2 * a, 2 * b), A(pz, 0, 2 * n), ACT.Identity, -ZC, None)

    def turned(bank, c0, a, b, const, m=0):
        return [(A(bank, c0 + u - a, c0 + u - a + 64), A("zc", 2 * u, 2 * u + 128), A(const, m, m + 64)) for u in range(a, b, 64)]

    def rounded(out):
        return [(out, ident, A("top", 0, out["n"])), (out, A("nI", 0, 128), A("top", 0, out["n"]))]

    def elist(t, a, b):
        return A("doff", 16 * t + 4 + a // 16, 16 * t + 4 + b // 16)

    def phase_e(t, a, b):
        ph[0] += 1
        n, py, e0 = b - a, "pq" if a else "py", 192 * t
        new = [(A(py, n + u - a, n + u - a + 64), A(x, 128 * t, 128 * t + 128, 1, 0, 12), A("Sr", (u + U * t) % S, (u + U * t) % S + 64, 1, 0, 12))
               for u in range(a, b, 64) for x in ("bz", "gz")]
        group(turned(py, n, a, b, "MF", 64) + rounded(A(py, n, 2 * n)) + turned(py, n, a, b, "MF") + new)
        scan(A("se", e0 + a, e0 + b), A("Cz", 0, n), A(py, n, 2 * n), ALU.mult, ALU.max)
        if (t, a) in cfg["g_e"]:
            plain(elist(t, a, b), A("se", e0 + a + 15, e0 + b, 16))
        elif t or a == 0:
            act(elist(t, a, b), A("se", e0 + a + 15, e0 + b, 16), ACT.Copy, None, None, "v")

    def phase_s(t, a, b, pz):
        ph[0] += 1
        n = b - a
        group(turned(pz, 3 * n, a, b, "MA", 64) + rounded(A(pz, 3 * n, 4 * n)) + turned(pz, 3 * n, a, b, "MA"))
        act(A("aoff", 192 * t + a, 192 * t + b), A(pz, 3 * n, 4 * n), ACT.Identity, 2048.0, None, "v")

    def phase_w(t, a, b):
        ph[0] += 1
        n, py, nk = b - a, "pq" if a else "py", 16 if (t, a) in cfg["wide"] else 8
        at = 384 if a else 256
        if t or not a:
            tt(A("tv", a, b), IND(A("ptr", 0, 192), elist(t, a, b)), A("dm", 0, n), ALU.mult)
            p0, p1, pick, start = 128 - n, 128, "Bq", 2048.0
            mm(A(py, at, at + 128, 1, p0, p1), [(A("tv", a, b), A("I1", 0, 128))])
        else:
            p0, p1, pick, start = 0, 8, "B8", -16.0 * U
            mm(A(py, at, at + 128, 1, p0, p1), [(A("se", a + 15, b, 16), ident)])
        sv = A("sv", 128 + 2 * a, 256 + 2 * a, 1, p0, p1)
        act(sv, A(py, at, at + 128, 1, p0, p1), ACT.Copy)
        items = []
        for u in range(0, n, 64):
            c = 2 * n + u // 16 * nk
            items += [(A(py, c, c + 4 * nk), ident, A("kk", 0, 4 * nk)), (A(py, c, c + 4 * nk), sv, A(pick, p0 + u, p0 + u + 4 * nk, 1, p0, p1))]
        group(items)
        act(A("woff", 192 * t + a, 192 * t + a + n // 16 * nk), A(py, 2 * n, 2 * n + n // 16 * nk), ACT.Identity, start, None, "v")

    def repeats(t, k, lanes, target):
        group([(A("py", 252, 256), target[0], target[1]), (A("py", 256, 512), A("sv", 128 * k, 128 * k + 128), A("Dq", 4, 260))]
              + [(A("py", 256 + q, 512, 4), A("B1", 128, 256), lanes) for q in range(4)])
        if not k:
            act(A("doff", 16 * t, 16 * t + 4), A("py", 252, 256), ACT.Identity, -1.0 * U, None, "v")
        cs = [("tensor_reduce", A("so", 4 * k + q, 4 * k + q + 1), A("py", 252 + q, 320 + 64 * q, 4), ALU.min, True) for q in range(4)]
        add("v", cs, sum(vcost(x[2], [x[2]]) for x in cs))
        if (t, k) in cfg["g_l"]:
            plain(A("soff", 4 * k, 4 * k + 4), A("so", 4 * k, 4 * k + 4))
        else:
            act(A("soff", 4 * k, 4 * k + 4), A("so", 4 * k, 4 * k + 4), ACT.Copy, None, None, "v")

    def phase_c(t):
        ph[0] += 1
        s0 = 192 * t
        tt(A("src", 0, 64), IND(A("Oh", 0, 192), elist(t, 0, U)), A("cj", s0, s0 + 64), ALU.mult)
        mm(A("py", 256, 384, 1, 64, 128), [(A("src", 0, 64), A("B1", 0, 128))])
        tt(A("sv", 0, 128, 1, 64, 128), A("py", 256, 384, 1, 64, 128), A("dm", 0, 128, 1, 64, 128), ALU.mult)
        repeats(t, 0, A("src", 0, 64), (A("sv", 0, 128), A("Dq", 0, 4)))
        gather(A("hold", 0, 64), A("Hs", U, U + CH), A("doff", 16 * t, 16 * t + 4))
        new = (lane0, A("Xl", 384 * t - 192 + U * t, 384 * t - 128 + U * t)) if t else (lane_in(0), comc(0, 0, U))
        mm(A("py", 0, 64), [new, (A("Sh", 128, 256), A("hold", 0, 64))])
        act(A("hnew", 0, 64), A("py", 0, 64), ACT.Copy)

    def phase_m(t):
        ph[0] += 1
        if t < STEPS - 1 or cfg["log"]:
            mm(A("py", 0, 64), [(A("B1", 0, 128), A("tv", 0, 64))])
            act(A("wold", 64 * t, 64 * t + 64), A("py", 0, 64), ACT.Identity, col(L2), 16.0)
        repeats(t, 1, A("tv", 0, 64), (ident, A("se", 192 * t + 15, 192 * t + 64, 16)))

    def phase_u(t):
        ph[0] += 1
        if t < STEPS - 1:
            cp(IND(A("Hs", 0, U + CH), A("soff", 0, 4)), A("hnew", 0, 64))
        if t < STEPS - 1 or cfg["log"]:
            cp(IND(A("ptr", 0, 192), A("soff", 4, 8)), A("pval", 64 * t, 64 * t + 64))
        else:
            cp(IND(A("pts", 0, 192), A("soff", 4, 8)), A("pval", 256, 320))

    def phase_r(t):
        s0, g0, f0 = 192 * t, 3072 * t, 3072 * (t % cfg["npw"])
        win = A("Wt", 0, 2048 + 1024 * t) if t else A("W0", 0, 2048)
        last = t == STEPS - 1
        if last:
            act(A("foff", 0, 128), A("ptr", U, 192), ACT.Identity, col(L2), 16.0)
        if last and not cfg["log"]:
            act(A("foff", 128, 256), A("pts", U, 192), ACT.Identity, col(LANE), None)
            for a, b in zip(cfg["bcut"], cfg["bcut"][1:]):
                gather(A("wb", 16 * a, 16 * b), win, A("foff", a, b))

        prods = []

        def update():
            ph[0] += 1
            for k0 in range(0, 16, 4):
                cs = [("tensor_tensor", A("pd", k, 1024, 16), A("pg", g0 + 64 * k, g0 + 64 * k + 64), A("pl0", 64, 128), ALU.mult) for k in range(k0, k0 + 4)]
                i = add("v", cs, sum(vcost(x[1], [x[2], x[3]], True) for x in cs))
            if not last or cfg["log"]:
                i = tt(A("Wt", 2048 + 1024 * t, 3072 + 1024 * t), IND(win, A("wold", 64 * t, 64 * t + 64)), A("pd", 0, 1024), ALU.add)
                if t in cfg["after"]:
                    ops[i]["ord"].add(prods[-1])
        for n in cfg["blocks"][t] + (3,):
            if n == 3:
                update()
                break
            ph[0] += 1
            c, b0, gr = 64 * n, g0 + 1024 * n, (t + n) % 3
            cut = cfg["pcut"][t][n]
            for k, l in zip(cut, cut[1:]):
                gather(A("pg", b0 + 64 * k, b0 + 64 * l), A("Ps", 0, CP), A("aoff", s0 + c + 4 * k, s0 + c + 4 * l), 1.0 / 32)
            cut, f = cfg["wcut"][t][n], f0 + 1024 * n
            for k, l in zip(cut, cut[1:]):
                wide = (t, min(c, U)) in cfg["wide"]
                h = 0 if wide else 8 * (k // 8)
                w0 = s0 + (c if wide or n < 2 else 96) - 4 * h
                i = tt(A("pw", f + 64 * k, f + 64 * l), IND(A(win["b"], h, win["c1"]), A("woff", w0 + 4 * k, w0 + 4 * l)), A("pg", b0 + 64 * k, b0 + 64 * l), ALU.mult)
                if t in cfg["chain"] and prods:
                    ops[i]["ord"].add(prods[-1])
                prods.append(i)
            parts = [A("pw", f + 64 * k, f + 64 * k + 64) for k in range(16)]
            if PLACE[gr][t] != t:
                parts = []
                for (k, l, m) in cfg["parts"][t][n]:
                    c0 = spare[0]
                    spare[0] += 64 * m
                    rem([([A("pw", f + 64 * j, f + 64 * (j + m)) for j in range(k, l, m)], A("sp", c0, c0 + 64 * m), HOP * (PLACE[gr][t] - t))])
                    parts += [A("sp", c0 + 64 * j, c0 + 64 * j + 64) for j in range(m)]
            for j in range(cfg["fold"].get((t, n), 0)):
                parts = parts[:len(parts) // 2]
                dma_add(A("pw", f, f + 64 * len(parts)), A("pw", f + 64 * len(parts), f + 128 * len(parts)))
            m = cfg["pre"].get((t, n), 0)
            if m:
                low = A("pw", f + 1024 - 128 * m, f + 1024 - 64 * m)
                tt(low, low, A("pw", f + 1024 - 64 * m, f + 1024), ALU.add)
                parts = parts[:16 - m]
            outcome(gr, t, parts, "pl%d" % n)

    spare, held = [0], []

    def tile(name, gr, t):
        return A(name, 192 * t + 64 * gr, 192 * t + 64 * gr + 64)

    def moves(gr, t):
        return PLACE[gr][t] != (PLACE[gr] + [0])[t + 1]

    def known(gr, t, pl):
        mm(A(pl, 128, 192), [(posI, hot(gr, t))] + ([(halfI, tile("Bi", gr, t - 1))] if t else []))

    def outcome(gr, t, parts, pl):
        ph[0] += 1
        lg, ys = A(pl, 0, 64), tile("ys", gr, t)
        if t and not moves(gr, t):
            known(gr, t, pl)
        group([(lg, posI, x) for x in parts] + ([(lg, posS, tile("Bi", gr, t - 1))] if t else []))
        act(ys, lg, ACT.Sigmoid, None, -32.0)
        if gr == t % 3:
            mm(A(pl, 64, 128), [(posI, hot(gr, t)), (posI, ys)])
        if moves(gr, t):
            if t:
                act(tile("Bo", gr, t), tile("Bi", gr, t - 1), ACT.Identity, None, 0.5)
            sides = [tile("Bi", gr, t)] + [tile("Bo", gr, t)] * (t > 0) + [hot(gr, t), ys]
            d = gr - cfg["pair"].get(t, 9)
            if d in (0, 1):
                held.append(gr)
                if len(held) % 2:
                    return
                sides = [A(x["b"], x["c0"] - 64 * d, x["c0"] - 64 * d + 128) for x in sides]
            rem([(sides[1:], sides[0], HOP * ((PLACE[gr] + [0])[t + 1] - PLACE[gr][t]))])
        else:
            sides = [tile("Bi", gr, t)]
            tt(sides[0], ys, A(pl, 128, 192) if t else hot(gr, t), ALU.add)
        if t + 1 == STEPS:
            dma(cfg["ybq"], [(EXT("yb", sides[0]["c0"] - 192 * t, sides[0]["c1"] - 192 * t), sides[0])], 512 * sides[0]["n"])

    phase_a(0)
    at_home()
    for t in range(STEPS):
        ch = (((0, U), "pz0"), ((U, S), "pz1"))

        def ahead(place):
            for s in range(1, STEPS):
                if cfg["a_at"][s] == (t, place):
                    phase_a(s)
        ahead(0)
        for ((a, b), pz) in ch:
            phase_h(t, a, b, pz)
            phase_e(t, a, b)
            phase_s(t, a, b, pz)
            if a == 0 and t < STEPS - 1:
                phase_c(t)
            phase_w(t, a, b)
        ahead(1)
        phase_m(t)
        ahead(2)
        phase_u(t)
        phase_r(t)
    ph[0] += 1
    for a, b in zip(cfg["fin"], cfg["fin"][1:]):
        if cfg["log"]:
            gather(A("wo", 16 * a, 16 * b), A("Wt", 0, 2048 + 1024 * STEPS), A("foff", a, b))
        elif a in cfg["late"]:
            old = dma("sync", [(EXT("yw", 16 * a, 16 * b), A("wb", 16 * a, 16 * b))], 8192 * (b - a))
            gather(A("wo", 16 * a, 16 * b), A("pd", 0, 1040), A("foff", 128 + a, 128 + b))
            ops[dma_add(EXT("yw", 16 * a, 16 * b), A("wo", 16 * a, 16 * b))]["sem"].add(old)
            continue
        else:
            tt(A("wo", 16 * a, 16 * b), IND(A("pd", 0, 1040), A("foff", 128 + a, 128 + b)), A("wb", 16 * a, 16 * b), ALU.add)
        dma("sync", [(EXT("yw", 16 * a, 16 * b), A("wo", 16 * a, 16 * b))], 8192 * (b - a))
    return ops


def landing(o, issued, pipe, cfg):
    first, own = issued + (cfg["RF"] if o["kind"] == "rem" else cfg["DF"]) - 500.0, o["bytes"] / cfg["BW"] + o["rows"] * cfg["RC"]
    first += o.get("once", 0.0)
    after = max(pipe, first) + own
    return (min(after, first + 2 * own) if o.get("raw", o["bytes"]) < cfg["SH"] else after) + 500.0, max(pipe, issued + cfg["DF"] - 500.0) + own


def replay(ops, order, cfg):
    free, done, pipe, end, wk = {}, {}, 0.0, 0.0, cfg["WK"]
    for i in order:
        o = ops[i]
        t = free.get(o["eng"], 0.0)
        for j in o["sem"]:
            if done[j] + wk > t:
                t = done[j] + wk
        d = free[o["eng"]] = t + o["dur"]
        if o["kind"] != "c":
            d, pipe = landing(o, d, pipe, cfg)
        done[i] = o["t1"] = d
        o["t0"] = t
        end = max(end, d)
    return end


def assign(opss, i, eng):
    for ops in opss:
        ops[i].update(eng=eng, calls=ops[i]["both"][eng][0], dur=ops[i]["both"][eng][1])


def direct(ops):
    above, sems, soft = [0] * len(ops), [], []
    for i, o in enumerate(ops):
        for j in o["sem"] | o["ord"]:
            above[i] |= above[j]
        near = {j for j in o["bank"] & o["sem"] if "pe" not in (ops[j]["eng"], o["eng"])}
        sems.append([j for j in sorted(o["sem"] - near) if not above[i] >> j & 1])
        soft.append([j for j in sorted(near) if not above[i] >> j & 1])
        for j in o["sem"] - near:
            above[i] |= 1 << j
    return sems, soft


def shuttle(opss, cfgs, order, rounds, seed=0):
    n = len(opss[0])
    rnd = np.random.RandomState(seed)
    keys = sorted({o["key"] for o in opss[0]})
    pred = [[(j, j in o["sem"]) for j in sorted(o["sem"] | o["ord"])] for o in opss[0]]
    succ = [[] for i in range(n)]
    for i in range(n):
        for (j, w) in pred[i]:
            succ[j].append((i, w))

    def fit(line, t, dur):
        p = len(line)
        while p and line[p - 1][1] > t:
            p -= 1
        while p < len(line) and line[p][0] < t + dur:
            if line[p][1] > t:
                t = line[p][1]
            p += 1
        return t, p

    def pack(ops, prio, walk, before, first, out, into, choose):
        for i in walk:
            for (j, w) in before[i]:
                if prio[i] <= prio[j]:
                    prio[i] = prio[j] + 0.001
        busy = {e: [] for e in QUEUES}
        end = [0.0] * n
        for i in sorted(walk, key=lambda i: prio[i]):
            t, o = first[i], ops[i]
            for (j, w) in before[i]:
                x = end[j] + out[j] + into[i] if w else end[j]
                if x > t:
                    t = x
            if choose and "both" in o:
                e = min(sorted(o["both"]), key=lambda e: fit(busy[e], t, o["both"][e][1])[0] + o["both"][e][1] + (choose if e != o["eng"] else 0.0))
                if e != o["eng"]:
                    assign(opss, i, e)
            t, p = fit(busy[o["eng"]], t, o["dur"])
            end[i] = t + o["dur"]
            busy[o["eng"]].insert(p, (t, end[i]))
        return end

    sems, soft = direct(opss[0])
    part = [0.0] * len(cfgs)

    def value(od, bar=None):
        got = []
        for ops, c in zip(opss, cfgs):
            free, ready, pipe, wk = {e: 0.0 for e in QUEUES}, [0.0] * n, 0.0, c["WK"]
            for i in od:
                o = ops[i]
                t = free[o["eng"]]
                for j in sems[i]:
                    if ready[j] > t:
                        t = ready[j]
                for j in soft[i]:
                    if ready[j] > t and ops[j]["eng"] != o["eng"]:
                        t = ready[j]
                free[o["eng"]] = t = t + o["dur"]
                if o["kind"] != "c":
                    t, pipe = landing(o, t, pipe, c)
                ready[i] = t + wk
            got.append(math.log(max(ready) - wk))
            if bar is not None and sum(got) - sum(part[:len(got)]) > len(cfgs) * bar + 0.02:
                return 1e9, got
        return sum(got) / len(cfgs), got
    zero = [0.0] * n
    if order is None:
        replay(opss[0], range(n), cfgs[0])
        wait = [cfgs[0]["WK"] + min(o["t1"] - o["t0"] - o["dur"], cfgs[0]["DF"] + o["bytes"] / cfgs[0]["BW"]) for o in opss[0]]
        way = [0.0] * n
        for i in range(n - 1, -1, -1):
            way[i] = opss[0][i]["dur"] + max([wait[i]] + [way[j] + (wait[i] if w else 0.0) for (j, w) in succ[i]])
        fore = pack(opss[0], [-x for x in way], range(n), pred, zero, wait, zero, 0.0)
        order = sorted(range(n), key=lambda i: (fore[i] - opss[0][i]["dur"], i))
    cur, part[:] = value(order)
    best = cur
    keep = (order, [o["eng"] for o in opss[0]])
    either = [o["i"] for o in opss[0] if "both" in o]
    for r in range(rounds):
        v = cfgs[0]["packs"][int(rnd.randint(len(cfgs[0]["packs"])))] % len(cfgs)
        ops, wk = opss[v], cfgs[v]["WK"] + cfgs[0]["slack"]
        was = [ops[i]["eng"] for i in either]
        replay(ops, order, cfgs[v])
        lat = [o["t1"] - o["t0"] - o["dur"] for o in ops]
        push = {keys[int(rnd.randint(len(keys)))]: float(rnd.normal()) * 1500.0 for s in range(1 + int(rnd.randint(6)))}
        whole = {int(rnd.randint(ops[-1]["key"][1] + 1)): float(rnd.normal()) * cfgs[0]["far"] for s in range(int(rnd.randint(4)))}
        ends = [-(o["t1"] + push.get(o["key"], 0.0) + whole.get(o["key"][1], 0.0)) for o in ops]
        for i in rnd.choice(either, int(rnd.randint(3)), False):
            assign(opss, int(i), [e for e in ops[i]["both"] if e != ops[i]["eng"]][0])
        pick, wait = rnd.rand(), [x + wk for x in lat]
        back = pack(ops, ends, range(n - 1, -1, -1), succ, lat, zero, wait, 600.0 * rnd.rand() + 300.0 if pick < cfgs[0]["pick"] else 0.0)
        whole = {int(rnd.randint(ops[-1]["key"][1] + 1)): float(rnd.normal()) * cfgs[0]["far"] for s in range(int(rnd.randint(2)))}
        fore = pack(ops, [whole.get(o["key"][1], 0.0) - x for o, x in zip(ops, back)], range(n), pred, zero, wait, zero, 600.0 * rnd.rand() + 300.0 if pick > 1 - cfgs[0]["pick"] else 0.0)
        od = sorted(range(n), key=lambda i: (fore[i] - ops[i]["dur"], i))
        room = cfgs[0]["heat2"] * (1 - r / rounds) * rnd.exponential()
        x, got = value(od, room)
        if x <= cur + room:
            order, cur, part[:] = od, x, got
            if x < best:
                best, keep = x, (od, [o["eng"] for o in ops])
        else:
            for i, e in zip(either, was):
                if ops[i]["eng"] != e:
                    assign(opss, i, e)
    for i in either:
        assign(opss, i, keep[1][i])
    return keep[0], [replay(o, keep[0], c) for o, c in zip(opss, cfgs)]


def polish(opss, cfgs, order, rounds, seed=0):
    ops, nv = opss[0], len(cfgs)
    n = len(ops)
    pred = [sorted(o["sem"] | o["ord"]) for o in ops]
    succ = [[] for o in ops]
    sems, soft = direct(ops)
    for i in range(n):
        for j in pred[i]:
            succ[j].append(i)
    engs = sorted({o["eng"] for o in ops})
    eng = [engs.index(o["eng"]) for o in ops]
    durs = [[o["dur"] for o in x] for x in opss]
    moving = [o["kind"] != "c" for o in ops]
    rnd = np.random.RandomState(seed)
    mix, heat, aim = cfgs[0]["mix"] / n, cfgs[0]["heat"], cfgs[0]["aim"]

    def prior(od, p0):
        seen = {}
        for p in range(p0 - 1, -1, -1):
            i = od[p]
            if eng[i] not in seen:
                seen[eng[i]] = i
            if moving[i] and -1 not in seen:
                seen[-1] = i
            if len(seen) > len(engs):
                break
        return seen

    def run(rest, v, seen, span, marked, stirred, flow, bar):
        wk, dur, free, pipe = wks[v], durs[v], [0.0] * len(engs), 0.0
        fin, ready, load = state[v]
        for e, i in seen.items():
            if e < 0:
                pipe = load[i]
            else:
                free[e] = fin[i]
        way, mark, stir, log, more, left, tail = ways[v], bytearray(marked), stirred[:], [], 0.0, span, tails[v]
        for i in rest:
            e = eng[i]
            if mark[i]:
                left -= 1
            elif not (stir[e] or (flow and moving[i])):
                free[e] = fin[i]
                if moving[i]:
                    pipe = load[i]
                continue
            t = free[e]
            for j in waits[i]:
                if ready[j] > t:
                    t = ready[j]
            free[e] = t = t + dur[i]
            span -= 1
            old = fin[i]
            if t != old or moving[i]:
                if span < 0 and t + tail[i] > bar:
                    return log, None
                stir[e] = span >= 0 or t != old
                log.append((i, old, ready[i], load[i]))
                fin[i] = t
                if moving[i]:
                    first, own, small, lead = way[i]
                    first += t
                    x = (pipe if pipe > first else first) + own
                    pipe = (pipe if pipe > t + lead else t + lead) + own
                    flow = span >= 0 or pipe != load[i]
                    load[i] = pipe
                    t = (first + 2 * own if small and first + 2 * own < x else x) + 500.0
                t += wk
                if t != ready[i]:
                    more += (t - ready[i]) * weight[i]
                    ready[i] = t
                    for k in heed[i]:
                        if not mark[k]:
                            mark[k] = 1
                            left += 1
            elif span < 0:
                stir[e] = False
                if not (left or flow or True in stir):
                    break
        return log, more

    def anew(od):
        for v in range(nv):
            state[v] = ([-1.0] * n, [0.0] * n, [0.0] * n)
            total[v] = run(od, v, {}, n, b"\1" * n, [True] * len(engs), True, 0.0)[1]
            part[v] = worth(v, total[v])
            fin, ready, dur, tail, ahead = state[v][0], state[v][1], durs[v], tails[v], [0.0] * len(engs)
            for i in od[::-1]:
                t = 0.0
                for k in waiting[i]:
                    if dur[k] + tail[k] > t:
                        t = dur[k] + tail[k]
                t += ready[i] - fin[i]
                tail[i] = t = t if t > ahead[eng[i]] else ahead[eng[i]]
                ahead[eng[i]] = t + dur[i]
    ways = [{o["i"]: ((c["RF"] if o["kind"] == "rem" else c["DF"]) - 500.0 + o.get("once", 0.0), o["bytes"] / c["BW"] + o["rows"] * c["RC"], o.get("raw", o["bytes"]) < c["SH"],
                      c["DF"] - 500.0) for o in x if o["kind"] != "c"} for x, c in zip(opss, cfgs)]
    waits = [sems[i] + [j for j in soft[i] if eng[j] != eng[i]] for i in range(n)]
    beside = [[i] + [k for k in succ[i] if i in soft[k]] for i in range(n)]
    heed = [[k for k in succ[i] if i in sems[k] or i in soft[k]] for i in range(n)]
    wks, ends = [c["WK"] for c in cfgs], [i for i in range(n) if not succ[i] and moving[i]]
    weight = [cfgs[0]["heavy"] if o["key"][0] in ("ys", "Bi", "Bo", "sp", "pl0", "pl1", "pl2", "pd", "Wt") else 1.0 for o in ops]
    state, total, part, norm = [None] * nv, [0.0] * nv, [0.0] * nv, [1.0] * nv
    waiting, tails = [[k for k in succ[i] if i in sems[k]] for i in range(n)], [[0.0] * n for v in range(nv)]

    def worth(v, s):
        ready = state[v][1]
        return (max([ready[i] for i in ends]) + mix * s) / norm[v]
    anew(order)
    norm = [nv * max(s[1]) for s in state]
    anew(order)

    def better(od, p0, span, room, both):
        logs, val, seen, rest, worse = [], [], prior(od, p0), od[p0:], 0.0
        marked, stirred, flow = bytearray(n), [both and e in ("v", "s", "g") for e in engs], False
        for i in rest[:span]:
            marked[i] = stirred[eng[i]] = True
            flow = flow or moving[i]
        for v in range(nv):
            bar = room + ahead * (nv - 1 - v)
            logs.append(run(rest, v, seen, span, marked, stirred, flow, (part[v] + bar - worse + spare) * norm[v] - mix * total[v]))
            if logs[v][1] is not None:
                val.append(worth(v, total[v] + logs[v][1]))
                worse += val[v] - part[v]
            if logs[v][1] is None or worse > bar:
                for (fin, ready, load), (log, more) in zip(state, logs):
                    for (i, a, b, c) in log:
                        fin[i], ready[i], load[i] = a, b, c
                return False
        for v in range(nv):
            total[v] += logs[v][1]
        part[:] = val
        return True
    ahead, spare, every, leap = cfgs[0]["ahead"], cfgs[0]["spare"], cfgs[0]["every"], cfgs[0]["leap"]

    def tight(od, v):
        fin, ready = state[v][0], state[v][1]
        before, last = {}, {}
        for i in od:
            before[i] = last.get(eng[i])
            last[eng[i]] = i
        i, pairs = ready.index(max(ready)), []
        while fin[i] - durs[v][i] > 0.01:
            a = before[i]
            if a is not None and fin[a] >= fin[i] - durs[v][i] - 0.01:
                if a not in pred[i]:
                    pairs.append((a, i))
                i = a
            else:
                i = max(sems[i] + soft[i], key=lambda j: ready[j])
        return pairs

    def turn(i):
        assign(opss, i, [e for e in ops[i]["both"] if e != ops[i]["eng"]][0])
        eng[i] = engs.index(ops[i]["eng"])
        for k in beside[i]:
            waits[k] = sems[k] + [j for j in soft[k] if eng[j] != eng[k]]
        for x, d in zip(opss, durs):
            d[i] = x[i]["dur"]
    best, keep, held = sum(part), (order, list(eng)), [None] * nv
    for r in range(rounds):
        if r % every == 0:
            v = (r // every) % nv
            rank = {i: p for p, i in enumerate(order)}
            order = sorted(order, key=lambda i: (state[v][0][i] - durs[v][i], rank[i]))
            anew(order)
        if r % 40 == 0:
            held = [None] * nv
        x = rnd.rand(5)
        room = -heat * (1 - r / rounds) * np.log(1 - x[0])
        od = None
        if x[1] < aim:
            v = int(x[2] * nv)
            if held[v] is None:
                held[v] = tight(order, v)
            if not held[v]:
                continue
            a, b = held[v][int(x[3] * len(held[v]))]
            i = a if x[4] < 0.15 else b
            p0 = order.index(i)
            if "both" not in ops[i] or x[4] > 0.3:
                p0, pb = order.index(a), p0 if i == b else order.index(b)
                if p0 > pb or eng[a] != eng[b]:
                    continue
                move, need, queues = [b], set(pred[b]), set()
                for y in order[pb - 1:p0:-1]:
                    if y in need or eng[y] in queues:
                        move.append(y)
                        need.update(pred[y])
                        queues.add(eng[y])
                if a in need or eng[a] in queues:
                    continue
                od = order[:p0] + move[::-1] + [y for y in order[p0:pb] if y not in move] + order[pb + 1:]
                span = pb - p0 + 1
        else:
            p0 = int(x[2] * n)
            i = order[p0]
            if "both" not in ops[i] or x[4] > 0.15:
                step, hops, q, stop = (1 if x[3] < 0.5 else -1), int(rnd.geometric(0.4)), p0, False
                bar = set(succ[i] if step > 0 else pred[i])
                if step < 0 and x[4] > 1 - leap:
                    fin, ready = state[0][0], state[0][1]
                    t = max([ready[j] for j in waits[i]] + [0.0])
                    hops = sum(1 for y in order[max(0, p0 - 150):p0] if eng[y] == eng[i] and fin[y] - durs[0][y] >= t)
                    if not hops:
                        continue
                while hops and not stop:
                    q += step
                    stop = q < 0 or q >= n or order[q] in bar
                    if not stop and eng[order[q]] == eng[i]:
                        hops -= 1
                if stop:
                    continue
                od = order[:p0] + order[p0 + 1:]
                od.insert(q, i)
                p0, span = min(p0, q), abs(q - p0) + 1
        turned = []
        if od is None:
            turned = [i]
            if rnd.rand() < cfgs[0]["swap"]:
                near = [q for q in range(max(0, p0 - 40), min(n, p0 + 40)) if "both" in ops[order[q]] and eng[order[q]] != eng[i]]
                if near:
                    q = near[int(rnd.randint(len(near)))]
                    turned.append(order[q])
                    p0 = min(p0, q)
            span = max(order.index(k) for y in turned for k in beside[y]) - p0 + 1
        for y in turned:
            turn(y)
        if better(od or order, p0, span, room, od is None):
            order = od or order
            if sum(part) < best:
                best, keep = sum(part), (order, list(eng))
        else:
            for y in turned:
                turn(y)
    for i in range(n):
        if eng[i] != keep[1][i]:
            turn(i)
    anew(keep[0])
    return keep[0], [max(state[v][1]) - wks[v] for v in range(nv)]


def arrange(cfg):
    cfgs = [dict(cfg, **v) for v in VARIANTS]
    found = []
    for seed in range(cfg["seed"], cfg["seed"] + cfg["tries"]):
        opss = [build(c) for c in cfgs]
        order = shuttle(opss, cfgs, None, cfg["shuttle"], seed)[0]
        order, ends = polish(opss, cfgs, order, cfg["trim"], seed)
        found.append((float(np.sum(np.log(ends))), seed, opss, order))
    opss, order = min(found)[2:]
    for seed in range(cfg["passes"]):
        order, ends = polish(opss, cfgs, order, cfg["polish"], seed)
    for ops in opss:
        for o in ops:
            near = {j for j in o["bank"] if ops[j]["eng"] == o["eng"] != "pe"}
            for j in near:
                o["sem"] = (o["sem"] - {j}) | (ops[j]["bank"] & ops[j]["sem"])
            o["ord"] |= near
    ends = [replay(x, order, c) for x, c in zip(opss, cfgs)]
    return opss[0], order, ends


def plan(cfg):
    ops, order, ends = arrange(cfg)
    need = set()
    for o in ops:
        need |= o["sem"]
    count = {}
    know = {}
    for i in order:
        o = ops[i]
        k = know.setdefault(o["eng"], {})
        want = {}
        for j in sorted(o["sem"], key=lambda j: -ops[j]["t1"]):
            p = ops[j]
            name, val = p["sig"]
            if k.get(name, 0) >= val:
                continue
            want[name] = max(want.get(name, 0), val)
            if p["kind"] != "rem":
                for a, b in p["clock"].items():
                    k[a] = max(k.get(a, 0), b)
            k[name] = max(k.get(name, 0), val)
        o["waits"] = sorted(want.items())
        o["clock"] = dict(k)
        if o["kind"] == "c":
            o["inc"] = i in need
            name = "e_" + o["eng"]
            if o["inc"]:
                count[name] = count.get(name, 0) + (1 if o["eng"] == "pe" else len(o["calls"]))
            o["sig"] = (name, count.get(name, 0))
        else:
            o["sig"] = (o["tok"], 1)
    return ops, order


PLAN = []


def rank_program(g, core, T, topo):
    rank = T.rank_of(core)
    if rank is None:
        return
    if not PLAN:
        PLAN.append(plan(CFG))
    ops, order = PLAN[0]
    cores = list(T.cores)
    queue = {"pe": g.tensor, "v": g.vector, "s": g.scalar, "g": g, "sync": g.sync}

    def masks(src, hops):
        to = [cores[(cores.index(src) + h) % NR] for h in hops]
        free, out = [e for e in topo.engines(src, to[0]) if all(e in topo.engines(src, c) for c in to)], []
        total = len(free)
        for p in SHARE[len(hops)]:
            out.append(sum(1 << e for e in free[:total // p]))
            free = free[total // p:]
        return out

    def bits(m):
        return bin(m).count("1")
    full = {}
    for o in ops:
        if o["kind"] == "dma":
            full[o["tok"]] = 16 * len(o["calls"])
        elif o["kind"] == "rem":
            hops = [m[2] for m in o["calls"][0][1]]
            full[o["tok"]] = sum(bits(masks(cores[(rank - h) % NR], hops)[n]) for n, h in enumerate(hops))
    sent = 0
    outs = []
    for i in order:
        o = ops[i]
        q = queue[o["eng"]]
        for name, val in o["waits"]:
            q.wait_ge(T.sem[name], full.get(name, val))
        for c in o["calls"]:
            if c[0] == "remote":
                ms = masks(core, [m[2] for m in c[1]])
                to = [topo.addr(cores[(rank + m[2]) % NR]) for m in c[1]]
                if len(ms) == 1 and len(c[1][0][0]) == 1:
                    g.remote_dma(real(T, c[1][0][1]), real(T, c[1][0][0][0]), T.sem[o["tok"]], T.sem.loc, to[0][1], to[0][0], ms[0])
                else:
                    g.remote_dma_fused([RemoteDMATransfer(dst_ids=[DstId(rid=a[0], pnc=a[1])], dma_engine_mask=e, remote_sem=T.sem[o["tok"]],
                                                          srcs=[real(T, x) for x in m[0]], dsts=[real(T, m[1])], alu_op=1 if len(m[0]) > 1 else 0)
                                        for m, a, e in zip(c[1], to, ms)], local_sem=T.sem.loc)
                sent += sum(bits(e) for e in ms)
                continue
            x = [real(T, a) if isinstance(a, dict) else a for a in c[1:]]
            if c[0] == "dma_start":
                q.dma_start(x[0], x[1]).then_inc(T.sem[o["tok"]], 16)
                if "ext" in c[1]:
                    outs.append(o)
                continue
            if c[0] == "dma_add":
                q.dma_start(x[0], x[1], accum_op=ALU.add).then_inc(T.sem[o["tok"]], 16)
                if "ext" in c[1]:
                    outs.append(o)
                continue
            if c[0] == "activation":
                kw = {}
                if x[3] is not None:
                    kw["bias"] = x[3]
                if x[4] is not None:
                    kw["scale"] = x[4]
                ins = q.activation(x[0], x[1], x[2], **kw)
            elif c[0] == "iota":
                if SCRATCH[c[1]["b"]][2] == IN:
                    ins = q.iota(*x)
                else:
                    ins = q.iota(*x, allow_small_or_imprecise_dtypes=True)
            elif c[0] == "affine_select":
                ins = q.affine_select(*x)
            elif c[0] == "matmul":
                ins = q.matmul(*x)
            elif c[0] == "tensor_copy":
                ins = q.tensor_copy(*x)
            elif c[0] == "tensor_scalar":
                ins = q.tensor_scalar(*x)
            elif c[0] == "tensor_tensor":
                ins = q.tensor_tensor(*x)
            elif c[0] == "tensor_reduce":
                ins = q.tensor_reduce(x[0], x[1], AxisListType.X, x[2], apply_absolute_value=x[3])
            elif c[0] == "tensor_tensor_scan":
                ins = q.tensor_tensor_scan(*x)
            else:
                ins = q.memset(*x)
            if o["inc"] and (o["eng"] != "pe" or c is o["calls"][-1]):
                ins.then_inc(T.sem["e_" + o["eng"]], 1)
    g.wait_ge(T.sem.loc, sent)
    for o in outs:
        queue[o["eng"]].wait_ge(T.sem[o["tok"]], 16)
